import numpy as np, ml_dtypes
CORES = [23,119,17,113]
N = 4
BF = ml_dtypes.bfloat16
V, M, C, B, VIS, H, ST = 4096, 256, 2048, 16, 6, 9, 1
def pack(v, words, rel, om, th):
    return {"x": np.ascontiguousarray(v.reshape(N, 128, V)).astype(np.float32).astype(BF), "wd": np.ascontiguousarray(words.reshape(N, 128, M)).astype(np.int32),
            "rt": np.ascontiguousarray(rel.reshape(N, 128, C)).astype(np.int32), "wt": np.ascontiguousarray(om.reshape(N, 128, 1)).astype(np.int32), "th": np.ascontiguousarray(th.reshape(N, 128, 1)).astype(np.int32)}
def setup_inputs(rng):
    return pack(rng.integers(0, 256, (N, 8, 16, V)), rng.integers(0, V, (N, 8, 16, M)), rng.integers(0, V, (N, 8, 16, C)), rng.integers(0, 4096, (N, 8, 16)), rng.integers(1500, 1751, (N, 8, 16)))
def setup_inputs_spread(rng):
    v = np.floor(256 * rng.random((N, 8, 16, V)) * np.exp2(-8 * rng.random((N, 8, 1, V)))).astype(np.int64)
    om = np.floor(4096 * np.exp2(-12.5 * rng.random((N, 8, 16)))).astype(np.int64)
    lev = rng.choice(np.array([300, 700, 1200, 2500, 4080]), (N, 8, 1)); th = np.floor(lev * (0.6 + 0.4 * rng.random((N, 8, 16)))).astype(np.int64)
    pw = rng.choice(np.array([1.0, 1.5, 2.0, 3.0]), (N, 8, 1, 1))
    words = np.floor(V * rng.random((N, 8, 16, M)) ** pw).astype(np.int64); rel = np.floor(V * rng.random((N, 8, 16, C)) ** pw).astype(np.int64)
    return pack(np.minimum(v, 255), np.minimum(words, V - 1), np.minimum(rel, V - 1), np.minimum(om, 4095), np.minimum(th, 4080))
def setup_inputs_ends(rng):
    v = 255 * rng.integers(0, 2, (N, 8, 16, V)); full = rng.random((N, 8)) < 0.5; full[:, 6:] = True
    v[full, :, V - 16:] = 255; v[full, :, 0] = 0
    om = 4095 * rng.integers(0, 2, (N, 8, 16))
    for q in range(N):
        a = 7 - (N - 1 - q) % 2; om[q, 6:] = 4095; om[q, 13 - a, 15] = 272
    hit = [((u * u >> 5) + 37 * u) & (C - 1) for u in (0, 16, 4095)]
    words = (V - 1) * rng.integers(0, 2, (N, 8, 16, M)); mix = rng.random((N, 8, 1, M)) < 0.2; mix[..., 0] = False; mix[..., M - 1] = False
    words = np.where(mix, rng.integers(0, V, (N, 8, 16, M)), words); words[:, :, 0, M - 1] = V - 1; words[:, :, 0, 0] = 0
    rel = (V - 1) * rng.integers(0, 2, (N, 8, 16, C)); mix = rng.random((N, 8, 1, C)) < 0.2; mix[..., hit] = False
    rel = np.where(mix, rng.integers(0, V, (N, 8, 16, C)), rel)
    rel[:, 6:, :, 0] = V - 16 + np.arange(16)
    for c in hit[1:]:
        rel[:, 6:, :, c] = 0; rel[:, 6:, 6, c] = V - 1; rel[:, 6:, 15, c] = V - 1
    pre = rng.choice(np.array([0, 4, H - 1, H, 12, 16]), (N, 8)); pre[:, 0] = 0; pre[:, 6] = 12; pre[:, 7] = 16
    th = 4080 * (np.arange(16) < pre[:, :, None]).astype(np.int64)
    for q in range(N):
        if (N - 1 - q) % 2 == 1:
            th[q, 7, 15] = 4079; th[q, 6, H - 1] = 4079
        else:
            th[q, 6, 11] = 4079
    return pack(v, words, rel, om, th)
def setup_inputs_corners(rng):
    val = np.array([0, 8, 9, 247, 248, 249]); cls = rng.choice(6, (N, 8, V), p=[0.4, 0.1, 0.1, 0.1, 0.2, 0.1])
    cls[:, ::2, 0] = 0; cls[:, 1::2, 0] = 4; cls[:, ::2, V - 1] = 4; cls[:, 1::2, V - 1] = 0
    ft = rng.integers(0, 16, (N, 8, 1, V)); v = rng.integers(0, 7, (N, 8, 16, 1)) + np.where(np.arange(16).reshape(16, 1) == ft, val[cls][:, :, None, :], 0)
    cnt = np.array([31, 8 * M, 33, 0, 63, 32, 1, 64]); order = rng.permutation(N); kk = np.arange(16).reshape(16, 1)
    words = np.zeros((N, 8, 16, M), np.int64); rel = np.zeros((N, 8, 16, C), np.int64); om = np.zeros((N, 8, 16), np.int64)
    for q in range(N):
        hit = (rng.permutation(8 * M) < int(cnt[order[q]])).reshape(8, M)
        lw = np.where(hit, rng.choice(np.array([H, 12, 15, 16]), (8, M)), rng.choice(np.array([0, 1, H - 1]), (8, M)))
        for g in range(8):
            z = np.flatnonzero(cls[q, g] == 0); b = np.flatnonzero(cls[q, g] != 0)
            za = z[rng.integers(0, len(z), (16, M))]; bb = b[rng.integers(0, len(b), (16, M))]
            words[q, g] = np.where(kk < lw[g], za, np.where(kk == lw[g], bb, rng.integers(0, V, (16, M))))
            rel[q, g] = z[rng.integers(0, len(z), (16, C))]
            m = (q + g) % 4
            if m == 1: om[q, g, int(rng.integers(0, 16))] = 4095
            if m == 2: om[q, g] = 4095
            if m == 3: om[q, g] = rng.integers(0, 4096, 16)
    return pack(v, words, rel, om, rng.choice(np.array([0, 0, 1]), (N, 8, 16)))
def setup_inputs_ties(rng):
    pr = rng.integers(0, 256, (N, 8, 16, 6)); v = np.take_along_axis(pr, rng.integers(0, 6, (N, 8, 1, V)), 3)
    dd = np.sort(np.add.reduce(np.abs(pr[:, :, :, :, None] - pr[:, :, :, None, :]), axis=2).reshape(N, 8, 36), axis=2)
    ix = np.minimum(rng.choice(np.array([20, 28, 33]), (N, 8, 1)) + rng.integers(0, 8, (N, 8, 16)), 35)
    th = np.maximum(np.take_along_axis(dd, ix, 2) - rng.integers(0, 2, (N, 8, 16)), 0)
    words = rng.integers(0, V, (N, 8, 16, M)); words[:, :, :, ::3] = words[:, :, :1, ::3].copy()
    rel = rng.integers(0, V, (N, 8, 16, C)); rel[:, :, :, ::4] = rel[:, :, :1, ::4].copy()
    om = rng.integers(0, 4096, (N, 8, 16))
    for q in range(N):
        for g in range(1, 8, 2):
            b = int(rng.integers(1, V - 2)); a = rng.integers(0, 100, 16)
            v[q, g, :, b] = a; v[q, g, :, b + 1] = a + 150; v[q, g, :, V - 1] = a + 100; v[q, g, :, 0] = a + 100; v[q, g, int(rng.integers(0, 16)), 0] += 1
            u = int(np.add.reduce(om[q, g] * a)) & 4095; c = ((u * u >> 5) + 37 * u) & (C - 1)
            rel[q, g, :, c] = b + 1; rel[q, g, 0, c] = 0; rel[q, g, 15, c] = V - 1
            words[q, g, 0, 1::8] = b; th[q, g, 0] = 1600
    return pack(v, words, rel, om, th)
def setup_inputs_still(rng):
    far = V // 2 + rng.permutation(V // 2)[:V // 4]; zero = rng.permutation(np.setdiff1d(np.arange(V), far))[:V // 4]
    val = rng.choice(np.array([1, 8, 9, 100, 248]), (N, 8, V)); val[..., zero] = 0; val[..., far] = 0
    ft = rng.integers(0, 16, (N, 8, 1, V)); kk = np.arange(16).reshape(16, 1)
    v = rng.integers(0, 7, (N, 8, 16, 1)) + np.where(kk == ft, val[:, :, None, :], 0)
    v[:, :, 2:5, far] = 255 - rng.integers(0, 7, (N, 8, 3, V // 4))
    words = np.where((kk + rng.integers(0, 4, (N, 8, 1, M))) % 4 == 0, far[rng.integers(0, V // 4, (N, 8, 16, M))], rng.integers(0, V, (N, 8, 16, M)))
    rel = zero[rng.integers(0, V // 4, (N, 8, 16, C))]
    cnt = rng.permutation(np.array([1, 31, 33, 63])); par = int(rng.integers(0, 2))
    for q in range(par, N, 2):
        hit = np.zeros((8, M), bool); hit[:, :M // 2] = (rng.permutation(8 * (M // 2)) < int(cnt[q // 2])).reshape(8, M // 2)
        lw = rng.choice(np.array([H, 12, 16]), (8, 1, M))
        w = np.where(kk < lw, zero[rng.integers(0, V // 4, (8, 16, M))], far[rng.integers(0, V // 4, (8, 16, M))])
        words[q] = np.where(hit[:, None, :], w, words[q])
    return pack(v, words, rel, rng.integers(0, 4096, (N, 8, 16)), rng.choice(np.array([0, 0, 1]), (N, 8, 16)))
def check_inputs(d):
    bad = []
    for k, hi in (("x", 255), ("wd", V - 1), ("rt", V - 1), ("wt", 4095), ("th", 4080)):
        v = np.asarray(d[k]).astype(np.float64)
        if not (np.min(v) >= 0 and np.max(v) <= hi): bad.append("range of " + k)
        elif np.any(v != np.floor(v)): bad.append("whole numbers of " + k)
    return bad
def reference(x, wd, rt, wt, th):
    X = x.astype(np.float32).astype(np.int32).reshape(N, 8, 16, V)
    W = wd.astype(np.int64).reshape(N, 8, 16, M); RT = rt.astype(np.int64).reshape(N, 8, 16, C)
    om = wt.astype(np.int64).reshape(N, 8, 16, 1); lim = th.astype(np.int64).reshape(N, 8, 16, 1)
    A = np.zeros(N, np.int64); k = np.arange(16).reshape(1, 1, 16, 1); i = np.arange(M).reshape(1, 1, M)
    def pick(c):
        return np.take_along_axis(X, c.reshape(N, 8, 1, 16 * M), 3).reshape(N, 8, 16, 16, M)
    for t in range(VIS):
        if t > 0:
            W = np.roll(np.roll(W, ST, axis=0), (t + t // N) - (t - 1 + (t - 1) // N), axis=1)
        xw = pick(W); x0 = xw[:, :, :, 0]
        u = np.add.reduce(om * x0, axis=2) & 4095
        c = ((u * u >> 5) + 37 * u) & (C - 1)
        R = np.take_along_axis(RT, c[:, :, None, :], 3)
        s = np.argmin(np.add.reduce(np.abs(pick(R) - x0[:, :, :, None, :]), axis=2), axis=2)
        Q = np.take_along_axis(R, (s[:, :, None, :] + k) & 15, 2)
        xq = pick(Q); gap = np.add.reduce(np.abs(xw - xq), axis=2)
        ok = (gap <= lim + 8 * (A & 31).reshape(N, 1, 1, 1)).astype(np.int64)
        l = np.add.reduce(np.minimum.accumulate(ok, axis=2), axis=2)[:, :, None, :]
        rep = l >= H; uu = u[:, :, None, :]
        new = np.where(k < 16 - l, Q[:, :, ::-1] ^ 1, np.where(k < 32 - 2 * l, np.take_along_axis(W, (k + 2 * l - 16) & 15, 2), ((Q * uu >> 5) + Q) & (V - 1)))
        W = np.where(rep, new, np.take_along_axis(W, (k + l + 1) & 15, 2))
        at = (B * i + (u & (B - 1)))[:, :, None, :]
        np.put_along_axis(X, at, np.where(rep, (x0 + xq[:, :, :, 15]) >> 1, np.take_along_axis(X, at, 3)), 3)
        A = np.add.reduce(rep.reshape(N, 8 * M).astype(np.int64), axis=1)
    return {"yx": X.reshape(N, 128, V).astype(np.float32).astype(BF), "yw": W.reshape(N, 128, M).astype(np.float32)}

@@ -1,0 +1,659 @@
+from concourse.mybir import dt, AluOpType as OP, AxisListType, ActivationFunctionType as AF
+
+VIS = 6
+NC = 2
+CW = 128
+CYCLE, FIXED, MM, GATHER, SCATTER = 0.83, 20.0, 0.0, 1.7, 3.5
+OWN, WAKE, LOOK = 180.0, 250.0, 60.0
+QV = 1536
+BIAS = {
+    "rows": -8.0, "constants_3": -8.0, "allow": -1.5,
+    "a.wcopy": -1.5, "a.wwin": 0.7, "a.gather_w": -0.7, "a.weigh": -3.0, "a.gather_r": -3.0, "a.letters": 0.7, "a.tail": 0.7, "a.pwin": -1.5,
+    "a.keys_r": 6.0, "a.least": -1.5, "a.turn_list": -3.0, "a.sizes": 0.7, "a.unpack": 3.0, "a.moves": -1.5, "a.tally": -3.0, "a.write_x": 3.0,
+    "b.wcopy": -0.7, "b.gather_w": -6.0, "b.spread": 3.0, "b.gather_r": -0.7, "b.letters": 3.0, "b.pwin": -3.0, "b.turn_list": -6.0,
+    "b.halves": -6.0, "b.unpack": -3.0, "b.turned": 1.5, "b.tally": 3.0, "b.write_x": -3.0}
+
+ORDER = """
+a.wcopy a.wwin a.gather_w:1v a.gather_w:0s a.weigh a.relator b.gather_w:1s a.spread b.gather_w:0v a.gather_r:0 b.wcopy b.wwin a.letters
+a.gather_r:1 b.weigh a.tail a.pwin a.keys_r b.relator a.biggest:9 a.keys_m b.gather_r:0 b.gather_r:1v b.letters
+a.least a.gather_q:0 b.spread a.gather_q:1 allow b.tail b.pwin a.turn_list b.biggest:9 b.keys_r a.sizes:0 b.keys_m a.sizes:1
+b.least a.halves a.match b.gather_q:0 a.moves a.turned b.gather_q:1 a.unpack b.turn_list b.sizes:0
+a.renew b.sizes:1 b.halves b.match b.moves a.write_x a.tally b.write_x b.unpack b.turned b.renew b.tally
+"""
+FIRST = "constants_1 constants_3 tables rows constants_2 " + ORDER.replace(" allow", "")
+
+SCRATCH = {
+    "xs": ("sbuf", [128, 4352], "bfloat16"),
+    "rts": ("sbuf", [128, 2048], "int32"),
+    "wdi": ("sbuf", [128, 256], "int32"),
+    "wti": ("sbuf", [128, 2], "int32"),
+    "thi": ("sbuf", [128, 2], "int32"),
+    "wl": ("sbuf", [128, 256 * VIS], "uint16"),
+    "wo": ("sbuf", [128, 256 * VIS], "uint16"),
+    "ywf": ("sbuf", [128, 256], "float32"),
+    "nvi": ("sbuf", [128, 256], "int32"),
+    "ones": ("sbuf", [128, 256], "bfloat16"),
+    "zerf": ("sbuf", [128, 128], "float32"),
+    "blk": ("sbuf", [128, 128], "bfloat16"),
+    "blk0": ("sbuf", [128, 128], "bfloat16"),
+    "i2": ("sbuf", [128, 256], "bfloat16"),
+    "an2": ("sbuf", [128, 256], "bfloat16"),
+    "i2h": ("sbuf", [128, 256], "float16"),
+    "an2h": ("sbuf", [128, 256], "float16"),
+    "hid": ("sbuf", [128, 128], "bfloat16"),
+    "ni": ("sbuf", [128, 128], "bfloat16"),
+    "wbh": ("sbuf", [128, 128], "bfloat16"),
+    "wbl": ("sbuf", [128, 128], "bfloat16"),
+    "wa": ("sbuf", [128, 2], "int32"),
+    "tri": ("sbuf", [128, 128], "bfloat16"),
+    "m3": ("sbuf", [128, 128], "bfloat16"),
+    "e8": ("sbuf", [128, 128], "bfloat16"),
+    "m1a": ("sbuf", [128, 128], "bfloat16"),
+    "m1": ("sbuf", [128, 128], "bfloat16"),
+    "m2a": ("sbuf", [128, 128], "bfloat16"),
+    "m2b": ("sbuf", [128, 128], "bfloat16"),
+    "m2": ("sbuf", [128, 128], "bfloat16"),
+    "g8": ("sbuf", [128, 128], "float32"),
+    "b0": ("sbuf", [128, 144], "bfloat16"),
+    "c0": ("sbuf", [128, 144], "bfloat16"),
+    "m1b": ("sbuf", [128, 128], "bfloat16"),
+    "tabr": ("sbuf", [128, 2048], "float32"),
+    "tabc": ("sbuf", [128, 2048], "float32"),
+    "tabi": ("sbuf", [128, 2048], "int32"),
+
+    "bm": ("sbuf", [128, 2048], "bfloat16"),
+    "bmh": ("sbuf", [128, 2048], "float16"),
+    "k2h": ("sbuf", [128, 128], "float16"),
+    "oneh": ("sbuf", [128, 128], "float16"),
+    "y0": ("sbuf", [128, 8], "float16"),
+    "y1": ("sbuf", [128, 8], "float16"),
+    "wt0": ("sbuf", [128, 144], "float16"),
+    "wb": ("sbuf", [128, 128], "float16"),
+    "s32": ("sbuf", [128, 8], "bfloat16"),
+    "s16": ("sbuf", [128, 8], "bfloat16"),
+    "s128": ("sbuf", [128, 8], "bfloat16"),
+    "kt": ("sbuf", [128, 128], "bfloat16"),
+    "row16": ("sbuf", [128, 128], "bfloat16"),
+    "md": ("sbuf", [128, 128], "bfloat16"),
+    "rs": ("sbuf", [128, 128], "float32"),
+    "keep": ("sbuf", [128, 128], "bfloat16"),
+    "pi": ("sbuf", [128, 2], "int32"),
+    "pj": ("sbuf", [128, 2], "int32"),
+    "cols": ("sbuf", [128, 64], "float32"),
+    "ihi": ("sbuf", [128, 8], "float32"),
+    "it": ("sbuf", [128, 8], "bfloat16"),
+    "m128": ("sbuf", [128, 8], "bfloat16"),
+    "itg": ("sbuf", [128, 16], "float32"),
+    "itf": ("sbuf", [128, 16], "float32"),
+    "ite": ("sbuf", [128, 16], "float32"),
+    "itd": ("sbuf", [128, 16], "float32"),
+    "cnt": ("sbuf", [128, 2], "float32"),
+    "ai": ("sbuf", [128, 2], "int32"),
+    "aj": ("sbuf", [128, 2], "int32"),
+}
+for _c in range(NC):
+    SCRATCH.update({
+        "xw%d" % _c: ("sbuf", [128, 2048], "bfloat16"),
+        "xr%d" % _c: ("sbuf", [128, 2048], "bfloat16"),
+        "mx%d" % _c: ("sbuf", [128, 2048], "bfloat16"),
+        "df%d" % _c: ("sbuf", [128, 2048], "bfloat16"),
+        "ww%d" % _c: ("sbuf", [128, 2048], "float32"),
+        "pw%d" % _c: ("sbuf", [128, 2048], "float32"),
+        "dw%d" % _c: ("dram", [8, 32, 128], "float32"),
+        "wf%d" % _c: ("sbuf", [128, 128], "float32"),
+        "pk%d" % _c: ("sbuf", [128, 128], "float32"),
+        "dp%d" % _c: ("dram", [8, 32, 128], "float32"),
+        "x0%d" % _c: ("sbuf", [128, 128], "float16"),
+        "ti%d" % _c: ("sbuf", [128, 1024], "int32"),
+        "tf%d" % _c: ("sbuf", [128, 512], "float32"),
+        "ui%d" % _c: ("sbuf", [128, 64], "int32"),
+        "uf%d" % _c: ("sbuf", [128, 64], "float32"),
+        "ls%d" % _c: ("sbuf", [128, 64], "uint16"),
+        "r16%d" % _c: ("sbuf", [128, 128], "uint16"),
+        "l2%d" % _c: ("sbuf", [128, 128], "uint16"),
+        "sc%d" % _c: ("sbuf", [128, 128], "float32"),
+        "zs%d" % _c: ("sbuf", [128, 128], "bfloat16"),
+        "sb%d" % _c: ("sbuf", [128, 384], "bfloat16"),
+        "pp%d" % _c: ("sbuf", [128, 384], "bfloat16"),
+        "tl%d" % _c: ("sbuf", [128, 128], "int32"),
+        "ff%d" % _c: ("sbuf", [128, 384], "float32"),
+        "ph%d" % _c: ("sbuf", [128, 384], "float16"),
+    })
+for _b in range(8):
+    SCRATCH["ps%d" % _b] = ("psum", [128, 512], "float32")
+
+SEMAPHORES = ["v", "s", "pe", "gp", "sent", "dacc", "ldx", "ldx2", "ldr", "ldw", "ldt", "ldh", "outw", "outx"]
+SEMAPHORES += ["d%s%d%d" % (w, st, c) for w in "wp" for st in (1, 2) for c in range(NC)]
+SEMAPHORES += ["ar%d_%d" % (t, c) for t in range(1, VIS) for c in range(NC)]
+
+
+def rank_program(g, core, T, topo):
+    rank = T.rank_of(core)
+    if rank is None:
+        return
+    nrank = len(T.cores)
+    nxt = T.cores[(rank + 1) % nrank]
+    V, S, PE, SY = g.vector, g.scalar, g.tensor, g.sync
+    queue = {"v": V, "s": S, "pe": PE, "gp": g, "sy": SY}
+    total = {}
+    know = {q: {} for q in queue}
+    wrote, seen = {}, {}
+
+    def need(q, tok):
+        if tok is None:
+            return
+        sem, val, clock, _ = tok
+        if know[q].get(sem, 0) < val:
+            queue[q].wait_ge(T.sem[sem], val)
+            for s2, v2 in clock.items():
+                if know[q].get(s2, 0) < v2:
+                    know[q][s2] = v2
+            know[q][sem] = val
+
+    def sync_for(q, reads, writes, banks):
+        toks = []
+        for r in reads:
+            toks.append(wrote[r])
+        for w in writes:
+            if w in wrote and not (q == "pe" and wrote[w][3] == q):
+                toks.append(wrote[w])
+            for tok in seen.get(w, {}).values():
+                if tok[3] != q or q == "sy":
+                    toks.append(tok)
+        for b in banks:
+            for q2, tok in seen.get(b, {}).items():
+                if q2 != q:
+                    toks.append(tok)
+        toks.sort(key=lambda z: -z[1])
+        for tok in toks:
+            need(q, tok)
+
+    def note(q, tok, reads, writes, banks):
+        for w in writes:
+            wrote[w] = tok
+            seen[w] = {}
+        for r in reads:
+            seen.setdefault(r, {})[tok[0]] = tok
+        for b in banks:
+            seen.setdefault(b, {})[q] = tok
+
+    nodes = []
+    label, now = [], [""]
+
+    def op(q, call, reads, writes, banks=(), cost=100.0):
+        def emit():
+            sync_for(q, reads, writes, banks)
+            total[q] = total.get(q, 0) + 1
+            call().then_inc(T.sem[q], 1)
+            note(q, (q, total[q], dict(know[q]), q), reads, writes, banks)
+        nodes.append((q, emit, list(reads), list(writes), list(banks), cost, 0.0))
+
+    def dmas(q, calls, sem, reads, writes, extra=2300.0):
+        def emit():
+            sync_for(q, reads, writes, ())
+            for call in calls:
+                total[sem] = total.get(sem, 0) + 16
+                call().then_inc(T.sem[sem], 16)
+            note(q, (sem, total[sem], dict(know[q]), "dma"), reads, writes, ())
+        nodes.append((q, emit, list(reads), list(writes), [], 70.0 * len(calls), extra))
+
+    def span(ap):
+        return ap.shape[1]
+
+    def vcost(n, kind, wide):
+        return {"": FIXED + max(64, n * wide) * CYCLE, "g": FIXED + n * GATHER * CYCLE, "s": FIXED + n * SCATTER * CYCLE}[kind]
+
+    def mm(out, lhsT, rhs, reads, bank, start=True, stop=True, tag=None):
+        op("pe", lambda: PE.matmul(out, lhsT, rhs, start, stop), reads, [tag] if tag else [], [bank], MM + max(64, span(rhs)) * CYCLE * 0.7)
+
+    def tt(out, a, b, o, reads, writes, banks=(), kind=""):
+        op("v", lambda: V.tensor_tensor(out, a, b, o), reads, writes, banks, vcost(span(out), kind, 1 if banks else 2))
+
+    def ts(out, a, s1, o1, reads, writes, banks=(), s2=None, o2=None, kind=""):
+        cost = vcost(span(out), kind, 1)
+        if o2 is None:
+            op("v", lambda: V.tensor_scalar(out, a, s1, None, o1), reads, writes, banks, cost)
+        else:
+            op("v", lambda: V.tensor_scalar(out, a, s1, s2, o1, o2), reads, writes, banks, cost)
+
+    def cp(out, a, reads, writes, banks=(), kind=""):
+        op("v", lambda: V.tensor_copy(out, a), reads, writes, banks, vcost(span(a if kind == "s" else out), kind, 1))
+
+    def act(out, a, f, reads, writes, banks=(), kind="", **more):
+        op("s", lambda: S.activation(out, a, f, **more), reads, writes, banks, vcost(span(out), kind, 1) + 30.0)
+
+    def plan():
+        n = len(nodes)
+        preds = [dict() for _ in range(n)]
+        last, rd, bk = {}, {}, {}
+        for i, (q, _, reads, writes, banks, _, _) in enumerate(nodes):
+            def edge(j, hard):
+                preds[i][j] = preds[i].get(j, False) or hard
+            for x in reads:
+                edge(last[x], True)
+                rd.setdefault(x, []).append(i)
+            for x in writes:
+                if x in last:
+                    edge(last[x], not (q == "pe" and nodes[last[x]][0] == "pe"))
+                for j in rd.get(x, ()):
+                    if j != i:
+                        edge(j, nodes[j][0] != q or q == "sy")
+                last[x], rd[x] = i, []
+            for b in banks:
+                for q2, j in bk.setdefault(b, {}).items():
+                    if j != i and (q2 != q or q == "pe"):
+                        edge(j, q2 != q)
+                bk[b][q] = i
+        succs = [[] for _ in range(n)]
+        left = [len(p) for p in preds]
+        for i, p in enumerate(preds):
+            for j, hard in p.items():
+                succs[j].append((i, hard))
+
+        def lag(j, i, hard):
+            return (nodes[j][6] + (OWN if nodes[j][0] == nodes[i][0] else WAKE)) if hard else 0.0
+        prio = [0.0] * n
+        for i in range(n - 1, -1, -1):
+            prio[i] = nodes[i][5] + max([prio[k] + lag(i, k, hard) for k, hard in succs[i]] + [0.0])
+        for i in range(n):
+            prio[i] += 1000.0 * BIAS.get(label[i], 0.0)
+        ready = {q: [] for q in queue}
+        at = [0.0] * n
+        free = {q: 0.0 for q in queue}
+        for i in range(n):
+            if left[i] == 0:
+                ready[nodes[i][0]].append(i)
+        order = []
+        while len(order) < n:
+            best = None
+            for q, c in ready.items():
+                if c:
+                    t0 = min(max(free[q], at[i]) for i in c)
+                    if best is None or t0 < best[0]:
+                        best = (t0, q)
+            t0, q = best
+            i = max((i for i in ready[q] if max(free[q], at[i]) <= t0 + LOOK), key=lambda z: prio[z] - (max(free[q], at[z]) - t0))
+            ready[q].remove(i)
+            t1 = max(free[q], at[i])
+            free[q] = t1 + nodes[i][5]
+            order.append(i)
+            for k, hard in succs[i]:
+                at[k] = max(at[k], free[q] + lag(i, k, hard) if hard else t1)
+                left[k] -= 1
+                if left[k] == 0:
+                    ready[nodes[k][0]].append(k)
+        return order
+
+    dmas("sy", [lambda: SY.dma_start(T.wdi[:], T.wd[:])], "ldw", [], ["wdi"])
+    dmas("s", [lambda: S.dma_start(T.xs[:, 0:2048], T.x[:, 0:2048])], "ldx", [], ["x_lo"], 4000.0)
+    dmas("sy", [lambda: SY.dma_start(T.xs[:, 2048:4096], T.x[:, 2048:4096])], "ldx2", [], ["x_hi"], 4000.0)
+    dmas("sy", [lambda: SY.dma_start(T.wti[:, 0:1], T.wt[:])], "ldt", [], ["wti"])
+    dmas("sy", [lambda: SY.dma_start(T.rts[:], T.rt[:])], "ldr", [], ["rts"], 6000.0)
+    dmas("sy", [lambda: SY.dma_start(T.thi[:, 0:1], T.th[:])], "ldh", [], ["thi"])
+
+    def col(n):
+        return T.cols[:, n:n + 1]
+
+    def sel(out, in_, pattern, cmp, fill, base, cm, reads, writes):
+        op("gp", lambda: g.affine_select(out, in_, pattern, cmp, fill, base, cm), reads, writes, (), 170.0 + 2 * span(out) * CYCLE)
+
+    op("v", lambda: V.memset(T.ones[:], 1.0), [], ["ones"])
+    op("gp", lambda: g.iota(T.pi[:], [[0, 2]], 0, 1), [], ["pi"])
+    sel(T.blk0[:], T.ones[:, 0:128], [[-16, 8], [0, 16]], OP.is_ge, 0.0, 0, 1, ["ones"], ["blk0"])
+    sel(T.blk[:], T.blk0[:], [[16, 8], [0, 16]], OP.is_ge, 0.0, 15, -1, ["blk0"], ["blk"])
+    sel(T.i2[:], T.ones[:], [[0, 2], [-1, 128]], OP.is_equal, 0.0, 0, 1, ["ones"], ["i2"])
+    op("v", lambda: V.memset(T.zerf[:], 0.0), [], ["zerf"])
+    op("v", lambda: V.memset(T.b0[:], 0.0), [], ["b0"])
+    for c in range(NC):
+        op("v", (lambda c: lambda: V.memset(T["zs%d" % c][:], 1.0))(c), [], ["zs%d" % c])
+    ts(T.pj[:], T.pi[:], 15, OP.bitwise_and, ["pi"], ["pj"])
+    cp(col(0), T.pj[:, 0:1], ["pj"], ["k0"])
+    op("gp", lambda: g.iota(T.kt[:], [[0, 8], [1, 16]], 0, 0, allow_small_or_imprecise_dtypes=True), [], ["kt"])
+    sel(T.keep[:], T.ones[:, 0:128], [[0, 8], [1, 16]], OP.not_equal, 0.0, 0, 0, ["ones"], ["keep"])
+    cp(T.b0[:, 15:143:16], T.blk[:, 0:128:16], ["blk"], ["b0"])
+    cp(T.wl[:, 0:256], T.wdi[:], ["wdi"], ["wl0_0", "wl0_1"])
+    cp(col(1), T.wti[:, 0:1], ["wti"], ["w1"])
+    ts(col(2), col(1), 2048.0, OP.is_ge, ["w1"], ["w2"], (), -4096.0, OP.mult)
+    tt(col(3), col(1), col(2), OP.add, ["w1", "w2"], ["w3"])
+    ts(T.wt0[:], T.b0[:], col(3), OP.mult, ["b0", "w3"], ["wt0"])
+    cp(T.i2h[:], T.i2[:], ["i2"], ["i2h"])
+    ts(T.wa[:, 0:1], T.wti[:, 0:1], 15, OP.bitwise_and, ["wti"], ["wa"])
+    cp(col(12), T.wa[:, 0:1], ["wa"], ["wlo"])
+    tt(col(11), col(1), col(12), OP.subtract, ["w1", "wlo"], ["whi"])
+    ts(T.wbl[:], T.blk[:], col(12), OP.mult, ["blk", "wlo"], ["wbl"])
+    ts(T.wbh[:], T.blk[:], col(11), OP.mult, ["blk", "whi"], ["wbh"])
+    ts(T.md[:], T.kt[:], col(0), OP.is_equal, ["kt", "k0"], ["md"])
+    ts(T.k2h[:], T.ones[:, 0:128], 2048.0, OP.mult, ["ones"], ["k2h"])
+    cp(T.oneh[:], T.ones[:, 0:128], ["ones"], ["oneh"])
+
+    def tables():
+        ts(T.tabi[:], T.rts[:], 1, OP.bitwise_and, ["rts"], ["tabi"])
+        ts(T.tabc[:], T.tabi[:], -2.0, OP.mult, ["tabi"], ["tabc"], (), -2047.0, OP.add)
+        cp(T.tabr[:], T.rts[:], ["rts"], ["tabr"])
+        dmas("gp", [lambda: g.dma_start(T.tabc[:], T.tabr[:], accum_op=OP.add)], "dacc", ["tabr", "tabc"], ["tabc"], 6000.0)
+
+    def rows():
+        cp(T.bmh[:], T.bm[:], ["bm%d" % n for n in range(8)], ["bmh"])
+
+    def constants_1():
+        sel(T.rs[:], T.zerf[:], [[0, 8], [1, 16]], OP.not_equal, 524288.0, 0, 0, ["zerf"], ["rs"])
+        op("gp", lambda: g.iota(T.row16[:], [[16, 128]], 0, 0, allow_small_or_imprecise_dtypes=True), [], ["row16"])
+        op("gp", lambda: g.iota(T.ihi[:], [[16, 8]], 0, 0, allow_small_or_imprecise_dtypes=True), [], ["ihi"])
+        op("gp", lambda: g.iota(T.itg[:], [[16, 16]], 0, 0, allow_small_or_imprecise_dtypes=True), [], ["itg"])
+        sel(T.tri[:], T.blk[:], [[1, 128]], OP.is_ge, 0.0, 0, -1, ["blk"], ["tri"])
+        sel(T.e8[:], T.ones[:, 0:128], [[-16, 8], [0, 16]], OP.is_equal, 0.0, -8, 1, ["ones"], ["e8"])
+        sel(T.an2[:], T.ones[:], [[0, 2], [-16, 8], [1, 16]], OP.is_equal, 0.0, -15, 1, ["ones"], ["an2"])
+        sel(T.m3[:], T.ones[:, 0:128], [[-16, 8], [1, 8], [0, 2]], OP.is_equal, 0.0, -15, 1, ["ones"], ["m3"])
+        ts(T.s32[:], T.blk[:, 0:128:16], 32.0, OP.mult, ["blk"], ["s32"])
+        ts(T.s16[:], T.blk[:, 0:128:16], -16.0, OP.mult, ["blk"], ["s16"])
+        ts(T.s128[:], T.blk[:, 0:128:16], 128.0, OP.mult, ["blk"], ["s128"])
+        ts(T.m128[:], T.ones[:, 0:8], col(0), OP.mult, ["ones", "k0"], ["m128"], (), -128.0, OP.mult)
+        ts(T.it[:], T.ihi[:], col(0), OP.add, ["ihi", "k0"], ["it"])
+        ts(T.hid[:], T.i2[:, 0:128], 0.5, OP.mult, ["i2"], ["hid"])
+        ts(T.ni[:], T.i2[:, 0:128], -1.0, OP.mult, ["i2"], ["ni"])
+
+    def constants_3():
+        for n in range(8):
+            sel(T.bm[:, 256 * n:256 * n + 256], T.ones[:], [[-1, 2], [-16, 8], [0, 16]], OP.is_equal, 0.0, -2 * n, 1, ["ones"], ["bm%d" % n])
+
+    def constants_2():
+        cp(col(8), T.thi[:, 0:1], ["thi"], ["thf"])
+        ts(col(4), col(0), 1.0, OP.add, ["k0"], ["k1"])
+        ts(T.itf[:], T.itg[:], col(0), OP.add, ["itg", "k0"], ["itf"], (), 4096.0, OP.add)
+        ts(T.itd[:], T.itg[:], col(0), OP.add, ["itg", "k0"], ["itd"], (), 15.0, OP.mult)
+        ts(T.ite[:], T.itd[:], -4096.0, OP.add, ["itd"], ["ite"])
+        ts(col(5), col(0), 8.0, OP.is_equal, ["k0"], ["q8"])
+        ts(col(6), col(0), 9.0, OP.is_ge, ["k0"], ["q9"], (), 1.0, OP.add)
+        ts(col(7), col(5), -8.0, OP.mult, ["q8"], ["q7"])
+        tt(col(9), col(6), col(7), OP.add, ["q9", "q7"], ["qc"])
+        ts(T.c0[:], T.b0[:], col(9), OP.mult, ["b0", "qc"], ["c0"], (), 128.0, OP.mult)
+        ts(T.g8[:], T.ones[:, 0:128], col(5), OP.mult, ["ones", "q8"], ["g8"])
+        cp(T.an2h[:], T.an2[:], ["an2"], ["an2h"])
+        tt(T.m1a[:], T.e8[:], T.i2[:, 0:128], OP.subtract, ["e8", "i2"], ["m1a"])
+        tt(T.m2a[:], T.an2[:, 0:128], T.e8[:], OP.subtract, ["an2", "e8"], ["m2a"])
+        sel(T.m1b[:], T.m1a[:], [[0, 8], [1, 16]], OP.is_ge, 0.0, -8, 0, ["m1a"], ["m1b"])
+        ts(T.m1[:], T.m1b[:], 4096.0, OP.mult, ["m1b"], ["m1"])
+        sel(T.m2b[:], T.m2a[:], [[0, 8], [-1, 16]], OP.is_ge, 0.0, 7, 0, ["m2a"], ["m2b"])
+        tt(T.m2[:], T.m2b[:], T.m3[:], OP.subtract, ["m2b", "m3"], ["m2"])
+
+    XR = ["x_lo", "x_hi"]
+
+    def stages(t, c):
+        B = ["ps%d" % (4 * c + b) for b in range(4)]
+        P = [T[b] for b in B]
+        r = lambda name: "%s_%d" % (name, c)
+        xw, xr, mx, df = T["xw%d" % c], T["xr%d" % c], T["mx%d" % c], T["df%d" % c]
+        ti, tf, ui, uf, ls = T["ti%d" % c], T["tf%d" % c], T["ui%d" % c], T["uf%d" % c], T["ls%d" % c]
+        w0 = 256 * t + CW * c
+        wres = "wl%d_%d" % (t, c)
+        TI = lambda n: ti[:, 128 * n:128 * n + 128]
+        TF = lambda n: tf[:, 128 * n:128 * n + 128]
+        UI = lambda n: ui[:, 8 * n:8 * n + 8]
+        UF = lambda n: uf[:, 8 * n:8 * n + 8]
+        LS = lambda n: ls[:, 8 * n:8 * n + 8]
+        last = t == VIS - 1
+
+        def gather_w(h, q):
+            o = xw[:, 1024 * h:1024 * h + 1024]
+            i = T.xs[:, 0:4096].indirect(T.wl[:, w0 + 64 * h:w0 + 64 * h + 64])
+            if q == "s":
+                act(o, i, AF.Copy, XR + [wres], [r("xw%d" % h)], kind="g")
+            else:
+                cp(o, i, XR + [wres], [r("xw%d" % h)], kind="g")
+
+        def wcopy():
+            ts(T["wf%d" % c][:], T.wl[:, w0:w0 + CW], -2048.0, OP.add, [wres], [r("wf")])
+
+
+        def window(kind, src, win, dram, off):
+            d, w, s = T[dram], T[win], T[src]
+            rs = [r(kind + "f")]
+            dmas("sy", [lambda: SY.dma_start(d[:, 0:16, :], s[:]), lambda: SY.dma_start(d[:, 16:32, :], s[:])],
+                 "d%s1%d" % (kind, c), rs, [r(kind + "d")])
+            dmas("sy", [(lambda k: lambda: SY.dma_start(w[k:128:16, :], d[:, k + off:k + off + 16, :]))(k) for k in range(16)],
+                 "d%s2%d" % (kind, c), [r(kind + "d")], [r(kind + "w")], 5000.0)
+
+        def wwin():
+            window("w", "wf%d" % c, "ww%d" % c, "dw%d" % c, 1)
+
+        def pwin():
+            window("p", "pk%d" % c, "pw%d" % c, "dp%d" % c, 0)
+
+        def pick(src, srcs, banks, tmp, out):
+            a, b2 = TF(tmp), TF(tmp + 1)
+            tt(a, src, T.md[:], OP.mult, srcs + ["md"], [r("f%d" % tmp)], banks)
+            op("v", lambda: V.tensor_tensor_scan(b2, T.keep[:], a, 0.0, OP.mult, OP.add), ["keep", r("f%d" % tmp)], [r("f%d" % (tmp + 1))])
+            return tf[:, 128 * tmp + 143:128 * tmp + 256:16], r("f%d" % (tmp + 1))
+
+        def weigh():
+            x0 = T["x0%d" % c]
+            XW = [r("xw0"), r("xw1")]
+            if c == 0:
+                mm(P[1][:, 8:136], T.wbh[:], xw[:, 0:2048:16], ["wbh"] + XW, B[1], True, False, r("ub"))
+                mm(P[1][:, 8:136], T.wbl[:], xw[:, 0:2048:16], ["wbl"] + XW, B[1], False, True, r("ub"))
+            else:
+                cp(x0[:], xw[:, 0:2048:16], XW, [r("x0")])
+                for m in range(16):
+                    mm(P[1][:, 0:8], T.wt0[:, 15 - m:143 - m], x0[:, m:128:16], ["wt0", r("x0")], B[1], m == 0, m == 15, r("uw"))
+            mm(P[0][:, 0:128], T.i2[:, 0:128], xw[:, 0:2048:16], ["i2"] + XW, B[0], True, True, r("x0p"))
+
+        def relator():
+            if c == 0:
+                src, res = pick(P[1][:, 8:136], [r("ub")], [B[1]], 0, None)
+                cp(UI(0), src, [res], [r("u0")])
+            else:
+                cp(UI(0), P[1][:, 0:8], [r("uw")], [r("u0")], [B[1]])
+            ts(UI(1), UI(0), 4095, OP.bitwise_and, [r("u0")], [r("u1")])
+            ts(T["y%d" % c][:], UI(1), -2048.0, OP.add, [r("u1")], [r("y")])
+            ts(UF(1), UI(1), 3232.0, OP.add, [r("u1")], [r("uz")])
+            tt(UI(2), T["y%d" % c][:], UF(1), OP.mult, [r("y"), r("uz")], [r("u2")])
+            ts(UI(3), UI(2), 5, OP.arith_shift_right, [r("u2")], [r("u3")], (), 2047, OP.bitwise_and)
+            cp(LS(0), UI(3), [r("u3")], [r("cl")])
+            cp(T["r16%d" % c][:], T.rts[:].indirect(LS(0)), ["rts", r("cl")], [r("r16")])
+            ts(UI(4), UI(1), 15, OP.bitwise_and, [r("u1")], [r("u4")])
+
+        def spread():
+            y = T["y%d" % c]
+            mm(P[0][:, 384:512], T.k2h[0:1, :], T.oneh[0:1, :], ["k2h", "oneh"], B[0], True, False, r("us"))
+            for m in range(16):
+                mm(P[0][:, 384 + m:512:16], T.bmh[:, 128 * m:128 * m + 128], y[:], ["bmh", r("y")], B[0], False, m == 15, r("us"))
+
+        def letters():
+            act(TF(0), T.tabr[:].indirect(LS(0)), AF.Copy, ["tabr", r("cl")], [r("f0")], kind="g")
+            act(TF(1), T.tabc[:].indirect(LS(0)), AF.Copy, ["tabc", r("cl")], [r("f1")], kind="g", scale=1.0 / 4096, bias=-2048.0)
+
+        def gather_r(h, q="s"):
+            o = xr[:, 1024 * h:1024 * h + 1024]
+            i = T.xs[:, 0:4096].indirect(T["r16%d" % c][:, 64 * h:64 * h + 64])
+            if q == "s":
+                act(o, i, AF.Copy, XR + [r("r16")], [r("xr%d" % h)], kind="g")
+            else:
+                cp(o, i, XR + [r("r16")], [r("xr%d" % h)], kind="g")
+
+        def tail():
+            tt(TI(0), TF(0), P[0][:, 384:512], OP.mult, [r("f0"), r("us")], [r("t0")], [B[0]])
+            ts(TI(1), TI(0), 5, OP.arith_shift_right, [r("t0")], [r("t1")], (), 4095, OP.bitwise_and)
+            tt(TI(2), TI(1), TF(0), OP.add, [r("t1"), r("f0")], [r("t2")])
+            ts(TI(3), TI(2), 4095, OP.bitwise_and, [r("t2")], [r("t3")])
+            tt(T["pk%d" % c][:], TI(3), TF(1), OP.add, [r("t3"), r("f1")], [r("pf")])
+            tt(UF(2), UI(4), T.ite[:, 8 * c:8 * c + 8], OP.add, [r("u4"), "ite"], [r("e")])
+
+        def keys_r():
+            K = P[1][:, 256:384]
+            mm(K, T.ones[0:1, 0:128], T.kt[0:1, :], ["ones", "kt"], B[1], True, False, r("key"))
+            for j in range(16):
+                mm(P[1][:, 256 + j:384:16], xr[:, j:2048:16], T.s16[:], [r("xr0"), r("xr1"), "s16"], B[1], False, False, r("key"))
+
+        def biggest(h):
+            h0, h1 = (0, 2) if h == 9 else (h, h + 1)
+            hs = range(h0, h1)
+            for j in range(16):
+                a = slice(1024 * h0 + j, 1024 * h1, 16)
+                tt(mx[:, a], xr[:, a], P[0][:, 64 * h0:64 * h1], OP.max, [r("xr%d" % h) for h in hs] + [r("x0p")],
+                   [r("mx%d_%d" % (h, j)) for h in hs] + [r("mz_%d" % j)] * (h1 - 1), [B[0]])
+
+        def keys_m():
+            for j in range(16):
+                mm(P[1][:, 256 + j:384:16], mx[:, j:2048:16], T.s32[:], [r("mx0_%d" % j), r("mx1_%d" % j), r("mz_%d" % j), "s32"], B[1], False, j == 15, r("key"))
+
+        def least():
+            sc, zs, sb = T["sc%d" % c], T["zs%d" % c], T["sb%d" % c]
+            op("v", lambda: V.tensor_tensor_scan(sc[:], T.rs[:], P[1][:, 256:384], 0.0, OP.max, OP.min), ["rs", r("key")], [r("sc")], [B[1]])
+            cp(UI(5), sc[:, 15:128:16], [r("sc")], [r("u5")])
+            ts(UI(6), UI(5), 15, OP.bitwise_and, [r("u5")], [r("u6")])
+            cp(zs[:, 0:128:16], UI(6), [r("u6")], ["zs%d" % c])
+            op("v", lambda: V.tensor_tensor_scan(sb[:, 0:128], T.keep[:], zs[:], 0.0, OP.mult, OP.add), ["keep", "zs%d" % c], [r("sk")])
+            ts(sb[:, 128:256], sb[:, 0:128], 16.0, OP.is_ge, [r("sk")], [r("sk16")], (), -16.0, OP.mult)
+            L = P[2][:, 0:128]
+            mm(L, T.ones[0:1, 0:128], T.row16[0:1, :], ["ones", "row16"], B[2], True, False, r("l2p"))
+            mm(L, sb[:, 0:128], T.i2[:, 0:128], [r("sk"), "i2"], B[2], False, False, r("l2p"))
+            mm(L, sb[:, 128:256], T.i2[:, 0:128], [r("sk16"), "i2"], B[2], False, True, r("l2p"))
+            tt(sb[:, 256:384], sb[:, 0:128], T.md[:], OP.mult, [r("sk"), "md"], [r("skd")])
+            cp(T["l2%d" % c][:], L, [r("l2p")], [r("l2")], [B[2]])
+
+        def turn_list():
+            sb = T["sb%d" % c]
+            o = P[1][:, 136:144]
+            mm(o, sb[:, 256:384], T.s128[:], [r("skd"), "s128"], B[1], True, False, r("slp"))
+            mm(o, T.i2[:, 0:128], T.it[:], ["i2", "it"], B[1], False, False, r("slp"))
+            mm(o, T.i2[:, 0:128], T.m128[:], ["i2", "m128"], B[1], False, True, r("slp"))
+            cp(LS(1), o, [r("slp")], [r("sl")], [B[1]])
+
+        def gather_q(h):
+            lo, hi = 1024 * h, (1024, QV)[h]
+            tt(df[:, lo:hi], xr[:].indirect(T["l2%d" % c][:, lo // 16:hi // 16]), xw[:, lo:hi], OP.subtract,
+               [r("xr0"), r("xr1"), r("l2"), r("xw%d" % h)], [r("df%d" % h)], kind="g")
+            if h == 1:
+                act(df[:, QV:2048], xr[:].indirect(T["l2%d" % c][:, QV // 16:128]), AF.Copy, [r("xr0"), r("xr1"), r("l2")], [r("df2")], kind="g")
+                o = P[3][:, 0:2048 - QV]
+                mm(o, T.i2[:, 0:128], df[:, QV:2048], ["i2", r("df2")], B[3], True, False, r("dq"))
+                mm(o, T.ni[:], xw[:, QV:2048], ["ni", r("xw1")], B[3], False, True, r("dq"))
+                act(mx[:, QV:2048], o, AF.Abs, [r("dq")], [r("mz_%d" % j) for j in range(16)], [B[3]])
+
+        def sizes(h):
+            a = slice(1024 * h, (1024, QV)[h])
+            act(mx[:, a], df[:, a], AF.Abs, [r("df%d" % h)], [r("mx%d_%d" % (h, j)) for j in range(16)])
+            for k in range(16):
+                mm(P[2][:, 128 + 64 * h:192 + 64 * h], T.b0[:, 15 - k:143 - k], mx[:, 1024 * h + k:1024 * h + 1024:16],
+                   ["b0", r("mx%d_%d" % (h, k))] + [r("mz_%d" % k)] * h, B[2], k == 0, k == 15, r("d2"))
+
+        def halves():
+            v = 128 + QV // 16
+            XW = [r("xw0"), r("xw1")]
+            mm(P[0][:, 128:256], T.hid[:], xw[:, 0:2048:16], ["hid"] + XW, B[0], True, False, r("nvp"))
+            mm(P[0][:, 128:v], T.hid[:], xw[:, 15:QV:16], ["hid"] + XW, B[0], False, False, r("nvp"))
+            mm(P[0][:, 128:v], T.hid[:], df[:, 15:QV:16], ["hid", r("df0"), r("df1")], B[0], False, False, r("nvp"))
+            mm(P[0][:, v:256], T.hid[:], df[:, QV + 15:2048:16], ["hid", r("df2")], B[0], False, True, r("nvp"))
+            ts(T.nvi[:, CW * c:CW * c + CW], P[0][:, 128:256], -0.25, OP.add, [r("nvp")], [r("nv")], [B[0]])
+
+        def unpack():
+            pw, ff = T["pw%d" % c], T["ff%d" % c]
+            ts(T["tl%d" % c][:], pw[:].indirect(LS(1)), 1.0 / 8192, OP.add, [r("pw"), r("sl")], [r("tl")], kind="g")
+            tt(ff[:, 128:256], pw[:].indirect(LS(1)), T["tl%d" % c][:], OP.subtract, [r("pw"), r("sl"), r("tl")], [r("rc")], kind="g")
+
+        def match():
+            pp = T["pp%d" % c]
+            ts(pp[:, 0:128], P[2][:, 128:256], col(8 if t == 0 else 10), OP.is_le, [r("d2"), "thf" if t == 0 else "thr"], [r("ag")], [B[2]])
+            mm(P[2][:, 256:384], T.tri[:], pp[:, 0:128], ["tri", r("ag")], B[2], True, True, r("pre"))
+            ts(pp[:, 128:256], P[2][:, 256:384], col(4), OP.is_ge, [r("pre"), "k1"], [r("P")], [B[2]])
+            mm(P[1][:, 384:512], T.e8[:], pp[:, 128:256], ["e8", r("P")], B[1], True, True, r("rep"))
+
+        def write_x():
+            src, res = pick(P[1][:, 384:512], [r("rep")], [B[1]], 2, None)
+            tt(UF(3), src, UF(2), OP.mult, [res, r("e")], [r("er")])
+            tt(UF(4), UF(3), T.itf[:, 8 * c:8 * c + 8], OP.add, [r("er"), "itf"], [r("at")])
+            cp(LS(2), UF(4), [r("at")], [r("al")])
+            cp(T.xs[:].indirect(LS(2)), T.nvi[:, CW * c:CW * c + CW], [r("nv"), r("al")], XR, kind="s")
+
+        def moves():
+            pp = T["pp%d" % c]
+            for m in range(16):
+                mm(P[0][:, 256:264], T.c0[:, 15 - m:143 - m], pp[:, 128 + m:256:16], ["c0", r("P")], B[0], m == 0, False, r("rho"))
+            mm(P[0][:, 256:264], T.i2[:, 0:128], T.it[:], ["i2", "it"], B[0], False, True, r("rho"))
+            Pk = pp[:, 128:256]
+            mm(P[3][:, 0:128], T.m1[:], Pk, ["m1", r("P")], B[3], True, True, r("k1"))
+            mm(P[3][:, 256:384], T.m3[:], Pk, ["m3", r("P")], B[3], True, True, r("k3"))
+            mm(P[3][:, 128:256], T.m2[:], Pk, ["m2", r("P")], B[3], True, False, r("k2"))
+            mm(P[3][:, 128:256], T.ones[0:1, 0:128], T.ones[0:1, 0:128], ["ones"], B[3], False, True, r("k2"))
+
+        def turned():
+            ff = T["ff%d" % c]
+            cp(LS(3), P[0][:, 256:264], [r("rho")], [r("rl")], [B[0]])
+            act(ff[:, 256:384], T["ww%d" % c][:].indirect(LS(3)), AF.Copy, [r("ww"), r("rl")], [r("wr")], kind="g")
+
+        def renew():
+            ff, ph = T["ff%d" % c], T["ph%d" % c]
+            tt(ph[:, 128:256], ff[:, 128:256], P[3][:, 0:128], OP.mult, [r("rc"), r("k1")], [r("h1")], [B[3]])
+            tt(ph[:, 256:384], T["tl%d" % c][:], P[3][:, 256:384], OP.mult, [r("tl"), r("k3")], [r("h2")], [B[3]])
+            tt(ph[:, 0:128], ff[:, 256:384], P[3][:, 128:256], OP.mult, [r("wr"), r("k2")], [r("h0")], [B[3]])
+            d = 0 if last else 16 * ((t + 1 + (t + 1) // nrank) - (t + t // nrank))
+            F = P[2][:, 384:512]
+            mm(F, T.an2h[:, 128 - d:256 - d], ph[:, 128:256], ["an2h", r("h1")], B[2], True, False, r("fin"))
+            mm(F, T.i2h[:, 128 - d:256 - d], ph[:, 256:384], ["i2h", r("h2")], B[2], False, False, r("fin"))
+            mm(F, T.i2h[:, 128 - d:256 - d], ph[:, 0:128], ["i2h", r("h0")], B[2], False, True, r("fin"))
+            if last:
+                ts(T.ywf[:, CW * c:CW * c + CW], F, 2048.0, OP.add, [r("fin")], [r("yw")], [B[2]])
+                return
+            wo = T.wo[:, w0:w0 + CW]
+            ts(wo, F, 2048.0, OP.add, [r("fin")], [r("wo%d" % t)], [B[2]])
+            rid, pid, _ = topo.addr(nxt)
+            sem = "ar%d_%d" % (t + 1, c)
+            lands = "wl%d_%d" % (t + 1, c)
+
+            def send():
+                sync_for("gp", [r("wo%d" % t)], [], ())
+                g.remote_dma(T.wl[:, w0 + 256:w0 + 256 + CW], wo, T.sem[sem], T.sem.sent, pid, rid, topo.mask(core, nxt))
+                total["sent"] = total.get("sent", 0) + len(topo.engines(core, nxt))
+                total[sem] = len(topo.engines(T.cores[(rank - 1) % nrank], core))
+                wrote[lands] = (sem, total[sem], {}, "net")
+            nodes.append(("gp", send, [r("wo%d" % t)], [lands], [], 1000.0, 1600.0))
+
+        def tally():
+            pp = T["pp%d" % c]
+            op("s", lambda: S.activation(pp[:, 256:384], pp[:, 128:256], AF.Copy, accum_out=T.cnt[:, c:c + 1]), [r("P")], [r("cnt"), r("junk")])
+
+        return {"gather_w": gather_w, "wcopy": wcopy, "wwin": wwin, "pwin": pwin, "weigh": weigh, "relator": relator,
+                "gather_r": gather_r, "tail": tail, "keys_r": keys_r, "biggest": biggest, "keys_m": keys_m, "least": least,
+                "turn_list": turn_list, "gather_q": gather_q, "sizes": sizes, "halves": halves, "unpack": unpack, "match": match,
+                "write_x": write_x, "moves": moves, "turned": turned, "renew": renew, "tally": tally, "spread": spread, "letters": letters}
+
+    def allow():
+        o = T.ps4[:, 264:265]
+        mm(o, T.g8[:], T.cnt[:, 0:1], ["g8", "cnt_0"], "ps4", True, False, "A")
+        mm(o, T.g8[:], T.cnt[:, 1:2], ["g8", "cnt_1"], "ps4", False, True, "A")
+        cp(T.ai[:, 0:1], o, ["A"], ["ai"], ["ps4"])
+        ts(T.aj[:, 0:1], T.ai[:, 0:1], 31, OP.bitwise_and, ["ai"], ["aj"])
+        ts(col(10), T.aj[:, 0:1], 8.0, OP.mult, ["aj", "thf"], ["thr"], (), col(8), OP.add)
+
+    for t in range(VIS):
+        a, b = stages(t, 0), stages(t, 1)
+        once = {"constants_1": constants_1, "constants_2": constants_2, "constants_3": constants_3, "tables": tables, "rows": rows}
+        for word in (ORDER if t > 0 else FIRST).split():
+            label.extend([now[0]] * (len(nodes) - len(label)))
+            now[0] = ("" if t > 0 else "0") + word.partition(":")[0]
+            name, _, arg = word.partition(":")
+            if name in once:
+                if t == 0:
+                    once[name]()
+            elif name == "allow":
+                if t > 0:
+                    allow()
+            elif name.endswith(".tally") and t == VIS - 1:
+                pass
+            else:
+                part = (a if name[0] == "a" else b)[name[2:]]
+                if arg == "":
+                    part()
+                elif len(arg) == 1:
+                    part(int(arg))
+                else:
+                    part(int(arg[0]), arg[1])
+
+    dmas("sy", [lambda: SY.dma_start(T.yx[:, 0:2048], T.xs[:, 0:2048]), lambda: SY.dma_start(T.yx[:, 2048:4096], T.xs[:, 2048:4096])],
+         "outx", XR, [])
+    dmas("sy", [lambda: SY.dma_start(T.yw[:], T.ywf[:])], "outw", ["yw_0", "yw_1"], [])
+    label.extend([""] * (len(nodes) - len(label)))
+    for i in plan():
+        nodes[i][1]()
+    for sem, val in total.items():
+        g.wait_ge(T.sem[sem], val)

@@ -3,49 +3,56 @@ from concourse.mybir import dt, AluOpType as OP, AxisListType, ActivationFunctio
 VIS = 6
 NC = 2
 CW = 128
-CYCLE, FIXED, MM, GATHER, SCATTER = 0.83, 20.0, 0.0, 1.7, 3.5
-OWN, WAKE, LOOK = 180.0, 250.0, 60.0
-QV = 1536
-BIAS = {
-    "rows": -8.0, "constants_3": -8.0, "allow": -1.5,
-    "a.wcopy": -1.5, "a.wwin": 0.7, "a.gather_w": -0.7, "a.weigh": -3.0, "a.gather_r": -3.0, "a.letters": 0.7, "a.tail": 0.7, "a.pwin": -1.5,
-    "a.keys_r": 6.0, "a.least": -1.5, "a.turn_list": -3.0, "a.sizes": 0.7, "a.unpack": 3.0, "a.moves": -1.5, "a.tally": -3.0, "a.write_x": 3.0,
-    "b.wcopy": -0.7, "b.gather_w": -6.0, "b.spread": 3.0, "b.gather_r": -0.7, "b.letters": 3.0, "b.pwin": -3.0, "b.turn_list": -6.0,
-    "b.halves": -6.0, "b.unpack": -3.0, "b.turned": 1.5, "b.tally": 3.0, "b.write_x": -3.0}
+WHOLE = 1.5 * 2 ** 23
+CYCLE, PECYCLE, GATHER, SCATTER = 0.83, 0.46, 1.56, 3.8
+OWN, WAKE, DMA = 130.0, 190.0, 2.0
+GR = [[(512 * n, 512 * n + 512, q) for n, q in enumerate(qs)] for qs in ("vssv", "svss")]
+MJ = (8, 10)
+GW = [[(512 * n, 512 * n + 512, q) for n, q in enumerate(qs)] for qs in ("saas", "asaa")]
+ROUNDS = 1
+SPAN = []
 
 ORDER = """
-a.wcopy a.wwin a.gather_w:1v a.gather_w:0s a.weigh a.relator b.gather_w:1s a.spread b.gather_w:0v a.gather_r:0 b.wcopy b.wwin a.letters
-a.gather_r:1 b.weigh a.tail a.pwin a.keys_r b.relator a.biggest:9 a.keys_m b.gather_r:0 b.gather_r:1v b.letters
-a.least a.gather_q:0 b.spread a.gather_q:1 allow b.tail b.pwin a.turn_list b.biggest:9 b.keys_r a.sizes:0 b.keys_m a.sizes:1
-b.least a.halves a.match b.gather_q:0 a.moves a.turned b.gather_q:1 a.unpack b.turn_list b.sizes:0
-a.renew b.sizes:1 b.halves b.match b.moves a.write_x a.tally b.write_x b.unpack b.turned b.renew b.tally
+b.first a.first a.weigh a.relator a.gather_r:2 -b.tally -b.turned a.gather_r:3 a.wwin -b.masks -b.renew a.letters b.wwin b.weigh b.relator b.gather_r:0 b.spread a.gather_r:0 b.gather_r:1 a.gather_r:1 a.spread a.biggest a.apart:1 a.tail a.apart:0 b.gather_r:2 b.gather_r:3 b.apart:0 b.letters a.keys b.tail a.least a.turn b.biggest a.gather_w:2 b.apart:1 b.keys b.least allow a.limit a.halves a.gather_w:1 a.gather_w:0 b.turn b.gather_w:3 a.pwin a.unpack a.sizes:0 b.pwin b.gather_w:1 a.gather_w:3 a.sizes:1 b.gather_w:0 b.halves a.match a.offer b.gather_w:2 a.lead a.turned b.sizes:0 b.sizes:1 b.unpack b.offer b.limit a.tally b.match b.aim b.lead a.masks a.renew a.aim a.write_x b.write_x
 """
-FIRST = "constants_1 constants_3 tables rows constants_2 " + ORDER.replace(" allow", "")
+ONCE = {"first": "constants_1 start", "spread": "constants_3 rows", "letters": "tables", "tail": "tables", "limit": "limits",
+        "gather_w": "constants_2", "halves": "constants_2", "offer": "constants_2"}
 
 SCRATCH = {
-    "xs": ("sbuf", [128, 4352], "bfloat16"),
+    "xs": ("sbuf", [128, 8192], "bfloat16"),
     "rts": ("sbuf", [128, 2048], "int32"),
     "wdi": ("sbuf", [128, 256], "int32"),
     "wti": ("sbuf", [128, 2], "int32"),
     "thi": ("sbuf", [128, 2], "int32"),
-    "wl": ("sbuf", [128, 256 * VIS], "uint16"),
-    "wo": ("sbuf", [128, 256 * VIS], "uint16"),
+    "wl": ("sbuf", [128, NC * CW * VIS], "float32"),
+    "wo": ("sbuf", [128, NC * CW * VIS], "float32"),
+    "ll": ("sbuf", [128, NC * 8 * VIS], "uint16"),
+    "lo": ("sbuf", [128, NC * 8 * VIS], "uint16"),
+    "b0h": ("sbuf", [128, 288], "float16"),
+    "cw": ("sbuf", [128, 128], "float32"),
+    "ct": ("sbuf", [128, 128], "float32"),
+    "cc": ("sbuf", [128, 128], "float32"),
+    "mc": ("sbuf", [128, 128], "bfloat16"),
+    "q1": ("sbuf", [128, 128], "bfloat16"),
     "ywf": ("sbuf", [128, 256], "float32"),
     "nvi": ("sbuf", [128, 256], "int32"),
     "ones": ("sbuf", [128, 256], "bfloat16"),
     "zerf": ("sbuf", [128, 128], "float32"),
-    "blk": ("sbuf", [128, 128], "bfloat16"),
-    "blk0": ("sbuf", [128, 128], "bfloat16"),
-    "i2": ("sbuf", [128, 256], "bfloat16"),
-    "an2": ("sbuf", [128, 256], "bfloat16"),
-    "i2h": ("sbuf", [128, 256], "float16"),
-    "an2h": ("sbuf", [128, 256], "float16"),
-    "hid": ("sbuf", [128, 128], "bfloat16"),
+    "blk": ("sbuf", [128, 256], "bfloat16"),
+    "blk0": ("sbuf", [128, 256], "bfloat16"),
+    "idn": ("sbuf", [128, 128], "bfloat16"),
+    "an": ("sbuf", [128, 128], "bfloat16"),
+    "idh": ("sbuf", [128, 128], "float16"),
+    "anh": ("sbuf", [128, 128], "float16"),
+    "nih": ("sbuf", [128, 128], "float16"),
+    "n16h": ("sbuf", [128, 128], "float16"),
     "ni": ("sbuf", [128, 128], "bfloat16"),
-    "wbh": ("sbuf", [128, 128], "bfloat16"),
-    "wbl": ("sbuf", [128, 128], "bfloat16"),
-    "wa": ("sbuf", [128, 2], "int32"),
-    "tri": ("sbuf", [128, 128], "bfloat16"),
+    "pa": ("sbuf", [128, 256], "bfloat16"),
+    "pb": ("sbuf", [128, 256], "bfloat16"),
+    "pc": ("sbuf", [128, 256], "bfloat16"),
+    "pd": ("sbuf", [128, 256], "bfloat16"),
+    "rvh": ("sbuf", [128, 256], "float16"),
+    "shh": ("sbuf", [128, 256], "float16"),
     "m3": ("sbuf", [128, 128], "bfloat16"),
     "e8": ("sbuf", [128, 128], "bfloat16"),
     "m1a": ("sbuf", [128, 128], "bfloat16"),
@@ -53,78 +60,76 @@ SCRATCH = {
     "m2a": ("sbuf", [128, 128], "bfloat16"),
     "m2b": ("sbuf", [128, 128], "bfloat16"),
     "m2": ("sbuf", [128, 128], "bfloat16"),
+    "m1b": ("sbuf", [128, 128], "bfloat16"),
     "g8": ("sbuf", [128, 128], "float32"),
     "b0": ("sbuf", [128, 144], "bfloat16"),
+    "b2": ("sbuf", [128, 144], "bfloat16"),
+    "bn": ("sbuf", [128, 144], "bfloat16"),
     "c0": ("sbuf", [128, 144], "bfloat16"),
-    "m1b": ("sbuf", [128, 128], "bfloat16"),
+    "c8": ("sbuf", [128, 144], "bfloat16"),
+    "z0h": ("sbuf", [128, 144], "float16"),
+    "wt0": ("sbuf", [128, 144], "float16"),
     "tabr": ("sbuf", [128, 2048], "float32"),
     "tabc": ("sbuf", [128, 2048], "float32"),
-    "tabi": ("sbuf", [128, 2048], "int32"),
-
+    "tabi": ("sbuf", [128, 2048], "float32"),
     "bm": ("sbuf", [128, 2048], "bfloat16"),
     "bmh": ("sbuf", [128, 2048], "float16"),
     "k2h": ("sbuf", [128, 128], "float16"),
     "oneh": ("sbuf", [128, 128], "float16"),
-    "y0": ("sbuf", [128, 8], "float16"),
-    "y1": ("sbuf", [128, 8], "float16"),
-    "wt0": ("sbuf", [128, 144], "float16"),
-    "wb": ("sbuf", [128, 128], "float16"),
-    "s32": ("sbuf", [128, 8], "bfloat16"),
-    "s16": ("sbuf", [128, 8], "bfloat16"),
-    "s128": ("sbuf", [128, 8], "bfloat16"),
+    "s2": ("sbuf", [128, 8], "bfloat16"),
+    "sn": ("sbuf", [128, 8], "bfloat16"),
+    "sx0": ("sbuf", [128, 128], "float16"),
+    "sx1": ("sbuf", [128, 128], "float16"),
     "kt": ("sbuf", [128, 128], "bfloat16"),
-    "row16": ("sbuf", [128, 128], "bfloat16"),
+    "ktk": ("sbuf", [128, 128], "bfloat16"),
     "md": ("sbuf", [128, 128], "bfloat16"),
     "rs": ("sbuf", [128, 128], "float32"),
     "keep": ("sbuf", [128, 128], "bfloat16"),
     "pi": ("sbuf", [128, 2], "int32"),
     "pj": ("sbuf", [128, 2], "int32"),
     "cols": ("sbuf", [128, 64], "float32"),
-    "ihi": ("sbuf", [128, 8], "float32"),
-    "it": ("sbuf", [128, 8], "bfloat16"),
-    "m128": ("sbuf", [128, 8], "bfloat16"),
     "itg": ("sbuf", [128, 16], "float32"),
-    "itf": ("sbuf", [128, 16], "float32"),
-    "ite": ("sbuf", [128, 16], "float32"),
-    "itd": ("sbuf", [128, 16], "float32"),
+    "rl": ("sbuf", [128, 32], "bfloat16"),
+    "cl": ("sbuf", [128, 32], "bfloat16"),
+    "row": ("sbuf", [128, 32], "bfloat16"),
+    "rh": ("sbuf", [128, 8], "float16"),
+    "ata": ("sbuf", [128, 16], "float32"),
+    "ath": ("sbuf", [128, 16], "float16"),
+    "two": ("sbuf", [128, 48], "float32"),
+    "txh": ("sbuf", [128, 8], "float16"),
+    "tx": ("sbuf", [128, 8], "float32"),
+    "dx": ("dram", [8, 32, 8], "float32"),
+    "tw": ("sbuf", [128, 128], "float32"),
     "cnt": ("sbuf", [128, 2], "float32"),
     "ai": ("sbuf", [128, 2], "int32"),
     "aj": ("sbuf", [128, 2], "int32"),
 }
 for _c in range(NC):
     SCRATCH.update({
-        "xw%d" % _c: ("sbuf", [128, 2048], "bfloat16"),
         "xr%d" % _c: ("sbuf", [128, 2048], "bfloat16"),
         "mx%d" % _c: ("sbuf", [128, 2048], "bfloat16"),
         "df%d" % _c: ("sbuf", [128, 2048], "bfloat16"),
         "ww%d" % _c: ("sbuf", [128, 2048], "float32"),
         "pw%d" % _c: ("sbuf", [128, 2048], "float32"),
         "dw%d" % _c: ("dram", [8, 32, 128], "float32"),
-        "wf%d" % _c: ("sbuf", [128, 128], "float32"),
-        "pk%d" % _c: ("sbuf", [128, 128], "float32"),
         "dp%d" % _c: ("dram", [8, 32, 128], "float32"),
-        "x0%d" % _c: ("sbuf", [128, 128], "float16"),
-        "ti%d" % _c: ("sbuf", [128, 1024], "int32"),
-        "tf%d" % _c: ("sbuf", [128, 512], "float32"),
+        "pk%d" % _c: ("sbuf", [128, 128], "float32"),
+        "ti%d" % _c: ("sbuf", [128, 640], "int32"),
+        "tf%d" % _c: ("sbuf", [128, 640], "float32"),
+        "tb%d" % _c: ("sbuf", [128, 1024], "bfloat16"),
+        "hh%d" % _c: ("sbuf", [128, 768], "float16"),
         "ui%d" % _c: ("sbuf", [128, 64], "int32"),
-        "uf%d" % _c: ("sbuf", [128, 64], "float32"),
+        "uf%d" % _c: ("sbuf", [128, 16], "float32"),
+        "uh%d" % _c: ("sbuf", [128, 16], "float16"),
         "ls%d" % _c: ("sbuf", [128, 64], "uint16"),
-        "r16%d" % _c: ("sbuf", [128, 128], "uint16"),
-        "l2%d" % _c: ("sbuf", [128, 128], "uint16"),
-        "sc%d" % _c: ("sbuf", [128, 128], "float32"),
-        "zs%d" % _c: ("sbuf", [128, 128], "bfloat16"),
-        "sb%d" % _c: ("sbuf", [128, 384], "bfloat16"),
-        "pp%d" % _c: ("sbuf", [128, 384], "bfloat16"),
-        "tl%d" % _c: ("sbuf", [128, 128], "int32"),
-        "ff%d" % _c: ("sbuf", [128, 384], "float32"),
-        "ph%d" % _c: ("sbuf", [128, 384], "float16"),
+        "lu%d" % _c: ("sbuf", [128, 256], "uint16"),
     })
 for _b in range(8):
     SCRATCH["ps%d" % _b] = ("psum", [128, 512], "float32")
 
-SEMAPHORES = ["v", "s", "pe", "gp", "sent", "dacc", "ldx", "ldx2", "ldr", "ldw", "ldt", "ldh", "outw", "outx"]
+SEMAPHORES = ["v", "s", "pe", "gp", "sent", "dacc", "ldx", "ldr", "ldw", "ldt", "ldh", "outw", "outx", "dx1", "dx2"]
 SEMAPHORES += ["d%s%d%d" % (w, st, c) for w in "wp" for st in (1, 2) for c in range(NC)]
-SEMAPHORES += ["ar%d_%d" % (t, c) for t in range(1, VIS) for c in range(NC)]
+SEMAPHORES += ["%s%d_%d" % (w, t, c) for w in ("ar", "al") for t in range(1, VIS) for c in range(NC)]
 
 
 def rank_program(g, core, T, topo):
@@ -186,25 +191,29 @@ def rank_program(g, core, T, topo):
             total[q] = total.get(q, 0) + 1
             call().then_inc(T.sem[q], 1)
             note(q, (q, total[q], dict(know[q]), q), reads, writes, banks)
-        nodes.append((q, emit, list(reads), list(writes), list(banks), cost, 0.0))
+        nodes.append((q, emit, list(reads), list(writes), list(banks), cost, 60.0 if q == "pe" else 0.0))
 
-    def dmas(q, calls, sem, reads, writes, extra=2300.0):
+    moving = {}
+
+    def dmas(q, calls, sem, reads, writes, kib=64):
         def emit():
             sync_for(q, reads, writes, ())
             for call in calls:
                 total[sem] = total.get(sem, 0) + 16
                 call().then_inc(T.sem[sem], 16)
             note(q, (sem, total[sem], dict(know[q]), "dma"), reads, writes, ())
-        nodes.append((q, emit, list(reads), list(writes), [], 70.0 * len(calls), extra))
+        moving[len(nodes)] = 100.0 + DMA * kib
+        issue = (900.0 if q == "gp" else 60.0) * len(calls)
+        nodes.append((q, emit, list(reads), list(writes), [], issue, 600.0))
 
     def span(ap):
         return ap.shape[1]
 
     def vcost(n, kind, wide):
-        return {"": FIXED + max(64, n * wide) * CYCLE, "g": FIXED + n * GATHER * CYCLE, "s": FIXED + n * SCATTER * CYCLE}[kind]
+        return {"": max(64, n * wide) * CYCLE, "h": max(64, n / 2) * CYCLE, "g": 50 + n * GATHER * CYCLE, "s": 50 + n * SCATTER * CYCLE}[kind]
 
     def mm(out, lhsT, rhs, reads, bank, start=True, stop=True, tag=None):
-        op("pe", lambda: PE.matmul(out, lhsT, rhs, start, stop), reads, [tag] if tag else [], [bank], MM + max(64, span(rhs)) * CYCLE * 0.7)
+        op("pe", lambda: PE.matmul(out, lhsT, rhs, start, stop), reads, [tag] if tag else [], [bank], max(64, span(rhs)) * PECYCLE)
 
     def tt(out, a, b, o, reads, writes, banks=(), kind=""):
         op("v", lambda: V.tensor_tensor(out, a, b, o), reads, writes, banks, vcost(span(out), kind, 1 if banks else 2))
@@ -218,6 +227,12 @@ def rank_program(g, core, T, topo):
 
     def cp(out, a, reads, writes, banks=(), kind=""):
         op("v", lambda: V.tensor_copy(out, a), reads, writes, banks, vcost(span(a if kind == "s" else out), kind, 1))
+
+    def scan(out, a, b, first, o0, o1, reads, writes, banks=(), kind=""):
+        op("v", lambda: V.tensor_tensor_scan(out, a, b, first, o0, o1), reads, writes, banks, vcost(span(out), kind, 1))
+
+    def fill(out, value, name):
+        op("v", lambda: V.memset(out, value), [], [name], (), vcost(span(out), "h", 1))
 
     def act(out, a, f, reads, writes, banks=(), kind="", **more):
         op("s", lambda: S.activation(out, a, f, **more), reads, writes, banks, vcost(span(out), kind, 1) + 30.0)
@@ -244,410 +259,477 @@ def rank_program(g, core, T, topo):
                     if j != i and (q2 != q or q == "pe"):
                         edge(j, q2 != q)
                 bk[b][q] = i
-        succs = [[] for _ in range(n)]
-        left = [len(p) for p in preds]
-        for i, p in enumerate(preds):
-            for j, hard in p.items():
-                succs[j].append((i, hard))
+        where, cost, ins, ids, ends = [], [], [], [], []
+        for i, node in enumerate(nodes):
+            ids.append(len(where))
+            where.append(node[0])
+            cost.append(node[5])
+            ins.append([(ends[j], nodes[j][6] + (OWN if nodes[j][0] == node[0] and j not in moving else WAKE)) if hard else (ids[j], 0.0)
+                        for j, hard in preds[i].items()])
+            if i in moving:
+                where.append("engines")
+                cost.append(moving[i])
+                ins.append([(ids[i], max(900.0 - node[5], 900.0 - moving[i]))])
+            ends.append(len(where) - 1)
+        m = len(where)
+        outs = [[] for _ in range(m)]
+        for i in range(m):
+            for j, lag in ins[i]:
+                outs[j].append((i, lag))
 
-        def lag(j, i, hard):
-            return (nodes[j][6] + (OWN if nodes[j][0] == nodes[i][0] else WAKE)) if hard else 0.0
-        prio = [0.0] * n
-        for i in range(n - 1, -1, -1):
-            prio[i] = nodes[i][5] + max([prio[k] + lag(i, k, hard) for k, hard in succs[i]] + [0.0])
-        for i in range(n):
-            prio[i] += 1000.0 * BIAS.get(label[i], 0.0)
-        ready = {q: [] for q in queue}
-        at = [0.0] * n
-        free = {q: 0.0 for q in queue}
-        for i in range(n):
-            if left[i] == 0:
-                ready[nodes[i][0]].append(i)
-        order = []
-        while len(order) < n:
-            best = None
-            for q, c in ready.items():
-                if c:
-                    t0 = min(max(free[q], at[i]) for i in c)
-                    if best is None or t0 < best[0]:
-                        best = (t0, q)
-            t0, q = best
-            i = max((i for i in ready[q] if max(free[q], at[i]) <= t0 + LOOK), key=lambda z: prio[z] - (max(free[q], at[z]) - t0))
-            ready[q].remove(i)
-            t1 = max(free[q], at[i])
-            free[q] = t1 + nodes[i][5]
-            order.append(i)
-            for k, hard in succs[i]:
-                at[k] = max(at[k], free[q] + lag(i, k, hard) if hard else t1)
-                left[k] -= 1
-                if left[k] == 0:
-                    ready[nodes[k][0]].append(k)
-        return order
+        def place(order, before):
+            end, busy = [0.0] * m, {}
+            for i in order:
+                t = max([end[j] + lag for j, lag in before[i]] + [0.0])
+                los, his = busy.setdefault(where[i], ([], []))
+                a, b = 0, len(his)
+                while a < b:
+                    mid = (a + b) // 2
+                    a, b = (mid + 1, b) if his[mid] <= t else (a, mid)
+                while a < len(los) and los[a] < t + cost[i]:
+                    t = his[a]
+                    a += 1
+                los.insert(a, t)
+                his.insert(a, t + cost[i])
+                end[i] = t + cost[i]
+            return end
+
+        key = list(range(m))
+        best = None
+        for _ in range(ROUNDS):
+            end = place(sorted(range(m), key=lambda z: key[z]), ins)
+            if best is None or max(end) < max(best):
+                best = end
+            back = place(sorted(range(m), key=lambda z: (-end[z], -z)), outs)
+            key = [-back[i] + 1e-7 * i for i in range(m)]
+        SPAN.append((max(best), nodes, label))
+        return sorted(range(n), key=lambda z: (best[ids[z]] - cost[ids[z]], z))
 
     dmas("sy", [lambda: SY.dma_start(T.wdi[:], T.wd[:])], "ldw", [], ["wdi"])
-    dmas("s", [lambda: S.dma_start(T.xs[:, 0:2048], T.x[:, 0:2048])], "ldx", [], ["x_lo"], 4000.0)
-    dmas("sy", [lambda: SY.dma_start(T.xs[:, 2048:4096], T.x[:, 2048:4096])], "ldx2", [], ["x_hi"], 4000.0)
-    dmas("sy", [lambda: SY.dma_start(T.wti[:, 0:1], T.wt[:])], "ldt", [], ["wti"])
-    dmas("sy", [lambda: SY.dma_start(T.rts[:], T.rt[:])], "ldr", [], ["rts"], 6000.0)
+    dmas("s", [lambda: S.dma_start(T.wti[:, 0:1], T.wt[:])], "ldt", [], ["wti"], 1)
+    dmas("sy", [lambda: SY.dma_start(T.rts[:], T.rt[:])], "ldr", [], ["rts"], 1024)
+    dmas("sy", [lambda: SY.dma_start(T.xs[:, 0:4096], T.x[:])], "ldx", [], ["x_lo", "x_hi"], 1024)
     dmas("sy", [lambda: SY.dma_start(T.thi[:, 0:1], T.th[:])], "ldh", [], ["thi"])
 
     def col(n):
         return T.cols[:, n:n + 1]
 
-    def sel(out, in_, pattern, cmp, fill, base, cm, reads, writes):
-        op("gp", lambda: g.affine_select(out, in_, pattern, cmp, fill, base, cm), reads, writes, (), 170.0 + 2 * span(out) * CYCLE)
+    def sel(out, in_, pattern, cmp, fill_, base, cm, reads, writes):
+        op("gp", lambda: g.affine_select(out, in_, pattern, cmp, fill_, base, cm), reads, writes, (), 170.0 + 2 * span(out) * CYCLE)
 
-    op("v", lambda: V.memset(T.ones[:], 1.0), [], ["ones"])
-    op("gp", lambda: g.iota(T.pi[:], [[0, 2]], 0, 1), [], ["pi"])
-    sel(T.blk0[:], T.ones[:, 0:128], [[-16, 8], [0, 16]], OP.is_ge, 0.0, 0, 1, ["ones"], ["blk0"])
-    sel(T.blk[:], T.blk0[:], [[16, 8], [0, 16]], OP.is_ge, 0.0, 15, -1, ["blk0"], ["blk"])
-    sel(T.i2[:], T.ones[:], [[0, 2], [-1, 128]], OP.is_equal, 0.0, 0, 1, ["ones"], ["i2"])
-    op("v", lambda: V.memset(T.zerf[:], 0.0), [], ["zerf"])
-    op("v", lambda: V.memset(T.b0[:], 0.0), [], ["b0"])
-    for c in range(NC):
-        op("v", (lambda c: lambda: V.memset(T["zs%d" % c][:], 1.0))(c), [], ["zs%d" % c])
-    ts(T.pj[:], T.pi[:], 15, OP.bitwise_and, ["pi"], ["pj"])
-    cp(col(0), T.pj[:, 0:1], ["pj"], ["k0"])
-    op("gp", lambda: g.iota(T.kt[:], [[0, 8], [1, 16]], 0, 0, allow_small_or_imprecise_dtypes=True), [], ["kt"])
-    sel(T.keep[:], T.ones[:, 0:128], [[0, 8], [1, 16]], OP.not_equal, 0.0, 0, 0, ["ones"], ["keep"])
-    cp(T.b0[:, 15:143:16], T.blk[:, 0:128:16], ["blk"], ["b0"])
-    cp(T.wl[:, 0:256], T.wdi[:], ["wdi"], ["wl0_0", "wl0_1"])
-    cp(col(1), T.wti[:, 0:1], ["wti"], ["w1"])
-    ts(col(2), col(1), 2048.0, OP.is_ge, ["w1"], ["w2"], (), -4096.0, OP.mult)
-    tt(col(3), col(1), col(2), OP.add, ["w1", "w2"], ["w3"])
-    ts(T.wt0[:], T.b0[:], col(3), OP.mult, ["b0", "w3"], ["wt0"])
-    cp(T.i2h[:], T.i2[:], ["i2"], ["i2h"])
-    ts(T.wa[:, 0:1], T.wti[:, 0:1], 15, OP.bitwise_and, ["wti"], ["wa"])
-    cp(col(12), T.wa[:, 0:1], ["wa"], ["wlo"])
-    tt(col(11), col(1), col(12), OP.subtract, ["w1", "wlo"], ["whi"])
-    ts(T.wbl[:], T.blk[:], col(12), OP.mult, ["blk", "wlo"], ["wbl"])
-    ts(T.wbh[:], T.blk[:], col(11), OP.mult, ["blk", "whi"], ["wbh"])
-    ts(T.md[:], T.kt[:], col(0), OP.is_equal, ["kt", "k0"], ["md"])
-    ts(T.k2h[:], T.ones[:, 0:128], 2048.0, OP.mult, ["ones"], ["k2h"])
-    cp(T.oneh[:], T.ones[:, 0:128], ["ones"], ["oneh"])
+    def iota(out, pattern, name):
+        op("gp", lambda: g.iota(out, pattern, 0, 0, allow_small_or_imprecise_dtypes=True), [], [name], (), 130.0 + 2 * span(out) * CYCLE)
 
-    def tables():
-        ts(T.tabi[:], T.rts[:], 1, OP.bitwise_and, ["rts"], ["tabi"])
-        ts(T.tabc[:], T.tabi[:], -2.0, OP.mult, ["tabi"], ["tabc"], (), -2047.0, OP.add)
-        cp(T.tabr[:], T.rts[:], ["rts"], ["tabr"])
-        dmas("gp", [lambda: g.dma_start(T.tabc[:], T.tabr[:], accum_op=OP.add)], "dacc", ["tabr", "tabc"], ["tabc"], 6000.0)
-
-    def rows():
-        cp(T.bmh[:], T.bm[:], ["bm%d" % n for n in range(8)], ["bmh"])
+    one, blk, s1 = T.ones[:, 0:128], T.blk[:, 0:128], T.blk[:, 0:128:16]
+    UP, DOWN = [[0, 2], [-16, 8], [1, 16]], [[0, 2], [16, 8], [1, 16]]
 
     def constants_1():
+        fill(T.ones[:], 1.0, "ones")
+        op("gp", lambda: g.iota(T.pi[:], [[0, 2]], 0, 1), [], ["pi"])
+        sel(T.blk0[:], T.ones[:], [[0, 2], [-16, 8], [0, 16]], OP.is_ge, 0.0, 0, 1, ["ones"], ["blk0"])
+        sel(T.blk[:], T.blk0[:], [[0, 2], [16, 8], [0, 16]], OP.is_ge, 0.0, 15, -1, ["blk0"], ["blk"])
+        sel(T.idn[:], one, [[-1, 128]], OP.is_equal, 0.0, 0, 1, ["ones"], ["idn"])
+        sel(T.pa[:], T.blk[:], UP, OP.is_equal, 0.0, 0, 1, ["blk"], ["pa"])
+        sel(T.pb[:], T.blk[:], UP, OP.is_equal, 0.0, -16, 1, ["blk"], ["pb"])
+        tt(T.rvh[:], T.pa[:], T.pb[:], OP.add, ["pa", "pb"], ["rvh"])
+        fill(T.zerf[:], 0.0, "zerf")
+        fill(T.b0[:], 0.0, "b0")
+        for c in range(NC):
+            fill(T["tb%d" % c][:, 0:128], 0.0, "zs_%d" % c)
+        ts(T.pj[:], T.pi[:], 15, OP.bitwise_and, ["pi"], ["pj"])
+        cp(col(0), T.pj[:, 0:1], ["pj"], ["k0"])
+        iota(T.kt[:], [[0, 8], [1, 16]], "kt")
+        sel(T.keep[:], one, [[0, 8], [1, 16]], OP.not_equal, 0.0, 0, 0, ["ones"], ["keep"])
+        cp(T.b0[:, 15:143:16], s1, ["blk"], ["b0"])
+        ts(col(13), col(0), 0.0, OP.is_equal, ["k0"], ["q0"])
+        ts(T.z0h[:], T.b0[:], col(13), OP.mult, ["b0", "q0"], ["z0h"])
+        cp(col(1), T.wti[:, 0:1], ["wti"], ["w1"])
+        ts(col(2), col(1), 2048.0, OP.is_ge, ["w1"], ["w2"], (), -4096.0, OP.mult)
+        tt(col(3), col(1), col(2), OP.add, ["w1", "w2"], ["w3"])
+        ts(T.wt0[:], T.b0[:], col(3), OP.mult, ["b0", "w3"], ["wt0"])
+        cp(T.idh[:], T.idn[:], ["idn"], ["idh"], kind="h")
+        ts(T.nih[:], T.idn[:], -1.0, OP.mult, ["idn"], ["nih"], kind="h")
+        ts(T.md[:], T.kt[:], col(0), OP.is_equal, ["kt", "k0"], ["md"])
+        ts(T.k2h[:], one, 2048.0, OP.mult, ["ones"], ["k2h"], kind="h")
+        cp(T.oneh[:], one, ["ones"], ["oneh"], kind="h")
         sel(T.rs[:], T.zerf[:], [[0, 8], [1, 16]], OP.not_equal, 524288.0, 0, 0, ["zerf"], ["rs"])
-        op("gp", lambda: g.iota(T.row16[:], [[16, 128]], 0, 0, allow_small_or_imprecise_dtypes=True), [], ["row16"])
-        op("gp", lambda: g.iota(T.ihi[:], [[16, 8]], 0, 0, allow_small_or_imprecise_dtypes=True), [], ["ihi"])
-        op("gp", lambda: g.iota(T.itg[:], [[16, 16]], 0, 0, allow_small_or_imprecise_dtypes=True), [], ["itg"])
-        sel(T.tri[:], T.blk[:], [[1, 128]], OP.is_ge, 0.0, 0, -1, ["blk"], ["tri"])
-        sel(T.e8[:], T.ones[:, 0:128], [[-16, 8], [0, 16]], OP.is_equal, 0.0, -8, 1, ["ones"], ["e8"])
-        sel(T.an2[:], T.ones[:], [[0, 2], [-16, 8], [1, 16]], OP.is_equal, 0.0, -15, 1, ["ones"], ["an2"])
-        sel(T.m3[:], T.ones[:, 0:128], [[-16, 8], [1, 8], [0, 2]], OP.is_equal, 0.0, -15, 1, ["ones"], ["m3"])
-        ts(T.s32[:], T.blk[:, 0:128:16], 32.0, OP.mult, ["blk"], ["s32"])
-        ts(T.s16[:], T.blk[:, 0:128:16], -16.0, OP.mult, ["blk"], ["s16"])
-        ts(T.s128[:], T.blk[:, 0:128:16], 128.0, OP.mult, ["blk"], ["s128"])
-        ts(T.m128[:], T.ones[:, 0:8], col(0), OP.mult, ["ones", "k0"], ["m128"], (), -128.0, OP.mult)
-        ts(T.it[:], T.ihi[:], col(0), OP.add, ["ihi", "k0"], ["it"])
-        ts(T.hid[:], T.i2[:, 0:128], 0.5, OP.mult, ["i2"], ["hid"])
-        ts(T.ni[:], T.i2[:, 0:128], -1.0, OP.mult, ["i2"], ["ni"])
+        iota(T.itg[:], [[16, 16]], "itg")
+        ts(T.ktk[:], T.kt[:], 7.5, OP.add, ["kt"], ["ktk"], (), 1.0 / 16, OP.mult, kind="h")
+        ts(T.s2[:], s1, 2.0, OP.mult, ["blk"], ["s2"])
+        ts(T.sn[:], s1, -1.0, OP.mult, ["blk"], ["sn"])
+        for c in range(NC):
+            if MJ[c]:
+                sel(T.m1a[:], blk, [[0, 8], [-1, 16]], OP.is_gt, 0.0, MJ[c], 0, ["blk"], ["m1a"])
+                ts(T["sx%d" % c][:], T.m1a[:], -1.0, OP.mult, ["m1a"], ["sx_%d" % c], kind="h")
+        fill(T.cl[:], 0.0, "cl")
+        for n, (scale, base) in enumerate([(2048.0, 960.0), (128.0, 60.0), (128.0, 61.0), (16.0, 7.5)]):
+            ts(T.rl[:, 8 * n:8 * n + 8], s1, scale, OP.mult, ["blk"], ["rl%d" % n])
+            fill(T.row[:, 8 * n:8 * n + 8], base, "row%d" % n)
+        ts(T.cl[:, 0:8], T.itg[:, 0:8], col(0), OP.add, ["itg", "k0", "cl"], ["cl"])
+        ts(T.cl[:, 24:32], T.itg[:, 0:8], col(0), OP.add, ["itg", "k0", "cl"], ["cl"], (), 16.0, OP.mult)
+
+    def tables():
+        cuts = [slice(512 * n, 512 * n + 512) for n in range(4)]
+        for n, a in enumerate(cuts):
+            cp(T.tabr[:, a], T.rts[:, a], ["rts"], ["tabr%d" % n])
+            act(T.pw1[:, a], T.tabr[:, a], AF.Copy, ["tabr%d" % n], ["frac%d" % n], scale=-1.0 / 4096, bias=-2047.0 / 4096)
+        for n, a in enumerate(cuts):
+            ts(T.tabi[:, a], T.rts[:, a], 0.5 - 1.0 / 8192, OP.mult, ["rts"], ["tabi%d" % n], (), WHOLE, OP.add)
+            act(T.tabc[:, a], T.tabi[:, a], AF.Copy, ["tabi%d" % n], ["tabc%d" % n], scale=1.0 / 1024, bias=-WHOLE / 1024 - 2048.0)
+        dmas("gp", [lambda: g.dma_start(T.tabc[:], T.pw1[:], accum_op=OP.add)], "dacc",
+             ["%s%d" % (w, n) for w in ("tabc", "frac") for n in range(4)], ["tabc", "pw_1"], 1024)
+
+    def rows():
+        cp(T.bmh[:], T.bm[:], ["bm%d" % n for n in range(8)], ["bmh"], kind="h")
 
     def constants_3():
         for n in range(8):
             sel(T.bm[:, 256 * n:256 * n + 256], T.ones[:], [[-1, 2], [-16, 8], [0, 16]], OP.is_equal, 0.0, -2 * n, 1, ["ones"], ["bm%d" % n])
 
     def constants_2():
-        cp(col(8), T.thi[:, 0:1], ["thi"], ["thf"])
-        ts(col(4), col(0), 1.0, OP.add, ["k0"], ["k1"])
-        ts(T.itf[:], T.itg[:], col(0), OP.add, ["itg", "k0"], ["itf"], (), 4096.0, OP.add)
-        ts(T.itd[:], T.itg[:], col(0), OP.add, ["itg", "k0"], ["itd"], (), 15.0, OP.mult)
-        ts(T.ite[:], T.itd[:], -4096.0, OP.add, ["itd"], ["ite"])
+        sel(T.e8[:], one, [[-16, 8], [0, 16]], OP.is_equal, 0.0, -8, 1, ["ones"], ["e8"])
+        sel(T.an[:], one, [[-16, 8], [1, 16]], OP.is_equal, 0.0, -15, 1, ["ones"], ["an"])
+        sel(T.m3[:], one, [[-16, 8], [1, 8], [0, 2]], OP.is_equal, 0.0, -15, 1, ["ones"], ["m3"])
+        sel(T.pc[:], T.blk[:], DOWN, OP.is_equal, 0.0, -1, -1, ["blk"], ["pc"])
+        sel(T.pd[:], T.blk[:], DOWN, OP.is_equal, 0.0, 15, -1, ["blk"], ["pd"])
+        tt(T.shh[:], T.pc[:], T.pd[:], OP.add, ["pc", "pd"], ["shh"])
+        ts(T.ni[:], T.idn[:], -1.0, OP.mult, ["idn"], ["ni"], kind="h")
+        ts(T.n16h[:], T.idn[:], -16.0, OP.mult, ["idn"], ["n16h"], kind="h")
+        ts(T.b2[:], T.b0[:], 2.0, OP.mult, ["b0"], ["b2"], kind="h")
+        ts(T.bn[:], T.b0[:], -1.0, OP.mult, ["b0"], ["bn"], kind="h")
+        ts(T.rh[:], T.itg[:, 0:8], col(0), OP.add, ["itg", "k0"], ["rh"], (), 1792.0, OP.add)
+        ts(T.ata[:], T.itg[:], col(0), OP.add, ["itg", "k0"], ["ata"], (), 1409.0, OP.add)
+        ts(T.ath[:], T.ata[:], 16.0, OP.mult, ["ata"], ["ath"])
         ts(col(5), col(0), 8.0, OP.is_equal, ["k0"], ["q8"])
         ts(col(6), col(0), 9.0, OP.is_ge, ["k0"], ["q9"], (), 1.0, OP.add)
         ts(col(7), col(5), -8.0, OP.mult, ["q8"], ["q7"])
         tt(col(9), col(6), col(7), OP.add, ["q9", "q7"], ["qc"])
-        ts(T.c0[:], T.b0[:], col(9), OP.mult, ["b0", "qc"], ["c0"], (), 128.0, OP.mult)
-        ts(T.g8[:], T.ones[:, 0:128], col(5), OP.mult, ["ones", "q8"], ["g8"])
-        cp(T.an2h[:], T.an2[:], ["an2"], ["an2h"])
-        tt(T.m1a[:], T.e8[:], T.i2[:, 0:128], OP.subtract, ["e8", "i2"], ["m1a"])
-        tt(T.m2a[:], T.an2[:, 0:128], T.e8[:], OP.subtract, ["an2", "e8"], ["m2a"])
+        ts(col(14), col(0), 15.0, OP.is_lt, ["k0"], ["qd"], (), -128.0, OP.mult)
+        ts(T.c0[:], T.b0[:], col(9), OP.mult, ["b0", "qc", "qd"], ["c0"], (), col(14), OP.mult)
+        ts(T.c8[:], T.b0[:], col(5), OP.mult, ["b0", "q8"], ["c8"], (), -4096.0, OP.mult)
+        ts(T.g8[:], one, col(5), OP.mult, ["ones", "q8"], ["g8"])
+        cp(T.anh[:], T.an[:], ["an"], ["anh"], kind="h")
+        tt(T.m1a[:], T.e8[:], T.idn[:], OP.subtract, ["e8", "idn"], ["m1a"])
+        tt(T.m2a[:], T.an[:], T.e8[:], OP.subtract, ["an", "e8"], ["m2a"])
         sel(T.m1b[:], T.m1a[:], [[0, 8], [1, 16]], OP.is_ge, 0.0, -8, 0, ["m1a"], ["m1b"])
-        ts(T.m1[:], T.m1b[:], 4096.0, OP.mult, ["m1b"], ["m1"])
+        ts(T.m1[:], T.m1b[:], 4096.0, OP.mult, ["m1b"], ["m1"], kind="h")
         sel(T.m2b[:], T.m2a[:], [[0, 8], [-1, 16]], OP.is_ge, 0.0, 7, 0, ["m2a"], ["m2b"])
         tt(T.m2[:], T.m2b[:], T.m3[:], OP.subtract, ["m2b", "m3"], ["m2"])
+        fill(T.b0h[:], 0.0, "b0h")
+        cp(T.b0h[:, 15:271:16], T.blk[:, 0:256:16], ["blk", "b0h"], ["b0h"])
+        ts(T.cw[:], T.rvh[:, 0:128], col(0), OP.mult, ["rvh", "k0"], ["cw0"], (), 6.5, OP.is_gt)
+        ts(T.ct[:], T.idn[:], col(13), OP.mult, ["idn", "q0"], ["ct"])
+        ts(col(15), col(0), 15.0, OP.is_equal, ["k0"], ["q15"], (), 4096.0, OP.mult)
+        tt(col(16), col(15), col(13), OP.subtract, ["q15", "q0"], ["q16"])
+        ts(T.cc[:], T.idn[:], col(16), OP.mult, ["idn", "q16", "cw0"], ["cc", "cw"])
+        ts(T.q1[:], T.kt[:], 1.0, OP.is_equal, ["kt"], ["q1"], kind="h")
+        sel(T.pa[:, 0:128], blk, DOWN[1:], OP.is_equal, 0.0, -2, -1, ["blk"], ["pa"])
+        tt(T.pb[:, 0:128], T.pa[:, 0:128], T.pc[:, 0:128], OP.subtract, ["pa", "pc"], ["pb"])
+        sel(T.pa[:, 128:256], T.pb[:, 0:128], [[0, 8], [-1, 16]], OP.is_ge, 0.0, 9, 0, ["pb"], ["pa2"])
+        sel(T.pb[:, 128:256], T.m1a[:], [[0, 8], [1, 16]], OP.is_equal, 0.0, -15, 0, ["m1a"], ["pb2"])
+        tt(T.blk0[:, 0:128], T.pa[:, 128:256], T.pb[:, 128:256], OP.add, ["pa2", "pb2", "blk"], ["blk0"])
+        tt(T.mc[:], T.blk0[:, 0:128], T.pd[:, 0:128], OP.add, ["blk0", "pd"], ["mc"])
 
-    XR = ["x_lo", "x_hi"]
+    def window(sem, src, dram, win, start, read, name):
+        dmas("sy", [lambda: SY.dma_start(dram[:, 0:16, :], src), lambda: SY.dma_start(dram[:, 16:32, :], src)], sem % 1, [read], [name + "d"], span(src))
+        dmas("sy", [(lambda k: lambda: SY.dma_start(win[k:128:16, :], dram[:, start(k):start(k) + 16, :]))(k) for k in range(16)],
+             sem % 2, [name + "d"], [name], 8 * span(src))
+
+    def back(k):
+        return (17 - k) % 16
+
+    def limits():
+        ts(T.two[:, 0:16], T.kt[:, 0:16], col(0), OP.add, ["kt", "k0"], ["two0"], (), 15.0, OP.is_lt)
+        ts(T.two[:, 16:32], T.two[:, 0:16], 1.0, OP.add, ["two0"], ["two1"])
+        scan(T.two[:, 32:48], T.two[:, 16:32], T.zerf[:, 0:16], 1.0, OP.mult, OP.add, ["two1", "zerf"], ["two"])
+        fill(T.txh[:], 0.0, "txh")
+        ts(T.txh[:, 0:1], T.thi[:, 0:1], -2048.0, OP.add, ["thi", "txh"], ["txh"])
+        cp(T.txh[:, 1:2], T.two[:, 47:48], ["two", "txh"], ["txh"])
+        mm(T.ps7[:, 0:8], T.rvh[:, 0:128], T.txh[:], ["rvh", "txh"], "ps7", True, True, "ps7d")
+        act(T.tx[:], T.ps7[:, 0:8], AF.Copy, ["ps7d"], ["tx"], ["ps7"])
+        window("dx%d", T.tx[:], T.dx, T.tw, back, "tx", "tw")
+
+    XR, TABR = ["x_lo", "x_hi"], ["tabr%d" % n for n in range(4)]
+    spare = [0]
 
     def stages(t, c):
-        B = ["ps%d" % (4 * c + b) for b in range(4)]
-        P = [T[b] for b in B]
+        X, Y, Z = ["ps%d" % (3 * c + b) for b in range(3)]
+        PX, PY, PZ = T[X], T[Y], T[Z]
         r = lambda name: "%s_%d" % (name, c)
-        xw, xr, mx, df = T["xw%d" % c], T["xr%d" % c], T["mx%d" % c], T["df%d" % c]
-        ti, tf, ui, uf, ls = T["ti%d" % c], T["tf%d" % c], T["ui%d" % c], T["uf%d" % c], T["ls%d" % c]
-        w0 = 256 * t + CW * c
-        wres = "wl%d_%d" % (t, c)
-        TI = lambda n: ti[:, 128 * n:128 * n + 128]
-        TF = lambda n: tf[:, 128 * n:128 * n + 128]
-        UI = lambda n: ui[:, 8 * n:8 * n + 8]
-        UF = lambda n: uf[:, 8 * n:8 * n + 8]
-        LS = lambda n: ls[:, 8 * n:8 * n + 8]
+        xr, mx, df = T["xr%d" % c], T["mx%d" % c], T["df%d" % c]
+        part = lambda name, n, w=128: T["%s%d" % (name, c)][:, w * n:w * n + w]
+        TI, TF, TB, HH = [(lambda name: lambda n: part(name, n))(name) for name in ("ti", "tf", "tb", "hh")]
+        UI, UF, UH, LS = [(lambda name: lambda n: part(name, n, 8))(name) for name in ("ui", "uf", "uh", "ls")]
+        lu, hh, tb = T["lu%d" % c], T["hh%d" % c], T["tb%d" % c]
+        w0, l0 = CW * (NC * t + c), 8 * (NC * t + c)
+        wres, lres = "wl%d_%d" % (t, c), "ll%d_%d" % (t, c)
         last = t == VIS - 1
+        x0 = HH(4)
+        blocks = lambda name, lo, hi: [r("%s%d" % (name, b)) for b in range(lo // 128, hi // 128)]
+        XRS = blocks("xr", 0, 2048)
+        x = T.xs[:, 0:4096]
 
-        def gather_w(h, q):
-            o = xw[:, 1024 * h:1024 * h + 1024]
-            i = T.xs[:, 0:4096].indirect(T.wl[:, w0 + 64 * h:w0 + 64 * h + 64])
-            if q == "s":
-                act(o, i, AF.Copy, XR + [wres], [r("xw%d" % h)], kind="g")
-            else:
-                cp(o, i, XR + [wres], [r("xw%d" % h)], kind="g")
+        shift = 128 - 16 * ((t + 1 + (t + 1) // nrank) - (t + t // nrank))
 
-        def wcopy():
-            ts(T["wf%d" % c][:], T.wl[:, w0:w0 + CW], -2048.0, OP.add, [wres], [r("wf")])
-
-
-        def window(kind, src, win, dram, off):
-            d, w, s = T[dram], T[win], T[src]
-            rs = [r(kind + "f")]
-            dmas("sy", [lambda: SY.dma_start(d[:, 0:16, :], s[:]), lambda: SY.dma_start(d[:, 16:32, :], s[:])],
-                 "d%s1%d" % (kind, c), rs, [r(kind + "d")])
-            dmas("sy", [(lambda k: lambda: SY.dma_start(w[k:128:16, :], d[:, k + off:k + off + 16, :]))(k) for k in range(16)],
-                 "d%s2%d" % (kind, c), [r(kind + "d")], [r(kind + "w")], 5000.0)
-
-        def wwin():
-            window("w", "wf%d" % c, "ww%d" % c, "dw%d" % c, 1)
-
-        def pwin():
-            window("p", "pk%d" % c, "pw%d" % c, "dp%d" % c, 0)
-
-        def pick(src, srcs, banks, tmp, out):
-            a, b2 = TF(tmp), TF(tmp + 1)
-            tt(a, src, T.md[:], OP.mult, srcs + ["md"], [r("f%d" % tmp)], banks)
-            op("v", lambda: V.tensor_tensor_scan(b2, T.keep[:], a, 0.0, OP.mult, OP.add), ["keep", r("f%d" % tmp)], [r("f%d" % (tmp + 1))])
-            return tf[:, 128 * tmp + 143:128 * tmp + 256:16], r("f%d" % (tmp + 1))
-
-        def weigh():
-            x0 = T["x0%d" % c]
-            XW = [r("xw0"), r("xw1")]
-            if c == 0:
-                mm(P[1][:, 8:136], T.wbh[:], xw[:, 0:2048:16], ["wbh"] + XW, B[1], True, False, r("ub"))
-                mm(P[1][:, 8:136], T.wbl[:], xw[:, 0:2048:16], ["wbl"] + XW, B[1], False, True, r("ub"))
-            else:
-                cp(x0[:], xw[:, 0:2048:16], XW, [r("x0")])
-                for m in range(16):
-                    mm(P[1][:, 0:8], T.wt0[:, 15 - m:143 - m], x0[:, m:128:16], ["wt0", r("x0")], B[1], m == 0, m == 15, r("uw"))
-            mm(P[0][:, 0:128], T.i2[:, 0:128], xw[:, 0:2048:16], ["i2"] + XW, B[0], True, True, r("x0p"))
-
-        def relator():
-            if c == 0:
-                src, res = pick(P[1][:, 8:136], [r("ub")], [B[1]], 0, None)
-                cp(UI(0), src, [res], [r("u0")])
-            else:
-                cp(UI(0), P[1][:, 0:8], [r("uw")], [r("u0")], [B[1]])
-            ts(UI(1), UI(0), 4095, OP.bitwise_and, [r("u0")], [r("u1")])
-            ts(T["y%d" % c][:], UI(1), -2048.0, OP.add, [r("u1")], [r("y")])
-            ts(UF(1), UI(1), 3232.0, OP.add, [r("u1")], [r("uz")])
-            tt(UI(2), T["y%d" % c][:], UF(1), OP.mult, [r("y"), r("uz")], [r("u2")])
-            ts(UI(3), UI(2), 5, OP.arith_shift_right, [r("u2")], [r("u3")], (), 2047, OP.bitwise_and)
-            cp(LS(0), UI(3), [r("u3")], [r("cl")])
-            cp(T["r16%d" % c][:], T.rts[:].indirect(LS(0)), ["rts", r("cl")], [r("r16")])
-            ts(UI(4), UI(1), 15, OP.bitwise_and, [r("u1")], [r("u4")])
-
-        def spread():
-            y = T["y%d" % c]
-            mm(P[0][:, 384:512], T.k2h[0:1, :], T.oneh[0:1, :], ["k2h", "oneh"], B[0], True, False, r("us"))
-            for m in range(16):
-                mm(P[0][:, 384 + m:512:16], T.bmh[:, 128 * m:128 * m + 128], y[:], ["bmh", r("y")], B[0], False, m == 15, r("us"))
-
-        def letters():
-            act(TF(0), T.tabr[:].indirect(LS(0)), AF.Copy, ["tabr", r("cl")], [r("f0")], kind="g")
-            act(TF(1), T.tabc[:].indirect(LS(0)), AF.Copy, ["tabc", r("cl")], [r("f1")], kind="g", scale=1.0 / 4096, bias=-2048.0)
-
-        def gather_r(h, q="s"):
-            o = xr[:, 1024 * h:1024 * h + 1024]
-            i = T.xs[:, 0:4096].indirect(T["r16%d" % c][:, 64 * h:64 * h + 64])
-            if q == "s":
-                act(o, i, AF.Copy, XR + [r("r16")], [r("xr%d" % h)], kind="g")
-            else:
-                cp(o, i, XR + [r("r16")], [r("xr%d" % h)], kind="g")
-
-        def tail():
-            tt(TI(0), TF(0), P[0][:, 384:512], OP.mult, [r("f0"), r("us")], [r("t0")], [B[0]])
-            ts(TI(1), TI(0), 5, OP.arith_shift_right, [r("t0")], [r("t1")], (), 4095, OP.bitwise_and)
-            tt(TI(2), TI(1), TF(0), OP.add, [r("t1"), r("f0")], [r("t2")])
-            ts(TI(3), TI(2), 4095, OP.bitwise_and, [r("t2")], [r("t3")])
-            tt(T["pk%d" % c][:], TI(3), TF(1), OP.add, [r("t3"), r("f1")], [r("pf")])
-            tt(UF(2), UI(4), T.ite[:, 8 * c:8 * c + 8], OP.add, [r("u4"), "ite"], [r("e")])
-
-        def keys_r():
-            K = P[1][:, 256:384]
-            mm(K, T.ones[0:1, 0:128], T.kt[0:1, :], ["ones", "kt"], B[1], True, False, r("key"))
-            for j in range(16):
-                mm(P[1][:, 256 + j:384:16], xr[:, j:2048:16], T.s16[:], [r("xr0"), r("xr1"), "s16"], B[1], False, False, r("key"))
-
-        def biggest(h):
-            h0, h1 = (0, 2) if h == 9 else (h, h + 1)
-            hs = range(h0, h1)
-            for j in range(16):
-                a = slice(1024 * h0 + j, 1024 * h1, 16)
-                tt(mx[:, a], xr[:, a], P[0][:, 64 * h0:64 * h1], OP.max, [r("xr%d" % h) for h in hs] + [r("x0p")],
-                   [r("mx%d_%d" % (h, j)) for h in hs] + [r("mz_%d" % j)] * (h1 - 1), [B[0]])
-
-        def keys_m():
-            for j in range(16):
-                mm(P[1][:, 256 + j:384:16], mx[:, j:2048:16], T.s32[:], [r("mx0_%d" % j), r("mx1_%d" % j), r("mz_%d" % j), "s32"], B[1], False, j == 15, r("key"))
-
-        def least():
-            sc, zs, sb = T["sc%d" % c], T["zs%d" % c], T["sb%d" % c]
-            op("v", lambda: V.tensor_tensor_scan(sc[:], T.rs[:], P[1][:, 256:384], 0.0, OP.max, OP.min), ["rs", r("key")], [r("sc")], [B[1]])
-            cp(UI(5), sc[:, 15:128:16], [r("sc")], [r("u5")])
-            ts(UI(6), UI(5), 15, OP.bitwise_and, [r("u5")], [r("u6")])
-            cp(zs[:, 0:128:16], UI(6), [r("u6")], ["zs%d" % c])
-            op("v", lambda: V.tensor_tensor_scan(sb[:, 0:128], T.keep[:], zs[:], 0.0, OP.mult, OP.add), ["keep", "zs%d" % c], [r("sk")])
-            ts(sb[:, 128:256], sb[:, 0:128], 16.0, OP.is_ge, [r("sk")], [r("sk16")], (), -16.0, OP.mult)
-            L = P[2][:, 0:128]
-            mm(L, T.ones[0:1, 0:128], T.row16[0:1, :], ["ones", "row16"], B[2], True, False, r("l2p"))
-            mm(L, sb[:, 0:128], T.i2[:, 0:128], [r("sk"), "i2"], B[2], False, False, r("l2p"))
-            mm(L, sb[:, 128:256], T.i2[:, 0:128], [r("sk16"), "i2"], B[2], False, True, r("l2p"))
-            tt(sb[:, 256:384], sb[:, 0:128], T.md[:], OP.mult, [r("sk"), "md"], [r("skd")])
-            cp(T["l2%d" % c][:], L, [r("l2p")], [r("l2")], [B[2]])
-
-        def turn_list():
-            sb = T["sb%d" % c]
-            o = P[1][:, 136:144]
-            mm(o, sb[:, 256:384], T.s128[:], [r("skd"), "s128"], B[1], True, False, r("slp"))
-            mm(o, T.i2[:, 0:128], T.it[:], ["i2", "it"], B[1], False, False, r("slp"))
-            mm(o, T.i2[:, 0:128], T.m128[:], ["i2", "m128"], B[1], False, True, r("slp"))
-            cp(LS(1), o, [r("slp")], [r("sl")], [B[1]])
-
-        def gather_q(h):
-            lo, hi = 1024 * h, (1024, QV)[h]
-            tt(df[:, lo:hi], xr[:].indirect(T["l2%d" % c][:, lo // 16:hi // 16]), xw[:, lo:hi], OP.subtract,
-               [r("xr0"), r("xr1"), r("l2"), r("xw%d" % h)], [r("df%d" % h)], kind="g")
-            if h == 1:
-                act(df[:, QV:2048], xr[:].indirect(T["l2%d" % c][:, QV // 16:128]), AF.Copy, [r("xr0"), r("xr1"), r("l2")], [r("df2")], kind="g")
-                o = P[3][:, 0:2048 - QV]
-                mm(o, T.i2[:, 0:128], df[:, QV:2048], ["i2", r("df2")], B[3], True, False, r("dq"))
-                mm(o, T.ni[:], xw[:, QV:2048], ["ni", r("xw1")], B[3], False, True, r("dq"))
-                act(mx[:, QV:2048], o, AF.Abs, [r("dq")], [r("mz_%d" % j) for j in range(16)], [B[3]])
-
-        def sizes(h):
-            a = slice(1024 * h, (1024, QV)[h])
-            act(mx[:, a], df[:, a], AF.Abs, [r("df%d" % h)], [r("mx%d_%d" % (h, j)) for j in range(16)])
-            for k in range(16):
-                mm(P[2][:, 128 + 64 * h:192 + 64 * h], T.b0[:, 15 - k:143 - k], mx[:, 1024 * h + k:1024 * h + 1024:16],
-                   ["b0", r("mx%d_%d" % (h, k))] + [r("mz_%d" % k)] * h, B[2], k == 0, k == 15, r("d2"))
-
-        def halves():
-            v = 128 + QV // 16
-            XW = [r("xw0"), r("xw1")]
-            mm(P[0][:, 128:256], T.hid[:], xw[:, 0:2048:16], ["hid"] + XW, B[0], True, False, r("nvp"))
-            mm(P[0][:, 128:v], T.hid[:], xw[:, 15:QV:16], ["hid"] + XW, B[0], False, False, r("nvp"))
-            mm(P[0][:, 128:v], T.hid[:], df[:, 15:QV:16], ["hid", r("df0"), r("df1")], B[0], False, False, r("nvp"))
-            mm(P[0][:, v:256], T.hid[:], df[:, QV + 15:2048:16], ["hid", r("df2")], B[0], False, True, r("nvp"))
-            ts(T.nvi[:, CW * c:CW * c + CW], P[0][:, 128:256], -0.25, OP.add, [r("nvp")], [r("nv")], [B[0]])
-
-        def unpack():
-            pw, ff = T["pw%d" % c], T["ff%d" % c]
-            ts(T["tl%d" % c][:], pw[:].indirect(LS(1)), 1.0 / 8192, OP.add, [r("pw"), r("sl")], [r("tl")], kind="g")
-            tt(ff[:, 128:256], pw[:].indirect(LS(1)), T["tl%d" % c][:], OP.subtract, [r("pw"), r("sl"), r("tl")], [r("rc")], kind="g")
-
-        def match():
-            pp = T["pp%d" % c]
-            ts(pp[:, 0:128], P[2][:, 128:256], col(8 if t == 0 else 10), OP.is_le, [r("d2"), "thf" if t == 0 else "thr"], [r("ag")], [B[2]])
-            mm(P[2][:, 256:384], T.tri[:], pp[:, 0:128], ["tri", r("ag")], B[2], True, True, r("pre"))
-            ts(pp[:, 128:256], P[2][:, 256:384], col(4), OP.is_ge, [r("pre"), "k1"], [r("P")], [B[2]])
-            mm(P[1][:, 384:512], T.e8[:], pp[:, 128:256], ["e8", r("P")], B[1], True, True, r("rep"))
-
-        def write_x():
-            src, res = pick(P[1][:, 384:512], [r("rep")], [B[1]], 2, None)
-            tt(UF(3), src, UF(2), OP.mult, [res, r("e")], [r("er")])
-            tt(UF(4), UF(3), T.itf[:, 8 * c:8 * c + 8], OP.add, [r("er"), "itf"], [r("at")])
-            cp(LS(2), UF(4), [r("at")], [r("al")])
-            cp(T.xs[:].indirect(LS(2)), T.nvi[:, CW * c:CW * c + CW], [r("nv"), r("al")], XR, kind="s")
-
-        def moves():
-            pp = T["pp%d" % c]
-            for m in range(16):
-                mm(P[0][:, 256:264], T.c0[:, 15 - m:143 - m], pp[:, 128 + m:256:16], ["c0", r("P")], B[0], m == 0, False, r("rho"))
-            mm(P[0][:, 256:264], T.i2[:, 0:128], T.it[:], ["i2", "it"], B[0], False, True, r("rho"))
-            Pk = pp[:, 128:256]
-            mm(P[3][:, 0:128], T.m1[:], Pk, ["m1", r("P")], B[3], True, True, r("k1"))
-            mm(P[3][:, 256:384], T.m3[:], Pk, ["m3", r("P")], B[3], True, True, r("k3"))
-            mm(P[3][:, 128:256], T.m2[:], Pk, ["m2", r("P")], B[3], True, False, r("k2"))
-            mm(P[3][:, 128:256], T.ones[0:1, 0:128], T.ones[0:1, 0:128], ["ones"], B[3], False, True, r("k2"))
-
-        def turned():
-            ff = T["ff%d" % c]
-            cp(LS(3), P[0][:, 256:264], [r("rho")], [r("rl")], [B[0]])
-            act(ff[:, 256:384], T["ww%d" % c][:].indirect(LS(3)), AF.Copy, [r("ww"), r("rl")], [r("wr")], kind="g")
-
-        def renew():
-            ff, ph = T["ff%d" % c], T["ph%d" % c]
-            tt(ph[:, 128:256], ff[:, 128:256], P[3][:, 0:128], OP.mult, [r("rc"), r("k1")], [r("h1")], [B[3]])
-            tt(ph[:, 256:384], T["tl%d" % c][:], P[3][:, 256:384], OP.mult, [r("tl"), r("k3")], [r("h2")], [B[3]])
-            tt(ph[:, 0:128], ff[:, 256:384], P[3][:, 128:256], OP.mult, [r("wr"), r("k2")], [r("h0")], [B[3]])
-            d = 0 if last else 16 * ((t + 1 + (t + 1) // nrank) - (t + t // nrank))
-            F = P[2][:, 384:512]
-            mm(F, T.an2h[:, 128 - d:256 - d], ph[:, 128:256], ["an2h", r("h1")], B[2], True, False, r("fin"))
-            mm(F, T.i2h[:, 128 - d:256 - d], ph[:, 256:384], ["i2h", r("h2")], B[2], False, False, r("fin"))
-            mm(F, T.i2h[:, 128 - d:256 - d], ph[:, 0:128], ["i2h", r("h0")], B[2], False, True, r("fin"))
-            if last:
-                ts(T.ywf[:, CW * c:CW * c + CW], F, 2048.0, OP.add, [r("fin")], [r("yw")], [B[2]])
-                return
-            wo = T.wo[:, w0:w0 + CW]
-            ts(wo, F, 2048.0, OP.add, [r("fin")], [r("wo%d" % t)], [B[2]])
+        def send(out, src, name, sem, lands, extra):
             rid, pid, _ = topo.addr(nxt)
-            sem = "ar%d_%d" % (t + 1, c)
-            lands = "wl%d_%d" % (t + 1, c)
 
-            def send():
-                sync_for("gp", [r("wo%d" % t)], [], ())
-                g.remote_dma(T.wl[:, w0 + 256:w0 + 256 + CW], wo, T.sem[sem], T.sem.sent, pid, rid, topo.mask(core, nxt))
+            def emit():
+                sync_for("gp", [name], [], ())
+                g.remote_dma(out, src, T.sem[sem], T.sem.sent, pid, rid, topo.mask(core, nxt))
                 total["sent"] = total.get("sent", 0) + len(topo.engines(core, nxt))
                 total[sem] = len(topo.engines(T.cores[(rank - 1) % nrank], core))
                 wrote[lands] = (sem, total[sem], {}, "net")
-            nodes.append(("gp", send, [r("wo%d" % t)], [lands], [], 1000.0, 1600.0))
+            nodes.append(("gp", emit, [name], [lands], [], 1000.0, extra))
+
+        def start():
+            ts(HH(3), T.wdi[:, CW * c:CW * c + CW], -2048.0, OP.add, ["wdi"], [r("h3")])
+            for m in range(16):
+                mm(PX[:, 8:16], T.z0h[:, 15 - m:143 - m], hh[:, 384 + m:512:16], ["z0h", r("h3")], X, m == 0, m == 15, r("w0p"))
+            ts(T.ll[:, l0:l0 + 8], PX[:, 8:16], 2048.0, OP.add, [r("w0p")], [lres], [X])
+            mm(PZ[:, 384:512], T.rvh[:, 0:128], HH(3), ["rvh", r("h3")], Z, True, True, r("zf"))
+            act(T.wl[:, w0:w0 + 128], PZ[:, 384:512], AF.Copy, [r("zf")], [wres], [Z])
+
+        def first():
+            cp(x0, x.indirect(T.ll[:, l0:l0 + 8]), XR + [lres], [r("x0")], kind="g")
+
+        def offer():
+            o = PX[:, 384:512]
+            mm(o, T.cw[:], T.wl[:, w0:w0 + 128], ["cw", wres], X, True, False, r("cp"))
+            mm(o, T.ct[:], TF(0), ["ct", r("f0")], X, False, False, r("cp"))
+            mm(o, T.cc[:], TF(3), ["cc", r("rc")], X, False, True, r("cp"))
+            cp(HH(3), o, [r("cp")], [r("h3")], [X])
+
+        def lead():
+            o = PY[:, 0:128]
+            mm(o, T.q1[0:1, :], T.ones[0:1, 0:128], ["q1", "ones"], Y, True, False, r("nvp"))
+            mm(o, T.mc[:], TB(6), ["mc", r("P")], Y, False, True, r("nvp"))
+            tt(HH(5), HH(3), o, OP.mult, [r("h3"), r("nvp")], [r("h5")], [Y])
+            for m in range(16):
+                mm(PY[:, 400:408], T.b0h[:, shift + 15 - m:shift + 143 - m], hh[:, 640 + m:768:16], ["b0h", r("h5")], Y, m == 0, m == 15, r("x0p"))
+            ts(T.lo[:, l0:l0 + 8], PY[:, 400:408], 2048.0, OP.add, [r("x0p")], [r("lo%d" % t)], [Y])
+            send(T.ll[:, l0 + 8 * NC:l0 + 8 * NC + 8], T.lo[:, l0:l0 + 8], r("lo%d" % t), "al%d_%d" % (t + 1, c), "ll%d_%d" % (t + 1, c), 1700.0)
+
+        def wwin():
+            window("dw%d" + str(c), T.wl[:, w0:w0 + 128], T["dw%d" % c], T["ww%d" % c], back, wres, r("ww"))
+
+        def pwin():
+            window("dp%d" + str(c), T["pk%d" % c][:], T["dp%d" % c], T["pw%d" % c], lambda k: k + 1, r("pk"), r("pw"))
+
+        def weigh():
+            for m in range(16):
+                mm(PX[:, 0:8], T.wt0[:, 15 - m:143 - m], hh[:, 512 + m:640:16], ["wt0", r("x0")], X, m == 0, m == 15, r("uw"))
+            if MJ[c]:
+                mm(PY[:, 384:512], T.idh[:], x0, ["idh", r("x0")], Y, True, True, r("x0p"))
+
+        def relator():
+            cp(UI(0), PX[:, 0:8], [r("uw")], [r("u0")], [X])
+            ts(UI(1), UI(0), 4095, OP.bitwise_and, [r("u0")], [r("u1")])
+            ts(UH(0), UI(1), -2048.0, OP.add, [r("u1")], [r("y")])
+            ts(UF(0), UI(1), 3232.0, OP.add, [r("u1")], [r("uz")])
+            tt(UI(2), UH(0), UF(0), OP.mult, [r("y"), r("uz")], [r("u2")])
+            ts(UI(3), UI(2), 5, OP.arith_shift_right, [r("u2")], [r("u3")], (), 2047, OP.bitwise_and)
+            cp(LS(1), UI(3), [r("u3")], [r("cl")])
+            cp(lu[:, 0:128], T.rts[:].indirect(LS(1)), ["rts", r("cl")], [r("lr")], kind="g")
+            ts(UH(1), UI(1), 1.0 / 16, OP.mult, [r("u1")], [r("uq")], (), 1025.0 - 15.0 / 32, OP.add)
+
+        def spread():
+            mm(PZ[:, 384:512], T.k2h[0:1, :], T.oneh[0:1, :], ["k2h", "oneh"], Z, True, False, r("zf"))
+            for m in range(16):
+                mm(PZ[:, 384 + m:512:16], T.bmh[:, 128 * m:128 * m + 128], UH(0), ["bmh", r("y")], Z, False, m == 15, r("zf"))
+
+        def gather_r(n):
+            for lo, hi, q in GR[c][n:n + 1]:
+                i = x.indirect(lu[:, lo // 16:hi // 16])
+                if q == "s":
+                    act(xr[:, lo:hi], i, AF.Copy, XR + [r("lr")], blocks("xr", lo, hi), kind="g")
+                else:
+                    cp(xr[:, lo:hi], i, XR + [r("lr")], blocks("xr", lo, hi), kind="g")
+
+        def letters():
+            act(TF(0), T.tabr[:].indirect(LS(1)), AF.Copy, TABR + [r("cl")], [r("f0")], kind="g")
+
+        def tail():
+            tt(TI(0), TF(0), PZ[:, 384:512], OP.mult, [r("f0"), r("zf")], [r("t0")], [Z])
+            ts(TI(1), TI(0), 5, OP.arith_shift_right, [r("t0")], [r("t1")], (), 4095, OP.bitwise_and)
+            tt(TI(2), T.tabr[:].indirect(LS(1)), TI(1), OP.add, TABR + [r("cl"), r("t1")], [r("t2")], kind="g")
+            ts(TI(3), TI(2), 4095, OP.bitwise_and, [r("t2")], [r("t3")])
+            tt(T["pk%d" % c][:], T.tabc[:].indirect(LS(1)), TI(3), OP.add, ["tabc", r("cl"), r("t3")], [r("pk")], kind="g")
+
+        mj = MJ[c]
+
+        def biggest():
+            for j in range(mj):
+                tt(mx[:, 128 * j:128 * j + 128], xr[:, j:2048:16], PY[:, 384:512], OP.max, XRS + [r("x0p")], [r("mx%d" % j)], [Y])
+
+        def apart(n):
+            for j0 in range(mj, 16, 4)[n::2]:
+                js = range(j0, min(j0 + 4, 16))
+                D = "ps%d" % (6 + spare[0] % 2)
+                spare[0] += 1
+                for n, j in enumerate(js):
+                    o = T[D][:, 128 * n:128 * n + 128]
+                    mm(o, T.idn[:], xr[:, j:2048:16], ["idn"] + XRS, D, True, False, D + "d")
+                    mm(o, T.nih[:], x0, ["nih", r("x0")], D, False, True, D + "d")
+                act(mx[:, 128 * j0:128 * (js[-1] + 1)], T[D][:, 0:128 * len(js)], AF.Abs, [D + "d"], [r("mx%d" % j) for j in js], [D])
+
+        def keys():
+            mm(PX[:, 128:256], T.ones[0:1, 0:128], T.ktk[0:1, :], ["ones", "ktk"], X, True, False, r("key"))
+            if mj:
+                mm(PX[:, 128:256], x0, T["sx%d" % c][:], [r("x0"), r("sx")], X, False, False, r("key"))
+            for j in range(mj):
+                mm(PX[:, 128 + j:256:16], xr[:, j:2048:16], T.sn[:], XRS + ["sn"], X, False, False, r("key"))
+            for j in range(16):
+                mm(PX[:, 128 + j:256:16], mx[:, 128 * j:128 * j + 128], T.s2[:] if j < mj else s1, [r("mx%d" % j), "s2", "blk"], X, False, j == 15, r("key"))
+
+        def least():
+            sc = T["tf%d" % c][:, 128 + 15:256:16]
+            scan(TF(1), T.rs[:], PX[:, 128:256], 0.0, OP.max, OP.min, ["rs", r("key")], [r("f1")], [X])
+            cp(UI(5), sc, [r("f1")], [r("u5")])
+            tt(tb[:, 0:128:16], sc, UI(5), OP.subtract, [r("f1"), r("u5")], [r("zs")])
+            scan(TB(1), T.keep[:], TB(0), 0.0, OP.mult, OP.add, ["keep", r("zs")], [r("sk")], kind="h")
+            tt(TB(2), TB(1), T.md[:], OP.mult, [r("sk"), "md"], [r("skd")])
+            o = PX[:, 16:48]
+            mm(o, T.ones[0:1, 0:128], T.row[0:1, :], ["ones"] + ["row%d" % n for n in range(4)], X, True, False, r("slp"))
+            mm(o, T.idn[:], T.cl[:], ["idn", "cl"], X, False, False, r("slp"))
+            mm(o, TB(2), T.rl[:], [r("skd")] + ["rl%d" % n for n in range(4)], X, False, True, r("slp"))
+            cp(T["ls%d" % c][:, 16:48], o, [r("slp")], [r("sl")], [X])
+
+        def turn():
+            ts(lu[:, 128:256], T["ww%d" % c][:].indirect(LS(2)), 2048.0, OP.add, [r("ww"), r("sl")], [r("lw")], kind="g")
+
+        def limit():
+            if t == 0:
+                act(TF(2), T.tw[:].indirect(LS(3)), AF.Copy, ["tw", r("sl")], [r("f2")], kind="g", bias=2048.0)
+            else:
+                act(TF(2), T.tw[:].indirect(LS(3)), AF.Identity, ["tw", r("sl"), "thr"], [r("f2")], kind="g", bias=col(10))
+
+        def gather_w(n):
+            for lo, hi, how in GW[c][n:n + 1]:
+                i = x.indirect(lu[:, 128 + lo // 16:128 + hi // 16])
+                d, m = blocks("df", lo, hi), blocks("mx", lo, hi)
+                if how == "s":
+                    act(df[:, lo:hi], i, AF.Copy, XR + [r("lw")], d, kind="g")
+                    D = "ps%d" % (6 + spare[0] % 2)
+                    spare[0] += 1
+                    o = T[D][:, 0:hi - lo]
+                    mm(o, T.ni[:], xr[:, lo:hi], ["ni"] + blocks("xr", lo, hi), D, True, False, D + "d")
+                    mm(o, T.idn[:], df[:, lo:hi], ["idn"] + d, D, False, True, D + "d")
+                    act(mx[:, lo:hi], o, AF.Abs, [D + "d"], m, [D])
+                    continue
+                tt(df[:, lo:hi], i, xr[:, lo:hi], OP.subtract, XR + [r("lw")] + blocks("xr", lo, hi), d, kind="g")
+                if how == "a":
+                    act(mx[:, lo:hi], df[:, lo:hi], AF.Abs, d, m)
+                else:
+                    ts(mx[:, lo:hi], df[:, lo:hi], 0.0, OP.max, d, m, kind="h")
+
+        def sizes(h):
+            for lo in (1024 * h,):
+                relu = (lo, lo + 1024, "r") in GW[c]
+                o = PY[:, 128 + lo // 16:192 + lo // 16]
+                if relu:
+                    for k in range(16):
+                        mm(o, T.bn[:, 15 - k:143 - k], df[:, lo + k:lo + 1024:16], ["bn"] + blocks("df", lo, lo + 1024), Y, k == 0, False, r("d2"))
+                for k in range(16):
+                    mm(o, (T.b2 if relu else T.b0)[:, 15 - k:143 - k], mx[:, lo + k:lo + 1024:16], ["b0", "b2"] + blocks("mx", lo, lo + 1024),
+                       Y, k == 0 and not relu, k == 15, r("d2"))
+
+        def halves():
+            act(TB(3), xr[:].indirect(LS(5)), AF.Copy, XRS + [r("sl")], [r("q15")], kind="g")
+            mm(PY[:, 0:128], T.idh[:], x0, ["idh", r("x0")], Y, True, False, r("nvp"))
+            mm(PY[:, 0:128], T.idn[:], TB(3), ["idn", r("q15")], Y, False, True, r("nvp"))
+            ts(T.nvi[:, CW * c:CW * c + CW], PY[:, 0:128], 0.5, OP.mult, [r("nvp")], [r("nv")], [Y], -0.25, OP.add)
+
+        def unpack():
+            act(TF(0), T["pw%d" % c][:].indirect(LS(2)), AF.Copy, [r("pw"), r("sl")], [r("f0")], kind="g")
+            ts(TI(4), TF(0), 1.0 / 8192, OP.add, [r("f0")], [r("tl")])
+            tt(TF(3), TF(0), TI(4), OP.subtract, [r("f0"), r("tl")], [r("rc")])
+
+        def match():
+            tt(TB(4), PY[:, 128:256], TF(2), OP.is_gt, [r("d2"), r("f2")], [r("dis")], [Y])
+            tt(TB(5), T.tw[:].indirect(LS(4)), TB(4), OP.mult, ["tw", r("sl"), r("dis")], [r("dw")], kind="g")
+            mm(PY[:, 256:384], blk, TB(5), ["blk", r("dw")], Y, True, True, r("pre"))
+            ts(TB(6), PY[:, 256:384], T.two[:, 47:48], OP.is_lt, [r("pre"), "two"], [r("P")], [Y])
+
+        def aim():
+            o = PX[:, 256:264]
+            mm(o, T.idh[:], T.ath[:, 8 * c:8 * c + 8], ["idh", "ath"], X, True, False, r("atp"))
+            mm(o, T.idh[:], UH(0), ["idh", r("y")], X, False, False, r("atp"))
+            mm(o, T.n16h[:], UH(1), ["n16h", r("uq")], X, False, False, r("atp"))
+            for m in range(16):
+                mm(o, T.c8[:, 15 - m:143 - m], tb[:, 768 + m:896:16], ["c8", r("P")], X, False, m == 15, r("atp"))
+            cp(LS(6), o, [r("atp")], [r("al")], [X])
+
+        def masks():
+            mm(PZ[:, 0:128], T.m1[:], TB(6), ["m1", r("P")], Z, True, True, r("k1"))
+            mm(PZ[:, 256:384], T.m3[:], TB(6), ["m3", r("P")], Z, True, True, r("k3"))
+            mm(PZ[:, 128:256], T.ones[0:1, 0:128], T.ones[0:1, 0:128], ["ones"], Z, True, False, r("k2"))
+            mm(PZ[:, 128:256], T.m2[:], TB(6), ["m2", r("P")], Z, False, True, r("k2"))
+
+        def write_x():
+            cp(T.xs[:].indirect(LS(6)), T.nvi[:, CW * c:CW * c + CW], [r("nv"), r("al")], XR, kind="s")
+
+        def turned():
+            o = PX[:, 264:272]
+            mm(o, T.idh[:], T.rh[:], ["idh", "rh"], X, True, False, r("rho"))
+            for m in range(16):
+                mm(o, T.c0[:, 15 - m:143 - m], tb[:, 768 + m:896:16], ["c0", r("P")], X, False, m == 15, r("rho"))
+            cp(LS(7), o, [r("rho")], [r("rl")], [X])
+            act(TF(4), T["ww%d" % c][:].indirect(LS(7)), AF.Copy, [r("ww"), r("rl")], [r("wr")], kind="g")
+
+        def renew():
+            tt(HH(1), TF(3), PZ[:, 0:128], OP.mult, [r("rc"), r("k1")], [r("h1")], [Z])
+            tt(HH(2), TI(4), PZ[:, 256:384], OP.mult, [r("tl"), r("k3")], [r("h2")], [Z])
+            tt(HH(0), TF(4), PZ[:, 128:256], OP.mult, [r("wr"), r("k2")], [r("h0")], [Z])
+            F = PZ[:, 384:512]
+            flip, same = (T.anh[:], T.idh[:]) if last else (T.shh[:, shift:shift + 128], T.rvh[:, shift:shift + 128])
+            mm(F, flip, HH(1), ["anh", "shh", r("h1")], Z, True, False, r("zf"))
+            mm(F, same, HH(2), ["idh", "rvh", r("h2")], Z, False, False, r("zf"))
+            mm(F, same, HH(0), ["idh", "rvh", r("h0")], Z, False, True, r("zf"))
+            if last:
+                act(T.ywf[:, CW * c:CW * c + CW], F, AF.Copy, [r("zf")], [r("yw")], [Z], bias=2048.0)
+                return
+            act(T.wo[:, w0:w0 + CW], F, AF.Copy, [r("zf")], [r("wo%d" % t)], [Z])
+            send(T.wl[:, w0 + NC * CW:w0 + NC * CW + CW], T.wo[:, w0:w0 + CW], r("wo%d" % t), "ar%d_%d" % (t + 1, c), "wl%d_%d" % (t + 1, c), 2700.0)
 
         def tally():
-            pp = T["pp%d" % c]
-            op("s", lambda: S.activation(pp[:, 256:384], pp[:, 128:256], AF.Copy, accum_out=T.cnt[:, c:c + 1]), [r("P")], [r("cnt"), r("junk")])
+            op("s", lambda: S.activation(TB(7), TB(6), AF.Copy, accum_out=T.cnt[:, c:c + 1]), [r("P")], [r("cnt"), r("junk")], (), 160.0)
 
-        return {"gather_w": gather_w, "wcopy": wcopy, "wwin": wwin, "pwin": pwin, "weigh": weigh, "relator": relator,
-                "gather_r": gather_r, "tail": tail, "keys_r": keys_r, "biggest": biggest, "keys_m": keys_m, "least": least,
-                "turn_list": turn_list, "gather_q": gather_q, "sizes": sizes, "halves": halves, "unpack": unpack, "match": match,
-                "write_x": write_x, "moves": moves, "turned": turned, "renew": renew, "tally": tally, "spread": spread, "letters": letters}
+        return {"start": start, "first": first, "wwin": wwin, "pwin": pwin, "weigh": weigh, "relator": relator, "spread": spread,
+                "gather_r": gather_r, "letters": letters, "tail": tail, "keys": keys, "least": least, "turn": turn, "gather_w": gather_w,
+                "biggest": biggest, "apart": apart, "limit": limit, "aim": aim, "masks": masks,
+                "sizes": sizes, "halves": halves, "unpack": unpack, "match": match, "write_x": write_x, "turned": turned,
+                "renew": renew, "tally": tally, "offer": offer, "lead": lead}
 
     def allow():
-        o = T.ps4[:, 264:265]
-        mm(o, T.g8[:], T.cnt[:, 0:1], ["g8", "cnt_0"], "ps4", True, False, "A")
-        mm(o, T.g8[:], T.cnt[:, 1:2], ["g8", "cnt_1"], "ps4", False, True, "A")
-        cp(T.ai[:, 0:1], o, ["A"], ["ai"], ["ps4"])
+        o = T.ps0[:, 300:301]
+        mm(o, T.g8[:], T.cnt[:, 0:1], ["g8", "cnt_0"], "ps0", True, False, "A")
+        mm(o, T.g8[:], T.cnt[:, 1:2], ["g8", "cnt_1"], "ps0", False, True, "A")
+        cp(T.ai[:, 0:1], o, ["A"], ["ai"], ["ps0"])
         ts(T.aj[:, 0:1], T.ai[:, 0:1], 31, OP.bitwise_and, ["ai"], ["aj"])
-        ts(col(10), T.aj[:, 0:1], 8.0, OP.mult, ["aj", "thf"], ["thr"], (), col(8), OP.add)
+        ts(col(10), T.aj[:, 0:1], 8.0, OP.mult, ["aj"], ["thr"], (), 2048.0, OP.add)
 
-    for t in range(VIS):
-        a, b = stages(t, 0), stages(t, 1)
-        once = {"constants_1": constants_1, "constants_2": constants_2, "constants_3": constants_3, "tables": tables, "rows": rows}
-        for word in (ORDER if t > 0 else FIRST).split():
+    parts = [{"a": stages(t, 0), "b": stages(t, 1)} for t in range(VIS)]
+    once = {"constants_1": constants_1, "constants_2": constants_2, "constants_3": constants_3, "tables": tables, "rows": rows,
+            "limits": limits, "start": lambda: (parts[0]["a"]["start"](), parts[0]["b"]["start"]())}
+    for t in range(VIS + 1):
+        for word in ORDER.split():
             label.extend([now[0]] * (len(nodes) - len(label)))
-            now[0] = ("" if t > 0 else "0") + word.partition(":")[0]
-            name, _, arg = word.partition(":")
-            if name in once:
-                if t == 0:
-                    once[name]()
-            elif name == "allow":
+            now[0] = (t, word)
+            at = t - 1 if word[0] == "-" else t
+            chunk, _, name = word.lstrip("-").partition(".")
+            name, _, piece = name.partition(":")
+            for first in ONCE.get(name, "").split() if at == 0 else ():
+                once.pop(first, lambda: None)()
+            if not 0 <= at < VIS or (at == VIS - 1 and name in ("tally", "offer", "lead")):
+                continue
+            if chunk == "allow":
                 if t > 0:
                     allow()
-            elif name.endswith(".tally") and t == VIS - 1:
-                pass
+            elif piece:
+                parts[at][chunk][name](int(piece))
             else:
-                part = (a if name[0] == "a" else b)[name[2:]]
-                if arg == "":
-                    part()
-                elif len(arg) == 1:
-                    part(int(arg))
-                else:
-                    part(int(arg[0]), arg[1])
+                parts[at][chunk][name]()
 
     dmas("sy", [lambda: SY.dma_start(T.yx[:, 0:2048], T.xs[:, 0:2048]), lambda: SY.dma_start(T.yx[:, 2048:4096], T.xs[:, 2048:4096])],
          "outx", XR, [])

@@ -3,23 +3,30 @@ from concourse.mybir import dt, AluOpType as OP, AxisListType, ActivationFunctio
 VIS = 6
 NC = 2
 CW = 128
+XW = 2048 + 4096 + 9 * 2048
 WHOLE = 1.5 * 2 ** 23
 CYCLE, PECYCLE, GATHER, SCATTER = 0.83, 0.46, 1.56, 3.8
 OWN, WAKE, DMA = 130.0, 190.0, 2.0
-GR = [[(512 * n, 512 * n + 512, q) for n, q in enumerate(qs)] for qs in ("vssv", "svss")]
+GR = [[(512 * n, 512 * n + 512, q) for n, q in enumerate(qs)] for qs in ("sssv", "ssss")]
 MJ = (8, 10)
-GW = [[(512 * n, 512 * n + 512, q) for n, q in enumerate(qs)] for qs in ("saas", "asaa")]
-ROUNDS = 1
+GW = [[(512 * n, 512 * n + 512, q) for n, q in enumerate(qs)] for qs in ("saaa", "asaa")]
+STEP = {"v": 512, "s": 512}
+JOIN = 4
+ROUNDS = 2
 SPAN = []
 
 ORDER = """
-b.first a.first a.weigh a.relator a.gather_r:2 -b.tally -b.turned a.gather_r:3 a.wwin -b.masks -b.renew a.letters b.wwin b.weigh b.relator b.gather_r:0 b.spread a.gather_r:0 b.gather_r:1 a.gather_r:1 a.spread a.biggest a.apart:1 a.tail a.apart:0 b.gather_r:2 b.gather_r:3 b.apart:0 b.letters a.keys b.tail a.least a.turn b.biggest a.gather_w:2 b.apart:1 b.keys b.least allow a.limit a.halves a.gather_w:1 a.gather_w:0 b.turn b.gather_w:3 a.pwin a.unpack a.sizes:0 b.pwin b.gather_w:1 a.gather_w:3 a.sizes:1 b.gather_w:0 b.halves a.match a.offer b.gather_w:2 a.lead a.turned b.sizes:0 b.sizes:1 b.unpack b.offer b.limit a.tally b.match b.aim b.lead a.masks a.renew a.aim a.write_x b.write_x
+-b.lead a.first b.first -b.tally a.weigh a.relator -b.masks a.gather_r:3 allow -b.turned -b.renew b.weigh a.gather_r:1 a.gather_r:0 b.relator a.gather_r:2 a.biggest a.apart:1 a.wwin a.apart:0 a.keys a.spread a.least b.letters a.limit b.gather_r:0 b.gather_r:2 b.gather_r:3 b.gather_r:1 b.apart:0 b.apart:1 a.turn a.gather_w:1 a.gather_w:3 a.letters a.tail a.gather_w:0 b.spread b.biggest a.gather_w:2 a.pwin b.keys b.tail a.unpack b.least b.halves b.wwin a.sizes:0 b.turn b.gather_w:2 b.gather_w:1 b.pwin a.sizes:1 a.match a.masks a.offer a.lead b.limit b.gather_w:0 b.sizes:0 a.aim b.unpack b.gather_w:3 b.sizes:1 a.turned a.halves a.write_x a.tally a.renew b.aim b.write_x b.offer b.match
 """
-ONCE = {"first": "constants_1 start", "spread": "constants_3 rows", "letters": "tables", "tail": "tables", "limit": "limits",
+ONCE = {"first": "constants_1 start", "weigh": "tables", "spread": "rows", "limit": "limits",
         "gather_w": "constants_2", "halves": "constants_2", "offer": "constants_2"}
+HALF = "vv"
+XFIRST = False
+LEAD = "ff"
+FAST = "sf"
 
 SCRATCH = {
-    "xs": ("sbuf", [128, 8192], "bfloat16"),
+    "xs": ("sbuf", [128, XW], "bfloat16"),
     "rts": ("sbuf", [128, 2048], "int32"),
     "wdi": ("sbuf", [128, 256], "int32"),
     "wti": ("sbuf", [128, 2], "int32"),
@@ -36,6 +43,8 @@ SCRATCH = {
     "q1": ("sbuf", [128, 128], "bfloat16"),
     "ywf": ("sbuf", [128, 256], "float32"),
     "nvi": ("sbuf", [128, 256], "int32"),
+    "nvb": ("sbuf", [128, 256], "bfloat16"),
+    "neg": ("sbuf", [128, 128], "bfloat16"),
     "ones": ("sbuf", [128, 256], "bfloat16"),
     "zerf": ("sbuf", [128, 128], "float32"),
     "blk": ("sbuf", [128, 256], "bfloat16"),
@@ -72,7 +81,6 @@ SCRATCH = {
     "tabr": ("sbuf", [128, 2048], "float32"),
     "tabc": ("sbuf", [128, 2048], "float32"),
     "tabi": ("sbuf", [128, 2048], "float32"),
-    "bm": ("sbuf", [128, 2048], "bfloat16"),
     "bmh": ("sbuf", [128, 2048], "float16"),
     "k2h": ("sbuf", [128, 128], "float16"),
     "oneh": ("sbuf", [128, 128], "float16"),
@@ -89,12 +97,13 @@ SCRATCH = {
     "pj": ("sbuf", [128, 2], "int32"),
     "cols": ("sbuf", [128, 64], "float32"),
     "itg": ("sbuf", [128, 16], "float32"),
-    "rl": ("sbuf", [128, 32], "bfloat16"),
-    "cl": ("sbuf", [128, 32], "bfloat16"),
-    "row": ("sbuf", [128, 32], "bfloat16"),
+    "rl": ("sbuf", [128, 40], "bfloat16"),
+    "cl": ("sbuf", [128, 40], "bfloat16"),
+    "row": ("sbuf", [128, 40], "bfloat16"),
+    "bk": ("sbuf", [128, 144], "bfloat16"),
     "rh": ("sbuf", [128, 8], "float16"),
-    "ata": ("sbuf", [128, 16], "float32"),
-    "ath": ("sbuf", [128, 16], "float16"),
+    "ata": ("sbuf", [128, 8], "float32"),
+    "ath": ("sbuf", [128, 8], "float16"),
     "two": ("sbuf", [128, 48], "float32"),
     "txh": ("sbuf", [128, 8], "float16"),
     "tx": ("sbuf", [128, 8], "float32"),
@@ -115,13 +124,13 @@ for _c in range(NC):
         "dp%d" % _c: ("dram", [8, 32, 128], "float32"),
         "pk%d" % _c: ("sbuf", [128, 128], "float32"),
         "ti%d" % _c: ("sbuf", [128, 640], "int32"),
-        "tf%d" % _c: ("sbuf", [128, 640], "float32"),
-        "tb%d" % _c: ("sbuf", [128, 1024], "bfloat16"),
+        "tf%d" % _c: ("sbuf", [128, 896], "float32"),
+        "tb%d" % _c: ("sbuf", [128, 1152], "bfloat16"),
         "hh%d" % _c: ("sbuf", [128, 768], "float16"),
         "ui%d" % _c: ("sbuf", [128, 64], "int32"),
         "uf%d" % _c: ("sbuf", [128, 16], "float32"),
         "uh%d" % _c: ("sbuf", [128, 16], "float16"),
-        "ls%d" % _c: ("sbuf", [128, 64], "uint16"),
+        "ls%d" % _c: ("sbuf", [128, 72], "uint16"),
         "lu%d" % _c: ("sbuf", [128, 256], "uint16"),
     })
 for _b in range(8):
@@ -202,8 +211,8 @@ def rank_program(g, core, T, topo):
                 total[sem] = total.get(sem, 0) + 16
                 call().then_inc(T.sem[sem], 16)
             note(q, (sem, total[sem], dict(know[q]), "dma"), reads, writes, ())
-        moving[len(nodes)] = 100.0 + DMA * kib
-        issue = (900.0 if q == "gp" else 60.0) * len(calls)
+        issue, busy = (900.0 if q == "gp" else 60.0) * len(calls), 100.0 + DMA * kib
+        moving[len(nodes)] = (busy, 900.0 - min(issue, busy))
         nodes.append((q, emit, list(reads), list(writes), [], issue, 600.0))
 
     def span(ap):
@@ -212,8 +221,19 @@ def rank_program(g, core, T, topo):
     def vcost(n, kind, wide):
         return {"": max(64, n * wide) * CYCLE, "h": max(64, n / 2) * CYCLE, "g": 50 + n * GATHER * CYCLE, "s": 50 + n * SCATTER * CYCLE}[kind]
 
-    def mm(out, lhsT, rhs, reads, bank, start=True, stop=True, tag=None):
-        op("pe", lambda: PE.matmul(out, lhsT, rhs, start, stop), reads, [tag] if tag else [], [bank], max(64, span(rhs)) * PECYCLE)
+    def mm(out, lhsT, rhs, reads, bank, start=True, stop=True, tag=None, join=None):
+        call, cost = lambda: PE.matmul(out, lhsT, rhs, start, stop), max(64, span(rhs)) * PECYCLE * (4 if "float32" in str(lhsT.dtype) else 1)
+        if ((not start) if join is None else join) and len(run[-1]) < JOIN:
+            q, _, before, writes, banks, so_far, _ = nodes.pop()
+            assert q == "pe" and writes == [tag]
+            calls = run.pop() + [call]
+            reads, cost = before + [x for x in reads if x not in before], so_far + cost
+        else:
+            calls = [call]
+        run.append(calls)
+        op("pe", lambda: [c() for c in calls][-1], reads, [tag], [bank], cost)
+
+    run = []
 
     def tt(out, a, b, o, reads, writes, banks=(), kind=""):
         op("v", lambda: V.tensor_tensor(out, a, b, o), reads, writes, banks, vcost(span(out), kind, 1 if banks else 2))
@@ -268,8 +288,8 @@ def rank_program(g, core, T, topo):
                         for j, hard in preds[i].items()])
             if i in moving:
                 where.append("engines")
-                cost.append(moving[i])
-                ins.append([(ids[i], max(900.0 - node[5], 900.0 - moving[i]))])
+                cost.append(moving[i][0])
+                ins.append([(ids[i], moving[i][1])])
             ends.append(len(where) - 1)
         m = len(where)
         outs = [[] for _ in range(m)]
@@ -302,13 +322,16 @@ def rank_program(g, core, T, topo):
                 best = end
             back = place(sorted(range(m), key=lambda z: (-end[z], -z)), outs)
             key = [-back[i] + 1e-7 * i for i in range(m)]
-        SPAN.append((max(best), nodes, label))
+        SPAN.append((max(best), nodes, label, moving))
         return sorted(range(n), key=lambda z: (best[ids[z]] - cost[ids[z]], z))
 
     dmas("sy", [lambda: SY.dma_start(T.wdi[:], T.wd[:])], "ldw", [], ["wdi"])
     dmas("s", [lambda: S.dma_start(T.wti[:, 0:1], T.wt[:])], "ldt", [], ["wti"], 1)
-    dmas("sy", [lambda: SY.dma_start(T.rts[:], T.rt[:])], "ldr", [], ["rts"], 1024)
-    dmas("sy", [lambda: SY.dma_start(T.xs[:, 0:4096], T.x[:])], "ldx", [], ["x_lo", "x_hi"], 1024)
+    if not XFIRST:
+        dmas("sy", [lambda: SY.dma_start(T.rts[:], T.rt[:])], "ldr", [], ["rts"], 1024)
+    dmas("sy", [lambda: SY.dma_start(T.xs[:, 2048:6144], T.x[:])], "ldx", [], ["x_lo", "x_hi"], 1024)
+    if XFIRST:
+        dmas("sy", [lambda: SY.dma_start(T.rts[:], T.rt[:])], "ldr", [], ["rts"], 1024)
     dmas("sy", [lambda: SY.dma_start(T.thi[:, 0:1], T.th[:])], "ldh", [], ["thi"])
 
     def col(n):
@@ -333,6 +356,7 @@ def rank_program(g, core, T, topo):
         sel(T.pb[:], T.blk[:], UP, OP.is_equal, 0.0, -16, 1, ["blk"], ["pb"])
         tt(T.rvh[:], T.pa[:], T.pb[:], OP.add, ["pa", "pb"], ["rvh"])
         fill(T.zerf[:], 0.0, "zerf")
+        fill(T.neg[:], -0.5, "neg")
         fill(T.b0[:], 0.0, "b0")
         for c in range(NC):
             fill(T["tb%d" % c][:, 0:128], 0.0, "zs_%d" % c)
@@ -362,7 +386,7 @@ def rank_program(g, core, T, topo):
                 sel(T.m1a[:], blk, [[0, 8], [-1, 16]], OP.is_gt, 0.0, MJ[c], 0, ["blk"], ["m1a"])
                 ts(T["sx%d" % c][:], T.m1a[:], -1.0, OP.mult, ["m1a"], ["sx_%d" % c], kind="h")
         fill(T.cl[:], 0.0, "cl")
-        for n, (scale, base) in enumerate([(2048.0, 960.0), (128.0, 60.0), (128.0, 61.0), (16.0, 7.5)]):
+        for n, (scale, base) in enumerate([(2048.0, 960.0), (128.0, 60.0), (128.0, 61.0), (16.0, 7.5), (128.0, 62.0)]):
             ts(T.rl[:, 8 * n:8 * n + 8], s1, scale, OP.mult, ["blk"], ["rl%d" % n])
             fill(T.row[:, 8 * n:8 * n + 8], base, "row%d" % n)
         ts(T.cl[:, 0:8], T.itg[:, 0:8], col(0), OP.add, ["itg", "k0", "cl"], ["cl"])
@@ -371,20 +395,16 @@ def rank_program(g, core, T, topo):
     def tables():
         cuts = [slice(512 * n, 512 * n + 512) for n in range(4)]
         for n, a in enumerate(cuts):
-            cp(T.tabr[:, a], T.rts[:, a], ["rts"], ["tabr%d" % n])
-            act(T.pw1[:, a], T.tabr[:, a], AF.Copy, ["tabr%d" % n], ["frac%d" % n], scale=-1.0 / 4096, bias=-2047.0 / 4096)
+            ts(T.tabr[:, a], T.rts[:, a], 2047.0, OP.add, ["rts"], ["tabr%d" % n], (), -1.0 / 4096, OP.mult)
         for n, a in enumerate(cuts):
             ts(T.tabi[:, a], T.rts[:, a], 0.5 - 1.0 / 8192, OP.mult, ["rts"], ["tabi%d" % n], (), WHOLE, OP.add)
             act(T.tabc[:, a], T.tabi[:, a], AF.Copy, ["tabi%d" % n], ["tabc%d" % n], scale=1.0 / 1024, bias=-WHOLE / 1024 - 2048.0)
-        dmas("gp", [lambda: g.dma_start(T.tabc[:], T.pw1[:], accum_op=OP.add)], "dacc",
-             ["%s%d" % (w, n) for w in ("tabc", "frac") for n in range(4)], ["tabc", "pw_1"], 1024)
+        dmas("gp", [lambda: g.dma_start(T.tabc[:], T.tabr[:], accum_op=OP.add)], "dacc",
+             ["%s%d" % (w, n) for w in ("tabc", "tabr") for n in range(4)], ["tabc"], 1024)
 
     def rows():
-        cp(T.bmh[:], T.bm[:], ["bm%d" % n for n in range(8)], ["bmh"], kind="h")
-
-    def constants_3():
-        for n in range(8):
-            sel(T.bm[:, 256 * n:256 * n + 256], T.ones[:], [[-1, 2], [-16, 8], [0, 16]], OP.is_equal, 0.0, -2 * n, 1, ["ones"], ["bm%d" % n])
+        for m in range(16):
+            ts(T.bmh[:, 128 * m:128 * m + 128], blk, T.md[:, m:m + 1], OP.mult, ["blk", "md"], ["bm%d" % m], kind="h")
 
     def constants_2():
         sel(T.e8[:], one, [[-16, 8], [0, 16]], OP.is_equal, 0.0, -8, 1, ["ones"], ["e8"])
@@ -398,15 +418,16 @@ def rank_program(g, core, T, topo):
         ts(T.b2[:], T.b0[:], 2.0, OP.mult, ["b0"], ["b2"], kind="h")
         ts(T.bn[:], T.b0[:], -1.0, OP.mult, ["b0"], ["bn"], kind="h")
         ts(T.rh[:], T.itg[:, 0:8], col(0), OP.add, ["itg", "k0"], ["rh"], (), 1792.0, OP.add)
-        ts(T.ata[:], T.itg[:], col(0), OP.add, ["itg", "k0"], ["ata"], (), 1409.0, OP.add)
+        ts(T.ata[:], T.itg[:, 0:8], col(0), OP.add, ["itg", "k0"], ["ata"], (), 1153.0, OP.add)
         ts(T.ath[:], T.ata[:], 16.0, OP.mult, ["ata"], ["ath"])
+        ts(T.bk[:], T.b0[:], 2048.0, OP.mult, ["b0"], ["bk"], kind="h")
         ts(col(5), col(0), 8.0, OP.is_equal, ["k0"], ["q8"])
         ts(col(6), col(0), 9.0, OP.is_ge, ["k0"], ["q9"], (), 1.0, OP.add)
         ts(col(7), col(5), -8.0, OP.mult, ["q8"], ["q7"])
         tt(col(9), col(6), col(7), OP.add, ["q9", "q7"], ["qc"])
         ts(col(14), col(0), 15.0, OP.is_lt, ["k0"], ["qd"], (), -128.0, OP.mult)
         ts(T.c0[:], T.b0[:], col(9), OP.mult, ["b0", "qc", "qd"], ["c0"], (), col(14), OP.mult)
-        ts(T.c8[:], T.b0[:], col(5), OP.mult, ["b0", "q8"], ["c8"], (), -4096.0, OP.mult)
+        ts(T.c8[:], T.b0[:], col(5), OP.mult, ["b0", "q8"], ["c8"], (), 2048.0, OP.mult)
         ts(T.g8[:], one, col(5), OP.mult, ["ones", "q8"], ["g8"])
         cp(T.anh[:], T.an[:], ["an"], ["anh"], kind="h")
         tt(T.m1a[:], T.e8[:], T.idn[:], OP.subtract, ["e8", "idn"], ["m1a"])
@@ -445,12 +466,17 @@ def rank_program(g, core, T, topo):
         fill(T.txh[:], 0.0, "txh")
         ts(T.txh[:, 0:1], T.thi[:, 0:1], -2048.0, OP.add, ["thi", "txh"], ["txh"])
         cp(T.txh[:, 1:2], T.two[:, 47:48], ["two", "txh"], ["txh"])
+        ts(col(17), col(0), 9.0, OP.is_ge, ["k0"], ["far"], (), 8192.0, OP.mult)
+        ts(col(18), col(17), -4096.0, OP.add, ["far"], ["far2"])
+        tt(T.txh[:, 2:3], T.txh[:, 0:1], col(18), OP.max, ["far2", "txh"], ["txh"])
         mm(T.ps7[:, 0:8], T.rvh[:, 0:128], T.txh[:], ["rvh", "txh"], "ps7", True, True, "ps7d")
         act(T.tx[:], T.ps7[:, 0:8], AF.Copy, ["ps7d"], ["tx"], ["ps7"])
         window("dx%d", T.tx[:], T.dx, T.tw, back, "tx", "tw")
 
     XR, TABR = ["x_lo", "x_hi"], ["tabr%d" % n for n in range(4)]
-    spare = [0]
+    def finer(lo, hi, q):
+        return [(a, a + STEP[q], q) for a in range(lo, hi, STEP[q])]
+
 
     def stages(t, c):
         X, Y, Z = ["ps%d" % (3 * c + b) for b in range(3)]
@@ -467,7 +493,7 @@ def rank_program(g, core, T, topo):
         x0 = HH(4)
         blocks = lambda name, lo, hi: [r("%s%d" % (name, b)) for b in range(lo // 128, hi // 128)]
         XRS = blocks("xr", 0, 2048)
-        x = T.xs[:, 0:4096]
+        x = T.xs[:, 2048:6144]
 
         shift = 128 - 16 * ((t + 1 + (t + 1) // nrank) - (t + t // nrank))
 
@@ -480,7 +506,8 @@ def rank_program(g, core, T, topo):
                 total["sent"] = total.get("sent", 0) + len(topo.engines(core, nxt))
                 total[sem] = len(topo.engines(T.cores[(rank - 1) % nrank], core))
                 wrote[lands] = (sem, total[sem], {}, "net")
-            nodes.append(("gp", emit, [name], [lands], [], 1000.0, extra))
+            moving[len(nodes)] = (extra, 750.0)
+            nodes.append(("gp", emit, [name], [lands], [], 1000.0, 900.0 + extra))
 
         def start():
             ts(HH(3), T.wdi[:, CW * c:CW * c + CW], -2048.0, OP.add, ["wdi"], [r("h3")])
@@ -494,21 +521,27 @@ def rank_program(g, core, T, topo):
             cp(x0, x.indirect(T.ll[:, l0:l0 + 8]), XR + [lres], [r("x0")], kind="g")
 
         def offer():
+            if LEAD[c] == "s":
+                return
             o = PX[:, 384:512]
             mm(o, T.cw[:], T.wl[:, w0:w0 + 128], ["cw", wres], X, True, False, r("cp"))
-            mm(o, T.ct[:], TF(0), ["ct", r("f0")], X, False, False, r("cp"))
-            mm(o, T.cc[:], TF(3), ["cc", r("rc")], X, False, True, r("cp"))
+            mm(o, T.ct[:], TF(0), ["ct", r("f0")], X, False, False, r("cp"), False)
+            mm(o, T.cc[:], TF(3), ["cc", r("rc")], X, False, True, r("cp"), False)
             cp(HH(3), o, [r("cp")], [r("h3")], [X])
 
         def lead():
             o = PY[:, 0:128]
-            mm(o, T.q1[0:1, :], T.ones[0:1, 0:128], ["q1", "ones"], Y, True, False, r("nvp"))
-            mm(o, T.mc[:], TB(6), ["mc", r("P")], Y, False, True, r("nvp"))
-            tt(HH(5), HH(3), o, OP.mult, [r("h3"), r("nvp")], [r("h5")], [Y])
+            if LEAD[c] == "s":
+                cp(HH(5), PZ[:, 384:512], [r("zf")], [r("h5")], [Z])
+            else:
+                mm(o, T.q1[0:1, :], T.ones[0:1, 0:128], ["q1", "ones"], Y, True, False, r("nvp"))
+                mm(o, T.mc[:], TB(6), ["mc", r("P")], Y, False, True, r("nvp"))
+                tt(HH(5), HH(3), o, OP.mult, [r("h3"), r("nvp")], [r("h5")], [Y])
             for m in range(16):
-                mm(PY[:, 400:408], T.b0h[:, shift + 15 - m:shift + 143 - m], hh[:, 640 + m:768:16], ["b0h", r("h5")], Y, m == 0, m == 15, r("x0p"))
+                pick = T.z0h[:, 15 - m:143 - m] if LEAD[c] == "s" else T.b0h[:, shift + 15 - m:shift + 143 - m]
+                mm(PY[:, 400:408], pick, hh[:, 640 + m:768:16], ["b0h", "z0h", r("h5")], Y, m == 0, m == 15, r("x0p"))
             ts(T.lo[:, l0:l0 + 8], PY[:, 400:408], 2048.0, OP.add, [r("x0p")], [r("lo%d" % t)], [Y])
-            send(T.ll[:, l0 + 8 * NC:l0 + 8 * NC + 8], T.lo[:, l0:l0 + 8], r("lo%d" % t), "al%d_%d" % (t + 1, c), "ll%d_%d" % (t + 1, c), 1700.0)
+            send(T.ll[:, l0 + 8 * NC:l0 + 8 * NC + 8], T.lo[:, l0:l0 + 8], r("lo%d" % t), "al%d_%d" % (t + 1, c), "ll%d_%d" % (t + 1, c), 20.0)
 
         def wwin():
             window("dw%d" + str(c), T.wl[:, w0:w0 + 128], T["dw%d" % c], T["ww%d" % c], back, wres, r("ww"))
@@ -536,10 +569,10 @@ def rank_program(g, core, T, topo):
         def spread():
             mm(PZ[:, 384:512], T.k2h[0:1, :], T.oneh[0:1, :], ["k2h", "oneh"], Z, True, False, r("zf"))
             for m in range(16):
-                mm(PZ[:, 384 + m:512:16], T.bmh[:, 128 * m:128 * m + 128], UH(0), ["bmh", r("y")], Z, False, m == 15, r("zf"))
+                mm(PZ[:, 384 + m:512:16], T.bmh[:, 128 * m:128 * m + 128], UH(0), ["bm%d" % m, r("y")], Z, False, m == 15, r("zf"))
 
         def gather_r(n):
-            for lo, hi, q in GR[c][n:n + 1]:
+            for lo, hi, q in finer(*GR[c][n]):
                 i = x.indirect(lu[:, lo // 16:hi // 16])
                 if q == "s":
                     act(xr[:, lo:hi], i, AF.Copy, XR + [r("lr")], blocks("xr", lo, hi), kind="g")
@@ -547,16 +580,18 @@ def rank_program(g, core, T, topo):
                     cp(xr[:, lo:hi], i, XR + [r("lr")], blocks("xr", lo, hi), kind="g")
 
         def letters():
-            act(TF(0), T.tabr[:].indirect(LS(1)), AF.Copy, TABR + [r("cl")], [r("f0")], kind="g")
+            act(TF(0), T.tabr[:].indirect(LS(1)), AF.Copy, TABR + [r("cl")], [r("f0")], kind="g", scale=-4096.0, bias=-2047.0)
 
         def tail():
             tt(TI(0), TF(0), PZ[:, 384:512], OP.mult, [r("f0"), r("zf")], [r("t0")], [Z])
             ts(TI(1), TI(0), 5, OP.arith_shift_right, [r("t0")], [r("t1")], (), 4095, OP.bitwise_and)
-            tt(TI(2), T.tabr[:].indirect(LS(1)), TI(1), OP.add, TABR + [r("cl"), r("t1")], [r("t2")], kind="g")
+            tt(TI(2), TF(0), TI(1), OP.add, [r("f0"), r("t1")], [r("t2")])
             ts(TI(3), TI(2), 4095, OP.bitwise_and, [r("t2")], [r("t3")])
             tt(T["pk%d" % c][:], T.tabc[:].indirect(LS(1)), TI(3), OP.add, ["tabc", r("cl"), r("t3")], [r("pk")], kind="g")
 
         mj = MJ[c]
+        positive = [any(how == "r" for lo, _, how in GW[c] if lo // 1024 == h) for h in range(2)]
+        spare = [("ps6", "ps6d"), ("ps7", "ps7d")]
 
         def biggest():
             for j in range(mj):
@@ -565,22 +600,22 @@ def rank_program(g, core, T, topo):
         def apart(n):
             for j0 in range(mj, 16, 4)[n::2]:
                 js = range(j0, min(j0 + 4, 16))
-                D = "ps%d" % (6 + spare[0] % 2)
-                spare[0] += 1
-                for n, j in enumerate(js):
-                    o = T[D][:, 128 * n:128 * n + 128]
-                    mm(o, T.idn[:], xr[:, j:2048:16], ["idn"] + XRS, D, True, False, D + "d")
-                    mm(o, T.nih[:], x0, ["nih", r("x0")], D, False, True, D + "d")
-                act(mx[:, 128 * j0:128 * (js[-1] + 1)], T[D][:, 0:128 * len(js)], AF.Abs, [D + "d"], [r("mx%d" % j) for j in js], [D])
+                D, tag = spare[n]
+                for j in js:
+                    o = T[D][:, 128 * (j - j0):128 * (j - j0) + 128]
+                    mm(o, T.idn[:], xr[:, j:2048:16], ["idn"] + XRS, D, True, False, tag, j > j0)
+                    mm(o, T.nih[:], x0, ["nih", r("x0")], D, False, True, tag)
+                act(mx[:, 128 * j0:128 * (js[-1] + 1)], T[D][:, 0:128 * len(js)], AF.Abs, [tag], [r("mx%d" % j) for j in js], [D])
 
         def keys():
             mm(PX[:, 128:256], T.ones[0:1, 0:128], T.ktk[0:1, :], ["ones", "ktk"], X, True, False, r("key"))
             if mj:
                 mm(PX[:, 128:256], x0, T["sx%d" % c][:], [r("x0"), r("sx")], X, False, False, r("key"))
             for j in range(mj):
-                mm(PX[:, 128 + j:256:16], xr[:, j:2048:16], T.sn[:], XRS + ["sn"], X, False, False, r("key"))
+                mm(PX[:, 128 + j:256:16], xr[:, j:2048:16], T.sn[:], XRS + ["sn"], X, False, False, r("key"), j > 0)
             for j in range(16):
-                mm(PX[:, 128 + j:256:16], mx[:, 128 * j:128 * j + 128], T.s2[:] if j < mj else s1, [r("mx%d" % j), "s2", "blk"], X, False, j == 15, r("key"))
+                mm(PX[:, 128 + j:256:16], mx[:, 128 * j:128 * j + 128], T.s2[:] if j < mj else s1, [r("mx%d" % j), "s2", "blk"], X, False, j == 15,
+                   r("key"), j % 4 != mj % 4 and j > 0)
 
         def least():
             sc = T["tf%d" % c][:, 128 + 15:256:16]
@@ -589,20 +624,21 @@ def rank_program(g, core, T, topo):
             tt(tb[:, 0:128:16], sc, UI(5), OP.subtract, [r("f1"), r("u5")], [r("zs")])
             scan(TB(1), T.keep[:], TB(0), 0.0, OP.mult, OP.add, ["keep", r("zs")], [r("sk")], kind="h")
             tt(TB(2), TB(1), T.md[:], OP.mult, [r("sk"), "md"], [r("skd")])
-            o = PX[:, 16:48]
-            mm(o, T.ones[0:1, 0:128], T.row[0:1, :], ["ones"] + ["row%d" % n for n in range(4)], X, True, False, r("slp"))
+            o = PX[:, 16:56]
+            mm(o, T.ones[0:1, 0:128], T.row[0:1, :], ["ones"] + ["row%d" % n for n in range(5)], X, True, False, r("slp"))
             mm(o, T.idn[:], T.cl[:], ["idn", "cl"], X, False, False, r("slp"))
-            mm(o, TB(2), T.rl[:], [r("skd")] + ["rl%d" % n for n in range(4)], X, False, True, r("slp"))
-            cp(T["ls%d" % c][:, 16:48], o, [r("slp")], [r("sl")], [X])
+            mm(o, TB(2), T.rl[:], [r("skd")] + ["rl%d" % n for n in range(5)], X, False, True, r("slp"), False)
+            cp(T["ls%d" % c][:, 16:56], o, [r("slp")], [r("sl")], [X])
 
         def turn():
             ts(lu[:, 128:256], T["ww%d" % c][:].indirect(LS(2)), 2048.0, OP.add, [r("ww"), r("sl")], [r("lw")], kind="g")
 
         def limit():
-            if t == 0:
-                act(TF(2), T.tw[:].indirect(LS(3)), AF.Copy, ["tw", r("sl")], [r("f2")], kind="g", bias=2048.0)
-            else:
-                act(TF(2), T.tw[:].indirect(LS(3)), AF.Identity, ["tw", r("sl"), "thr"], [r("f2")], kind="g", bias=col(10))
+            for out, by in [(2, 3), (5, 6)][:2 if FAST[c] == "f" else 1]:
+                if t == 0:
+                    act(TF(out), T.tw[:].indirect(LS(by)), AF.Copy, ["tw", r("sl")], [r("f%d" % out)], kind="g", bias=2048.0)
+                else:
+                    act(TF(out), T.tw[:].indirect(LS(by)), AF.Identity, ["tw", r("sl"), "thr"], [r("f%d" % out)], kind="g", bias=col(10))
 
         def gather_w(n):
             for lo, hi, how in GW[c][n:n + 1]:
@@ -610,22 +646,23 @@ def rank_program(g, core, T, topo):
                 d, m = blocks("df", lo, hi), blocks("mx", lo, hi)
                 if how == "s":
                     act(df[:, lo:hi], i, AF.Copy, XR + [r("lw")], d, kind="g")
-                    D = "ps%d" % (6 + spare[0] % 2)
-                    spare[0] += 1
+                    D, tag = spare[n % 2]
                     o = T[D][:, 0:hi - lo]
-                    mm(o, T.ni[:], xr[:, lo:hi], ["ni"] + blocks("xr", lo, hi), D, True, False, D + "d")
-                    mm(o, T.idn[:], df[:, lo:hi], ["idn"] + d, D, False, True, D + "d")
-                    act(mx[:, lo:hi], o, AF.Abs, [D + "d"], m, [D])
+                    mm(o, T.ni[:], xr[:, lo:hi], ["ni"] + blocks("xr", lo, hi), D, True, False, tag)
+                    mm(o, T.idn[:], df[:, lo:hi], ["idn"] + d, D, False, True, tag, False)
+                    act(mx[:, lo:hi], o, AF.Abs, [tag], m, [D])
                     continue
-                tt(df[:, lo:hi], i, xr[:, lo:hi], OP.subtract, XR + [r("lw")] + blocks("xr", lo, hi), d, kind="g")
+                for a, b, _ in finer(lo, hi, "v"):
+                    tt(df[:, a:b], x.indirect(lu[:, 128 + a // 16:128 + b // 16]), xr[:, a:b], OP.subtract,
+                       XR + [r("lw")] + blocks("xr", a, b), blocks("df", a, b), kind="g")
                 if how == "a":
-                    act(mx[:, lo:hi], df[:, lo:hi], AF.Abs, d, m)
+                    act(mx[:, lo:hi], df[:, lo:hi], AF.Relu if positive[lo // 1024] else AF.Abs, d, m)
                 else:
                     ts(mx[:, lo:hi], df[:, lo:hi], 0.0, OP.max, d, m, kind="h")
 
         def sizes(h):
             for lo in (1024 * h,):
-                relu = (lo, lo + 1024, "r") in GW[c]
+                relu = positive[h]
                 o = PY[:, 128 + lo // 16:192 + lo // 16]
                 if relu:
                     for k in range(16):
@@ -637,8 +674,14 @@ def rank_program(g, core, T, topo):
         def halves():
             act(TB(3), xr[:].indirect(LS(5)), AF.Copy, XRS + [r("sl")], [r("q15")], kind="g")
             mm(PY[:, 0:128], T.idh[:], x0, ["idh", r("x0")], Y, True, False, r("nvp"))
-            mm(PY[:, 0:128], T.idn[:], TB(3), ["idn", r("q15")], Y, False, True, r("nvp"))
-            ts(T.nvi[:, CW * c:CW * c + CW], PY[:, 0:128], 0.5, OP.mult, [r("nvp")], [r("nv")], [Y], -0.25, OP.add)
+            if HALF[c] == "s":
+                mm(PY[:, 0:128], T.ones[0:1, 0:128], T.neg[0:1, :], ["ones", "neg"], Y, False, False, r("nvp"))
+            mm(PY[:, 0:128], T.idn[:], TB(3), ["idn", r("q15")], Y, False, True, r("nvp"), False)
+            if HALF[c] == "s":
+                act(TF(6), PY[:, 0:128], AF.Copy, [r("nvp")], [r("f6")], [Y], scale=0.5, bias=WHOLE)
+                act(T.nvb[:, CW * c:CW * c + CW], TF(6), AF.Copy, [r("f6")], [r("nv")], bias=-WHOLE)
+            else:
+                ts(T.nvi[:, CW * c:CW * c + CW], PY[:, 0:128], 0.5, OP.mult, [r("nvp")], [r("nv")], [Y], -0.25, OP.add)
 
         def unpack():
             act(TF(0), T["pw%d" % c][:].indirect(LS(2)), AF.Copy, [r("pw"), r("sl")], [r("f0")], kind="g")
@@ -653,12 +696,17 @@ def rank_program(g, core, T, topo):
 
         def aim():
             o = PX[:, 256:264]
-            mm(o, T.idh[:], T.ath[:, 8 * c:8 * c + 8], ["idh", "ath"], X, True, False, r("atp"))
+            if FAST[c] == "f":
+                tt(TB(8), PY[:, 128:256], TF(5), OP.is_gt, [r("d2"), r("f5")], [r("far")], [Y])
+            mm(o, T.idh[:], T.ath[:], ["idh", "ath"], X, True, False, r("atp"))
             mm(o, T.idh[:], UH(0), ["idh", r("y")], X, False, False, r("atp"))
             mm(o, T.n16h[:], UH(1), ["n16h", r("uq")], X, False, False, r("atp"))
             for m in range(16):
-                mm(o, T.c8[:, 15 - m:143 - m], tb[:, 768 + m:896:16], ["c8", r("P")], X, False, m == 15, r("atp"))
-            cp(LS(6), o, [r("atp")], [r("al")], [X])
+                if FAST[c] == "f":
+                    mm(o, T.bk[:, 15 - m:143 - m], tb[:, 1024 + m:1152:16], ["bk", r("far")], X, False, m == 15, r("atp"), m > 0)
+                else:
+                    mm(o, T.c8[:, 15 - m:143 - m], tb[:, 768 + m:896:16], ["c8", r("P")], X, False, m == 15, r("atp"), m > 0)
+            cp(LS(8), o, [r("atp")], [r("al")], [X])
 
         def masks():
             mm(PZ[:, 0:128], T.m1[:], TB(6), ["m1", r("P")], Z, True, True, r("k1"))
@@ -667,7 +715,7 @@ def rank_program(g, core, T, topo):
             mm(PZ[:, 128:256], T.m2[:], TB(6), ["m2", r("P")], Z, False, True, r("k2"))
 
         def write_x():
-            cp(T.xs[:].indirect(LS(6)), T.nvi[:, CW * c:CW * c + CW], [r("nv"), r("al")], XR, kind="s")
+            cp(T.xs[:, 4096 * c:(4096, XW)[c]].indirect(LS(8)), (T.nvb if HALF[c] == "s" else T.nvi)[:, CW * c:CW * c + CW], [r("nv"), r("al")], XR[c:c + 1], kind="s")
 
         def turned():
             o = PX[:, 264:272]
@@ -685,12 +733,12 @@ def rank_program(g, core, T, topo):
             flip, same = (T.anh[:], T.idh[:]) if last else (T.shh[:, shift:shift + 128], T.rvh[:, shift:shift + 128])
             mm(F, flip, HH(1), ["anh", "shh", r("h1")], Z, True, False, r("zf"))
             mm(F, same, HH(2), ["idh", "rvh", r("h2")], Z, False, False, r("zf"))
-            mm(F, same, HH(0), ["idh", "rvh", r("h0")], Z, False, True, r("zf"))
+            mm(F, same, HH(0), ["idh", "rvh", r("h0")], Z, False, True, r("zf"), False)
             if last:
                 act(T.ywf[:, CW * c:CW * c + CW], F, AF.Copy, [r("zf")], [r("yw")], [Z], bias=2048.0)
                 return
             act(T.wo[:, w0:w0 + CW], F, AF.Copy, [r("zf")], [r("wo%d" % t)], [Z])
-            send(T.wl[:, w0 + NC * CW:w0 + NC * CW + CW], T.wo[:, w0:w0 + CW], r("wo%d" % t), "ar%d_%d" % (t + 1, c), "wl%d_%d" % (t + 1, c), 2700.0)
+            send(T.wl[:, w0 + NC * CW:w0 + NC * CW + CW], T.wo[:, w0:w0 + CW], r("wo%d" % t), "ar%d_%d" % (t + 1, c), "wl%d_%d" % (t + 1, c), 550.0)
 
         def tally():
             op("s", lambda: S.activation(TB(7), TB(6), AF.Copy, accum_out=T.cnt[:, c:c + 1]), [r("P")], [r("cnt"), r("junk")], (), 160.0)
@@ -710,7 +758,7 @@ def rank_program(g, core, T, topo):
         ts(col(10), T.aj[:, 0:1], 8.0, OP.mult, ["aj"], ["thr"], (), 2048.0, OP.add)
 
     parts = [{"a": stages(t, 0), "b": stages(t, 1)} for t in range(VIS)]
-    once = {"constants_1": constants_1, "constants_2": constants_2, "constants_3": constants_3, "tables": tables, "rows": rows,
+    once = {"constants_1": constants_1, "constants_2": constants_2, "tables": tables, "rows": rows,
             "limits": limits, "start": lambda: (parts[0]["a"]["start"](), parts[0]["b"]["start"]())}
     for t in range(VIS + 1):
         for word in ORDER.split():
@@ -731,9 +779,9 @@ def rank_program(g, core, T, topo):
             else:
                 parts[at][chunk][name]()
 
-    dmas("sy", [lambda: SY.dma_start(T.yx[:, 0:2048], T.xs[:, 0:2048]), lambda: SY.dma_start(T.yx[:, 2048:4096], T.xs[:, 2048:4096])],
-         "outx", XR, [])
-    dmas("sy", [lambda: SY.dma_start(T.yw[:], T.ywf[:])], "outw", ["yw_0", "yw_1"], [])
+    dmas("sy", [lambda: SY.dma_start(T.yx[:, 0:2048], T.xs[:, 2048:4096])], "outx", XR[:1], [], 512)
+    dmas("sy", [lambda: SY.dma_start(T.yx[:, 2048:4096], T.xs[:, 4096:6144])], "outx", XR[1:], [], 512)
+    dmas("s", [lambda: S.dma_start(T.yw[:], T.ywf[:])], "outw", ["yw_0", "yw_1"], [], 128)
     label.extend([""] * (len(nodes) - len(label)))
     for i in plan():
         nodes[i][1]()

@@ -1,29 +1,36 @@
+import math
 from concourse.mybir import dt, AluOpType as OP, AxisListType, ActivationFunctionType as AF
 
 VIS = 6
 NC = 2
 CW = 128
 XW = 2048 + 4096 + 9 * 2048
+BIG = 1.5 * 2 ** 35
 WHOLE = 1.5 * 2 ** 23
-CYCLE, PECYCLE, GATHER, SCATTER = 0.83, 0.46, 1.56, 3.8
-OWN, WAKE, DMA = 130.0, 190.0, 2.0
-GR = [[(512 * n, 512 * n + 512, q) for n, q in enumerate(qs)] for qs in ("sssv", "ssss")]
+CYCLE, PECYCLE, GATHER, SCATTER = 0.95, 0.53, 1.56, 3.8
+OWN, WAKE, DMA, NET = 120.0, 200.0, 2.3, 1.1
+GR, GR0 = ("sssv", "sssv"), ("svsv", "svsv")
 MJ = (8, 10)
-GW = [[(512 * n, 512 * n + 512, q) for n, q in enumerate(qs)] for qs in ("saaa", "asaa")]
-STEP = {"v": 512, "s": 512}
+GW = ("saaa", "asaa")
+FINE = (256, 256)
+FIRST, OFFER, RENEW = "vv", "ss", "sv"
+FAST = "sf"
 JOIN = 4
 ROUNDS = 2
-SPAN = []
+TRIES, STEPS, MORE, HEAT, SEED = 1, 4000, 12000, 250.0, 11
+PLAN = {}
 
 ORDER = """
--b.lead a.first b.first -b.tally a.weigh a.relator -b.masks a.gather_r:3 allow -b.turned -b.renew b.weigh a.gather_r:1 a.gather_r:0 b.relator a.gather_r:2 a.biggest a.apart:1 a.wwin a.apart:0 a.keys a.spread a.least b.letters a.limit b.gather_r:0 b.gather_r:2 b.gather_r:3 b.gather_r:1 b.apart:0 b.apart:1 a.turn a.gather_w:1 a.gather_w:3 a.letters a.tail a.gather_w:0 b.spread b.biggest a.gather_w:2 a.pwin b.keys b.tail a.unpack b.least b.halves b.wwin a.sizes:0 b.turn b.gather_w:2 b.gather_w:1 b.pwin a.sizes:1 a.match a.masks a.offer a.lead b.limit b.gather_w:0 b.sizes:0 a.aim b.unpack b.gather_w:3 b.sizes:1 a.turned a.halves a.write_x a.tally a.renew b.aim b.write_x b.offer b.match
+-b.lead -b.lists a.first b.first -b.tally a.weigh a.relator a.wwin -b.masks a.gather_r:0 allow -b.turned -b.renew b.weigh a.gather_r:1
+a.gather_r:3 b.relator a.gather_r:2 a.letters a.pwin a.biggest:0 a.apart:0 a.biggest:1 a.apart:1 a.keys a.spread a.least b.wwin b.letters
+a.limit b.gather_r:0 b.gather_r:1 b.gather_r:2 b.gather_r:3 b.apart:0 b.apart:1 a.turn a.gather_w:1 a.gather_w:3 a.gather_w:0 b.pwin
+b.spread b.biggest:0 b.biggest:1 a.gather_w:2 b.keys a.unpack a.tail a.other b.least b.halves a.sizes:0 b.turn b.gather_w:2 b.gather_w:1
+a.sizes:1 a.match a.offer a.lead a.lists a.masks b.limit b.gather_w:0 b.sizes:0 a.turned b.unpack b.gather_w:3 b.sizes:1 a.halves
+a.write_x a.renew a.tally b.aim b.write_x b.tail b.other b.offer b.match
 """
-ONCE = {"first": "constants_1 start", "weigh": "tables", "spread": "rows", "limit": "limits",
-        "gather_w": "constants_2", "halves": "constants_2", "offer": "constants_2"}
-HALF = "vv"
-XFIRST = False
-LEAD = "ff"
-FAST = "sf"
+CHAIN = """first weigh relator letters pwin gather_r:0 gather_r:1 gather_r:2 gather_r:3 biggest:0 apart:0 biggest:1 apart:1 keys least turn
+gather_w:0 gather_w:1 gather_w:2 gather_w:3 sizes:0 sizes:1 limit match lead lists turned masks renew wwin spread unpack tail other offer
+halves aim write_x tally""".split()
 
 SCRATCH = {
     "xs": ("sbuf", [128, XW], "bfloat16"),
@@ -34,34 +41,29 @@ SCRATCH = {
     "wl": ("sbuf", [128, NC * CW * VIS], "float32"),
     "wo": ("sbuf", [128, NC * CW * VIS], "float32"),
     "ll": ("sbuf", [128, NC * 8 * VIS], "uint16"),
-    "lo": ("sbuf", [128, NC * 8 * VIS], "uint16"),
-    "b0h": ("sbuf", [128, 288], "float16"),
-    "cw": ("sbuf", [128, 128], "float32"),
-    "ct": ("sbuf", [128, 128], "float32"),
-    "cc": ("sbuf", [128, 128], "float32"),
-    "mc": ("sbuf", [128, 128], "bfloat16"),
-    "q1": ("sbuf", [128, 128], "bfloat16"),
+    "lo": ("sbuf", [128, NC * 24 * VIS], "uint16"),
     "ywf": ("sbuf", [128, 256], "float32"),
     "nvi": ("sbuf", [128, 256], "int32"),
-    "nvb": ("sbuf", [128, 256], "bfloat16"),
-    "neg": ("sbuf", [128, 128], "bfloat16"),
+    "cw": ("sbuf", [128, 256], "float32"),
+    "ct": ("sbuf", [128, 256], "bfloat16"),
+    "cc": ("sbuf", [128, 256], "bfloat16"),
+    "mc": ("sbuf", [128, 256], "bfloat16"),
+    "q1": ("sbuf", [128, 128], "bfloat16"),
     "ones": ("sbuf", [128, 256], "bfloat16"),
-    "zerf": ("sbuf", [128, 128], "float32"),
+    "zerf": ("sbuf", [128, 16], "float32"),
     "blk": ("sbuf", [128, 256], "bfloat16"),
     "blk0": ("sbuf", [128, 256], "bfloat16"),
-    "idn": ("sbuf", [128, 128], "bfloat16"),
+    "id2": ("sbuf", [128, 256], "bfloat16"),
     "an": ("sbuf", [128, 128], "bfloat16"),
-    "idh": ("sbuf", [128, 128], "float16"),
-    "anh": ("sbuf", [128, 128], "float16"),
-    "nih": ("sbuf", [128, 128], "float16"),
-    "n16h": ("sbuf", [128, 128], "float16"),
+    "i128": ("sbuf", [128, 128], "bfloat16"),
+    "n16": ("sbuf", [128, 128], "bfloat16"),
     "ni": ("sbuf", [128, 128], "bfloat16"),
     "pa": ("sbuf", [128, 256], "bfloat16"),
     "pb": ("sbuf", [128, 256], "bfloat16"),
     "pc": ("sbuf", [128, 256], "bfloat16"),
     "pd": ("sbuf", [128, 256], "bfloat16"),
-    "rvh": ("sbuf", [128, 256], "float16"),
-    "shh": ("sbuf", [128, 256], "float16"),
+    "rv": ("sbuf", [128, 256], "bfloat16"),
+    "sh": ("sbuf", [128, 256], "bfloat16"),
     "m3": ("sbuf", [128, 128], "bfloat16"),
     "e8": ("sbuf", [128, 128], "bfloat16"),
     "m1a": ("sbuf", [128, 128], "bfloat16"),
@@ -69,29 +71,28 @@ SCRATCH = {
     "m2a": ("sbuf", [128, 128], "bfloat16"),
     "m2b": ("sbuf", [128, 128], "bfloat16"),
     "m2": ("sbuf", [128, 128], "bfloat16"),
-    "m1b": ("sbuf", [128, 128], "bfloat16"),
-    "g8": ("sbuf", [128, 128], "float32"),
+    "g8": ("sbuf", [128, 8], "bfloat16"),
     "b0": ("sbuf", [128, 144], "bfloat16"),
     "b2": ("sbuf", [128, 144], "bfloat16"),
     "bn": ("sbuf", [128, 144], "bfloat16"),
-    "c0": ("sbuf", [128, 144], "bfloat16"),
-    "c8": ("sbuf", [128, 144], "bfloat16"),
-    "z0h": ("sbuf", [128, 144], "float16"),
+    "bk": ("sbuf", [128, 144], "bfloat16"),
+    "z0": ("sbuf", [128, 144], "bfloat16"),
     "wt0": ("sbuf", [128, 144], "float16"),
-    "tabr": ("sbuf", [128, 2048], "float32"),
-    "tabc": ("sbuf", [128, 2048], "float32"),
-    "tabi": ("sbuf", [128, 2048], "float32"),
-    "bmh": ("sbuf", [128, 2048], "float16"),
-    "k2h": ("sbuf", [128, 128], "float16"),
-    "oneh": ("sbuf", [128, 128], "float16"),
+    "mod": ("sbuf", [128, 48], "bfloat16"),
+    "on6": ("sbuf", [128, 48], "bfloat16"),
+    "b18": ("sbuf", [128, 288], "bfloat16"),
+    "bm": ("sbuf", [128, 2048], "bfloat16"),
+    "k2": ("sbuf", [128, 128], "bfloat16"),
+    "oneh": ("sbuf", [128, 256], "float16"),
     "s2": ("sbuf", [128, 8], "bfloat16"),
     "sn": ("sbuf", [128, 8], "bfloat16"),
-    "sx0": ("sbuf", [128, 128], "float16"),
-    "sx1": ("sbuf", [128, 128], "float16"),
+    "sx0": ("sbuf", [128, 144], "bfloat16"),
+    "sx1": ("sbuf", [128, 144], "bfloat16"),
     "kt": ("sbuf", [128, 128], "bfloat16"),
-    "ktk": ("sbuf", [128, 128], "bfloat16"),
+    "ktk": ("sbuf", [128, 144], "bfloat16"),
     "md": ("sbuf", [128, 128], "bfloat16"),
-    "rs": ("sbuf", [128, 128], "float32"),
+    "mdf": ("sbuf", [128, 16], "float32"),
+    "rs": ("sbuf", [128, 144], "float32"),
     "keep": ("sbuf", [128, 128], "bfloat16"),
     "pi": ("sbuf", [128, 2], "int32"),
     "pj": ("sbuf", [128, 2], "int32"),
@@ -100,45 +101,250 @@ SCRATCH = {
     "rl": ("sbuf", [128, 40], "bfloat16"),
     "cl": ("sbuf", [128, 40], "bfloat16"),
     "row": ("sbuf", [128, 40], "bfloat16"),
-    "bk": ("sbuf", [128, 144], "bfloat16"),
-    "rh": ("sbuf", [128, 8], "float16"),
+    "base": ("sbuf", [128, 24], "float16"),
     "ata": ("sbuf", [128, 8], "float32"),
-    "ath": ("sbuf", [128, 8], "float16"),
     "two": ("sbuf", [128, 48], "float32"),
     "txh": ("sbuf", [128, 8], "float16"),
     "tx": ("sbuf", [128, 8], "float32"),
     "dx": ("dram", [8, 32, 8], "float32"),
     "tw": ("sbuf", [128, 128], "float32"),
-    "cnt": ("sbuf", [128, 2], "float32"),
+    "cnt": ("sbuf", [128, 2], "bfloat16"),
     "ai": ("sbuf", [128, 2], "int32"),
     "aj": ("sbuf", [128, 2], "int32"),
 }
 for _c in range(NC):
     SCRATCH.update({
         "xr%d" % _c: ("sbuf", [128, 2048], "bfloat16"),
-        "mx%d" % _c: ("sbuf", [128, 2048], "bfloat16"),
+        "mx%d" % _c: ("sbuf", [128, 16, 128], "bfloat16"),
         "df%d" % _c: ("sbuf", [128, 2048], "bfloat16"),
         "ww%d" % _c: ("sbuf", [128, 2048], "float32"),
         "pw%d" % _c: ("sbuf", [128, 2048], "float32"),
         "dw%d" % _c: ("dram", [8, 32, 128], "float32"),
         "dp%d" % _c: ("dram", [8, 32, 128], "float32"),
         "pk%d" % _c: ("sbuf", [128, 128], "float32"),
-        "ti%d" % _c: ("sbuf", [128, 640], "int32"),
-        "tf%d" % _c: ("sbuf", [128, 896], "float32"),
+        "ti%d" % _c: ("sbuf", [128, 384], "int32"),
+        "tf%d" % _c: ("sbuf", [128, 1280], "float32"),
         "tb%d" % _c: ("sbuf", [128, 1152], "bfloat16"),
-        "hh%d" % _c: ("sbuf", [128, 768], "float16"),
-        "ui%d" % _c: ("sbuf", [128, 64], "int32"),
-        "uf%d" % _c: ("sbuf", [128, 16], "float32"),
-        "uh%d" % _c: ("sbuf", [128, 16], "float16"),
+        "hh%d" % _c: ("sbuf", [128, 1024], "float16"),
+        "ui%d" % _c: ("sbuf", [128, 32], "int32"),
+        "uf%d" % _c: ("sbuf", [128, 56], "float32"),
+        "uh%d" % _c: ("sbuf", [128, 24], "float16"),
         "ls%d" % _c: ("sbuf", [128, 72], "uint16"),
         "lu%d" % _c: ("sbuf", [128, 256], "uint16"),
     })
 for _b in range(8):
     SCRATCH["ps%d" % _b] = ("psum", [128, 512], "float32")
 
-SEMAPHORES = ["v", "s", "pe", "gp", "sent", "dacc", "ldx", "ldr", "ldw", "ldt", "ldh", "outw", "outx", "dx1", "dx2"]
+SEMAPHORES = ["v", "s", "pe", "gp", "sent", "ldx", "ldr", "ldw", "ldt", "ldh", "outw", "outx", "dx1", "dx2"]
 SEMAPHORES += ["d%s%d%d" % (w, st, c) for w in "wp" for st in (1, 2) for c in range(NC)]
 SEMAPHORES += ["%s%d_%d" % (w, t, c) for w in ("ar", "al") for t in range(1, VIS) for c in range(NC)]
+
+
+def needs(nodes, banks_too):
+    preds = [dict() for _ in nodes]
+    last, rd, bk = {}, {}, {}
+    for i, (q, _, reads, writes, banks, _) in enumerate(nodes):
+        def edge(j, hard):
+            preds[i][j] = preds[i].get(j, False) or hard
+        for x in reads:
+            edge(last[x], True)
+            rd.setdefault(x, []).append(i)
+        for x in writes:
+            if x in last:
+                edge(last[x], not (q == "pe" and nodes[last[x]][0] == "pe"))
+            for j in rd.get(x, ()):
+                if j != i:
+                    edge(j, nodes[j][0] != q or q == "sy")
+            last[x], rd[x] = i, []
+        for b in banks:
+            for q2, j in bk.setdefault(b, {}).items():
+                if j != i and ((q2 != q and banks_too) or q2 == q == "pe"):
+                    edge(j, q2 != q)
+            bk[b][q] = i
+    return preds
+
+
+def lag(nodes, moving, j, i):
+    return OWN if nodes[j][0] == nodes[i][0] and j not in moving else WAKE + (60.0 if nodes[j][0] == "pe" else 0.0)
+
+
+def first_placing(nodes, moving):
+    where, cost, ins, ids, ends = [], [], [], [], []
+    for i, pred in enumerate(needs(nodes, True)):
+        ids.append(len(where))
+        where.append(nodes[i][0])
+        cost.append(nodes[i][5])
+        ins.append([(ends[j], lag(nodes, moving, j, i) + moving.get(j, (0, 0, 0.0))[2]) if hard else (ids[j], 0.0) for j, hard in pred.items()])
+        if i in moving:
+            where.append("engines")
+            cost.append(moving[i][1])
+            ins.append([(ids[i], moving[i][0] - min(nodes[i][5], moving[i][0]))])
+        ends.append(len(where) - 1)
+    m = len(where)
+    outs = [[] for _ in range(m)]
+    for i in range(m):
+        for j, wait in ins[i]:
+            outs[j].append((i, wait))
+
+    def place(order, before):
+        end, busy = [0.0] * m, {}
+        for i in order:
+            t = max([end[j] + wait for j, wait in before[i]] + [0.0])
+            los, his = busy.setdefault(where[i], ([], []))
+            a, b = 0, len(his)
+            while a < b:
+                mid = (a + b) // 2
+                a, b = (mid + 1, b) if his[mid] <= t else (a, mid)
+            while a < len(los) and los[a] < t + cost[i]:
+                t = his[a]
+                a += 1
+            los.insert(a, t)
+            his.insert(a, t + cost[i])
+            end[i] = t + cost[i]
+        return end
+
+    key, best = list(range(m)), None
+    for _ in range(ROUNDS):
+        end = place(sorted(range(m), key=lambda z: key[z]), ins)
+        if best is None or max(end) < max(best):
+            best = end
+        back = place(sorted(range(m), key=lambda z: (-end[z], -z)), outs)
+        key = [-back[i] + 1e-7 * i for i in range(m)]
+    return sorted(range(len(nodes)), key=lambda z: (best[ids[z]] - cost[ids[z]], z))
+
+
+def clock(nodes, moving):
+    n = len(nodes)
+    preds = needs(nodes, False)
+    names = ["v", "s", "pe", "gp", "sy"]
+    rows = []
+    for i, node in enumerate(nodes):
+        q = names.index(node[0])
+        rows.append((q, [(j, lag(nodes, moving, j, i)) for j, hard in preds[i].items() if hard], int(node[4][0][2:]) if node[4] else -1,
+                     node[5], moving.get(i), WAKE + (60.0 if q == 2 else 0.0)))
+
+    def run(order):
+        free, last = [0.0] * 5, [-1] * 5
+        start, end, why = [0.0] * n, [0.0] * n, [-1] * n
+        held = [[(-1e9, -1)] * 3 for _ in range(8)]
+        engines, mover, since = 0.0, -1, 0.0
+        for i in order:
+            q, hard, bank, cost, move, wake = rows[i]
+            t, w = free[q], last[q]
+            for j, wait in hard:
+                u = end[j] + wait
+                if u > t:
+                    t, w = u, j
+            if bank >= 0:
+                for z in (0, 1, 2):
+                    if z != q and held[bank][z][0] > t:
+                        t, w = held[bank][z]
+            u = free[q] = t + cost
+            last[q] = i
+            if move:
+                at = t + move[0]
+                if engines > at:
+                    if q == 3 and rows[mover][0] == 4:
+                        part = min(1.0, max(0.0, t - start[mover]) / rows[mover][3])
+                        at = max(at, since + part * rows[mover][4][1])
+                        end[mover] += move[1]
+                        engines += move[1]
+                        start[i], end[i], why[i] = t, at + move[1] + move[2], (mover if at > t + move[0] else w)
+                        continue
+                    at, w = engines, mover
+                since, engines, mover = at, at + move[1], i
+                u = engines + move[2]
+            elif bank >= 0:
+                held[bank][q] = (u + wake, i)
+            start[i], end[i], why[i] = t, u, w
+        return start, end, why
+    return preds, run
+
+
+def tighten(nodes, moving, label, given):
+    n = len(nodes)
+    preds, run = clock(nodes, moving)
+    lists = [list(p) for p in preds]
+    hard = [[(j, lag(nodes, moving, j, i)) for j, h in p.items() if h] for i, p in enumerate(preds)]
+    users = [[] for _ in nodes]
+    for i, p in enumerate(hard):
+        for j, wait in p:
+            users[j].append((i, wait))
+    kind, of, count, parts = [None] * n, {}, {}, {}
+    for i in range(n):
+        t, word = label[i]
+        t, word = t - (word[:1] == "-"), word.lstrip("-")
+        count[t, word] = count.get((t, word), 0) + 1
+        kind[i] = (t, (word, count[t, word], nodes[i][0]))
+        of[kind[i]] = i
+        parts.setdefault(word, []).append(i)
+    seed = [SEED]
+
+    def chance():
+        seed[0] = (seed[0] * 1103515245 + 12345) % 2 ** 31
+        return seed[0] / 2 ** 31
+
+    def attempt(order, steps, heat):
+        now = run(order)
+        length = max(now[1])
+        best, pairs = (length, order), None
+        for step in range(steps):
+            if pairs is None:
+                start, end, why = now
+                key = [0.0] * n
+                for r, i in enumerate(order):
+                    key[i] = start[i] + 1e-4 * r
+                pairs, i = [], end.index(length)
+                while why[i] >= 0:
+                    if why[i] not in preds[i]:
+                        pairs.append((why[i], i))
+                    i = why[i]
+            new = list(key)
+            j, i = pairs[int(len(pairs) * chance())]
+            up, far = chance() < 0.5, chance() ** 2
+            whole = chance() < 0.08
+            if whole:
+                first = int(len(CHAIN) * chance())
+                some = sorted(x for w in CHAIN[first:first + 1 + int(5 * chance() ** 2)] for x in parts.get("ab"[int(far > 0.25)] + "." + w, ())
+                              if (kind[x][0] > 0) == (kind[i][0] > 0))
+                when = {}
+                for x in (some if up else some[::-1]):
+                    if up:
+                        new[x] = max([when.get(p, end[p]) + wait for p, wait in hard[x]] + [0.0])
+                        when[x] = new[x] + end[x] - start[x]
+                    else:
+                        new[x] = when[x] = min([when.get(p, start[p]) - wait for p, wait in users[x]] + [length]) - (end[x] - start[x])
+            low = min(kind[i][0], kind[j][0])
+            for d in () if whole else range(1 - low, VIS) if low and chance() < 0.85 else (0,):
+                a, b = of.get((kind[j][0] + d, kind[j][1])), of.get((kind[i][0] + d, kind[i][1]))
+                if a is None or b is None or key[a] > key[b]:
+                    continue
+                if not up:
+                    late = min([start[x] - wait for x, wait in users[a]] + [length]) - (end[a] - start[a])
+                    new[a] = key[b] + 0.5 + far * max(0.0, late - key[b])
+                    continue
+                early = max([end[x] + wait for x, wait in hard[b]] + [0.0])
+                edge, stack = key[a] - 0.5 - far * max(0.0, key[a] - early), [b]
+                while stack:
+                    x = stack.pop()
+                    new[x] = edge - 0.4 + 1e-7 * key[x]
+                    stack.extend(p for p in lists[x] if new[p] > edge and p != a)
+            for i in range(n):
+                k = new[i]
+                for p in lists[i]:
+                    if new[p] >= k:
+                        k = new[p] + 1e-6
+                new[i] = k
+            other = sorted(range(n), key=lambda z: new[z])
+            then = run(other)
+            if max(then[1]) - length <= -heat * (1 - step / steps) * math.log(chance() + 1e-9):
+                order, now, length, pairs = other, then, max(then[1]), None
+                if length < best[0]:
+                    best = (length, order)
+        return best
+
+    best = min(attempt(given, STEPS, HEAT) for _ in range(TRIES))
+    return attempt(best[1], MORE, HEAT / 3)[1]
 
 
 def rank_program(g, core, T, topo):
@@ -154,12 +360,10 @@ def rank_program(g, core, T, topo):
     wrote, seen = {}, {}
 
     def need(q, tok):
-        if tok is None:
-            return
-        sem, val, clock, _ = tok
+        sem, val, past, _ = tok
         if know[q].get(sem, 0) < val:
             queue[q].wait_ge(T.sem[sem], val)
-            for s2, v2 in clock.items():
+            for s2, v2 in past.items():
                 if know[q].get(s2, 0) < v2:
                     know[q][s2] = v2
             know[q][sem] = val
@@ -192,7 +396,7 @@ def rank_program(g, core, T, topo):
             seen.setdefault(b, {})[q] = tok
 
     nodes = []
-    label, now = [], [""]
+    label, now = [], [(0, "")]
 
     def op(q, call, reads, writes, banks=(), cost=100.0):
         def emit():
@@ -200,7 +404,7 @@ def rank_program(g, core, T, topo):
             total[q] = total.get(q, 0) + 1
             call().then_inc(T.sem[q], 1)
             note(q, (q, total[q], dict(know[q]), q), reads, writes, banks)
-        nodes.append((q, emit, list(reads), list(writes), list(banks), cost, 60.0 if q == "pe" else 0.0))
+        nodes.append((q, emit, list(reads), list(writes), list(banks), cost))
 
     moving = {}
 
@@ -211,27 +415,26 @@ def rank_program(g, core, T, topo):
                 total[sem] = total.get(sem, 0) + 16
                 call().then_inc(T.sem[sem], 16)
             note(q, (sem, total[sem], dict(know[q]), "dma"), reads, writes, ())
-        issue, busy = (900.0 if q == "gp" else 60.0) * len(calls), 100.0 + DMA * kib
-        moving[len(nodes)] = (busy, 900.0 - min(issue, busy))
-        nodes.append((q, emit, list(reads), list(writes), [], issue, 600.0))
+        moving[len(nodes)] = (960.0, 100.0 + DMA * kib, 600.0)
+        nodes.append((q, emit, list(reads), list(writes), [], 60.0 * len(calls)))
 
     def span(ap):
-        return ap.shape[1]
+        return math.prod(ap.shape[1:])
 
     def vcost(n, kind, wide):
-        return {"": max(64, n * wide) * CYCLE, "h": max(64, n / 2) * CYCLE, "g": 50 + n * GATHER * CYCLE, "s": 50 + n * SCATTER * CYCLE}[kind]
+        return {"": max(64, n * wide) * CYCLE, "h": max(64, n / 2) * CYCLE, "g": 55 + n * GATHER * CYCLE, "s": 55 + n * SCATTER * CYCLE}[kind]
 
     def mm(out, lhsT, rhs, reads, bank, start=True, stop=True, tag=None, join=None):
         call, cost = lambda: PE.matmul(out, lhsT, rhs, start, stop), max(64, span(rhs)) * PECYCLE * (4 if "float32" in str(lhsT.dtype) else 1)
+        tags = tag if isinstance(tag, list) else [tag]
         if ((not start) if join is None else join) and len(run[-1]) < JOIN:
-            q, _, before, writes, banks, so_far, _ = nodes.pop()
-            assert q == "pe" and writes == [tag]
+            q, _, before, writes, banks, so_far = nodes.pop()
             calls = run.pop() + [call]
             reads, cost = before + [x for x in reads if x not in before], so_far + cost
         else:
             calls = [call]
         run.append(calls)
-        op("pe", lambda: [c() for c in calls][-1], reads, [tag], [bank], cost)
+        op("pe", lambda: [c() for c in calls][-1], reads, tags, [bank], cost)
 
     run = []
 
@@ -257,82 +460,23 @@ def rank_program(g, core, T, topo):
     def act(out, a, f, reads, writes, banks=(), kind="", **more):
         op("s", lambda: S.activation(out, a, f, **more), reads, writes, banks, vcost(span(out), kind, 1) + 30.0)
 
-    def plan():
-        n = len(nodes)
-        preds = [dict() for _ in range(n)]
-        last, rd, bk = {}, {}, {}
-        for i, (q, _, reads, writes, banks, _, _) in enumerate(nodes):
-            def edge(j, hard):
-                preds[i][j] = preds[i].get(j, False) or hard
-            for x in reads:
-                edge(last[x], True)
-                rd.setdefault(x, []).append(i)
-            for x in writes:
-                if x in last:
-                    edge(last[x], not (q == "pe" and nodes[last[x]][0] == "pe"))
-                for j in rd.get(x, ()):
-                    if j != i:
-                        edge(j, nodes[j][0] != q or q == "sy")
-                last[x], rd[x] = i, []
-            for b in banks:
-                for q2, j in bk.setdefault(b, {}).items():
-                    if j != i and (q2 != q or q == "pe"):
-                        edge(j, q2 != q)
-                bk[b][q] = i
-        where, cost, ins, ids, ends = [], [], [], [], []
-        for i, node in enumerate(nodes):
-            ids.append(len(where))
-            where.append(node[0])
-            cost.append(node[5])
-            ins.append([(ends[j], nodes[j][6] + (OWN if nodes[j][0] == node[0] and j not in moving else WAKE)) if hard else (ids[j], 0.0)
-                        for j, hard in preds[i].items()])
-            if i in moving:
-                where.append("engines")
-                cost.append(moving[i][0])
-                ins.append([(ids[i], moving[i][1])])
-            ends.append(len(where) - 1)
-        m = len(where)
-        outs = [[] for _ in range(m)]
-        for i in range(m):
-            for j, lag in ins[i]:
-                outs[j].append((i, lag))
+    def copy(who, out, a, reads, writes, banks=(), kind=""):
+        if who == "s":
+            act(out, a, AF.Copy, reads, writes, banks, kind)
+        else:
+            cp(out, a, reads, writes, banks, kind)
 
-        def place(order, before):
-            end, busy = [0.0] * m, {}
-            for i in order:
-                t = max([end[j] + lag for j, lag in before[i]] + [0.0])
-                los, his = busy.setdefault(where[i], ([], []))
-                a, b = 0, len(his)
-                while a < b:
-                    mid = (a + b) // 2
-                    a, b = (mid + 1, b) if his[mid] <= t else (a, mid)
-                while a < len(los) and los[a] < t + cost[i]:
-                    t = his[a]
-                    a += 1
-                los.insert(a, t)
-                his.insert(a, t + cost[i])
-                end[i] = t + cost[i]
-            return end
+    def together(k):
+        some = [nodes.pop() for _ in range(k)][::-1]
+        both = lambda z: list(dict.fromkeys(x for node in some for x in node[z]))
+        nodes.append((some[0][0], lambda: [node[1]() for node in some], both(2), both(3), both(4), sum(node[5] for node in some)))
 
-        key = list(range(m))
-        best = None
-        for _ in range(ROUNDS):
-            end = place(sorted(range(m), key=lambda z: key[z]), ins)
-            if best is None or max(end) < max(best):
-                best = end
-            back = place(sorted(range(m), key=lambda z: (-end[z], -z)), outs)
-            key = [-back[i] + 1e-7 * i for i in range(m)]
-        SPAN.append((max(best), nodes, label, moving))
-        return sorted(range(n), key=lambda z: (best[ids[z]] - cost[ids[z]], z))
-
-    dmas("sy", [lambda: SY.dma_start(T.wdi[:], T.wd[:])], "ldw", [], ["wdi"])
+    dmas("sy", [lambda: SY.dma_start(T.wdi[:], T.wd[:])], "ldw", [], ["wdi"], 128)
     dmas("s", [lambda: S.dma_start(T.wti[:, 0:1], T.wt[:])], "ldt", [], ["wti"], 1)
-    if not XFIRST:
-        dmas("sy", [lambda: SY.dma_start(T.rts[:], T.rt[:])], "ldr", [], ["rts"], 1024)
     dmas("sy", [lambda: SY.dma_start(T.xs[:, 2048:6144], T.x[:])], "ldx", [], ["x_lo", "x_hi"], 1024)
-    if XFIRST:
-        dmas("sy", [lambda: SY.dma_start(T.rts[:], T.rt[:])], "ldr", [], ["rts"], 1024)
-    dmas("sy", [lambda: SY.dma_start(T.thi[:, 0:1], T.th[:])], "ldh", [], ["thi"])
+    dmas("sy", [lambda: SY.dma_start(T.rts[:, 712:2048], T.rt[:, 0:1336]), lambda: SY.dma_start(T.rts[:, 0:712], T.rt[:, 1336:2048])],
+         "ldr", [], ["rts"], 1024)
+    dmas("sy", [lambda: SY.dma_start(T.thi[:, 0:1], T.th[:])], "ldh", [], ["thi"], 1)
 
     def col(n):
         return T.cols[:, n:n + 1]
@@ -343,20 +487,29 @@ def rank_program(g, core, T, topo):
     def iota(out, pattern, name):
         op("gp", lambda: g.iota(out, pattern, 0, 0, allow_small_or_imprecise_dtypes=True), [], [name], (), 130.0 + 2 * span(out) * CYCLE)
 
-    one, blk, s1 = T.ones[:, 0:128], T.blk[:, 0:128], T.blk[:, 0:128:16]
+    one, blk, s1, idn = T.ones[:, 0:128], T.blk[:, 0:128], T.blk[:, 0:128:16], T.id2[:, 0:128]
     UP, DOWN = [[0, 2], [-16, 8], [1, 16]], [[0, 2], [16, 8], [1, 16]]
+
+    def times(out, in_, by, reads, writes):
+        act(out, in_, AF.Copy, reads, writes, scale=by)
+
+    def join(out, terms, reads, name):
+        o = T.ps6[:, 0:span(out)]
+        for n, (sign, tile) in enumerate(terms):
+            mm(o, idn if sign > 0 else T.ni[:], tile, reads + ["idn", "ni"], "ps6", n == 0, n == len(terms) - 1, "ps6d")
+        act(out, o, AF.Copy, ["ps6d"], [name], ["ps6"])
 
     def constants_1():
         fill(T.ones[:], 1.0, "ones")
         op("gp", lambda: g.iota(T.pi[:], [[0, 2]], 0, 1), [], ["pi"])
         sel(T.blk0[:], T.ones[:], [[0, 2], [-16, 8], [0, 16]], OP.is_ge, 0.0, 0, 1, ["ones"], ["blk0"])
         sel(T.blk[:], T.blk0[:], [[0, 2], [16, 8], [0, 16]], OP.is_ge, 0.0, 15, -1, ["blk0"], ["blk"])
-        sel(T.idn[:], one, [[-1, 128]], OP.is_equal, 0.0, 0, 1, ["ones"], ["idn"])
+        sel(T.id2[:], T.blk[:], DOWN, OP.is_equal, 0.0, 0, -1, ["blk"], ["idn"])
         sel(T.pa[:], T.blk[:], UP, OP.is_equal, 0.0, 0, 1, ["blk"], ["pa"])
         sel(T.pb[:], T.blk[:], UP, OP.is_equal, 0.0, -16, 1, ["blk"], ["pb"])
-        tt(T.rvh[:], T.pa[:], T.pb[:], OP.add, ["pa", "pb"], ["rvh"])
+        times(T.ni[:], idn, -1.0, ["idn"], ["ni"])
+        join(T.rv[:], [(1, T.pa[:]), (1, T.pb[:])], ["pa", "pb"], "rv")
         fill(T.zerf[:], 0.0, "zerf")
-        fill(T.neg[:], -0.5, "neg")
         fill(T.b0[:], 0.0, "b0")
         for c in range(NC):
             fill(T["tb%d" % c][:, 0:128], 0.0, "zs_%d" % c)
@@ -366,45 +519,53 @@ def rank_program(g, core, T, topo):
         sel(T.keep[:], one, [[0, 8], [1, 16]], OP.not_equal, 0.0, 0, 0, ["ones"], ["keep"])
         cp(T.b0[:, 15:143:16], s1, ["blk"], ["b0"])
         ts(col(13), col(0), 0.0, OP.is_equal, ["k0"], ["q0"])
-        ts(T.z0h[:], T.b0[:], col(13), OP.mult, ["b0", "q0"], ["z0h"])
+        times(T.z0[:], T.b0[:], col(13), ["b0", "q0"], ["z0"])
         cp(col(1), T.wti[:, 0:1], ["wti"], ["w1"])
         ts(col(2), col(1), 2048.0, OP.is_ge, ["w1"], ["w2"], (), -4096.0, OP.mult)
         tt(col(3), col(1), col(2), OP.add, ["w1", "w2"], ["w3"])
         ts(T.wt0[:], T.b0[:], col(3), OP.mult, ["b0", "w3"], ["wt0"])
-        cp(T.idh[:], T.idn[:], ["idn"], ["idh"], kind="h")
-        ts(T.nih[:], T.idn[:], -1.0, OP.mult, ["idn"], ["nih"], kind="h")
+        fill(T.on6[:], 1.0, "on6")
+        fill(T.on6[:, 0:48:6], 0.0, "on6")
+        for n, step in enumerate([0.0, -2048.0, 0.5, BIG, -BIG, -592.0]):
+            fill(T.mod[0:1, n:48:6], step, "mod%d" % n)
+        together(6)
         ts(T.md[:], T.kt[:], col(0), OP.is_equal, ["kt", "k0"], ["md"])
-        ts(T.k2h[:], one, 2048.0, OP.mult, ["ones"], ["k2h"], kind="h")
-        cp(T.oneh[:], one, ["ones"], ["oneh"], kind="h")
-        sel(T.rs[:], T.zerf[:], [[0, 8], [1, 16]], OP.not_equal, 524288.0, 0, 0, ["zerf"], ["rs"])
+        times(T.k2[0:1, :], T.ones[0:1, 0:128], 128.0, ["ones"], ["k2"])
+        ts(T.oneh[0:1, 0:128], T.ones[0:1, 0:128], 2080.0 / 128, OP.mult, ["ones"], ["oneh"], kind="h")
+        ts(T.oneh[0:1, 128:256], T.ones[0:1, 0:128], 512.0, OP.mult, ["ones"], ["oneh2"], kind="h")
+        fill(T.rs[:], 0.0, "rs")
+        for n, step in [(0, 2.0 ** 20), (16, WHOLE), (17, -WHOLE)]:
+            fill(T.rs[:, n:144:18], step, "rs")
         iota(T.itg[:], [[16, 16]], "itg")
-        ts(T.ktk[:], T.kt[:], 7.5, OP.add, ["kt"], ["ktk"], (), 1.0 / 16, OP.mult, kind="h")
-        ts(T.s2[:], s1, 2.0, OP.mult, ["blk"], ["s2"])
-        ts(T.sn[:], s1, -1.0, OP.mult, ["blk"], ["sn"])
+        iota(T.ktk[0:1, :], [[0, 8], [1, 18]], "ktk")
+        ts(T.ktk[0:1, :], T.ktk[0:1, :], 7.5, OP.add, ["ktk"], ["ktk"], (), 1.0 / 16, OP.mult, kind="h")
+        fill(T.ktk[0:1, 16:144:18], 2.0 ** 40, "ktk")
+        fill(T.ktk[0:1, 17:144:18], 2.0 ** 40, "ktk")
+        fill(T.b18[:, 0:144], -1.0, "b18")
+        sel(T.b18[:, 144:288], T.b18[:, 0:144], [[-16, 8], [0, 18]], OP.is_ge, 0.0, 0, 1, ["b18"], ["b18a"])
+        sel(T.b18[:, 0:144], T.b18[:, 144:288], [[16, 8], [0, 18]], OP.is_ge, 0.0, 15, -1, ["b18a"], ["b18"])
+        times(T.s2[:], s1, 2.0, ["blk"], ["s2"])
+        times(T.sn[:], s1, -1.0, ["blk"], ["sn"])
         for c in range(NC):
             if MJ[c]:
-                sel(T.m1a[:], blk, [[0, 8], [-1, 16]], OP.is_gt, 0.0, MJ[c], 0, ["blk"], ["m1a"])
-                ts(T["sx%d" % c][:], T.m1a[:], -1.0, OP.mult, ["m1a"], ["sx_%d" % c], kind="h")
+                sel(T["sx%d" % c][:], T.b18[:, 0:144], [[0, 8], [-1, 18]], OP.is_gt, 0.0, MJ[c], 0, ["b18"], ["sx_%d" % c])
+            mm(T["ps%d" % (3 * c)][:, 256:384], idn, T.md[:], ["idn", "md"], "ps%d" % (3 * c), True, True, "mdp_%d" % c)
         fill(T.cl[:], 0.0, "cl")
-        for n, (scale, base) in enumerate([(2048.0, 960.0), (128.0, 60.0), (128.0, 61.0), (16.0, 7.5), (128.0, 62.0)]):
-            ts(T.rl[:, 8 * n:8 * n + 8], s1, scale, OP.mult, ["blk"], ["rl%d" % n])
-            fill(T.row[:, 8 * n:8 * n + 8], base, "row%d" % n)
+        for n, base in enumerate([960.0, 60.0, 61.0, 7.5, 62.0]):
+            fill(T.row[0:1, 8 * n:8 * n + 8], base, "row%d" % n)
+        together(5)
+        for n, scale in enumerate([2048.0, 128.0, 128.0, 16.0, 128.0]):
+            times(T.rl[:, 8 * n:8 * n + 8], s1, scale, ["blk"], ["rl%d" % n])
+        together(5)
         ts(T.cl[:, 0:8], T.itg[:, 0:8], col(0), OP.add, ["itg", "k0", "cl"], ["cl"])
         ts(T.cl[:, 24:32], T.itg[:, 0:8], col(0), OP.add, ["itg", "k0", "cl"], ["cl"], (), 16.0, OP.mult)
 
-    def tables():
-        cuts = [slice(512 * n, 512 * n + 512) for n in range(4)]
-        for n, a in enumerate(cuts):
-            ts(T.tabr[:, a], T.rts[:, a], 2047.0, OP.add, ["rts"], ["tabr%d" % n], (), -1.0 / 4096, OP.mult)
-        for n, a in enumerate(cuts):
-            ts(T.tabi[:, a], T.rts[:, a], 0.5 - 1.0 / 8192, OP.mult, ["rts"], ["tabi%d" % n], (), WHOLE, OP.add)
-            act(T.tabc[:, a], T.tabi[:, a], AF.Copy, ["tabi%d" % n], ["tabc%d" % n], scale=1.0 / 1024, bias=-WHOLE / 1024 - 2048.0)
-        dmas("gp", [lambda: g.dma_start(T.tabc[:], T.tabr[:], accum_op=OP.add)], "dacc",
-             ["%s%d" % (w, n) for w in ("tabc", "tabr") for n in range(4)], ["tabc"], 1024)
-
     def rows():
+        ts(T.mdf[:], T.md[:, 0:16], 128.0, OP.mult, ["md"], ["mdf"])
         for m in range(16):
-            ts(T.bmh[:, 128 * m:128 * m + 128], blk, T.md[:, m:m + 1], OP.mult, ["blk", "md"], ["bm%d" % m], kind="h")
+            times(T.bm[:, 128 * m:128 * m + 128], blk, T.mdf[:, m:m + 1], ["blk", "mdf"], ["bm%d" % m])
+            if m % 4 == 3:
+                together(4)
 
     def constants_2():
         sel(T.e8[:], one, [[-16, 8], [0, 16]], OP.is_equal, 0.0, -8, 1, ["ones"], ["e8"])
@@ -412,44 +573,41 @@ def rank_program(g, core, T, topo):
         sel(T.m3[:], one, [[-16, 8], [1, 8], [0, 2]], OP.is_equal, 0.0, -15, 1, ["ones"], ["m3"])
         sel(T.pc[:], T.blk[:], DOWN, OP.is_equal, 0.0, -1, -1, ["blk"], ["pc"])
         sel(T.pd[:], T.blk[:], DOWN, OP.is_equal, 0.0, 15, -1, ["blk"], ["pd"])
-        tt(T.shh[:], T.pc[:], T.pd[:], OP.add, ["pc", "pd"], ["shh"])
-        ts(T.ni[:], T.idn[:], -1.0, OP.mult, ["idn"], ["ni"], kind="h")
-        ts(T.n16h[:], T.idn[:], -16.0, OP.mult, ["idn"], ["n16h"], kind="h")
-        ts(T.b2[:], T.b0[:], 2.0, OP.mult, ["b0"], ["b2"], kind="h")
-        ts(T.bn[:], T.b0[:], -1.0, OP.mult, ["b0"], ["bn"], kind="h")
-        ts(T.rh[:], T.itg[:, 0:8], col(0), OP.add, ["itg", "k0"], ["rh"], (), 1792.0, OP.add)
+        join(T.sh[:], [(1, T.pc[:]), (1, T.pd[:])], ["pc", "pd"], "sh")
+        times(T.i128[:], idn, 128.0, ["idn"], ["i128"])
+        times(T.n16[:], idn, -16.0, ["idn"], ["n16"])
+        if "r" in "".join(GW):
+            times(T.b2[:], T.b0[:], 2.0, ["b0"], ["b2"])
+            times(T.bn[:], T.b0[:], -1.0, ["b0"], ["bn"])
+        ts(T.base[:, 0:8], T.ones[:, 0:8], 2048.0, OP.mult, ["ones"], ["base0"])
+        ts(T.base[:, 8:16], T.itg[:, 0:8], col(0), OP.add, ["itg", "k0"], ["base1"], (), 1792.0, OP.add)
         ts(T.ata[:], T.itg[:, 0:8], col(0), OP.add, ["itg", "k0"], ["ata"], (), 1153.0, OP.add)
-        ts(T.ath[:], T.ata[:], 16.0, OP.mult, ["ata"], ["ath"])
-        ts(T.bk[:], T.b0[:], 2048.0, OP.mult, ["b0"], ["bk"], kind="h")
+        ts(T.base[:, 16:24], T.ata[:], 16.0, OP.mult, ["ata"], ["base2"])
+        times(T.bk[:], T.b0[:], 2048.0, ["b0"], ["bk"])
         ts(col(5), col(0), 8.0, OP.is_equal, ["k0"], ["q8"])
         ts(col(6), col(0), 9.0, OP.is_ge, ["k0"], ["q9"], (), 1.0, OP.add)
         ts(col(7), col(5), -8.0, OP.mult, ["q8"], ["q7"])
         tt(col(9), col(6), col(7), OP.add, ["q9", "q7"], ["qc"])
         ts(col(14), col(0), 15.0, OP.is_lt, ["k0"], ["qd"], (), -128.0, OP.mult)
-        ts(T.c0[:], T.b0[:], col(9), OP.mult, ["b0", "qc", "qd"], ["c0"], (), col(14), OP.mult)
-        ts(T.c8[:], T.b0[:], col(5), OP.mult, ["b0", "q8"], ["c8"], (), 2048.0, OP.mult)
-        ts(T.g8[:], one, col(5), OP.mult, ["ones", "q8"], ["g8"])
-        cp(T.anh[:], T.an[:], ["an"], ["anh"], kind="h")
-        tt(T.m1a[:], T.e8[:], T.idn[:], OP.subtract, ["e8", "idn"], ["m1a"])
-        tt(T.m2a[:], T.an[:], T.e8[:], OP.subtract, ["an", "e8"], ["m2a"])
-        sel(T.m1b[:], T.m1a[:], [[0, 8], [1, 16]], OP.is_ge, 0.0, -8, 0, ["m1a"], ["m1b"])
-        ts(T.m1[:], T.m1b[:], 4096.0, OP.mult, ["m1b"], ["m1"], kind="h")
+        tt(col(11), col(9), col(14), OP.mult, ["qc", "qd"], ["c0"])
+        ts(col(12), col(5), 2048.0, OP.mult, ["q8"], ["c8"])
+        cp(T.g8[:, 0:1], col(5), ["q8"], ["g8"])
+        join(T.m1a[:], [(1, T.e8[:]), (-1, idn)], ["e8"], "m1a")
+        join(T.m2a[:], [(1, T.an[:]), (-1, T.e8[:])], ["an", "e8"], "m2a")
+        sel(T.m1[:], T.m1a[:], [[0, 8], [1, 16]], OP.is_ge, 0.0, -8, 0, ["m1a"], ["m1"])
         sel(T.m2b[:], T.m2a[:], [[0, 8], [-1, 16]], OP.is_ge, 0.0, 7, 0, ["m2a"], ["m2b"])
-        tt(T.m2[:], T.m2b[:], T.m3[:], OP.subtract, ["m2b", "m3"], ["m2"])
-        fill(T.b0h[:], 0.0, "b0h")
-        cp(T.b0h[:, 15:271:16], T.blk[:, 0:256:16], ["blk", "b0h"], ["b0h"])
-        ts(T.cw[:], T.rvh[:, 0:128], col(0), OP.mult, ["rvh", "k0"], ["cw0"], (), 6.5, OP.is_gt)
-        ts(T.ct[:], T.idn[:], col(13), OP.mult, ["idn", "q0"], ["ct"])
-        ts(col(15), col(0), 15.0, OP.is_equal, ["k0"], ["q15"], (), 4096.0, OP.mult)
-        tt(col(16), col(15), col(13), OP.subtract, ["q15", "q0"], ["q16"])
-        ts(T.cc[:], T.idn[:], col(16), OP.mult, ["idn", "q16", "cw0"], ["cc", "cw"])
-        ts(T.q1[:], T.kt[:], 1.0, OP.is_equal, ["kt"], ["q1"], kind="h")
+        join(T.m2[:], [(1, T.m2b[:]), (-1, T.m3[:])], ["m2b", "m3"], "m2")
+        ts(T.cw[:], T.rv[:], col(0), OP.mult, ["rv", "k0"], ["cw"], (), 6.5, OP.is_gt)
+        times(T.ct[:], T.id2[:], col(13), ["idn", "q0"], ["ct"])
+        ts(col(15), col(0), 15.0, OP.is_equal, ["k0"], ["q15"])
+        times(T.cc[:], T.id2[:], col(15), ["idn", "q15"], ["cc"])
+        ts(T.q1[0:1, :], T.kt[0:1, :], 1.0, OP.is_equal, ["kt"], ["q1"], kind="h")
         sel(T.pa[:, 0:128], blk, DOWN[1:], OP.is_equal, 0.0, -2, -1, ["blk"], ["pa"])
-        tt(T.pb[:, 0:128], T.pa[:, 0:128], T.pc[:, 0:128], OP.subtract, ["pa", "pc"], ["pb"])
-        sel(T.pa[:, 128:256], T.pb[:, 0:128], [[0, 8], [-1, 16]], OP.is_ge, 0.0, 9, 0, ["pb"], ["pa2"])
-        sel(T.pb[:, 128:256], T.m1a[:], [[0, 8], [1, 16]], OP.is_equal, 0.0, -15, 0, ["m1a"], ["pb2"])
-        tt(T.blk0[:, 0:128], T.pa[:, 128:256], T.pb[:, 128:256], OP.add, ["pa2", "pb2", "blk"], ["blk0"])
-        tt(T.mc[:], T.blk0[:, 0:128], T.pd[:, 0:128], OP.add, ["blk0", "pd"], ["mc"])
+        join(T.pb[:, 0:128], [(1, T.pa[:, 0:128]), (-1, T.pc[:, 0:128])], ["pa", "pc"], "pb")
+        sel(T.pa[:, 128:256], T.pb[:, 0:128], [[0, 8], [-1, 16]], OP.is_ge, 0.0, 9, 0, ["pb"], ["pa2", "pa"])
+        sel(T.pb[:, 128:256], T.m1a[:], [[0, 8], [1, 16]], OP.is_equal, 0.0, -15, 0, ["m1a"], ["pb2", "pb"])
+        join(T.mc[:, 0:128], [(1, T.pa[:, 128:256]), (1, T.pb[:, 128:256]), (1, T.pd[:, 0:128])], ["pa2", "pb2", "pd"], "mc0")
+        times(T.mc[:, 128:256], T.mc[:, 0:128], 1.0, ["mc0"], ["mc"])
 
     def window(sem, src, dram, win, start, read, name):
         dmas("sy", [lambda: SY.dma_start(dram[:, 0:16, :], src), lambda: SY.dma_start(dram[:, 16:32, :], src)], sem % 1, [read], [name + "d"], span(src))
@@ -469,14 +627,11 @@ def rank_program(g, core, T, topo):
         ts(col(17), col(0), 9.0, OP.is_ge, ["k0"], ["far"], (), 8192.0, OP.mult)
         ts(col(18), col(17), -4096.0, OP.add, ["far"], ["far2"])
         tt(T.txh[:, 2:3], T.txh[:, 0:1], col(18), OP.max, ["far2", "txh"], ["txh"])
-        mm(T.ps7[:, 0:8], T.rvh[:, 0:128], T.txh[:], ["rvh", "txh"], "ps7", True, True, "ps7d")
+        mm(T.ps7[:, 0:8], T.rv[:, 0:128], T.txh[:], ["rv", "txh"], "ps7", True, True, "ps7d")
         act(T.tx[:], T.ps7[:, 0:8], AF.Copy, ["ps7d"], ["tx"], ["ps7"])
         window("dx%d", T.tx[:], T.dx, T.tw, back, "tx", "tw")
 
-    XR, TABR = ["x_lo", "x_hi"], ["tabr%d" % n for n in range(4)]
-    def finer(lo, hi, q):
-        return [(a, a + STEP[q], q) for a in range(lo, hi, STEP[q])]
-
+    XR = ["x_lo", "x_hi"]
 
     def stages(t, c):
         X, Y, Z = ["ps%d" % (3 * c + b) for b in range(3)]
@@ -486,16 +641,19 @@ def rank_program(g, core, T, topo):
         part = lambda name, n, w=128: T["%s%d" % (name, c)][:, w * n:w * n + w]
         TI, TF, TB, HH = [(lambda name: lambda n: part(name, n))(name) for name in ("ti", "tf", "tb", "hh")]
         UI, UF, UH, LS = [(lambda name: lambda n: part(name, n, 8))(name) for name in ("ui", "uf", "uh", "ls")]
-        lu, hh, tb = T["lu%d" % c], T["hh%d" % c], T["tb%d" % c]
+        lu, hh, tb, tf, uf = [T["%s%d" % (name, c)] for name in ("lu", "hh", "tb", "tf", "uf")]
         w0, l0 = CW * (NC * t + c), 8 * (NC * t + c)
-        wres, lres = "wl%d_%d" % (t, c), "ll%d_%d" % (t, c)
+        wres, lres, made = "wl%d_%d" % (t, c), "ll%d_%d" % (t, c), r("lo%d" % t)
+        LO = lambda lo, hi: T.lo[:, 3 * l0 + 8 * lo:3 * l0 + 8 * hi]
         last = t == VIS - 1
-        x0 = HH(4)
+        x0 = TB(7)
         blocks = lambda name, lo, hi: [r("%s%d" % (name, b)) for b in range(lo // 128, hi // 128)]
+        sized = lambda js, hs=(0, 1): [r("mx%d.%d" % (j, h)) for j in js for h in hs]
         XRS = blocks("xr", 0, 2048)
         x = T.xs[:, 2048:6144]
 
         shift = 128 - 16 * ((t + 1 + (t + 1) // nrank) - (t + t // nrank))
+        moved = slice(shift, shift + 128)
 
         def send(out, src, name, sem, lands, extra):
             rid, pid, _ = topo.addr(nxt)
@@ -506,42 +664,49 @@ def rank_program(g, core, T, topo):
                 total["sent"] = total.get("sent", 0) + len(topo.engines(core, nxt))
                 total[sem] = len(topo.engines(T.cores[(rank - 1) % nrank], core))
                 wrote[lands] = (sem, total[sem], {}, "net")
-            moving[len(nodes)] = (extra, 750.0)
-            nodes.append(("gp", emit, [name], [lands], [], 1000.0, 900.0 + extra))
+            moving[len(nodes)] = (750.0 * NET, extra * NET, (900.0 + extra) * NET)
+            nodes.append(("gp", emit, [name], [lands], [], 1000.0 * NET))
 
         def start():
             ts(HH(3), T.wdi[:, CW * c:CW * c + CW], -2048.0, OP.add, ["wdi"], [r("h3")])
             for m in range(16):
-                mm(PX[:, 8:16], T.z0h[:, 15 - m:143 - m], hh[:, 384 + m:512:16], ["z0h", r("h3")], X, m == 0, m == 15, r("w0p"))
-            ts(T.ll[:, l0:l0 + 8], PX[:, 8:16], 2048.0, OP.add, [r("w0p")], [lres], [X])
-            mm(PZ[:, 384:512], T.rvh[:, 0:128], HH(3), ["rvh", r("h3")], Z, True, True, r("zf"))
+                mm(PX[:, 48:56], T.z0[:, 15 - m:143 - m], hh[:, 384 + m:512:16], ["z0", r("h3")], X, m == 0, m == 15, r("w0p"))
+            ts(T.ll[:, l0:l0 + 8], PX[:, 48:56], 2048.0, OP.add, [r("w0p")], [lres], [X])
+            mm(PZ[:, 384:512], T.rv[:, 0:128], HH(3), ["rv", r("h3")], Z, True, True, r("zf"))
             act(T.wl[:, w0:w0 + 128], PZ[:, 384:512], AF.Copy, [r("zf")], [wres], [Z])
 
         def first():
-            cp(x0, x.indirect(T.ll[:, l0:l0 + 8]), XR + [lres], [r("x0")], kind="g")
+            copy(FIRST[c], x0, x.indirect(T.ll[:, l0:l0 + 8]), XR + [lres], [r("x0")], kind="g")
 
         def offer():
-            if LEAD[c] == "s":
-                return
             o = PX[:, 384:512]
-            mm(o, T.cw[:], T.wl[:, w0:w0 + 128], ["cw", wres], X, True, False, r("cp"))
-            mm(o, T.ct[:], TF(0), ["ct", r("f0")], X, False, False, r("cp"), False)
-            mm(o, T.cc[:], TF(3), ["cc", r("rc")], X, False, True, r("cp"), False)
-            cp(HH(3), o, [r("cp")], [r("h3")], [X])
+            mm(o, T.cw[:, moved], T.wl[:, w0:w0 + 128], ["cw", wres], X, True, False, r("cp"))
+            mm(o, T.cc[:, moved], HH(3), ["cc", r("h3")], X, False, False, r("cp"), False)
+            mm(o, T.ct[:, moved], HH(4), ["ct", r("tl")], X, False, True, r("cp"), False)
+            copy(OFFER[c], TF(7), o, [r("cp")], [r("f7")], [X])
 
         def lead():
-            o = PY[:, 0:128]
-            if LEAD[c] == "s":
-                cp(HH(5), PZ[:, 384:512], [r("zf")], [r("h5")], [Z])
-            else:
-                mm(o, T.q1[0:1, :], T.ones[0:1, 0:128], ["q1", "ones"], Y, True, False, r("nvp"))
-                mm(o, T.mc[:], TB(6), ["mc", r("P")], Y, False, True, r("nvp"))
-                tt(HH(5), HH(3), o, OP.mult, [r("h3"), r("nvp")], [r("h5")], [Y])
+            o = PY[:, 128:256]
+            mm(o, T.q1[0:1, :], T.ones[0:1, 0:128], ["q1", "ones"], Y, True, False, r("d2"))
+            mm(o, T.mc[:, moved], TB(6), ["mc", r("P")], Y, False, True, r("d2"))
+            tt(HH(5), TF(7), o, OP.mult, [r("f7"), r("d2")], [r("h5")], [Y])
+
+        def lists():
+            lo, hi = (1 if last else 0), (2 if FAST[c] == "f" else 3)
+            ts(HH(6), TB(6), col(11), OP.mult, [r("P"), "c0"], [r("h6")], kind="h")
+            if hi == 3:
+                ts(HH(7), TB(6), col(12), OP.mult, [r("P"), "c8"], [r("h7")], kind="h")
+            o = PY[:, 400 + 8 * lo:400 + 8 * hi]
+            mm(o, idn, T.base[:, 8 * lo:8 * hi], ["idn", "base0", "base1", "base2"], Y, True, False, r("x0p"))
+            if hi == 3:
+                mm(PY[:, 416:424], T.i128[:], UH(0), ["i128", r("y")], Y, False, False, r("x0p"))
+                mm(PY[:, 416:424], T.n16[:], UH(2), ["n16", r("uq")], Y, False, False, r("x0p"))
             for m in range(16):
-                pick = T.z0h[:, 15 - m:143 - m] if LEAD[c] == "s" else T.b0h[:, shift + 15 - m:shift + 143 - m]
-                mm(PY[:, 400:408], pick, hh[:, 640 + m:768:16], ["b0h", "z0h", r("h5")], Y, m == 0, m == 15, r("x0p"))
-            ts(T.lo[:, l0:l0 + 8], PY[:, 400:408], 2048.0, OP.add, [r("x0p")], [r("lo%d" % t)], [Y])
-            send(T.ll[:, l0 + 8 * NC:l0 + 8 * NC + 8], T.lo[:, l0:l0 + 8], r("lo%d" % t), "al%d_%d" % (t + 1, c), "ll%d_%d" % (t + 1, c), 20.0)
+                mm(o, T.b0[:, 15 - m:143 - m], hh[:, 640 + 128 * lo + m:640 + 128 * hi:16], ["b0"] + [r("h%d" % (5 + n)) for n in range(lo, hi)],
+                   Y, False, m == 15, r("x0p"), m > 0)
+            cp(LO(lo, hi), o, [r("x0p")], [made], [Y])
+            if not last:
+                send(T.ll[:, l0 + 8 * NC:l0 + 8 * NC + 8], LO(0, 1), made, "al%d_%d" % (t + 1, c), "ll%d_%d" % (t + 1, c), 20.0)
 
         def wwin():
             window("dw%d" + str(c), T.wl[:, w0:w0 + 128], T["dw%d" % c], T["ww%d" % c], back, wres, r("ww"))
@@ -550,84 +715,88 @@ def rank_program(g, core, T, topo):
             window("dp%d" + str(c), T["pk%d" % c][:], T["dp%d" % c], T["pw%d" % c], lambda k: k + 1, r("pk"), r("pw"))
 
         def weigh():
+            mm(PX[:, 0:48], T.ones[0:1, 0:128], T.mod[0:1, :], ["ones"] + ["mod%d" % n for n in range(6)], X, True, False, r("uw"))
             for m in range(16):
-                mm(PX[:, 0:8], T.wt0[:, 15 - m:143 - m], hh[:, 512 + m:640:16], ["wt0", r("x0")], X, m == 0, m == 15, r("uw"))
+                mm(PX[:, 0:48:6], T.wt0[:, 15 - m:143 - m], tb[:, 896 + m:1024:16], ["wt0", r("x0")], X, False, m == 15, r("uw"), m > 0)
             if MJ[c]:
-                mm(PY[:, 384:512], T.idh[:], x0, ["idh", r("x0")], Y, True, True, r("x0p"))
+                mm(PY[:, 384:512], idn, x0, ["idn", r("x0")], Y, True, True, r("x0p"))
 
         def relator():
-            cp(UI(0), PX[:, 0:8], [r("uw")], [r("u0")], [X])
-            ts(UI(1), UI(0), 4095, OP.bitwise_and, [r("u0")], [r("u1")])
-            ts(UH(0), UI(1), -2048.0, OP.add, [r("u1")], [r("y")])
-            ts(UF(0), UI(1), 3232.0, OP.add, [r("u1")], [r("uz")])
-            tt(UI(2), UH(0), UF(0), OP.mult, [r("y"), r("uz")], [r("u2")])
+            scan(uf[:, 0:48], T.on6[:], PX[:, 0:48], 0.0, OP.mult, OP.add, ["on6", r("uw")], [r("u0")], [X])
+            tt(UF(6), PX[:, 0:48:6], uf[:, 5:48:6], OP.subtract, [r("uw"), r("u0")], [r("u1")], [X])
+            tt(UI(2), UF(6), UF(6), OP.mult, [r("u1")], [r("u2")])
             ts(UI(3), UI(2), 5, OP.arith_shift_right, [r("u2")], [r("u3")], (), 2047, OP.bitwise_and)
             cp(LS(1), UI(3), [r("u3")], [r("cl")])
             cp(lu[:, 0:128], T.rts[:].indirect(LS(1)), ["rts", r("cl")], [r("lr")], kind="g")
-            ts(UH(1), UI(1), 1.0 / 16, OP.mult, [r("u1")], [r("uq")], (), 1025.0 - 15.0 / 32, OP.add)
 
         def spread():
-            mm(PZ[:, 384:512], T.k2h[0:1, :], T.oneh[0:1, :], ["k2h", "oneh"], Z, True, False, r("zf"))
+            ts(UH(0), UF(6), 1.0 / 128, OP.mult, [r("u1")], [r("y")], (), -2640.0 / 128, OP.add)
+            ts(UH(1), UF(6), 16.0, OP.mult, [r("u1")], [r("y16")], (), -2640.0 * 16, OP.add)
+            ts(UH(2), UF(6), 1.0 / 16, OP.mult, [r("u1")], [r("uq")], (), 1025.0 - 37 - 15.0 / 32, OP.add)
+            together(3)
+            mm(PZ[:, 0:256], T.k2[0:1, :], T.oneh[0:1, :], ["k2", "oneh", "oneh2"], Z, True, False, [r("k1"), r("k2")])
             for m in range(16):
-                mm(PZ[:, 384 + m:512:16], T.bmh[:, 128 * m:128 * m + 128], UH(0), ["bm%d" % m, r("y")], Z, False, m == 15, r("zf"))
+                mm(PZ[:, m:256:16], T.bm[:, 128 * m:128 * m + 128], T["uh%d" % c][:, 0:16], ["bm%d" % m, r("y"), r("y16")], Z, False, m == 15,
+                   [r("k1"), r("k2")], m > 0)
 
         def gather_r(n):
-            for lo, hi, q in finer(*GR[c][n]):
-                i = x.indirect(lu[:, lo // 16:hi // 16])
-                if q == "s":
-                    act(xr[:, lo:hi], i, AF.Copy, XR + [r("lr")], blocks("xr", lo, hi), kind="g")
-                else:
-                    cp(xr[:, lo:hi], i, XR + [r("lr")], blocks("xr", lo, hi), kind="g")
+            lo, hi = 512 * n, 512 * n + 512
+            copy((GR if t else GR0)[c][n], xr[:, lo:hi], x.indirect(lu[:, lo // 16:hi // 16]), XR + [r("lr")], blocks("xr", lo, hi), kind="g")
 
         def letters():
-            act(TF(0), T.tabr[:].indirect(LS(1)), AF.Copy, TABR + [r("cl")], [r("f0")], kind="g", scale=-4096.0, bias=-2047.0)
+            ts(T["pk%d" % c][:], lu[:, 0:128], -2048.0, OP.add, [r("lr")], [r("pk")])
 
         def tail():
-            tt(TI(0), TF(0), PZ[:, 384:512], OP.mult, [r("f0"), r("zf")], [r("t0")], [Z])
+            tt(TF(6), TF(0), PZ[:, 0:128], OP.mult, [r("f0"), r("k1")], [r("f6")], [Z])
+            tt(TI(0), TF(6), PZ[:, 128:256], OP.add, [r("f6"), r("k2")], [r("t0")], [Z])
             ts(TI(1), TI(0), 5, OP.arith_shift_right, [r("t0")], [r("t1")], (), 4095, OP.bitwise_and)
-            tt(TI(2), TF(0), TI(1), OP.add, [r("f0"), r("t1")], [r("t2")])
-            ts(TI(3), TI(2), 4095, OP.bitwise_and, [r("t2")], [r("t3")])
-            tt(T["pk%d" % c][:], T.tabc[:].indirect(LS(1)), TI(3), OP.add, ["tabc", r("cl"), r("t3")], [r("pk")], kind="g")
+            ts(HH(4), TI(1), -2048.0, OP.add, [r("t1")], [r("tl")])
+
+        def other():
+            ts(TI(2), TF(0), 0.5, OP.mult, [r("f0")], [r("t2")], (), -0.25, OP.add)
+            ts(TF(3), TI(2), 4.0, OP.mult, [r("t2")], [r("t3")], (), 1.0, OP.add)
+            tt(HH(3), TF(3), TF(0), OP.subtract, [r("t3"), r("f0")], [r("h3")])
 
         mj = MJ[c]
-        positive = [any(how == "r" for lo, _, how in GW[c] if lo // 1024 == h) for h in range(2)]
+        positive = ["r" in GW[c][2 * h:2 * h + 2] for h in range(2)]
         spare = [("ps6", "ps6d"), ("ps7", "ps7d")]
 
-        def biggest():
+        def biggest(h):
             for j in range(mj):
-                tt(mx[:, 128 * j:128 * j + 128], xr[:, j:2048:16], PY[:, 384:512], OP.max, XRS + [r("x0p")], [r("mx%d" % j)], [Y])
+                tt(mx[:, j, 64 * h:64 * h + 64], xr[:, 1024 * h + j:1024 * h + 1024:16], PY[:, 384 + 64 * h:448 + 64 * h], OP.max,
+                   XRS[8 * h:8 * h + 8] + [r("x0p")], sized([j], [h]), [Y])
+                if j in (mj // 2 - 1, mj - 1):
+                    together(mj // 2)
 
-        def apart(n):
-            for j0 in range(mj, 16, 4)[n::2]:
-                js = range(j0, min(j0 + 4, 16))
-                D, tag = spare[n]
+        def apart(h):
+            D, tag = spare[h]
+            for j0 in range(mj, 16, 8):
+                js = range(j0, min(j0 + 8, 16))
                 for j in js:
-                    o = T[D][:, 128 * (j - j0):128 * (j - j0) + 128]
-                    mm(o, T.idn[:], xr[:, j:2048:16], ["idn"] + XRS, D, True, False, tag, j > j0)
-                    mm(o, T.nih[:], x0, ["nih", r("x0")], D, False, True, tag)
-                act(mx[:, 128 * j0:128 * (js[-1] + 1)], T[D][:, 0:128 * len(js)], AF.Abs, [tag], [r("mx%d" % j) for j in js], [D])
+                    o = T[D][:, 64 * (j - j0):64 * (j - j0) + 64]
+                    mm(o, idn, xr[:, 1024 * h + j:1024 * h + 1024:16], ["idn"] + XRS[8 * h:8 * h + 8], D, True, False, tag, j > j0)
+                    mm(o, T.ni[:], tb[:, 896 + 64 * h:960 + 64 * h], ["ni", r("x0")], D, False, True, tag)
+                act(mx[:, j0:js[-1] + 1, 64 * h:64 * h + 64], T[D][:, 0:64 * len(js)], AF.Abs, [tag], sized(js, [h]), [D])
 
         def keys():
-            mm(PX[:, 128:256], T.ones[0:1, 0:128], T.ktk[0:1, :], ["ones", "ktk"], X, True, False, r("key"))
+            mm(PX[:, 96:240], T.ones[0:1, 0:128], T.ktk[0:1, :], ["ones", "ktk"], X, True, False, r("key"))
             if mj:
-                mm(PX[:, 128:256], x0, T["sx%d" % c][:], [r("x0"), r("sx")], X, False, False, r("key"))
+                mm(PX[:, 96:240], x0, T["sx%d" % c][:], [r("x0"), r("sx")], X, False, False, r("key"))
             for j in range(mj):
-                mm(PX[:, 128 + j:256:16], xr[:, j:2048:16], T.sn[:], XRS + ["sn"], X, False, False, r("key"), j > 0)
+                mm(PX[:, 96 + j:240:18], xr[:, j:2048:16], T.sn[:], XRS + ["sn"], X, False, False, r("key"), j > 0)
             for j in range(16):
-                mm(PX[:, 128 + j:256:16], mx[:, 128 * j:128 * j + 128], T.s2[:] if j < mj else s1, [r("mx%d" % j), "s2", "blk"], X, False, j == 15,
+                mm(PX[:, 96 + j:240:18], mx[:, j, :], T.s2[:] if j < mj else s1, sized([j]) + ["s2", "blk"], X, False, j == 15,
                    r("key"), j % 4 != mj % 4 and j > 0)
 
         def least():
-            sc = T["tf%d" % c][:, 128 + 15:256:16]
-            scan(TF(1), T.rs[:], PX[:, 128:256], 0.0, OP.max, OP.min, ["rs", r("key")], [r("f1")], [X])
-            cp(UI(5), sc, [r("f1")], [r("u5")])
-            tt(tb[:, 0:128:16], sc, UI(5), OP.subtract, [r("f1"), r("u5")], [r("zs")])
+            scan(tf[:, 1024:1168], T.rs[:], PX[:, 96:240], 0.0, OP.add, OP.min, ["rs", r("key")], [r("f1")], [X])
+            tt(tb[:, 0:128:16], tf[:, 1024 + 15:1168:18], tf[:, 1024 + 17:1168:18], OP.subtract, [r("f1")], [r("zs")])
             scan(TB(1), T.keep[:], TB(0), 0.0, OP.mult, OP.add, ["keep", r("zs")], [r("sk")], kind="h")
-            tt(TB(2), TB(1), T.md[:], OP.mult, [r("sk"), "md"], [r("skd")])
-            o = PX[:, 16:56]
+            tt(TB(2), TB(1), PX[:, 256:384], OP.mult, [r("sk"), r("mdp")], [r("skd")], [X])
+            o = PX[:, 56:96]
             mm(o, T.ones[0:1, 0:128], T.row[0:1, :], ["ones"] + ["row%d" % n for n in range(5)], X, True, False, r("slp"))
-            mm(o, T.idn[:], T.cl[:], ["idn", "cl"], X, False, False, r("slp"))
-            mm(o, TB(2), T.rl[:], [r("skd")] + ["rl%d" % n for n in range(5)], X, False, True, r("slp"), False)
+            mm(o, idn, T.cl[:], ["idn", "cl"], X, False, False, r("slp"))
+            mm(o, TB(2), T.rl[:], [r("skd")] + ["rl%d" % n for n in range(5)], X, False, True, r("slp"))
             cp(T["ls%d" % c][:, 16:56], o, [r("slp")], [r("sl")], [X])
 
         def turn():
@@ -641,52 +810,42 @@ def rank_program(g, core, T, topo):
                     act(TF(out), T.tw[:].indirect(LS(by)), AF.Identity, ["tw", r("sl"), "thr"], [r("f%d" % out)], kind="g", bias=col(10))
 
         def gather_w(n):
-            for lo, hi, how in GW[c][n:n + 1]:
-                i = x.indirect(lu[:, 128 + lo // 16:128 + hi // 16])
-                d, m = blocks("df", lo, hi), blocks("mx", lo, hi)
-                if how == "s":
-                    act(df[:, lo:hi], i, AF.Copy, XR + [r("lw")], d, kind="g")
-                    D, tag = spare[n % 2]
-                    o = T[D][:, 0:hi - lo]
-                    mm(o, T.ni[:], xr[:, lo:hi], ["ni"] + blocks("xr", lo, hi), D, True, False, tag)
-                    mm(o, T.idn[:], df[:, lo:hi], ["idn"] + d, D, False, True, tag, False)
-                    act(mx[:, lo:hi], o, AF.Abs, [tag], m, [D])
-                    continue
-                for a, b, _ in finer(lo, hi, "v"):
-                    tt(df[:, a:b], x.indirect(lu[:, 128 + a // 16:128 + b // 16]), xr[:, a:b], OP.subtract,
-                       XR + [r("lw")] + blocks("xr", a, b), blocks("df", a, b), kind="g")
-                if how == "a":
-                    act(mx[:, lo:hi], df[:, lo:hi], AF.Relu if positive[lo // 1024] else AF.Abs, d, m)
-                else:
-                    ts(mx[:, lo:hi], df[:, lo:hi], 0.0, OP.max, d, m, kind="h")
+            lo, hi, how = 512 * n, 512 * n + 512, GW[c][n]
+            d, m, out = blocks("df", lo, hi), sized(range(4 * n, 4 * n + 4)), mx[:, 4 * n:4 * n + 4, :]
+            if how == "s":
+                act(df[:, lo:hi], x.indirect(lu[:, 128 + lo // 16:128 + hi // 16]), AF.Copy, XR + [r("lw")], d, kind="g")
+                D, tag = spare[n % 2]
+                mm(T[D][:], T.ni[:], xr[:, lo:hi], ["ni"] + blocks("xr", lo, hi), D, True, False, tag)
+                mm(T[D][:], idn, df[:, lo:hi], ["idn"] + d, D, False, True, tag, False)
+                act(out, T[D][:], AF.Abs, [tag], m, [D])
+                return
+            for a in range(lo, hi, FINE[c]):
+                b = a + FINE[c]
+                tt(df[:, a:b], x.indirect(lu[:, 128 + a // 16:128 + b // 16]), xr[:, a:b], OP.subtract,
+                   XR + [r("lw")] + blocks("xr", a, b), blocks("df", a, b), kind="g")
+            if how == "a":
+                act(out, df[:, lo:hi], AF.Relu if positive[n // 2] else AF.Abs, d, m)
+            else:
+                ts(out, df[:, lo:hi], 0.0, OP.max, d, m, kind="h")
 
         def sizes(h):
-            for lo in (1024 * h,):
-                relu = positive[h]
-                o = PY[:, 128 + lo // 16:192 + lo // 16]
-                if relu:
-                    for k in range(16):
-                        mm(o, T.bn[:, 15 - k:143 - k], df[:, lo + k:lo + 1024:16], ["bn"] + blocks("df", lo, lo + 1024), Y, k == 0, False, r("d2"))
+            lo, relu = 1024 * h, positive[h]
+            o = PY[:, 128 + lo // 16:192 + lo // 16]
+            if relu:
                 for k in range(16):
-                    mm(o, (T.b2 if relu else T.b0)[:, 15 - k:143 - k], mx[:, lo + k:lo + 1024:16], ["b0", "b2"] + blocks("mx", lo, lo + 1024),
-                       Y, k == 0 and not relu, k == 15, r("d2"))
+                    mm(o, T.bn[:, 15 - k:143 - k], df[:, lo + k:lo + 1024:16], ["bn"] + blocks("df", lo, lo + 1024), Y, k == 0, False, r("d2"))
+            for k in range(16):
+                mm(o, (T.b2 if relu else T.b0)[:, 15 - k:143 - k], mx[:, 8 * h:8 * h + 8, k:128:16],
+                   ["b2" if relu else "b0"] + sized(range(8 * h, 8 * h + 8)), Y, k == 0 and not relu, k == 15, r("d2"), False if k == 0 else None)
 
         def halves():
             act(TB(3), xr[:].indirect(LS(5)), AF.Copy, XRS + [r("sl")], [r("q15")], kind="g")
-            mm(PY[:, 0:128], T.idh[:], x0, ["idh", r("x0")], Y, True, False, r("nvp"))
-            if HALF[c] == "s":
-                mm(PY[:, 0:128], T.ones[0:1, 0:128], T.neg[0:1, :], ["ones", "neg"], Y, False, False, r("nvp"))
-            mm(PY[:, 0:128], T.idn[:], TB(3), ["idn", r("q15")], Y, False, True, r("nvp"), False)
-            if HALF[c] == "s":
-                act(TF(6), PY[:, 0:128], AF.Copy, [r("nvp")], [r("f6")], [Y], scale=0.5, bias=WHOLE)
-                act(T.nvb[:, CW * c:CW * c + CW], TF(6), AF.Copy, [r("f6")], [r("nv")], bias=-WHOLE)
-            else:
-                ts(T.nvi[:, CW * c:CW * c + CW], PY[:, 0:128], 0.5, OP.mult, [r("nvp")], [r("nv")], [Y], -0.25, OP.add)
+            mm(PY[:, 0:128], idn, x0, ["idn", r("x0")], Y, True, False, r("nvp"))
+            mm(PY[:, 0:128], idn, TB(3), ["idn", r("q15")], Y, False, True, r("nvp"))
+            ts(T.nvi[:, CW * c:CW * c + CW], PY[:, 0:128], 0.5, OP.mult, [r("nvp")], [r("nv")], [Y], -0.25, OP.add)
 
         def unpack():
             act(TF(0), T["pw%d" % c][:].indirect(LS(2)), AF.Copy, [r("pw"), r("sl")], [r("f0")], kind="g")
-            ts(TI(4), TF(0), 1.0 / 8192, OP.add, [r("f0")], [r("tl")])
-            tt(TF(3), TF(0), TI(4), OP.subtract, [r("f0"), r("tl")], [r("rc")])
 
         def match():
             tt(TB(4), PY[:, 128:256], TF(2), OP.is_gt, [r("d2"), r("f2")], [r("dis")], [Y])
@@ -695,17 +854,13 @@ def rank_program(g, core, T, topo):
             ts(TB(6), PY[:, 256:384], T.two[:, 47:48], OP.is_lt, [r("pre"), "two"], [r("P")], [Y])
 
         def aim():
-            o = PX[:, 256:264]
-            if FAST[c] == "f":
-                tt(TB(8), PY[:, 128:256], TF(5), OP.is_gt, [r("d2"), r("f5")], [r("far")], [Y])
-            mm(o, T.idh[:], T.ath[:], ["idh", "ath"], X, True, False, r("atp"))
-            mm(o, T.idh[:], UH(0), ["idh", r("y")], X, False, False, r("atp"))
-            mm(o, T.n16h[:], UH(1), ["n16h", r("uq")], X, False, False, r("atp"))
+            o = PX[:, 240:248]
+            tt(TB(8), PY[:, 128:256], TF(5), OP.is_gt, [r("d2"), r("f5")], [r("far")], [Y])
+            mm(o, idn, T.base[:, 16:24], ["idn", "base2"], X, True, False, r("atp"))
+            mm(o, T.i128[:], UH(0), ["i128", r("y")], X, False, False, r("atp"))
+            mm(o, T.n16[:], UH(2), ["n16", r("uq")], X, False, False, r("atp"))
             for m in range(16):
-                if FAST[c] == "f":
-                    mm(o, T.bk[:, 15 - m:143 - m], tb[:, 1024 + m:1152:16], ["bk", r("far")], X, False, m == 15, r("atp"), m > 0)
-                else:
-                    mm(o, T.c8[:, 15 - m:143 - m], tb[:, 768 + m:896:16], ["c8", r("P")], X, False, m == 15, r("atp"), m > 0)
+                mm(o, T.bk[:, 15 - m:143 - m], tb[:, 1024 + m:1152:16], ["bk", r("far")], X, False, m == 15, r("atp"), m > 0)
             cp(LS(8), o, [r("atp")], [r("al")], [X])
 
         def masks():
@@ -715,60 +870,59 @@ def rank_program(g, core, T, topo):
             mm(PZ[:, 128:256], T.m2[:], TB(6), ["m2", r("P")], Z, False, True, r("k2"))
 
         def write_x():
-            cp(T.xs[:, 4096 * c:(4096, XW)[c]].indirect(LS(8)), (T.nvb if HALF[c] == "s" else T.nvi)[:, CW * c:CW * c + CW], [r("nv"), r("al")], XR[c:c + 1], kind="s")
+            at, name = (LS(8), r("al")) if FAST[c] == "f" else (LO(2, 3), made)
+            cp(T.xs[:, 4096 * c:(4096, XW)[c]].indirect(at), T.nvi[:, CW * c:CW * c + CW], [r("nv"), name], XR[c:c + 1], kind="s")
 
         def turned():
-            o = PX[:, 264:272]
-            mm(o, T.idh[:], T.rh[:], ["idh", "rh"], X, True, False, r("rho"))
-            for m in range(16):
-                mm(o, T.c0[:, 15 - m:143 - m], tb[:, 768 + m:896:16], ["c0", r("P")], X, False, m == 15, r("rho"))
-            cp(LS(7), o, [r("rho")], [r("rl")], [X])
-            act(TF(4), T["ww%d" % c][:].indirect(LS(7)), AF.Copy, [r("ww"), r("rl")], [r("wr")], kind="g")
+            act(TF(4), T["ww%d" % c][:].indirect(LO(1, 2)), AF.Copy, [r("ww"), made], [r("wr")], kind="g")
 
         def renew():
-            tt(HH(1), TF(3), PZ[:, 0:128], OP.mult, [r("rc"), r("k1")], [r("h1")], [Z])
-            tt(HH(2), TI(4), PZ[:, 256:384], OP.mult, [r("tl"), r("k3")], [r("h2")], [Z])
+            tt(HH(1), HH(3), PZ[:, 0:128], OP.mult, [r("h3"), r("k1")], [r("h1")], [Z])
+            tt(HH(2), HH(4), PZ[:, 256:384], OP.mult, [r("tl"), r("k3")], [r("h2")], [Z])
+            together(2)
             tt(HH(0), TF(4), PZ[:, 128:256], OP.mult, [r("wr"), r("k2")], [r("h0")], [Z])
             F = PZ[:, 384:512]
-            flip, same = (T.anh[:], T.idh[:]) if last else (T.shh[:, shift:shift + 128], T.rvh[:, shift:shift + 128])
-            mm(F, flip, HH(1), ["anh", "shh", r("h1")], Z, True, False, r("zf"))
-            mm(F, same, HH(2), ["idh", "rvh", r("h2")], Z, False, False, r("zf"))
-            mm(F, same, HH(0), ["idh", "rvh", r("h0")], Z, False, True, r("zf"), False)
+            flip, same = (T.an[:], idn) if last else (T.sh[:, moved], T.rv[:, moved])
+            mm(F, flip, HH(1), ["an", "sh", r("h1")], Z, True, False, r("zf"))
+            mm(F, same, HH(2), ["idn", "rv", r("h2")], Z, False, False, r("zf"))
+            mm(F, same, HH(0), ["idn", "rv", r("h0")], Z, False, True, r("zf"))
             if last:
                 act(T.ywf[:, CW * c:CW * c + CW], F, AF.Copy, [r("zf")], [r("yw")], [Z], bias=2048.0)
                 return
-            act(T.wo[:, w0:w0 + CW], F, AF.Copy, [r("zf")], [r("wo%d" % t)], [Z])
+            copy(RENEW[c], T.wo[:, w0:w0 + CW], F, [r("zf")], [r("wo%d" % t)], [Z])
             send(T.wl[:, w0 + NC * CW:w0 + NC * CW + CW], T.wo[:, w0:w0 + CW], r("wo%d" % t), "ar%d_%d" % (t + 1, c), "wl%d_%d" % (t + 1, c), 550.0)
 
         def tally():
-            op("s", lambda: S.activation(TB(7), TB(6), AF.Copy, accum_out=T.cnt[:, c:c + 1]), [r("P")], [r("cnt"), r("junk")], (), 160.0)
+            mm(PY[:, 256:257], TB(6), T.g8[:, 0:1], [r("P"), "g8"], Y, True, True, r("pre"))
+            act(T.cnt[:, c:c + 1], PY[:, 256:257], AF.Copy, [r("pre")], [r("cnt")], [Y])
 
         return {"start": start, "first": first, "wwin": wwin, "pwin": pwin, "weigh": weigh, "relator": relator, "spread": spread,
-                "gather_r": gather_r, "letters": letters, "tail": tail, "keys": keys, "least": least, "turn": turn, "gather_w": gather_w,
-                "biggest": biggest, "apart": apart, "limit": limit, "aim": aim, "masks": masks,
+                "gather_r": gather_r, "letters": letters, "tail": tail, "other": other, "keys": keys, "least": least, "turn": turn,
+                "gather_w": gather_w, "biggest": biggest, "apart": apart, "limit": limit, "aim": aim, "masks": masks,
                 "sizes": sizes, "halves": halves, "unpack": unpack, "match": match, "write_x": write_x, "turned": turned,
-                "renew": renew, "tally": tally, "offer": offer, "lead": lead}
+                "renew": renew, "tally": tally, "offer": offer, "lead": lead, "lists": lists}
 
     def allow():
-        o = T.ps0[:, 300:301]
-        mm(o, T.g8[:], T.cnt[:, 0:1], ["g8", "cnt_0"], "ps0", True, False, "A")
-        mm(o, T.g8[:], T.cnt[:, 1:2], ["g8", "cnt_1"], "ps0", False, True, "A")
-        cp(T.ai[:, 0:1], o, ["A"], ["ai"], ["ps0"])
+        o = T.ps0[:, 48:49]
+        mm(o, one, T.cnt[:, 0:1], ["ones", "cnt_0"], "ps0", True, False, "w0p_0")
+        mm(o, one, T.cnt[:, 1:2], ["ones", "cnt_1"], "ps0", False, True, "w0p_0")
+        cp(T.ai[:, 0:1], o, ["w0p_0"], ["ai"], ["ps0"])
         ts(T.aj[:, 0:1], T.ai[:, 0:1], 31, OP.bitwise_and, ["ai"], ["aj"])
         ts(col(10), T.aj[:, 0:1], 8.0, OP.mult, ["aj"], ["thr"], (), 2048.0, OP.add)
 
+    def enter(name):
+        label.extend([now[0]] * (len(nodes) - len(label)))
+        now[0] = name
+
     parts = [{"a": stages(t, 0), "b": stages(t, 1)} for t in range(VIS)]
-    once = {"constants_1": constants_1, "constants_2": constants_2, "tables": tables, "rows": rows,
-            "limits": limits, "start": lambda: (parts[0]["a"]["start"](), parts[0]["b"]["start"]())}
+    for once in (constants_1, parts[0]["a"]["start"], parts[0]["b"]["start"], limits, rows, constants_2):
+        once()
     for t in range(VIS + 1):
         for word in ORDER.split():
-            label.extend([now[0]] * (len(nodes) - len(label)))
-            now[0] = (t, word)
             at = t - 1 if word[0] == "-" else t
             chunk, _, name = word.lstrip("-").partition(".")
             name, _, piece = name.partition(":")
-            for first in ONCE.get(name, "").split() if at == 0 else ():
-                once.pop(first, lambda: None)()
+            enter((t, word))
             if not 0 <= at < VIS or (at == VIS - 1 and name in ("tally", "offer", "lead")):
                 continue
             if chunk == "allow":
@@ -779,11 +933,15 @@ def rank_program(g, core, T, topo):
             else:
                 parts[at][chunk][name]()
 
+    enter((VIS, "out"))
     dmas("sy", [lambda: SY.dma_start(T.yx[:, 0:2048], T.xs[:, 2048:4096])], "outx", XR[:1], [], 512)
     dmas("sy", [lambda: SY.dma_start(T.yx[:, 2048:4096], T.xs[:, 4096:6144])], "outx", XR[1:], [], 512)
-    dmas("s", [lambda: S.dma_start(T.yw[:], T.ywf[:])], "outw", ["yw_0", "yw_1"], [], 128)
-    label.extend([""] * (len(nodes) - len(label)))
-    for i in plan():
+    for c in range(NC):
+        dmas("s", [(lambda a: lambda: S.dma_start(T.yw[:, a], T.ywf[:, a]))(slice(CW * c, CW * c + CW))], "outw", ["yw_%d" % c], [], 64)
+    enter(None)
+    if "order" not in PLAN:
+        PLAN["order"] = tighten(nodes, moving, label, first_placing(nodes, moving))
+    for i in PLAN["order"]:
         nodes[i][1]()
     for sem, val in total.items():
         g.wait_ge(T.sem[sem], val)

@@ -7,30 +7,38 @@ CW = 128
 XW = 2048 + 4096 + 9 * 2048
 BIG = 1.5 * 2 ** 35
 WHOLE = 1.5 * 2 ** 23
+EVEN = 1.5 * 2 ** 24
+OFF = 8192.0
 CYCLE, PECYCLE, GATHER, SCATTER = 0.95, 0.53, 1.56, 3.8
-OWN, WAKE, DMA, NET = 120.0, 200.0, 2.3, 1.1
+OWN, WAKE, DMA, NET = 120.0, 200.0, 2.1, 1.1
+MIXES = [(0.95, 1.0, 1.0, 1.0, 1.0, 1.0, 1.15, 20.0), (1.15, 0.8, 1.0, 1.0, 0.8, 0.9, 1.2, 0.0), (0.95, 1.1, 1.4, 1.0, 1.0, 1.1, 1.1, 50.0)]
 GR, GR0 = ("sssv", "sssv"), ("svsv", "svsv")
-MJ = (8, 10)
-GW = ("saaa", "asaa")
-FINE = (256, 256)
-FIRST, OFFER, RENEW = "vv", "ss", "sv"
+MJ = (10, 10)
+GW = ("saaa", "asar")
+FINE = (512, 512)
+FIRST, LETTERS, TAIL, OTHER, LIMIT, UNPACK, MATCH, TURNED = "vv", "vs", "ss", "ss", "ss", "ss", "vv", "ff"
+SPREAD, HALVES, LEAD, TURN, PICK, STEPS_BY = "ss", "vv", "XX", "vv", "vv", "vv"
+AIM = (0, 4)
 FAST = "sf"
+PACK = 0
+LOTS = 1
 JOIN = 4
+SLOW = (1.0, 1.0)
 ROUNDS = 2
-TRIES, STEPS, MORE, HEAT, SEED = 1, 4000, 12000, 250.0, 11
+TURNS, STEPS, MORE, HEAT, SEED = 5, 1000, 1000, 100.0, 12
 PLAN = {}
 
 ORDER = """
--b.lead -b.lists a.first b.first -b.tally a.weigh a.relator a.wwin -b.masks a.gather_r:0 allow -b.turned -b.renew b.weigh a.gather_r:1
-a.gather_r:3 b.relator a.gather_r:2 a.letters a.pwin a.biggest:0 a.apart:0 a.biggest:1 a.apart:1 a.keys a.spread a.least b.wwin b.letters
-a.limit b.gather_r:0 b.gather_r:1 b.gather_r:2 b.gather_r:3 b.apart:0 b.apart:1 a.turn a.gather_w:1 a.gather_w:3 a.gather_w:0 b.pwin
-b.spread b.biggest:0 b.biggest:1 a.gather_w:2 b.keys a.unpack a.tail a.other b.least b.halves a.sizes:0 b.turn b.gather_w:2 b.gather_w:1
-a.sizes:1 a.match a.offer a.lead a.lists a.masks b.limit b.gather_w:0 b.sizes:0 a.turned b.unpack b.gather_w:3 b.sizes:1 a.halves
-a.write_x a.renew a.tally b.aim b.write_x b.tail b.other b.offer b.match
+-b.sizes:2 -a.halves -b.tail -b.aim:0 -b.match -a.write_x -b.write_x:0 a.first -b.lead a.weigh -b.masks a.relator -b.lists b.first
+a.gather_r:2 b.weigh -b.renew a.gather_r:3 -b.tally a.gather_r:1 -a.renew a.wwin b.relator a.gather_r:0 a.apart:0 a.letters b.spread
+a.apart:1 b.gather_r:1 b.gather_r:0 a.pwin b.biggest:0 a.biggest:1 a.biggest:0 -a.tally b.gather_r:3 a.keys a.least b.letters
+b.gather_r:2 b.apart:1 a.turn b.apart:0 a.limit b.biggest:1 a.spread allow a.gather_w:1 a.gather_w:3 a.unpack a.gather_w:0 a.gather_w:2
+b.keys b.least a.sizes:3 b.wwin a.other a.sizes:1 b.turn b.gather_w:0 a.sizes:0 a.sizes:2 b.halves a.match b.limit b.gather_w:1
+b.gather_w:2 b.pwin a.tail a.masks b.sizes:1 b.gather_w:3 b.unpack b.other b.sizes:0 a.lead a.lists b.sizes:3
 """
 CHAIN = """first weigh relator letters pwin gather_r:0 gather_r:1 gather_r:2 gather_r:3 biggest:0 apart:0 biggest:1 apart:1 keys least turn
-gather_w:0 gather_w:1 gather_w:2 gather_w:3 sizes:0 sizes:1 limit match lead lists turned masks renew wwin spread unpack tail other offer
-halves aim write_x tally""".split()
+gather_w:0 gather_w:1 gather_w:2 gather_w:3 sizes:0 sizes:1 sizes:2 sizes:3 limit match lead lists turned masks renew wwin spread unpack tail other
+halves aim:0 aim:1 write_x write_x:0 write_x:1 tally""".split()
 
 SCRATCH = {
     "xs": ("sbuf", [128, XW], "bfloat16"),
@@ -55,33 +63,37 @@ SCRATCH = {
     "blk0": ("sbuf", [128, 256], "bfloat16"),
     "id2": ("sbuf", [128, 256], "bfloat16"),
     "an": ("sbuf", [128, 128], "bfloat16"),
-    "i128": ("sbuf", [128, 128], "bfloat16"),
     "n16": ("sbuf", [128, 128], "bfloat16"),
     "ni": ("sbuf", [128, 128], "bfloat16"),
     "pa": ("sbuf", [128, 256], "bfloat16"),
     "pb": ("sbuf", [128, 256], "bfloat16"),
-    "pc": ("sbuf", [128, 256], "bfloat16"),
-    "pd": ("sbuf", [128, 256], "bfloat16"),
-    "rv": ("sbuf", [128, 256], "bfloat16"),
-    "sh": ("sbuf", [128, 256], "bfloat16"),
+    "pc": ("sbuf", [128, 128], "bfloat16"),
+    "pd": ("sbuf", [128, 128], "bfloat16"),
+    "cn": ("sbuf", [128, 256], "bfloat16"),
+    "cr0": ("sbuf", [128, 256], "bfloat16"),
     "m3": ("sbuf", [128, 128], "bfloat16"),
     "e8": ("sbuf", [128, 128], "bfloat16"),
     "m1a": ("sbuf", [128, 128], "bfloat16"),
-    "m1": ("sbuf", [128, 128], "bfloat16"),
-    "m2a": ("sbuf", [128, 128], "bfloat16"),
+    "mo": ("sbuf", [128, 128], "bfloat16"),
     "m2b": ("sbuf", [128, 128], "bfloat16"),
-    "m2": ("sbuf", [128, 128], "bfloat16"),
+    "mt": ("sbuf", [128, 128], "bfloat16"),
+    "ann": ("sbuf", [128, 128], "bfloat16"),
+    "cth": ("sbuf", [128, 128], "float16"),
+    "cw2": ("sbuf", [128, 128], "bfloat16"),
+    "cw3": ("sbuf", [128, 128], "bfloat16"),
+    "tl": ("sbuf", [128, 24], "uint16"),
+    "rn": ("sbuf", [128, 32], "bfloat16"),
     "g8": ("sbuf", [128, 8], "bfloat16"),
     "b0": ("sbuf", [128, 144], "bfloat16"),
-    "b2": ("sbuf", [128, 144], "bfloat16"),
-    "bn": ("sbuf", [128, 144], "bfloat16"),
+    "sj": ("sbuf", [128, 192], "bfloat16"),
+    "wb": ("sbuf", [128, 128], "float16"),
+    "dg": ("sbuf", [128, 152], "bfloat16"),
+    "rd": ("sbuf", [128, 152], "float32"),
+    "bj": ("sbuf", [128, 256], "bfloat16"),
     "bk": ("sbuf", [128, 144], "bfloat16"),
     "z0": ("sbuf", [128, 144], "bfloat16"),
-    "wt0": ("sbuf", [128, 144], "float16"),
-    "mod": ("sbuf", [128, 48], "bfloat16"),
-    "on6": ("sbuf", [128, 48], "bfloat16"),
     "b18": ("sbuf", [128, 288], "bfloat16"),
-    "bm": ("sbuf", [128, 2048], "bfloat16"),
+    "bm": ("sbuf", [128, 384], "bfloat16"),
     "k2": ("sbuf", [128, 128], "bfloat16"),
     "oneh": ("sbuf", [128, 256], "float16"),
     "s2": ("sbuf", [128, 8], "bfloat16"),
@@ -91,20 +103,18 @@ SCRATCH = {
     "kt": ("sbuf", [128, 128], "bfloat16"),
     "ktk": ("sbuf", [128, 144], "bfloat16"),
     "md": ("sbuf", [128, 128], "bfloat16"),
-    "mdf": ("sbuf", [128, 16], "float32"),
     "rs": ("sbuf", [128, 144], "float32"),
     "keep": ("sbuf", [128, 128], "bfloat16"),
     "pi": ("sbuf", [128, 2], "int32"),
     "pj": ("sbuf", [128, 2], "int32"),
     "cols": ("sbuf", [128, 64], "float32"),
     "itg": ("sbuf", [128, 16], "float32"),
-    "rl": ("sbuf", [128, 40], "bfloat16"),
-    "cl": ("sbuf", [128, 40], "bfloat16"),
-    "row": ("sbuf", [128, 40], "bfloat16"),
+    "rl": ("sbuf", [128, 32], "bfloat16"),
+    "cl": ("sbuf", [128, 32], "bfloat16"),
+    "row": ("sbuf", [128, 32], "bfloat16"),
     "base": ("sbuf", [128, 24], "float16"),
     "ata": ("sbuf", [128, 8], "float32"),
     "two": ("sbuf", [128, 48], "float32"),
-    "txh": ("sbuf", [128, 8], "float16"),
     "tx": ("sbuf", [128, 8], "float32"),
     "dx": ("dram", [8, 32, 8], "float32"),
     "tw": ("sbuf", [128, 128], "float32"),
@@ -119,9 +129,11 @@ for _c in range(NC):
         "df%d" % _c: ("sbuf", [128, 2048], "bfloat16"),
         "ww%d" % _c: ("sbuf", [128, 2048], "float32"),
         "pw%d" % _c: ("sbuf", [128, 2048], "float32"),
-        "dw%d" % _c: ("dram", [8, 32, 128], "float32"),
+        "dw%d0" % _c: ("dram", [8, 32, 128 // LOTS], "float32"),
         "dp%d" % _c: ("dram", [8, 32, 128], "float32"),
         "pk%d" % _c: ("sbuf", [128, 128], "float32"),
+        "zs%d" % _c: ("sbuf", [128, 288], "bfloat16"),
+        "ys%d" % _c: ("sbuf", [128, 288], "float16"),
         "ti%d" % _c: ("sbuf", [128, 384], "int32"),
         "tf%d" % _c: ("sbuf", [128, 1280], "float32"),
         "tb%d" % _c: ("sbuf", [128, 1152], "bfloat16"),
@@ -132,11 +144,13 @@ for _c in range(NC):
         "ls%d" % _c: ("sbuf", [128, 72], "uint16"),
         "lu%d" % _c: ("sbuf", [128, 256], "uint16"),
     })
+if PACK:
+    SCRATCH.update({"pk1": ("sbuf", [128, 128], "int32"), "dp1": ("dram", [8, 32, 128], "int32"), "pw1": ("sbuf", [128, 2048], "int32")})
 for _b in range(8):
     SCRATCH["ps%d" % _b] = ("psum", [128, 512], "float32")
 
-SEMAPHORES = ["v", "s", "pe", "gp", "sent", "ldx", "ldr", "ldw", "ldt", "ldh", "outw", "outx", "dx1", "dx2"]
-SEMAPHORES += ["d%s%d%d" % (w, st, c) for w in "wp" for st in (1, 2) for c in range(NC)]
+SEMAPHORES = ["v", "s", "pe", "gp", "sent", "ldx", "ldr", "ldw", "ldt", "ldh", "outw", "outx", "dx0", "dx1"]
+SEMAPHORES += ["d%s%d%d" % (w, st, c) for w in "wp" for st in (0, 1, 2) for c in range(NC)]
 SEMAPHORES += ["%s%d_%d" % (w, t, c) for w in ("ar", "al") for t in range(1, VIS) for c in range(NC)]
 
 
@@ -170,15 +184,16 @@ def lag(nodes, moving, j, i):
 
 def first_placing(nodes, moving):
     where, cost, ins, ids, ends = [], [], [], [], []
+    moving = {i: [x * SLOW[1] for x in move] if nodes[i][0] == "gp" else [move[0], move[1] * SLOW[0], move[2]] for i, move in moving.items()}
     for i, pred in enumerate(needs(nodes, True)):
         ids.append(len(where))
         where.append(nodes[i][0])
-        cost.append(nodes[i][5])
+        cost.append(nodes[i][5].real + nodes[i][5].imag)
         ins.append([(ends[j], lag(nodes, moving, j, i) + moving.get(j, (0, 0, 0.0))[2]) if hard else (ids[j], 0.0) for j, hard in pred.items()])
         if i in moving:
             where.append("engines")
             cost.append(moving[i][1])
-            ins.append([(ids[i], moving[i][0] - min(nodes[i][5], moving[i][0]))])
+            ins.append([(ids[i], moving[i][0] - min(nodes[i][5].real, moving[i][0]))])
         ends.append(len(where) - 1)
     m = len(where)
     outs = [[] for _ in range(m)]
@@ -210,18 +225,22 @@ def first_placing(nodes, moving):
             best = end
         back = place(sorted(range(m), key=lambda z: (-end[z], -z)), outs)
         key = [-back[i] + 1e-7 * i for i in range(m)]
-    return sorted(range(len(nodes)), key=lambda z: (best[ids[z]] - cost[ids[z]], z))
+    return sorted(range(len(nodes)), key=lambda z: (best[ends[z]] - cost[ends[z]] - (moving[z][0] if z in moving else 0.0), z))
 
 
-def clock(nodes, moving):
+def clock(nodes, moving, mix=MIXES[0], preds=None):
     n = len(nodes)
-    preds = needs(nodes, False)
+    preds = preds or needs(nodes, False)
     names = ["v", "s", "pe", "gp", "sy"]
+    engine, lists, waits, moves, late, net, pe, short = mix
     rows = []
     for i, node in enumerate(nodes):
-        q = names.index(node[0])
-        rows.append((q, [(j, lag(nodes, moving, j, i)) for j, hard in preds[i].items() if hard], int(node[4][0][2:]) if node[4] else -1,
-                     node[5], moving.get(i), WAKE + (60.0 if q == 2 else 0.0)))
+        q, move, cost = names.index(node[0]), moving.get(i), node[5]
+        if move:
+            move = [x * net for x in move] if q == 3 else [move[0] * late, move[1] * moves, move[2] * late]
+        cost = cost.real * (net if q == 3 else 1.0) if move else engine * (cost.real + lists * cost.imag) * (pe if q == 2 else 1.0) + (short if q == 1 else 0.0)
+        rows.append((q, [(j, waits * lag(nodes, moving, j, i)) for j, hard in preds[i].items() if hard], int(node[4][0][2:]) if node[4] else -1,
+                     cost, move, waits * (WAKE + (60.0 if q == 2 else 0.0))))
 
     def run(order):
         free, last = [0.0] * 5, [-1] * 5
@@ -263,7 +282,8 @@ def clock(nodes, moving):
 
 def tighten(nodes, moving, label, given):
     n = len(nodes)
-    preds, run = clock(nodes, moving)
+    preds = needs(nodes, False)
+    runs = [clock(nodes, moving, mix, preds)[1] for mix in MIXES]
     lists = [list(p) for p in preds]
     hard = [[(j, lag(nodes, moving, j, i)) for j, h in p.items() if h] for i, p in enumerate(preds)]
     users = [[] for _ in nodes]
@@ -285,12 +305,13 @@ def tighten(nodes, moving, label, given):
         return seed[0] / 2 ** 31
 
     def attempt(order, steps, heat):
-        now = run(order)
-        length = max(now[1])
-        best, pairs = (length, order), None
+        now = [run(order) for run in runs]
+        total = [max(x[1]) for x in now]
+        best, pairs = (sum(total) / len(runs), order), None
         for step in range(steps):
-            if pairs is None:
-                start, end, why = now
+            if pairs is None or chance() < 0.05:
+                mix = int(len(runs) * chance())
+                (start, end, why), length = now[mix], total[mix]
                 key = [0.0] * n
                 for r, i in enumerate(order):
                     key[i] = start[i] + 1e-4 * r
@@ -336,15 +357,21 @@ def tighten(nodes, moving, label, given):
                         k = new[p] + 1e-6
                 new[i] = k
             other = sorted(range(n), key=lambda z: new[z])
-            then = run(other)
-            if max(then[1]) - length <= -heat * (1 - step / steps) * math.log(chance() + 1e-9):
-                order, now, length, pairs = other, then, max(then[1]), None
-                if length < best[0]:
-                    best = (length, order)
+            room = -len(runs) * heat * (1 - step / steps) * math.log(chance() + 1e-9)
+            mine = runs[mix](other)
+            if max(mine[1]) - length <= room + 300.0:
+                then = [mine if m == mix else run(other) for m, run in enumerate(runs)]
+                if sum(max(x[1]) for x in then) - sum(total) <= room:
+                    order, now, total, pairs = other, then, [max(x[1]) for x in then], None
+                    best = min(best, (sum(total) / len(runs), order))
         return best
 
-    best = min(attempt(given, STEPS, HEAT) for _ in range(TRIES))
-    return attempt(best[1], MORE, HEAT / 3)[1]
+    best = (1e18, given)
+    for _ in range(TURNS):
+        best = min(best, attempt(attempt(given, STEPS, HEAT)[1], MORE, HEAT / 3))
+        again = first_placing([nodes[i] for i in best[1]], {r: moving[i] for r, i in enumerate(best[1]) if i in moving})
+        given = [best[1][r] for r in again]
+    return best
 
 
 def rank_program(g, core, T, topo):
@@ -415,19 +442,20 @@ def rank_program(g, core, T, topo):
                 total[sem] = total.get(sem, 0) + 16
                 call().then_inc(T.sem[sem], 16)
             note(q, (sem, total[sem], dict(know[q]), "dma"), reads, writes, ())
-        moving[len(nodes)] = (960.0, 100.0 + DMA * kib, 600.0)
+        moving[len(nodes)] = (960.0, 20.0 * len(calls) + DMA * kib, 600.0)
         nodes.append((q, emit, list(reads), list(writes), [], 60.0 * len(calls)))
 
     def span(ap):
         return math.prod(ap.shape[1:])
 
     def vcost(n, kind, wide):
-        return {"": max(64, n * wide) * CYCLE, "h": max(64, n / 2) * CYCLE, "g": 55 + n * GATHER * CYCLE, "s": 55 + n * SCATTER * CYCLE}[kind]
+        return {"": max(64, n * wide) * CYCLE, "h": max(64, n / 2) * CYCLE, "g": 55 + 1j * n * GATHER * CYCLE, "s": 55 + 1j * n * SCATTER * CYCLE}[kind]
 
-    def mm(out, lhsT, rhs, reads, bank, start=True, stop=True, tag=None, join=None):
-        call, cost = lambda: PE.matmul(out, lhsT, rhs, start, stop), max(64, span(rhs)) * PECYCLE * (4 if "float32" in str(lhsT.dtype) else 1)
+    def mm(out, lhsT, rhs, reads, bank, start=True, stop=True, tag=None, join=None, most=JOIN):
+        call = lambda: PE.matmul(out, lhsT, rhs, start, stop)
+        cost = max(min(64, span(lhsT)), span(rhs)) * PECYCLE * (4 if "float32" in str(lhsT.dtype) else 1)
         tags = tag if isinstance(tag, list) else [tag]
-        if ((not start) if join is None else join) and len(run[-1]) < JOIN:
+        if ((not start) if join is None else join) and len(run[-1]) < most:
             q, _, before, writes, banks, so_far = nodes.pop()
             calls = run.pop() + [call]
             reads, cost = before + [x for x in reads if x not in before], so_far + cost
@@ -465,6 +493,18 @@ def rank_program(g, core, T, topo):
             act(out, a, AF.Copy, reads, writes, banks, kind)
         else:
             cp(out, a, reads, writes, banks, kind)
+
+    def plus(who, out, a, value, reads, writes):
+        if who == "s":
+            act(out, a, AF.Copy, reads, writes, bias=value)
+        else:
+            ts(out, a, value, OP.add, reads, writes)
+
+    def line(who, out, a, scale, bias, reads, writes, banks=()):
+        if who == "s":
+            act(out, a, AF.Copy, reads, writes, banks, scale=scale, bias=bias)
+        else:
+            ts(out, a, scale, OP.mult, reads, writes, banks, bias, OP.add)
 
     def together(k):
         some = [nodes.pop() for _ in range(k)][::-1]
@@ -505,30 +545,32 @@ def rank_program(g, core, T, topo):
         sel(T.blk0[:], T.ones[:], [[0, 2], [-16, 8], [0, 16]], OP.is_ge, 0.0, 0, 1, ["ones"], ["blk0"])
         sel(T.blk[:], T.blk0[:], [[0, 2], [16, 8], [0, 16]], OP.is_ge, 0.0, 15, -1, ["blk0"], ["blk"])
         sel(T.id2[:], T.blk[:], DOWN, OP.is_equal, 0.0, 0, -1, ["blk"], ["idn"])
-        sel(T.pa[:], T.blk[:], UP, OP.is_equal, 0.0, 0, 1, ["blk"], ["pa"])
-        sel(T.pb[:], T.blk[:], UP, OP.is_equal, 0.0, -16, 1, ["blk"], ["pb"])
         times(T.ni[:], idn, -1.0, ["idn"], ["ni"])
-        join(T.rv[:], [(1, T.pa[:]), (1, T.pb[:])], ["pa", "pb"], "rv")
         fill(T.zerf[:], 0.0, "zerf")
         fill(T.b0[:], 0.0, "b0")
         for c in range(NC):
-            fill(T["tb%d" % c][:, 0:128], 0.0, "zs_%d" % c)
+            fill(T["zs%d" % c][:], 0.0, "zs_%d" % c)
+            fill(T["ys%d" % c][:], 0.0, "y_%d" % c)
+        fill(col(10), 2048.0, "thr")
+        fill(col(19), -2048.0 * 32768, "thr2")
         ts(T.pj[:], T.pi[:], 15, OP.bitwise_and, ["pi"], ["pj"])
         cp(col(0), T.pj[:, 0:1], ["pj"], ["k0"])
         iota(T.kt[:], [[0, 8], [1, 16]], "kt")
-        sel(T.keep[:], one, [[0, 8], [1, 16]], OP.not_equal, 0.0, 0, 0, ["ones"], ["keep"])
+        ts(T.keep[:], T.kt[:], col(0), OP.is_le, ["kt", "k0"], ["kp0"], kind="h")
+        sel(T.keep[:], T.keep[:], [[0, 8], [1, 16]], OP.not_equal, 0.0, 0, 0, ["kp0"], ["keep"])
         cp(T.b0[:, 15:143:16], s1, ["blk"], ["b0"])
         ts(col(13), col(0), 0.0, OP.is_equal, ["k0"], ["q0"])
         times(T.z0[:], T.b0[:], col(13), ["b0", "q0"], ["z0"])
         cp(col(1), T.wti[:, 0:1], ["wti"], ["w1"])
         ts(col(2), col(1), 2048.0, OP.is_ge, ["w1"], ["w2"], (), -4096.0, OP.mult)
         tt(col(3), col(1), col(2), OP.add, ["w1", "w2"], ["w3"])
-        ts(T.wt0[:], T.b0[:], col(3), OP.mult, ["b0", "w3"], ["wt0"])
-        fill(T.on6[:], 1.0, "on6")
-        fill(T.on6[:, 0:48:6], 0.0, "on6")
-        for n, step in enumerate([0.0, -2048.0, 0.5, BIG, -BIG, -592.0]):
-            fill(T.mod[0:1, n:48:6], step, "mod%d" % n)
-        together(6)
+        times(T.wb[:], blk, col(3), ["blk", "w3"], ["wb"])
+        iota(T.dg[:], [[0, 8], [1, 19]], "dg")
+        ts(T.dg[:], T.dg[:], col(0), OP.not_equal, ["dg", "k0"], ["dg"], (), -2.0 ** 25, OP.mult, kind="h")
+        ts(T.dg[:], T.dg[:], 592.0, OP.add, ["dg"], ["dg"], kind="h")
+        fill(T.rd[:], 0.0, "rd")
+        for n, step in [(0, -2.0 ** 27), (16, -2639.5), (17, BIG), (18, -BIG)]:
+            fill(T.rd[:, n:152:19], step, "rd")
         ts(T.md[:], T.kt[:], col(0), OP.is_equal, ["kt", "k0"], ["md"])
         times(T.k2[0:1, :], T.ones[0:1, 0:128], 128.0, ["ones"], ["k2"])
         ts(T.oneh[0:1, 0:128], T.ones[0:1, 0:128], 2080.0 / 128, OP.mult, ["ones"], ["oneh"], kind="h")
@@ -549,87 +591,105 @@ def rank_program(g, core, T, topo):
         for c in range(NC):
             if MJ[c]:
                 sel(T["sx%d" % c][:], T.b18[:, 0:144], [[0, 8], [-1, 18]], OP.is_gt, 0.0, MJ[c], 0, ["b18"], ["sx_%d" % c])
-            mm(T["ps%d" % (3 * c)][:, 256:384], idn, T.md[:], ["idn", "md"], "ps%d" % (3 * c), True, True, "mdp_%d" % c)
         fill(T.cl[:], 0.0, "cl")
-        for n, base in enumerate([960.0, 60.0, 61.0, 7.5, 62.0]):
+        for n, base in enumerate([960.0, 960.0 / LOTS, 7.5, 7.5]):
             fill(T.row[0:1, 8 * n:8 * n + 8], base, "row%d" % n)
-        together(5)
-        for n, scale in enumerate([2048.0, 128.0, 128.0, 16.0, 128.0]):
+        together(4)
+        for n, scale in enumerate([2048.0, -2048.0 / LOTS, 16.0, 16.0]):
             times(T.rl[:, 8 * n:8 * n + 8], s1, scale, ["blk"], ["rl%d" % n])
-        together(5)
+        together(4)
+        times(T.rn[:], T.rl[:], -1.0, ["rl%d" % n for n in range(4)], ["rn"])
         ts(T.cl[:, 0:8], T.itg[:, 0:8], col(0), OP.add, ["itg", "k0", "cl"], ["cl"])
+        for n in range(0, 8, 8 // LOTS):
+            ts(T.cl[:, 8 + n:8 + n + 8 // LOTS], T.itg[:, 0:8 // LOTS], col(0), OP.add, ["itg", "k0", "cl"], ["cl"])
         ts(T.cl[:, 24:32], T.itg[:, 0:8], col(0), OP.add, ["itg", "k0", "cl"], ["cl"], (), 16.0, OP.mult)
 
     def rows():
-        ts(T.mdf[:], T.md[:, 0:16], 128.0, OP.mult, ["md"], ["mdf"])
-        for m in range(16):
-            times(T.bm[:, 128 * m:128 * m + 128], blk, T.mdf[:, m:m + 1], ["blk", "mdf"], ["bm%d" % m])
-            if m % 4 == 3:
-                together(4)
+        for n, by in enumerate([-1.0, 2048.0, -2048.0]):
+            times(T.bm[:, 128 * n:128 * n + 128], blk, by, ["blk"], ["bm"])
 
     def constants_2():
         sel(T.e8[:], one, [[-16, 8], [0, 16]], OP.is_equal, 0.0, -8, 1, ["ones"], ["e8"])
         sel(T.an[:], one, [[-16, 8], [1, 16]], OP.is_equal, 0.0, -15, 1, ["ones"], ["an"])
         sel(T.m3[:], one, [[-16, 8], [1, 8], [0, 2]], OP.is_equal, 0.0, -15, 1, ["ones"], ["m3"])
-        sel(T.pc[:], T.blk[:], DOWN, OP.is_equal, 0.0, -1, -1, ["blk"], ["pc"])
-        sel(T.pd[:], T.blk[:], DOWN, OP.is_equal, 0.0, 15, -1, ["blk"], ["pd"])
-        join(T.sh[:], [(1, T.pc[:]), (1, T.pd[:])], ["pc", "pd"], "sh")
-        times(T.i128[:], idn, 128.0, ["idn"], ["i128"])
+        sel(T.pc[:], blk, DOWN[1:], OP.is_equal, 0.0, -1, -1, ["blk"], ["pc"])
+        sel(T.pd[:], blk, DOWN[1:], OP.is_equal, 0.0, 15, -1, ["blk"], ["pd"])
+        times(T.ann[:], T.an[:], -1.0, ["an"], ["ann"])
+        times(T.mt[:], T.m3[:], -OFF, ["m3"], ["mt"])
+        fill(T.cr0[0:2, :], OFF - 2048, "cr0")
+        sel(T.cr0[0:2, 0:128], T.cr0[0:2, 0:128], [[0, 128]], OP.is_equal, -1.0, 0, 1, ["cr0"], ["cr1"])
+        sel(T.cr0[0:2, 128:256], T.cr0[0:2, 128:256], [[0, 128]], OP.is_equal, 0.0, 0, 1, ["cr0"], ["cr2"])
         times(T.n16[:], idn, -16.0, ["idn"], ["n16"])
-        if "r" in "".join(GW):
-            times(T.b2[:], T.b0[:], 2.0, ["b0"], ["b2"])
-            times(T.bn[:], T.b0[:], -1.0, ["b0"], ["bn"])
-        ts(T.base[:, 0:8], T.ones[:, 0:8], 2048.0, OP.mult, ["ones"], ["base0"])
-        ts(T.base[:, 8:16], T.itg[:, 0:8], col(0), OP.add, ["itg", "k0"], ["base1"], (), 1792.0, OP.add)
+        ts(T.base[:, 0:8], T.ones[:, 0:8], 16 * 2048.0, OP.mult, ["ones"], ["base0"])
+        for n in range(0, 8, 8 // LOTS):
+            ts(T.base[:, 8 + n:8 + n + 8 // LOTS], T.itg[:, 0:8 // LOTS], col(0), OP.add, ["itg", "k0"], ["base1"], (), 128.0 / LOTS + 256 * n, OP.add)
         ts(T.ata[:], T.itg[:, 0:8], col(0), OP.add, ["itg", "k0"], ["ata"], (), 1153.0, OP.add)
         ts(T.base[:, 16:24], T.ata[:], 16.0, OP.mult, ["ata"], ["base2"])
-        times(T.bk[:], T.b0[:], 2048.0, ["b0"], ["bk"])
+        fill(T.bk[:], 0.0, "bk")
+        times(T.bk[:, 15:143:16], T.bj[:, 128:256:16], 2048.0, ["bjt", "bk"], ["bk"])
+        fill(T.sj[:], 0.0, "sj")
+        for z, by in enumerate([1.0, 2.0, -1.0]):
+            times(T.sj[:, 64 * z + 24:64 * z + 32], s1, by, ["blk", "sj"], ["sj"])
         ts(col(5), col(0), 8.0, OP.is_equal, ["k0"], ["q8"])
         ts(col(6), col(0), 9.0, OP.is_ge, ["k0"], ["q9"], (), 1.0, OP.add)
         ts(col(7), col(5), -8.0, OP.mult, ["q8"], ["q7"])
         tt(col(9), col(6), col(7), OP.add, ["q9", "q7"], ["qc"])
-        ts(col(14), col(0), 15.0, OP.is_lt, ["k0"], ["qd"], (), -128.0, OP.mult)
+        ts(col(14), col(0), 15.0, OP.is_lt, ["k0"], ["qd"], (), 128.0 / LOTS, OP.mult)
         tt(col(11), col(9), col(14), OP.mult, ["qc", "qd"], ["c0"])
         ts(col(12), col(5), 2048.0, OP.mult, ["q8"], ["c8"])
         cp(T.g8[:, 0:1], col(5), ["q8"], ["g8"])
         join(T.m1a[:], [(1, T.e8[:]), (-1, idn)], ["e8"], "m1a")
-        join(T.m2a[:], [(1, T.an[:]), (-1, T.e8[:])], ["an", "e8"], "m2a")
-        sel(T.m1[:], T.m1a[:], [[0, 8], [1, 16]], OP.is_ge, 0.0, -8, 0, ["m1a"], ["m1"])
-        sel(T.m2b[:], T.m2a[:], [[0, 8], [-1, 16]], OP.is_ge, 0.0, 7, 0, ["m2a"], ["m2b"])
-        join(T.m2[:], [(1, T.m2b[:]), (-1, T.m3[:])], ["m2b", "m3"], "m2")
-        ts(T.cw[:], T.rv[:], col(0), OP.mult, ["rv", "k0"], ["cw"], (), 6.5, OP.is_gt)
+        join(T.m2b[:], [(1, T.an[:]), (-1, T.e8[:])], ["an", "e8"], "m2a")
+        sel(T.m2b[:], T.m2b[:], [[0, 8], [-1, 16]], OP.is_ge, 0.0, 7, 0, ["m2a"], ["m2b"])
+        times(T.mo[:], T.m2b[:], OFF, ["m2b"], ["mo"])
+        ts(col(20), col(0), 0.5, OP.is_gt, ["k0"], ["q20"])
+        ts(col(21), col(0), 9.5, OP.is_lt, ["k0", "q20"], ["q21"], (), col(20), OP.mult)
+        times(T.cw[:], T.id2[:], col(21), ["idn", "q21"], ["cw"])
         times(T.ct[:], T.id2[:], col(13), ["idn", "q0"], ["ct"])
         ts(col(15), col(0), 15.0, OP.is_equal, ["k0"], ["q15"])
         times(T.cc[:], T.id2[:], col(15), ["idn", "q15"], ["cc"])
-        ts(T.q1[0:1, :], T.kt[0:1, :], 1.0, OP.is_equal, ["kt"], ["q1"], kind="h")
+        times(T.cn[:], T.cc[:], -1.0, ["cc"], ["cn"])
+        ts(col(22), col(21), -2048.0, OP.mult, ["q21"], ["q22"], (), -OFF, OP.add)
+        ts(col(23), col(0), 1.0, OP.is_equal, ["k0"], ["q23"], (), OFF, OP.mult)
+        tt(T.g8[:, 2:3], col(22), col(23), OP.add, ["q22", "q23"], ["g82"])
+        cp(T.g8[:, 3:4], col(15), ["q15"], ["g83"])
+        mm(T.ps7[0:2, 0:128], T.g8[:, 2:4], idn, ["g82", "g83", "idn"], "ps7", True, True, "ps7d")
+        act(T.q1[0:2, :], T.ps7[0:2, 0:128], AF.Copy, ["ps7d"], ["q1"], ["ps7"])
         sel(T.pa[:, 0:128], blk, DOWN[1:], OP.is_equal, 0.0, -2, -1, ["blk"], ["pa"])
-        join(T.pb[:, 0:128], [(1, T.pa[:, 0:128]), (-1, T.pc[:, 0:128])], ["pa", "pc"], "pb")
+        join(T.pb[:, 0:128], [(1, T.pa[:, 0:128]), (-1, T.pc[:])], ["pa", "pc"], "pb")
         sel(T.pa[:, 128:256], T.pb[:, 0:128], [[0, 8], [-1, 16]], OP.is_ge, 0.0, 9, 0, ["pb"], ["pa2", "pa"])
         sel(T.pb[:, 128:256], T.m1a[:], [[0, 8], [1, 16]], OP.is_equal, 0.0, -15, 0, ["m1a"], ["pb2", "pb"])
-        join(T.mc[:, 0:128], [(1, T.pa[:, 128:256]), (1, T.pb[:, 128:256]), (1, T.pd[:, 0:128])], ["pa2", "pb2", "pd"], "mc0")
-        times(T.mc[:, 128:256], T.mc[:, 0:128], 1.0, ["mc0"], ["mc"])
+        join(T.mc[:, 0:128], [(1, T.pa[:, 128:256]), (1, T.pb[:, 128:256]), (1, T.pd[:])], ["pa2", "pb2", "pd"], "mc0")
+        times(T.mc[:, 128:256], T.mc[:, 0:128], OFF, ["mc0"], ["mc1"])
+        times(T.mc[:, 0:128], T.mc[:, 0:128], OFF, ["mc0"], ["mc", "mc0"])
 
-    def window(sem, src, dram, win, start, read, name):
-        dmas("sy", [lambda: SY.dma_start(dram[:, 0:16, :], src), lambda: SY.dma_start(dram[:, 16:32, :], src)], sem % 1, [read], [name + "d"], span(src))
-        dmas("sy", [(lambda k: lambda: SY.dma_start(win[k:128:16, :], dram[:, start(k):start(k) + 16, :]))(k) for k in range(16)],
-             sem % 2, [name + "d"], [name], 8 * span(src))
-
-    def back(k):
-        return (17 - k) % 16
+    def window(sem, src, cols, by, dram, win, start, read, name):
+        pieces = [(by, 8, 0), (0, by, 128 - 16 * by)][:2 if by else 1]
+        lots = len(dram)
+        wide = (cols.stop - cols.start) // lots
+        dmas("sy", [(lambda a, b, p, h, d, c0: lambda: SY.dma_start(d[a:b, h:h + 16, :], src[p:p + 16 * (b - a), c0:c0 + wide]))(a, b, p, h, d, cols.start + n * wide)
+                    for n, d in enumerate(dram) for h in (0, 16) for a, b, p in pieces], sem % 0, [read], [name + "d"], lots * wide)
+        for n, d in enumerate(dram):
+            dmas("sy", [(lambda k, d, n: lambda: SY.dma_start(win[k:128:16, 16 * wide * n:16 * wide * (n + 1)], d[:, start(k):start(k) + 16, :]))(k, d, n)
+                        for k in range(16)], sem % (n + 1), [name + "d"], [name + str(n)], 8 * wide)
 
     def limits():
         ts(T.two[:, 0:16], T.kt[:, 0:16], col(0), OP.add, ["kt", "k0"], ["two0"], (), 15.0, OP.is_lt)
         ts(T.two[:, 16:32], T.two[:, 0:16], 1.0, OP.add, ["two0"], ["two1"])
         scan(T.two[:, 32:48], T.two[:, 16:32], T.zerf[:, 0:16], 1.0, OP.mult, OP.add, ["two1", "zerf"], ["two"])
-        fill(T.txh[:], 0.0, "txh")
-        ts(T.txh[:, 0:1], T.thi[:, 0:1], -2048.0, OP.add, ["thi", "txh"], ["txh"])
-        cp(T.txh[:, 1:2], T.two[:, 47:48], ["two", "txh"], ["txh"])
-        ts(col(17), col(0), 9.0, OP.is_ge, ["k0"], ["far"], (), 8192.0, OP.mult)
-        ts(col(18), col(17), -4096.0, OP.add, ["far"], ["far2"])
-        tt(T.txh[:, 2:3], T.txh[:, 0:1], col(18), OP.max, ["far2", "txh"], ["txh"])
-        mm(T.ps7[:, 0:8], T.rv[:, 0:128], T.txh[:], ["rv", "txh"], "ps7", True, True, "ps7d")
-        act(T.tx[:], T.ps7[:, 0:8], AF.Copy, ["ps7d"], ["tx"], ["ps7"])
-        window("dx%d", T.tx[:], T.dx, T.tw, back, "tx", "tw")
+        fill(T.tx[:], 0.0, "tx")
+        ts(T.tx[:, 0:1], T.thi[:, 0:1], -1.0, OP.mult, ["thi", "tx"], ["tx"], (), 2048.0, OP.add)
+        cp(T.tx[:, 1:2], T.two[:, 47:48], ["two", "tx"], ["tx"])
+        ts(T.tx[:, 2:3], col(0), 9.0, OP.is_ge, ["k0", "tx"], ["tx"], (), 8192.0, OP.mult)
+        window("dx%d", T.tx, slice(0, 8), 0, [T.dx], T.tw, lambda m: 15 - m, "tx", "tw")
+        ts(col(17), col(0), 8.0, OP.is_ge, ["k0"], ["k8"], (), 8.0, OP.mult)
+        sel(T.bj[:, 128:256], one, [[0, 16], [-16, 8]], OP.is_ge, 0.0, 0, 1, ["ones"], ["bjt"])
+        sel(T.bj[:, 0:128], T.bj[:, 128:256], [[0, 16], [16, 8]], OP.is_ge, 0.0, 15, -1, ["bjt"], ["bj"])
+        mm(T.ps7[:, 0:128], T.bj[:, 0:128], idn, ["bj", "idn"], "ps7", True, True, "ps7d")
+        act(T.bj[:, 128:256], T.ps7[:, 0:128], AF.Copy, ["ps7d"], ["bjt"], ["ps7"])
+        for n, out in enumerate([T.cth, T.cw2, T.cw3]):
+            ts(T.tl[:, 8 * n:8 * n + 8], T.itg[:, 0:8], col(17), OP.add, ["itg", "k8"], ["tl%d" % n], (), float(n), OP.add)
+            tt(out[:], T.tw[:].indirect(T.tl[:, 8 * n:8 * n + 8]), T.bj[:, 0:128], OP.mult, ["tw0", "tl%d" % n, "bj"], ["circ%d" % n], kind="g")
 
     XR = ["x_lo", "x_hi"]
 
@@ -652,8 +712,12 @@ def rank_program(g, core, T, topo):
         XRS = blocks("xr", 0, 2048)
         x = T.xs[:, 2048:6144]
 
-        shift = 128 - 16 * ((t + 1 + (t + 1) // nrank) - (t + t // nrank))
-        moved = slice(shift, shift + 128)
+        step = lambda u: (u + u // nrank) - (u - 1 + (u - 1) // nrank) if u else 0
+        onward = lambda d: slice(128 - 16 * d, 256 - 16 * d)
+        moved = onward(step(t + 1))
+        zs, ys = T["zs%d" % c], T["ys%d" % c]
+        GAPS = [r("d2.%d" % n) for n in range(4)]
+        WW = [r("ww") + str(n) for n in range(LOTS)]
 
         def send(out, src, name, sem, lands, extra):
             rid, pid, _ = topo.addr(nxt)
@@ -672,34 +736,33 @@ def rank_program(g, core, T, topo):
             for m in range(16):
                 mm(PX[:, 48:56], T.z0[:, 15 - m:143 - m], hh[:, 384 + m:512:16], ["z0", r("h3")], X, m == 0, m == 15, r("w0p"))
             ts(T.ll[:, l0:l0 + 8], PX[:, 48:56], 2048.0, OP.add, [r("w0p")], [lres], [X])
-            mm(PZ[:, 384:512], T.rv[:, 0:128], HH(3), ["rv", r("h3")], Z, True, True, r("zf"))
-            act(T.wl[:, w0:w0 + 128], PZ[:, 384:512], AF.Copy, [r("zf")], [wres], [Z])
+            cp(T.wl[:, w0:w0 + 128], T.wdi[:, CW * c:CW * c + CW], ["wdi"], [wres])
 
         def first():
             copy(FIRST[c], x0, x.indirect(T.ll[:, l0:l0 + 8]), XR + [lres], [r("x0")], kind="g")
 
-        def offer():
-            o = PX[:, 384:512]
-            mm(o, T.cw[:, moved], T.wl[:, w0:w0 + 128], ["cw", wres], X, True, False, r("cp"))
-            mm(o, T.cc[:, moved], HH(3), ["cc", r("h3")], X, False, False, r("cp"), False)
-            mm(o, T.ct[:, moved], HH(4), ["ct", r("tl")], X, False, True, r("cp"), False)
-            copy(OFFER[c], TF(7), o, [r("cp")], [r("f7")], [X])
-
         def lead():
-            o = PY[:, 128:256]
-            mm(o, T.q1[0:1, :], T.ones[0:1, 0:128], ["q1", "ones"], Y, True, False, r("d2"))
-            mm(o, T.mc[:, moved], TB(6), ["mc", r("P")], Y, False, True, r("d2"))
-            tt(HH(5), TF(7), o, OP.mult, [r("f7"), r("d2")], [r("h5")], [Y])
+            B = {"X": X, "Z": Z}[LEAD[c]]
+            o = T[B][:, 384:512]
+            mm(o, T.q1[0:2, :], T.ones[0:2, 0:128], ["q1", "ones"], B, True, False, r("cp"))
+            mm(o, T.cw[:, onward(step(t) + step(t + 1))], T.wl[:, w0:w0 + 128], ["cw", wres], B, False, False, r("cp"))
+            mm(o, T.cn[:, moved], HH(0), ["cn", r("q")], B, False, False, r("cp"), False)
+            mm(o, T.cc[:, moved], HH(1), ["cc", r("ev")], B, False, False, r("cp"), False)
+            mm(o, T.ct[:, moved], HH(4), ["ct", r("tl")], B, False, False, r("cp"), False)
+            mm(o, T.mc[:, moved], TB(6), ["mc", "mc1", r("P")], B, False, True, r("cp"), False)
+            ts(HH(5), o, -2048.0, OP.max, [r("cp")], [r("h5")], [B])
 
         def lists():
             lo, hi = (1 if last else 0), (2 if FAST[c] == "f" else 3)
-            ts(HH(6), TB(6), col(11), OP.mult, [r("P"), "c0"], [r("h6")], kind="h")
-            if hi == 3:
-                ts(HH(7), TB(6), col(12), OP.mult, [r("P"), "c8"], [r("h7")], kind="h")
+            for n, (by, name) in enumerate([(11, "c0"), (12, "c8")][:hi - 1]):
+                if STEPS_BY[c] == "s":
+                    times(HH(6 + n), TB(6), col(by), [r("P"), name], [r("h%d" % (6 + n))])
+                else:
+                    ts(HH(6 + n), TB(6), col(by), OP.mult, [r("P"), name], [r("h%d" % (6 + n))], kind="h")
             o = PY[:, 400 + 8 * lo:400 + 8 * hi]
             mm(o, idn, T.base[:, 8 * lo:8 * hi], ["idn", "base0", "base1", "base2"], Y, True, False, r("x0p"))
             if hi == 3:
-                mm(PY[:, 416:424], T.i128[:], UH(0), ["i128", r("y")], Y, False, False, r("x0p"))
+                mm(PY[:, 416:424], idn, ys[:, 0:128:16], ["idn", r("y")], Y, False, False, r("x0p"))
                 mm(PY[:, 416:424], T.n16[:], UH(2), ["n16", r("uq")], Y, False, False, r("x0p"))
             for m in range(16):
                 mm(o, T.b0[:, 15 - m:143 - m], hh[:, 640 + 128 * lo + m:640 + 128 * hi:16], ["b0"] + [r("h%d" % (5 + n)) for n in range(lo, hi)],
@@ -709,56 +772,68 @@ def rank_program(g, core, T, topo):
                 send(T.ll[:, l0 + 8 * NC:l0 + 8 * NC + 8], LO(0, 1), made, "al%d_%d" % (t + 1, c), "ll%d_%d" % (t + 1, c), 20.0)
 
         def wwin():
-            window("dw%d" + str(c), T.wl[:, w0:w0 + 128], T["dw%d" % c], T["ww%d" % c], back, wres, r("ww"))
+            window("dw%d" + str(c), T.wl, slice(w0, w0 + 128), step(t), [T["dw%d%d" % (c, n)] for n in range(LOTS)], T["ww%d" % c], lambda k: k, wres, r("ww"))
 
         def pwin():
-            window("dp%d" + str(c), T["pk%d" % c][:], T["dp%d" % c], T["pw%d" % c], lambda k: k + 1, r("pk"), r("pw"))
+            if PACK and c == 0:
+                return
+            window("dp%d" + str(c), T["pk%d" % c], slice(0, 128), 0, [T["dp%d" % c]], T["pw%d" % c], lambda k: k + 1, r("pk"), r("pw"))
 
         def weigh():
-            mm(PX[:, 0:48], T.ones[0:1, 0:128], T.mod[0:1, :], ["ones"] + ["mod%d" % n for n in range(6)], X, True, False, r("uw"))
-            for m in range(16):
-                mm(PX[:, 0:48:6], T.wt0[:, 15 - m:143 - m], tb[:, 896 + m:1024:16], ["wt0", r("x0")], X, False, m == 15, r("uw"), m > 0)
+            mm(PX[:, 96:248], idn, T.dg[:], ["idn", "dg"], X, True, False, r("key"))
+            for h in range(8):
+                mm(PX[:, 96 + 19 * h:112 + 19 * h], T.wb[:], tb[:, 896 + 16 * h:912 + 16 * h], ["wb", r("x0")], X, False, h == 7, r("key"), h > 0, 8)
             if MJ[c]:
                 mm(PY[:, 384:512], idn, x0, ["idn", r("x0")], Y, True, True, r("x0p"))
 
         def relator():
-            scan(uf[:, 0:48], T.on6[:], PX[:, 0:48], 0.0, OP.mult, OP.add, ["on6", r("uw")], [r("u0")], [X])
-            tt(UF(6), PX[:, 0:48:6], uf[:, 5:48:6], OP.subtract, [r("uw"), r("u0")], [r("u1")], [X])
+            scan(tf[:, 1024:1176], T.rd[:], PX[:, 96:248], 0.0, OP.add, OP.max, ["rd", r("key")], [r("f1")], [X])
+            tt(UF(6), tf[:, 1024 + 15:1176:19], tf[:, 1024 + 18:1176:19], OP.subtract, [r("f1")], [r("u1")])
             tt(UI(2), UF(6), UF(6), OP.mult, [r("u1")], [r("u2")])
             ts(UI(3), UI(2), 5, OP.arith_shift_right, [r("u2")], [r("u3")], (), 2047, OP.bitwise_and)
             cp(LS(1), UI(3), [r("u3")], [r("cl")])
-            cp(lu[:, 0:128], T.rts[:].indirect(LS(1)), ["rts", r("cl")], [r("lr")], kind="g")
+            copy(PICK[c], lu[:, 0:128], T.rts[:].indirect(LS(1)), ["rts", r("cl")], [r("lr")], kind="g")
 
         def spread():
-            ts(UH(0), UF(6), 1.0 / 128, OP.mult, [r("u1")], [r("y")], (), -2640.0 / 128, OP.add)
-            ts(UH(1), UF(6), 16.0, OP.mult, [r("u1")], [r("y16")], (), -2640.0 * 16, OP.add)
-            ts(UH(2), UF(6), 1.0 / 16, OP.mult, [r("u1")], [r("uq")], (), 1025.0 - 37 - 15.0 / 32, OP.add)
-            together(3)
-            mm(PZ[:, 0:256], T.k2[0:1, :], T.oneh[0:1, :], ["k2", "oneh", "oneh2"], Z, True, False, [r("k1"), r("k2")])
-            for m in range(16):
-                mm(PZ[:, m:256:16], T.bm[:, 128 * m:128 * m + 128], T["uh%d" % c][:, 0:16], ["bm%d" % m, r("y"), r("y16")], Z, False, m == 15,
-                   [r("k1"), r("k2")], m > 0)
+            plus(SPREAD[c], ys[:, 0:128:16], UF(6), -2640.0, [r("u1")], [r("y")])
+            line(SPREAD[c], UH(2), UF(6), 1.0 / 16, 1025.0 - 37 - 15.0 / 32, [r("u1")], [r("uq")])
+            together(2)
+            scan(ys[:, 144:272], T.keep[:], ys[:, 0:128], 0.0, OP.mult, OP.add, ["keep", r("y")], [r("yk")], kind="h")
+            both = [r("k1"), r("k2")]
+            mm(PZ[:, 0:256], T.k2[0:1, :], T.oneh[0:1, :], ["k2", "oneh", "oneh2"], Z, True, False, both)
+            for n, (up, down) in enumerate([(blk, T.bm[:, 0:128]), (T.bm[:, 128:256], T.bm[:, 256:384])]):
+                o = PZ[:, 128 * n:128 * n + 128]
+                mm(o, up, ys[:, 1:129], ["blk", "bm", r("y"), r("yk")], Z, False, False, both, False)
+                mm(o, up, ys[:, 144:272], ["blk", "bm", r("yk")], Z, False, False, both)
+                mm(o, down, ys[:, 145:273], ["bm", r("yk")], Z, False, n == 1, both)
 
         def gather_r(n):
             lo, hi = 512 * n, 512 * n + 512
             copy((GR if t else GR0)[c][n], xr[:, lo:hi], x.indirect(lu[:, lo // 16:hi // 16]), XR + [r("lr")], blocks("xr", lo, hi), kind="g")
 
         def letters():
-            ts(T["pk%d" % c][:], lu[:, 0:128], -2048.0, OP.add, [r("lr")], [r("pk")])
+            if not PACK:
+                plus(LETTERS[c], T["pk%d" % c][:], lu[:, 0:128], -2048.0, [r("lr")], [r("pk")])
+            elif c == 0:
+                copy(LETTERS[c], T.pk0[:], lu[:, 0:128], [r("lr")], [r("pk")])
+            else:
+                act(PZ[:, 384:512], lu[:, 0:128], AF.Copy, [r("lr")], [r("up")], [Z], scale=4096.0)
+                tt(T.pk1[:], T.pk0[:], PZ[:, 384:512], OP.add, ["pk_0", r("up")], [r("pk")], [Z])
 
         def tail():
-            tt(TF(6), TF(0), PZ[:, 0:128], OP.mult, [r("f0"), r("k1")], [r("f6")], [Z])
+            tt(TF(6), HH(0), PZ[:, 0:128], OP.mult, [r("q"), r("k1")], [r("f6")], [Z])
             tt(TI(0), TF(6), PZ[:, 128:256], OP.add, [r("f6"), r("k2")], [r("t0")], [Z])
             ts(TI(1), TI(0), 5, OP.arith_shift_right, [r("t0")], [r("t1")], (), 4095, OP.bitwise_and)
-            ts(HH(4), TI(1), -2048.0, OP.add, [r("t1")], [r("tl")])
+            plus(TAIL[c], HH(4), TI(1), -2048.0, [r("t1")], [r("tl")])
 
         def other():
-            ts(TI(2), TF(0), 0.5, OP.mult, [r("f0")], [r("t2")], (), -0.25, OP.add)
-            ts(TF(3), TI(2), 4.0, OP.mult, [r("t2")], [r("t3")], (), 1.0, OP.add)
-            tt(HH(3), TF(3), TF(0), OP.subtract, [r("t3"), r("f0")], [r("h3")])
+            ts(TF(3), HH(0), -0.5, OP.add, [r("q")], [r("t3")], (), EVEN, OP.add)
+            if OTHER[c] == "s":
+                act(HH(1), TF(3), AF.Copy, [r("t3")], [r("ev")], scale=2.0, bias=-2 * EVEN)
+            else:
+                ts(HH(1), TF(3), -EVEN, OP.add, [r("t3")], [r("ev")], (), 2.0, OP.mult)
 
         mj = MJ[c]
-        positive = ["r" in GW[c][2 * h:2 * h + 2] for h in range(2)]
         spare = [("ps6", "ps6d"), ("ps7", "ps7d")]
 
         def biggest(h):
@@ -769,8 +844,8 @@ def rank_program(g, core, T, topo):
                     together(mj // 2)
 
         def apart(h):
-            D, tag = spare[h]
             for j0 in range(mj, 16, 8):
+                D, tag = spare[(h + (j0 - mj) // 8) % 2]
                 js = range(j0, min(j0 + 8, 16))
                 for j in js:
                     o = T[D][:, 64 * (j - j0):64 * (j - j0) + 64]
@@ -790,30 +865,34 @@ def rank_program(g, core, T, topo):
 
         def least():
             scan(tf[:, 1024:1168], T.rs[:], PX[:, 96:240], 0.0, OP.add, OP.min, ["rs", r("key")], [r("f1")], [X])
-            tt(tb[:, 0:128:16], tf[:, 1024 + 15:1168:18], tf[:, 1024 + 17:1168:18], OP.subtract, [r("f1")], [r("zs")])
-            scan(TB(1), T.keep[:], TB(0), 0.0, OP.mult, OP.add, ["keep", r("zs")], [r("sk")], kind="h")
-            tt(TB(2), TB(1), PX[:, 256:384], OP.mult, [r("sk"), r("mdp")], [r("skd")], [X])
-            o = PX[:, 56:96]
-            mm(o, T.ones[0:1, 0:128], T.row[0:1, :], ["ones"] + ["row%d" % n for n in range(5)], X, True, False, r("slp"))
+            tt(zs[:, 0:128:16], tf[:, 1024 + 15:1168:18], tf[:, 1024 + 17:1168:18], OP.subtract, [r("f1")], [r("zs")])
+            scan(zs[:, 144:272], T.keep[:], zs[:, 0:128], 0.0, OP.mult, OP.add, ["keep", r("zs")], [r("sk")], kind="h")
+            o, rl = PX[:, 56:88], ["rl%d" % n for n in range(4)]
+            mm(o, T.ones[0:1, 0:128], T.row[0:1, :], ["ones"] + ["row%d" % n for n in range(4)], X, True, False, r("slp"))
             mm(o, idn, T.cl[:], ["idn", "cl"], X, False, False, r("slp"))
-            mm(o, TB(2), T.rl[:], [r("skd")] + ["rl%d" % n for n in range(5)], X, False, True, r("slp"))
-            cp(T["ls%d" % c][:, 16:56], o, [r("slp")], [r("sl")], [X])
+            mm(o, zs[:, 1:129], T.rl[:], [r("zs")] + rl, X, False, False, r("slp"), False)
+            mm(o, zs[:, 144:272], T.rl[:], [r("sk")] + rl, X, False, False, r("slp"), False)
+            mm(o, zs[:, 145:273], T.rn[:], [r("sk"), "rn"], X, False, True, r("slp"))
+            cp(T["ls%d" % c][:, 16:48], o, [r("slp")], [r("sl")], [X])
 
         def turn():
-            ts(lu[:, 128:256], T["ww%d" % c][:].indirect(LS(2)), 2048.0, OP.add, [r("ww"), r("sl")], [r("lw")], kind="g")
+            for n in range(LOTS):
+                a, b = n * 128 // LOTS, (n + 1) * 128 // LOTS
+                copy(TURN[c], lu[:, 128 + a:128 + b], T["ww%d" % c][:, 16 * a:16 * b].indirect(T["ls%d" % c][:, 24 + a // 16:24 + b // 16]),
+                   [r("ww") + str(n), r("sl")], [r("lw%d" % h) for h in range(a // 64, b // 64)], kind="g")
 
         def limit():
-            for out, by in [(2, 3), (5, 6)][:2 if FAST[c] == "f" else 1]:
-                if t == 0:
-                    act(TF(out), T.tw[:].indirect(LS(by)), AF.Copy, ["tw", r("sl")], [r("f%d" % out)], kind="g", bias=2048.0)
-                else:
-                    act(TF(out), T.tw[:].indirect(LS(by)), AF.Identity, ["tw", r("sl"), "thr"], [r("f%d" % out)], kind="g", bias=col(10))
+            copy(LIMIT[c], TB(2), T.md[:, 0:16].indirect(LS(4)), ["md", r("sl")], [r("one")], kind="g")
+            mm(PX[:, 256:384], T.cw2[:], TB(2), ["circ1", r("one")], X, True, True, r("w2"))
+            if FAST[c] == "f":
+                mm(PZ[:, 256:384], T.cw3[:], TB(2), ["circ2", r("one")], Z, True, True, r("w3"))
+                act(TF(5), PZ[:, 256:384], AF.Identity, [r("w3"), "thr"], [r("f5")], [Z], bias=col(10))
 
         def gather_w(n):
             lo, hi, how = 512 * n, 512 * n + 512, GW[c][n]
             d, m, out = blocks("df", lo, hi), sized(range(4 * n, 4 * n + 4)), mx[:, 4 * n:4 * n + 4, :]
             if how == "s":
-                act(df[:, lo:hi], x.indirect(lu[:, 128 + lo // 16:128 + hi // 16]), AF.Copy, XR + [r("lw")], d, kind="g")
+                act(df[:, lo:hi], x.indirect(lu[:, 128 + lo // 16:128 + hi // 16]), AF.Copy, XR + [r("lw%d" % (n // 2))], d, kind="g")
                 D, tag = spare[n % 2]
                 mm(T[D][:], T.ni[:], xr[:, lo:hi], ["ni"] + blocks("xr", lo, hi), D, True, False, tag)
                 mm(T[D][:], idn, df[:, lo:hi], ["idn"] + d, D, False, True, tag, False)
@@ -822,74 +901,93 @@ def rank_program(g, core, T, topo):
             for a in range(lo, hi, FINE[c]):
                 b = a + FINE[c]
                 tt(df[:, a:b], x.indirect(lu[:, 128 + a // 16:128 + b // 16]), xr[:, a:b], OP.subtract,
-                   XR + [r("lw")] + blocks("xr", a, b), blocks("df", a, b), kind="g")
+                   XR + [r("lw%d" % (n // 2))] + blocks("xr", a, b), blocks("df", a, b), kind="g")
             if how == "a":
-                act(out, df[:, lo:hi], AF.Relu if positive[n // 2] else AF.Abs, d, m)
+                act(out, df[:, lo:hi], AF.Abs, d, m)
             else:
                 ts(out, df[:, lo:hi], 0.0, OP.max, d, m, kind="h")
 
-        def sizes(h):
-            lo, relu = 1024 * h, positive[h]
-            o = PY[:, 128 + lo // 16:192 + lo // 16]
+        def sizes(n):
+            lo, relu = 512 * n, GW[c][n] == "r"
+            o = lambda k: PY[32 * (k // 4):32 * (k // 4) + 32, 128 + 32 * n:160 + 32 * n]
+            by = lambda z, k: T.sj[:, 64 * z + 24 - 8 * (k % 4):64 * z + 56 - 8 * (k % 4)]
+            mm(PY[:, 128 + 32 * n:160 + 32 * n], T.cth[:], tb[:, 256 + 32 * n:288 + 32 * n], ["circ0", r("one")], Y, True, False, GAPS[n])
             if relu:
                 for k in range(16):
-                    mm(o, T.bn[:, 15 - k:143 - k], df[:, lo + k:lo + 1024:16], ["bn"] + blocks("df", lo, lo + 1024), Y, k == 0, False, r("d2"))
+                    mm(o(k), by(2, k), df[:, lo + k:lo + 512:16], ["sj"] + blocks("df", lo, lo + 512), Y, False, False, GAPS[n], k > 0, 8)
             for k in range(16):
-                mm(o, (T.b2 if relu else T.b0)[:, 15 - k:143 - k], mx[:, 8 * h:8 * h + 8, k:128:16],
-                   ["b2" if relu else "b0"] + sized(range(8 * h, 8 * h + 8)), Y, k == 0 and not relu, k == 15, r("d2"), False if k == 0 else None)
+                mm(o(k), by(int(relu), k), mx[:, 4 * n:4 * n + 4, k:128:16], ["sj"] + sized(range(4 * n, 4 * n + 4)), Y, False, k % 4 == 3, GAPS[n], k > 0, 8)
 
         def halves():
             act(TB(3), xr[:].indirect(LS(5)), AF.Copy, XRS + [r("sl")], [r("q15")], kind="g")
             mm(PY[:, 0:128], idn, x0, ["idn", r("x0")], Y, True, False, r("nvp"))
             mm(PY[:, 0:128], idn, TB(3), ["idn", r("q15")], Y, False, True, r("nvp"))
-            ts(T.nvi[:, CW * c:CW * c + CW], PY[:, 0:128], 0.5, OP.mult, [r("nvp")], [r("nv")], [Y], -0.25, OP.add)
+            line(HALVES[c], T.nvi[:, CW * c:CW * c + CW], PY[:, 0:128], 0.5, -0.25, [r("nvp")], [r("nv")], [Y])
 
         def unpack():
-            act(TF(0), T["pw%d" % c][:].indirect(LS(2)), AF.Copy, [r("pw"), r("sl")], [r("f0")], kind="g")
+            if PACK:
+                by, o = [(4095, OP.bitwise_and), (12, OP.arith_shift_right)][c]
+                ts(TI(2), T.pw1[:].indirect(LS(2)), by, o, ["pw_10", r("sl")], [r("t2")], kind="g")
+                plus(UNPACK[c], HH(0), TI(2), -2048.0, [r("t2")], [r("q")])
+            else:
+                copy(UNPACK[c], HH(0), T["pw%d" % c][:].indirect(LS(2)), [r("pw") + "0", r("sl")], [r("q")], kind="g")
 
         def match():
-            tt(TB(4), PY[:, 128:256], TF(2), OP.is_gt, [r("d2"), r("f2")], [r("dis")], [Y])
-            tt(TB(5), T.tw[:].indirect(LS(4)), TB(4), OP.mult, ["tw", r("sl"), r("dis")], [r("dw")], kind="g")
-            mm(PY[:, 256:384], blk, TB(5), ["blk", r("dw")], Y, True, True, r("pre"))
+            if MATCH[c] == "s":
+                act(TB(4), PY[:, 128:256], AF.Relu, GAPS + ["thr2"], [r("dis")], [Y], scale=32768.0, bias=col(19))
+                tt(TB(5), TB(4), PX[:, 256:384], OP.min, [r("dis"), r("w2")], [r("dw")], [X])
+            else:
+                ts(TB(4), PY[:, 128:256], col(10), OP.is_gt, GAPS + ["thr"], [r("dis")], [Y])
+                tt(TB(5), TB(4), PX[:, 256:384], OP.mult, [r("dis"), r("w2")], [r("dw")], [X])
+            mm(PY[:, 256:384], T.bj[:, 128:256], TB(5), ["bjt", r("dw")], Y, True, True, r("pre"))
             ts(TB(6), PY[:, 256:384], T.two[:, 47:48], OP.is_lt, [r("pre"), "two"], [r("P")], [Y])
 
-        def aim():
-            o = PX[:, 240:248]
-            tt(TB(8), PY[:, 128:256], TF(5), OP.is_gt, [r("d2"), r("f5")], [r("far")], [Y])
-            mm(o, idn, T.base[:, 16:24], ["idn", "base2"], X, True, False, r("atp"))
-            mm(o, T.i128[:], UH(0), ["i128", r("y")], X, False, False, r("atp"))
-            mm(o, T.n16[:], UH(2), ["n16", r("uq")], X, False, False, r("atp"))
-            for m in range(16):
-                mm(o, T.bk[:, 15 - m:143 - m], tb[:, 1024 + m:1152:16], ["bk", r("far")], X, False, m == 15, r("atp"), m > 0)
-            cp(LS(8), o, [r("atp")], [r("al")], [X])
+        def aim(n):
+            if n + 1 < len(AIM):
+                a, b, uh = 2 * AIM[n], 2 * AIM[n + 1], T["uh%d" % c]
+                o, far, tag = PX[:, a:b], r("far%d" % n), r("atp%d" % n)
+                tt(tb[:, 1024 + 16 * a:1024 + 16 * b], PY[:, 128 + 16 * a:128 + 16 * b], tf[:, 640 + 16 * a:640 + 16 * b], OP.is_gt,
+                   GAPS[AIM[n]:AIM[n + 1]] + [r("f5")], [far], [Y])
+                mm(o, idn, T.base[:, 16 + a:16 + b], ["idn", "base2"], X, True, False, tag)
+                mm(o, idn, ys[:, 16 * a:16 * b:16], ["idn", r("y")], X, False, False, tag)
+                mm(o, T.n16[:], uh[:, 16 + a:16 + b], ["n16", r("uq")], X, False, False, tag)
+                for m in range(16):
+                    mm(o, T.bk[:, 15 - m:143 - m], tb[:, 1024 + 16 * a + m:1024 + 16 * b:16], ["bk", far], X, False, m == 15, tag, m > 0)
+                cp(T["ls%d" % c][:, 64 + a:64 + b], o, [tag], [r("al%d" % n)], [X])
 
         def masks():
-            mm(PZ[:, 0:128], T.m1[:], TB(6), ["m1", r("P")], Z, True, True, r("k1"))
-            mm(PZ[:, 256:384], T.m3[:], TB(6), ["m3", r("P")], Z, True, True, r("k3"))
-            mm(PZ[:, 128:256], T.ones[0:1, 0:128], T.ones[0:1, 0:128], ["ones"], Z, True, False, r("k2"))
-            mm(PZ[:, 128:256], T.m2[:], TB(6), ["m2", r("P")], Z, False, True, r("k2"))
+            both = [r("k1"), r("k2")]
+            mm(PZ[:, 0:256], T.ones[0:2, 0:128], T.cr0[0:2, :], ["ones", "cr1", "cr2"], Z, True, False, both)
+            mm(PZ[:, 0:128], T.an[:], HH(0), ["an", r("q")], Z, False, False, both)
+            mm(PZ[:, 0:128], T.ann[:], HH(1), ["ann", r("ev")], Z, False, False, both)
+            mm(PZ[:, 128:256], T.ni[:], HH(4), ["ni", r("tl")], Z, False, False, both)
+            mm(PZ[:, 0:128], T.mo[:], TB(6), ["mo", r("P")], Z, False, False, both, False)
+            mm(PZ[:, 128:256], T.mt[:], TB(6), ["mt", r("P")], Z, False, True, both)
 
-        def write_x():
-            at, name = (LS(8), r("al")) if FAST[c] == "f" else (LO(2, 3), made)
-            cp(T.xs[:, 4096 * c:(4096, XW)[c]].indirect(at), T.nvi[:, CW * c:CW * c + CW], [r("nv"), name], XR[c:c + 1], kind="s")
+        def write_x(n=0):
+            if FAST[c] != "f":
+                cp(T.xs[:, 0:4096].indirect(LO(2, 3)), T.nvi[:, CW * c:CW * c + CW], [r("nv"), made], XR[c:c + 1], kind="s")
+            elif n + 1 < len(AIM):
+                a, b = 2 * AIM[n], 2 * AIM[n + 1]
+                cp(T.xs[:, 4096:XW].indirect(T["ls%d" % c][:, 64 + a:64 + b]), T.nvi[:, CW * c + 16 * a:CW * c + 16 * b], [r("nv"), r("al%d" % n)],
+                   XR[c:c + 1], kind="s")
 
         def turned():
-            act(TF(4), T["ww%d" % c][:].indirect(LO(1, 2)), AF.Copy, [r("ww"), made], [r("wr")], kind="g")
+            if TURNED[c] != "f":
+                copy(TURNED[c], TF(4), T["ww%d" % c][:].indirect(LO(1, 2)), WW + [made], [r("wr")], kind="g")
 
         def renew():
-            tt(HH(1), HH(3), PZ[:, 0:128], OP.mult, [r("h3"), r("k1")], [r("h1")], [Z])
-            tt(HH(2), HH(4), PZ[:, 256:384], OP.mult, [r("tl"), r("k3")], [r("h2")], [Z])
-            together(2)
-            tt(HH(0), TF(4), PZ[:, 128:256], OP.mult, [r("wr"), r("k2")], [r("h0")], [Z])
-            F = PZ[:, 384:512]
-            flip, same = (T.an[:], idn) if last else (T.sh[:, moved], T.rv[:, moved])
-            mm(F, flip, HH(1), ["an", "sh", r("h1")], Z, True, False, r("zf"))
-            mm(F, same, HH(2), ["idn", "rv", r("h2")], Z, False, False, r("zf"))
-            mm(F, same, HH(0), ["idn", "rv", r("h0")], Z, False, True, r("zf"))
+            if TURNED[c] == "f":
+                act(TF(4), PZ[:, 0:128], AF.Copy, [r("k1")], [r("wr")], [Z])
+                tt(TF(0), TF(4), PZ[:, 128:256], OP.min, [r("wr"), r("k2")], [r("n1")], [Z])
+                tt(TF(2), T["ww%d" % c][:].indirect(LO(1, 2)), TF(0), OP.min, WW + [made, r("n1")], [r("n2")], kind="g")
+            else:
+                tt(TF(0), TF(4), PZ[:, 0:128], OP.min, [r("wr"), r("k1")], [r("n1")], [Z])
+                tt(TF(2), TF(0), PZ[:, 128:256], OP.min, [r("n1"), r("k2")], [r("n2")], [Z])
             if last:
-                act(T.ywf[:, CW * c:CW * c + CW], F, AF.Copy, [r("zf")], [r("yw")], [Z], bias=2048.0)
+                act(T.ywf[:, CW * c:CW * c + CW], TF(2), AF.Abs, [r("n2")], [r("yw")])
                 return
-            copy(RENEW[c], T.wo[:, w0:w0 + CW], F, [r("zf")], [r("wo%d" % t)], [Z])
+            act(T.wo[:, w0:w0 + CW], TF(2), AF.Abs, [r("n2")], [r("wo%d" % t)])
             send(T.wl[:, w0 + NC * CW:w0 + NC * CW + CW], T.wo[:, w0:w0 + CW], r("wo%d" % t), "ar%d_%d" % (t + 1, c), "wl%d_%d" % (t + 1, c), 550.0)
 
         def tally():
@@ -900,7 +998,7 @@ def rank_program(g, core, T, topo):
                 "gather_r": gather_r, "letters": letters, "tail": tail, "other": other, "keys": keys, "least": least, "turn": turn,
                 "gather_w": gather_w, "biggest": biggest, "apart": apart, "limit": limit, "aim": aim, "masks": masks,
                 "sizes": sizes, "halves": halves, "unpack": unpack, "match": match, "write_x": write_x, "turned": turned,
-                "renew": renew, "tally": tally, "offer": offer, "lead": lead, "lists": lists}
+                "renew": renew, "tally": tally, "lead": lead, "lists": lists}
 
     def allow():
         o = T.ps0[:, 48:49]
@@ -909,6 +1007,8 @@ def rank_program(g, core, T, topo):
         cp(T.ai[:, 0:1], o, ["w0p_0"], ["ai"], ["ps0"])
         ts(T.aj[:, 0:1], T.ai[:, 0:1], 31, OP.bitwise_and, ["ai"], ["aj"])
         ts(col(10), T.aj[:, 0:1], 8.0, OP.mult, ["aj"], ["thr"], (), 2048.0, OP.add)
+        if "s" in MATCH:
+            ts(col(19), T.aj[:, 0:1], -8.0 * 32768, OP.mult, ["aj"], ["thr2"], (), -2048.0 * 32768, OP.add)
 
     def enter(name):
         label.extend([now[0]] * (len(nodes) - len(label)))
@@ -940,7 +1040,7 @@ def rank_program(g, core, T, topo):
         dmas("s", [(lambda a: lambda: S.dma_start(T.yw[:, a], T.ywf[:, a]))(slice(CW * c, CW * c + CW))], "outw", ["yw_%d" % c], [], 64)
     enter(None)
     if "order" not in PLAN:
-        PLAN["order"] = tighten(nodes, moving, label, first_placing(nodes, moving))
+        PLAN["len"], PLAN["order"] = tighten(nodes, moving, label, first_placing(nodes, moving))
     for i in PLAN["order"]:
         nodes[i][1]()
     for sem, val in total.items():

import math
from concourse.mybir import dt, AluOpType as OP, AxisListType, ActivationFunctionType as AF

VIS = 6
NC = 2
CW = 128
XW = 2048 + 4096 + 9 * 2048
BIG = 1.5 * 2 ** 35
WHOLE = 1.5 * 2 ** 23
EVEN = 1.5 * 2 ** 24
OFF = 8192.0
CYCLE, PECYCLE, GATHER, SCATTER = 0.95, 0.53, 1.56, 3.8
OWN, WAKE, DMA, NET = 120.0, 200.0, 2.1, 1.1
MIXES = [(0.95, 1.0, 1.0, 1.0, 1.0, 1.0, 1.15, 20.0), (1.15, 0.8, 1.0, 1.0, 0.8, 0.9, 1.2, 0.0), (0.95, 1.1, 1.4, 1.0, 1.0, 1.1, 1.1, 50.0)]
GR, GR0 = ("sssv", "sssv"), ("svsv", "svsv")
MJ = (10, 10)
GW = ("saaa", "asar")
FINE = (512, 512)
FIRST, LETTERS, TAIL, OTHER, LIMIT, UNPACK, MATCH, TURNED = "vv", "vs", "ss", "ss", "ss", "ss", "vv", "ff"
SPREAD, HALVES, LEAD, TURN, PICK, STEPS_BY = "ss", "vv", "XX", "vv", "vv", "vv"
AIM = (0, 4)
FAST = "sf"
PACK = 0
LOTS = 1
JOIN = 4
SLOW = (1.0, 1.0)
ROUNDS = 2
TURNS, STEPS, MORE, HEAT, SEED = 5, 1000, 1000, 100.0, 12
PLAN = {}

ORDER = """
-b.sizes:2 -a.halves -b.tail -b.aim:0 -b.match -a.write_x -b.write_x:0 a.first -b.lead a.weigh -b.masks a.relator -b.lists b.first
a.gather_r:2 b.weigh -b.renew a.gather_r:3 -b.tally a.gather_r:1 -a.renew a.wwin b.relator a.gather_r:0 a.apart:0 a.letters b.spread
a.apart:1 b.gather_r:1 b.gather_r:0 a.pwin b.biggest:0 a.biggest:1 a.biggest:0 -a.tally b.gather_r:3 a.keys a.least b.letters
b.gather_r:2 b.apart:1 a.turn b.apart:0 a.limit b.biggest:1 a.spread allow a.gather_w:1 a.gather_w:3 a.unpack a.gather_w:0 a.gather_w:2
b.keys b.least a.sizes:3 b.wwin a.other a.sizes:1 b.turn b.gather_w:0 a.sizes:0 a.sizes:2 b.halves a.match b.limit b.gather_w:1
b.gather_w:2 b.pwin a.tail a.masks b.sizes:1 b.gather_w:3 b.unpack b.other b.sizes:0 a.lead a.lists b.sizes:3
"""
CHAIN = """first weigh relator letters pwin gather_r:0 gather_r:1 gather_r:2 gather_r:3 biggest:0 apart:0 biggest:1 apart:1 keys least turn
gather_w:0 gather_w:1 gather_w:2 gather_w:3 sizes:0 sizes:1 sizes:2 sizes:3 limit match lead lists turned masks renew wwin spread unpack tail other
halves aim:0 aim:1 write_x write_x:0 write_x:1 tally""".split()

SCRATCH = {
    "xs": ("sbuf", [128, XW], "bfloat16"),
    "rts": ("sbuf", [128, 2048], "int32"),
    "wdi": ("sbuf", [128, 256], "int32"),
    "wti": ("sbuf", [128, 2], "int32"),
    "thi": ("sbuf", [128, 2], "int32"),
    "wl": ("sbuf", [128, NC * CW * VIS], "float32"),
    "wo": ("sbuf", [128, NC * CW * VIS], "float32"),
    "ll": ("sbuf", [128, NC * 8 * VIS], "uint16"),
    "lo": ("sbuf", [128, NC * 24 * VIS], "uint16"),
    "ywf": ("sbuf", [128, 256], "float32"),
    "nvi": ("sbuf", [128, 256], "int32"),
    "cw": ("sbuf", [128, 256], "float32"),
    "ct": ("sbuf", [128, 256], "bfloat16"),
    "cc": ("sbuf", [128, 256], "bfloat16"),
    "mc": ("sbuf", [128, 256], "bfloat16"),
    "q1": ("sbuf", [128, 128], "bfloat16"),
    "ones": ("sbuf", [128, 256], "bfloat16"),
    "zerf": ("sbuf", [128, 16], "float32"),
    "blk": ("sbuf", [128, 256], "bfloat16"),
    "blk0": ("sbuf", [128, 256], "bfloat16"),
    "id2": ("sbuf", [128, 256], "bfloat16"),
    "an": ("sbuf", [128, 128], "bfloat16"),
    "n16": ("sbuf", [128, 128], "bfloat16"),
    "ni": ("sbuf", [128, 128], "bfloat16"),
    "pa": ("sbuf", [128, 256], "bfloat16"),
    "pb": ("sbuf", [128, 256], "bfloat16"),
    "pc": ("sbuf", [128, 128], "bfloat16"),
    "pd": ("sbuf", [128, 128], "bfloat16"),
    "cn": ("sbuf", [128, 256], "bfloat16"),
    "cr0": ("sbuf", [128, 256], "bfloat16"),
    "m3": ("sbuf", [128, 128], "bfloat16"),
    "e8": ("sbuf", [128, 128], "bfloat16"),
    "m1a": ("sbuf", [128, 128], "bfloat16"),
    "mo": ("sbuf", [128, 128], "bfloat16"),
    "m2b": ("sbuf", [128, 128], "bfloat16"),
    "mt": ("sbuf", [128, 128], "bfloat16"),
    "ann": ("sbuf", [128, 128], "bfloat16"),
    "cth": ("sbuf", [128, 128], "float16"),
    "cw2": ("sbuf", [128, 128], "bfloat16"),
    "cw3": ("sbuf", [128, 128], "bfloat16"),
    "tl": ("sbuf", [128, 24], "uint16"),
    "rn": ("sbuf", [128, 32], "bfloat16"),
    "g8": ("sbuf", [128, 8], "bfloat16"),
    "b0": ("sbuf", [128, 144], "bfloat16"),
    "sj": ("sbuf", [128, 192], "bfloat16"),
    "wb": ("sbuf", [128, 128], "float16"),
    "dg": ("sbuf", [128, 152], "bfloat16"),
    "rd": ("sbuf", [128, 152], "float32"),
    "bj": ("sbuf", [128, 256], "bfloat16"),
    "bk": ("sbuf", [128, 144], "bfloat16"),
    "z0": ("sbuf", [128, 144], "bfloat16"),
    "b18": ("sbuf", [128, 288], "bfloat16"),
    "bm": ("sbuf", [128, 384], "bfloat16"),
    "k2": ("sbuf", [128, 128], "bfloat16"),
    "oneh": ("sbuf", [128, 256], "float16"),
    "s2": ("sbuf", [128, 8], "bfloat16"),
    "sn": ("sbuf", [128, 8], "bfloat16"),
    "sx0": ("sbuf", [128, 144], "bfloat16"),
    "sx1": ("sbuf", [128, 144], "bfloat16"),
    "kt": ("sbuf", [128, 128], "bfloat16"),
    "ktk": ("sbuf", [128, 144], "bfloat16"),
    "md": ("sbuf", [128, 128], "bfloat16"),
    "rs": ("sbuf", [128, 144], "float32"),
    "keep": ("sbuf", [128, 128], "bfloat16"),
    "pi": ("sbuf", [128, 2], "int32"),
    "pj": ("sbuf", [128, 2], "int32"),
    "cols": ("sbuf", [128, 64], "float32"),
    "itg": ("sbuf", [128, 16], "float32"),
    "rl": ("sbuf", [128, 32], "bfloat16"),
    "cl": ("sbuf", [128, 32], "bfloat16"),
    "row": ("sbuf", [128, 32], "bfloat16"),
    "base": ("sbuf", [128, 24], "float16"),
    "ata": ("sbuf", [128, 8], "float32"),
    "two": ("sbuf", [128, 48], "float32"),
    "tx": ("sbuf", [128, 8], "float32"),
    "dx": ("dram", [8, 32, 8], "float32"),
    "tw": ("sbuf", [128, 128], "float32"),
    "cnt": ("sbuf", [128, 2], "bfloat16"),
    "ai": ("sbuf", [128, 2], "int32"),
    "aj": ("sbuf", [128, 2], "int32"),
}
for _c in range(NC):
    SCRATCH.update({
        "xr%d" % _c: ("sbuf", [128, 2048], "bfloat16"),
        "mx%d" % _c: ("sbuf", [128, 16, 128], "bfloat16"),
        "df%d" % _c: ("sbuf", [128, 2048], "bfloat16"),
        "ww%d" % _c: ("sbuf", [128, 2048], "float32"),
        "pw%d" % _c: ("sbuf", [128, 2048], "float32"),
        "dw%d0" % _c: ("dram", [8, 32, 128 // LOTS], "float32"),
        "dp%d" % _c: ("dram", [8, 32, 128], "float32"),
        "pk%d" % _c: ("sbuf", [128, 128], "float32"),
        "zs%d" % _c: ("sbuf", [128, 288], "bfloat16"),
        "ys%d" % _c: ("sbuf", [128, 288], "float16"),
        "ti%d" % _c: ("sbuf", [128, 384], "int32"),
        "tf%d" % _c: ("sbuf", [128, 1280], "float32"),
        "tb%d" % _c: ("sbuf", [128, 1152], "bfloat16"),
        "hh%d" % _c: ("sbuf", [128, 1024], "float16"),
        "ui%d" % _c: ("sbuf", [128, 32], "int32"),
        "uf%d" % _c: ("sbuf", [128, 56], "float32"),
        "uh%d" % _c: ("sbuf", [128, 24], "float16"),
        "ls%d" % _c: ("sbuf", [128, 72], "uint16"),
        "lu%d" % _c: ("sbuf", [128, 256], "uint16"),
    })
if PACK:
    SCRATCH.update({"pk1": ("sbuf", [128, 128], "int32"), "dp1": ("dram", [8, 32, 128], "int32"), "pw1": ("sbuf", [128, 2048], "int32")})
for _b in range(8):
    SCRATCH["ps%d" % _b] = ("psum", [128, 512], "float32")

SEMAPHORES = ["v", "s", "pe", "gp", "sent", "ldx", "ldr", "ldw", "ldt", "ldh", "outw", "outx", "dx0", "dx1"]
SEMAPHORES += ["d%s%d%d" % (w, st, c) for w in "wp" for st in (0, 1, 2) for c in range(NC)]
SEMAPHORES += ["%s%d_%d" % (w, t, c) for w in ("ar", "al") for t in range(1, VIS) for c in range(NC)]


def needs(nodes, banks_too):
    preds = [dict() for _ in nodes]
    last, rd, bk = {}, {}, {}
    for i, (q, _, reads, writes, banks, _) in enumerate(nodes):
        def edge(j, hard):
            preds[i][j] = preds[i].get(j, False) or hard
        for x in reads:
            edge(last[x], True)
            rd.setdefault(x, []).append(i)
        for x in writes:
            if x in last:
                edge(last[x], not (q == "pe" and nodes[last[x]][0] == "pe"))
            for j in rd.get(x, ()):
                if j != i:
                    edge(j, nodes[j][0] != q or q == "sy")
            last[x], rd[x] = i, []
        for b in banks:
            for q2, j in bk.setdefault(b, {}).items():
                if j != i and ((q2 != q and banks_too) or q2 == q == "pe"):
                    edge(j, q2 != q)
            bk[b][q] = i
    return preds


def lag(nodes, moving, j, i):
    return OWN if nodes[j][0] == nodes[i][0] and j not in moving else WAKE + (60.0 if nodes[j][0] == "pe" else 0.0)


def first_placing(nodes, moving):
    where, cost, ins, ids, ends = [], [], [], [], []
    moving = {i: [x * SLOW[1] for x in move] if nodes[i][0] == "gp" else [move[0], move[1] * SLOW[0], move[2]] for i, move in moving.items()}
    for i, pred in enumerate(needs(nodes, True)):
        ids.append(len(where))
        where.append(nodes[i][0])
        cost.append(nodes[i][5].real + nodes[i][5].imag)
        ins.append([(ends[j], lag(nodes, moving, j, i) + moving.get(j, (0, 0, 0.0))[2]) if hard else (ids[j], 0.0) for j, hard in pred.items()])
        if i in moving:
            where.append("engines")
            cost.append(moving[i][1])
            ins.append([(ids[i], moving[i][0] - min(nodes[i][5].real, moving[i][0]))])
        ends.append(len(where) - 1)
    m = len(where)
    outs = [[] for _ in range(m)]
    for i in range(m):
        for j, wait in ins[i]:
            outs[j].append((i, wait))

    def place(order, before):
        end, busy = [0.0] * m, {}
        for i in order:
            t = max([end[j] + wait for j, wait in before[i]] + [0.0])
            los, his = busy.setdefault(where[i], ([], []))
            a, b = 0, len(his)
            while a < b:
                mid = (a + b) // 2
                a, b = (mid + 1, b) if his[mid] <= t else (a, mid)
            while a < len(los) and los[a] < t + cost[i]:
                t = his[a]
                a += 1
            los.insert(a, t)
            his.insert(a, t + cost[i])
            end[i] = t + cost[i]
        return end

    key, best = list(range(m)), None
    for _ in range(ROUNDS):
        end = place(sorted(range(m), key=lambda z: key[z]), ins)
        if best is None or max(end) < max(best):
            best = end
        back = place(sorted(range(m), key=lambda z: (-end[z], -z)), outs)
        key = [-back[i] + 1e-7 * i for i in range(m)]
    return sorted(range(len(nodes)), key=lambda z: (best[ends[z]] - cost[ends[z]] - (moving[z][0] if z in moving else 0.0), z))


def clock(nodes, moving, mix=MIXES[0], preds=None):
    n = len(nodes)
    preds = preds or needs(nodes, False)
    names = ["v", "s", "pe", "gp", "sy"]
    engine, lists, waits, moves, late, net, pe, short = mix
    rows = []
    for i, node in enumerate(nodes):
        q, move, cost = names.index(node[0]), moving.get(i), node[5]
        if move:
            move = [x * net for x in move] if q == 3 else [move[0] * late, move[1] * moves, move[2] * late]
        cost = cost.real * (net if q == 3 else 1.0) if move else engine * (cost.real + lists * cost.imag) * (pe if q == 2 else 1.0) + (short if q == 1 else 0.0)
        rows.append((q, [(j, waits * lag(nodes, moving, j, i)) for j, hard in preds[i].items() if hard], int(node[4][0][2:]) if node[4] else -1,
                     cost, move, waits * (WAKE + (60.0 if q == 2 else 0.0))))

    def run(order):
        free, last = [0.0] * 5, [-1] * 5
        start, end, why = [0.0] * n, [0.0] * n, [-1] * n
        held = [[(-1e9, -1)] * 3 for _ in range(8)]
        engines, mover, since = 0.0, -1, 0.0
        for i in order:
            q, hard, bank, cost, move, wake = rows[i]
            t, w = free[q], last[q]
            for j, wait in hard:
                u = end[j] + wait
                if u > t:
                    t, w = u, j
            if bank >= 0:
                for z in (0, 1, 2):
                    if z != q and held[bank][z][0] > t:
                        t, w = held[bank][z]
            u = free[q] = t + cost
            last[q] = i
            if move:
                at = t + move[0]
                if engines > at:
                    if q == 3 and rows[mover][0] == 4:
                        part = min(1.0, max(0.0, t - start[mover]) / rows[mover][3])
                        at = max(at, since + part * rows[mover][4][1])
                        end[mover] += move[1]
                        engines += move[1]
                        start[i], end[i], why[i] = t, at + move[1] + move[2], (mover if at > t + move[0] else w)
                        continue
                    at, w = engines, mover
                since, engines, mover = at, at + move[1], i
                u = engines + move[2]
            elif bank >= 0:
                held[bank][q] = (u + wake, i)
            start[i], end[i], why[i] = t, u, w
        return start, end, why
    return preds, run


def tighten(nodes, moving, label, given):
    n = len(nodes)
    preds = needs(nodes, False)
    runs = [clock(nodes, moving, mix, preds)[1] for mix in MIXES]
    lists = [list(p) for p in preds]
    hard = [[(j, lag(nodes, moving, j, i)) for j, h in p.items() if h] for i, p in enumerate(preds)]
    users = [[] for _ in nodes]
    for i, p in enumerate(hard):
        for j, wait in p:
            users[j].append((i, wait))
    kind, of, count, parts = [None] * n, {}, {}, {}
    for i in range(n):
        t, word = label[i]
        t, word = t - (word[:1] == "-"), word.lstrip("-")
        count[t, word] = count.get((t, word), 0) + 1
        kind[i] = (t, (word, count[t, word], nodes[i][0]))
        of[kind[i]] = i
        parts.setdefault(word, []).append(i)
    seed = [SEED]

    def chance():
        seed[0] = (seed[0] * 1103515245 + 12345) % 2 ** 31
        return seed[0] / 2 ** 31

    def attempt(order, steps, heat):
        now = [run(order) for run in runs]
        total = [max(x[1]) for x in now]
        best, pairs = (sum(total) / len(runs), order), None
        for step in range(steps):
            if pairs is None or chance() < 0.05:
                mix = int(len(runs) * chance())
                (start, end, why), length = now[mix], total[mix]
                key = [0.0] * n
                for r, i in enumerate(order):
                    key[i] = start[i] + 1e-4 * r
                pairs, i = [], end.index(length)
                while why[i] >= 0:
                    if why[i] not in preds[i]:
                        pairs.append((why[i], i))
                    i = why[i]
            new = list(key)
            j, i = pairs[int(len(pairs) * chance())]
            up, far = chance() < 0.5, chance() ** 2
            whole = chance() < 0.08
            if whole:
                first = int(len(CHAIN) * chance())
                some = sorted(x for w in CHAIN[first:first + 1 + int(5 * chance() ** 2)] for x in parts.get("ab"[int(far > 0.25)] + "." + w, ())
                              if (kind[x][0] > 0) == (kind[i][0] > 0))
                when = {}
                for x in (some if up else some[::-1]):
                    if up:
                        new[x] = max([when.get(p, end[p]) + wait for p, wait in hard[x]] + [0.0])
                        when[x] = new[x] + end[x] - start[x]
                    else:
                        new[x] = when[x] = min([when.get(p, start[p]) - wait for p, wait in users[x]] + [length]) - (end[x] - start[x])
            low = min(kind[i][0], kind[j][0])
            for d in () if whole else range(1 - low, VIS) if low and chance() < 0.85 else (0,):
                a, b = of.get((kind[j][0] + d, kind[j][1])), of.get((kind[i][0] + d, kind[i][1]))
                if a is None or b is None or key[a] > key[b]:
                    continue
                if not up:
                    late = min([start[x] - wait for x, wait in users[a]] + [length]) - (end[a] - start[a])
                    new[a] = key[b] + 0.5 + far * max(0.0, late - key[b])
                    continue
                early = max([end[x] + wait for x, wait in hard[b]] + [0.0])
                edge, stack = key[a] - 0.5 - far * max(0.0, key[a] - early), [b]
                while stack:
                    x = stack.pop()
                    new[x] = edge - 0.4 + 1e-7 * key[x]
                    stack.extend(p for p in lists[x] if new[p] > edge and p != a)
            for i in range(n):
                k = new[i]
                for p in lists[i]:
                    if new[p] >= k:
                        k = new[p] + 1e-6
                new[i] = k
            other = sorted(range(n), key=lambda z: new[z])
            room = -len(runs) * heat * (1 - step / steps) * math.log(chance() + 1e-9)
            mine = runs[mix](other)
            if max(mine[1]) - length <= room + 300.0:
                then = [mine if m == mix else run(other) for m, run in enumerate(runs)]
                if sum(max(x[1]) for x in then) - sum(total) <= room:
                    order, now, total, pairs = other, then, [max(x[1]) for x in then], None
                    best = min(best, (sum(total) / len(runs), order))
        return best

    best = (1e18, given)
    for _ in range(TURNS):
        best = min(best, attempt(attempt(given, STEPS, HEAT)[1], MORE, HEAT / 3))
        again = first_placing([nodes[i] for i in best[1]], {r: moving[i] for r, i in enumerate(best[1]) if i in moving})
        given = [best[1][r] for r in again]
    return best


def rank_program(g, core, T, topo):
    rank = T.rank_of(core)
    if rank is None:
        return
    nrank = len(T.cores)
    nxt = T.cores[(rank + 1) % nrank]
    V, S, PE, SY = g.vector, g.scalar, g.tensor, g.sync
    queue = {"v": V, "s": S, "pe": PE, "gp": g, "sy": SY}
    total = {}
    know = {q: {} for q in queue}
    wrote, seen = {}, {}

    def need(q, tok):
        sem, val, past, _ = tok
        if know[q].get(sem, 0) < val:
            queue[q].wait_ge(T.sem[sem], val)
            for s2, v2 in past.items():
                if know[q].get(s2, 0) < v2:
                    know[q][s2] = v2
            know[q][sem] = val

    def sync_for(q, reads, writes, banks):
        toks = []
        for r in reads:
            toks.append(wrote[r])
        for w in writes:
            if w in wrote and not (q == "pe" and wrote[w][3] == q):
                toks.append(wrote[w])
            for tok in seen.get(w, {}).values():
                if tok[3] != q or q == "sy":
                    toks.append(tok)
        for b in banks:
            for q2, tok in seen.get(b, {}).items():
                if q2 != q:
                    toks.append(tok)
        toks.sort(key=lambda z: -z[1])
        for tok in toks:
            need(q, tok)

    def note(q, tok, reads, writes, banks):
        for w in writes:
            wrote[w] = tok
            seen[w] = {}
        for r in reads:
            seen.setdefault(r, {})[tok[0]] = tok
        for b in banks:
            seen.setdefault(b, {})[q] = tok

    nodes = []
    label, now = [], [(0, "")]

    def op(q, call, reads, writes, banks=(), cost=100.0):
        def emit():
            sync_for(q, reads, writes, banks)
            total[q] = total.get(q, 0) + 1
            call().then_inc(T.sem[q], 1)
            note(q, (q, total[q], dict(know[q]), q), reads, writes, banks)
        nodes.append((q, emit, list(reads), list(writes), list(banks), cost))

    moving = {}

    def dmas(q, calls, sem, reads, writes, kib=64):
        def emit():
            sync_for(q, reads, writes, ())
            for call in calls:
                total[sem] = total.get(sem, 0) + 16
                call().then_inc(T.sem[sem], 16)
            note(q, (sem, total[sem], dict(know[q]), "dma"), reads, writes, ())
        moving[len(nodes)] = (960.0, 20.0 * len(calls) + DMA * kib, 600.0)
        nodes.append((q, emit, list(reads), list(writes), [], 60.0 * len(calls)))

    def span(ap):
        return math.prod(ap.shape[1:])

    def vcost(n, kind, wide):
        return {"": max(64, n * wide) * CYCLE, "h": max(64, n / 2) * CYCLE, "g": 55 + 1j * n * GATHER * CYCLE, "s": 55 + 1j * n * SCATTER * CYCLE}[kind]

    def mm(out, lhsT, rhs, reads, bank, start=True, stop=True, tag=None, join=None, most=JOIN):
        call = lambda: PE.matmul(out, lhsT, rhs, start, stop)
        cost = max(min(64, span(lhsT)), span(rhs)) * PECYCLE * (4 if "float32" in str(lhsT.dtype) else 1)
        tags = tag if isinstance(tag, list) else [tag]
        if ((not start) if join is None else join) and len(run[-1]) < most:
            q, _, before, writes, banks, so_far = nodes.pop()
            calls = run.pop() + [call]
            reads, cost = before + [x for x in reads if x not in before], so_far + cost
        else:
            calls = [call]
        run.append(calls)
        op("pe", lambda: [c() for c in calls][-1], reads, tags, [bank], cost)

    run = []

    def tt(out, a, b, o, reads, writes, banks=(), kind=""):
        op("v", lambda: V.tensor_tensor(out, a, b, o), reads, writes, banks, vcost(span(out), kind, 1 if banks else 2))

    def ts(out, a, s1, o1, reads, writes, banks=(), s2=None, o2=None, kind=""):
        cost = vcost(span(out), kind, 1)
        if o2 is None:
            op("v", lambda: V.tensor_scalar(out, a, s1, None, o1), reads, writes, banks, cost)
        else:
            op("v", lambda: V.tensor_scalar(out, a, s1, s2, o1, o2), reads, writes, banks, cost)

    def cp(out, a, reads, writes, banks=(), kind=""):
        op("v", lambda: V.tensor_copy(out, a), reads, writes, banks, vcost(span(a if kind == "s" else out), kind, 1))

    def scan(out, a, b, first, o0, o1, reads, writes, banks=(), kind=""):
        op("v", lambda: V.tensor_tensor_scan(out, a, b, first, o0, o1), reads, writes, banks, vcost(span(out), kind, 1))

    def fill(out, value, name):
        op("v", lambda: V.memset(out, value), [], [name], (), vcost(span(out), "h", 1))

    def act(out, a, f, reads, writes, banks=(), kind="", **more):
        op("s", lambda: S.activation(out, a, f, **more), reads, writes, banks, vcost(span(out), kind, 1) + 30.0)

    def copy(who, out, a, reads, writes, banks=(), kind=""):
        if who == "s":
            act(out, a, AF.Copy, reads, writes, banks, kind)
        else:
            cp(out, a, reads, writes, banks, kind)

    def plus(who, out, a, value, reads, writes):
        if who == "s":
            act(out, a, AF.Copy, reads, writes, bias=value)
        else:
            ts(out, a, value, OP.add, reads, writes)

    def line(who, out, a, scale, bias, reads, writes, banks=()):
        if who == "s":
            act(out, a, AF.Copy, reads, writes, banks, scale=scale, bias=bias)
        else:
            ts(out, a, scale, OP.mult, reads, writes, banks, bias, OP.add)

    def together(k):
        some = [nodes.pop() for _ in range(k)][::-1]
        both = lambda z: list(dict.fromkeys(x for node in some for x in node[z]))
        nodes.append((some[0][0], lambda: [node[1]() for node in some], both(2), both(3), both(4), sum(node[5] for node in some)))

    dmas("sy", [lambda: SY.dma_start(T.wdi[:], T.wd[:])], "ldw", [], ["wdi"], 128)
    dmas("s", [lambda: S.dma_start(T.wti[:, 0:1], T.wt[:])], "ldt", [], ["wti"], 1)
    dmas("sy", [lambda: SY.dma_start(T.xs[:, 2048:6144], T.x[:])], "ldx", [], ["x_lo", "x_hi"], 1024)
    dmas("sy", [lambda: SY.dma_start(T.rts[:, 712:2048], T.rt[:, 0:1336]), lambda: SY.dma_start(T.rts[:, 0:712], T.rt[:, 1336:2048])],
         "ldr", [], ["rts"], 1024)
    dmas("sy", [lambda: SY.dma_start(T.thi[:, 0:1], T.th[:])], "ldh", [], ["thi"], 1)

    def col(n):
        return T.cols[:, n:n + 1]

    def sel(out, in_, pattern, cmp, fill_, base, cm, reads, writes):
        op("gp", lambda: g.affine_select(out, in_, pattern, cmp, fill_, base, cm), reads, writes, (), 170.0 + 2 * span(out) * CYCLE)

    def iota(out, pattern, name):
        op("gp", lambda: g.iota(out, pattern, 0, 0, allow_small_or_imprecise_dtypes=True), [], [name], (), 130.0 + 2 * span(out) * CYCLE)

    one, blk, s1, idn = T.ones[:, 0:128], T.blk[:, 0:128], T.blk[:, 0:128:16], T.id2[:, 0:128]
    UP, DOWN = [[0, 2], [-16, 8], [1, 16]], [[0, 2], [16, 8], [1, 16]]

    def times(out, in_, by, reads, writes):
        act(out, in_, AF.Copy, reads, writes, scale=by)

    def join(out, terms, reads, name):
        o = T.ps6[:, 0:span(out)]
        for n, (sign, tile) in enumerate(terms):
            mm(o, idn if sign > 0 else T.ni[:], tile, reads + ["idn", "ni"], "ps6", n == 0, n == len(terms) - 1, "ps6d")
        act(out, o, AF.Copy, ["ps6d"], [name], ["ps6"])

    def constants_1():
        fill(T.ones[:], 1.0, "ones")
        op("gp", lambda: g.iota(T.pi[:], [[0, 2]], 0, 1), [], ["pi"])
        sel(T.blk0[:], T.ones[:], [[0, 2], [-16, 8], [0, 16]], OP.is_ge, 0.0, 0, 1, ["ones"], ["blk0"])
        sel(T.blk[:], T.blk0[:], [[0, 2], [16, 8], [0, 16]], OP.is_ge, 0.0, 15, -1, ["blk0"], ["blk"])
        sel(T.id2[:], T.blk[:], DOWN, OP.is_equal, 0.0, 0, -1, ["blk"], ["idn"])
        times(T.ni[:], idn, -1.0, ["idn"], ["ni"])
        fill(T.zerf[:], 0.0, "zerf")
        fill(T.b0[:], 0.0, "b0")
        for c in range(NC):
            fill(T["zs%d" % c][:], 0.0, "zs_%d" % c)
            fill(T["ys%d" % c][:], 0.0, "y_%d" % c)
        fill(col(10), 2048.0, "thr")
        fill(col(19), -2048.0 * 32768, "thr2")
        ts(T.pj[:], T.pi[:], 15, OP.bitwise_and, ["pi"], ["pj"])
        cp(col(0), T.pj[:, 0:1], ["pj"], ["k0"])
        iota(T.kt[:], [[0, 8], [1, 16]], "kt")
        ts(T.keep[:], T.kt[:], col(0), OP.is_le, ["kt", "k0"], ["kp0"], kind="h")
        sel(T.keep[:], T.keep[:], [[0, 8], [1, 16]], OP.not_equal, 0.0, 0, 0, ["kp0"], ["keep"])
        cp(T.b0[:, 15:143:16], s1, ["blk"], ["b0"])
        ts(col(13), col(0), 0.0, OP.is_equal, ["k0"], ["q0"])
        times(T.z0[:], T.b0[:], col(13), ["b0", "q0"], ["z0"])
        cp(col(1), T.wti[:, 0:1], ["wti"], ["w1"])
        ts(col(2), col(1), 2048.0, OP.is_ge, ["w1"], ["w2"], (), -4096.0, OP.mult)
        tt(col(3), col(1), col(2), OP.add, ["w1", "w2"], ["w3"])
        times(T.wb[:], blk, col(3), ["blk", "w3"], ["wb"])
        iota(T.dg[:], [[0, 8], [1, 19]], "dg")
        ts(T.dg[:], T.dg[:], col(0), OP.not_equal, ["dg", "k0"], ["dg"], (), -2.0 ** 25, OP.mult, kind="h")
        ts(T.dg[:], T.dg[:], 592.0, OP.add, ["dg"], ["dg"], kind="h")
        fill(T.rd[:], 0.0, "rd")
        for n, step in [(0, -2.0 ** 27), (16, -2639.5), (17, BIG), (18, -BIG)]:
            fill(T.rd[:, n:152:19], step, "rd")
        ts(T.md[:], T.kt[:], col(0), OP.is_equal, ["kt", "k0"], ["md"])
        times(T.k2[0:1, :], T.ones[0:1, 0:128], 128.0, ["ones"], ["k2"])
        ts(T.oneh[0:1, 0:128], T.ones[0:1, 0:128], 2080.0 / 128, OP.mult, ["ones"], ["oneh"], kind="h")
        ts(T.oneh[0:1, 128:256], T.ones[0:1, 0:128], 512.0, OP.mult, ["ones"], ["oneh2"], kind="h")
        fill(T.rs[:], 0.0, "rs")
        for n, step in [(0, 2.0 ** 20), (16, WHOLE), (17, -WHOLE)]:
            fill(T.rs[:, n:144:18], step, "rs")
        iota(T.itg[:], [[16, 16]], "itg")
        iota(T.ktk[0:1, :], [[0, 8], [1, 18]], "ktk")
        ts(T.ktk[0:1, :], T.ktk[0:1, :], 7.5, OP.add, ["ktk"], ["ktk"], (), 1.0 / 16, OP.mult, kind="h")
        fill(T.ktk[0:1, 16:144:18], 2.0 ** 40, "ktk")
        fill(T.ktk[0:1, 17:144:18], 2.0 ** 40, "ktk")
        fill(T.b18[:, 0:144], -1.0, "b18")
        sel(T.b18[:, 144:288], T.b18[:, 0:144], [[-16, 8], [0, 18]], OP.is_ge, 0.0, 0, 1, ["b18"], ["b18a"])
        sel(T.b18[:, 0:144], T.b18[:, 144:288], [[16, 8], [0, 18]], OP.is_ge, 0.0, 15, -1, ["b18a"], ["b18"])
        times(T.s2[:], s1, 2.0, ["blk"], ["s2"])
        times(T.sn[:], s1, -1.0, ["blk"], ["sn"])
        for c in range(NC):
            if MJ[c]:
                sel(T["sx%d" % c][:], T.b18[:, 0:144], [[0, 8], [-1, 18]], OP.is_gt, 0.0, MJ[c], 0, ["b18"], ["sx_%d" % c])
        fill(T.cl[:], 0.0, "cl")
        for n, base in enumerate([960.0, 960.0 / LOTS, 7.5, 7.5]):
            fill(T.row[0:1, 8 * n:8 * n + 8], base, "row%d" % n)
        together(4)
        for n, scale in enumerate([2048.0, -2048.0 / LOTS, 16.0, 16.0]):
            times(T.rl[:, 8 * n:8 * n + 8], s1, scale, ["blk"], ["rl%d" % n])
        together(4)
        times(T.rn[:], T.rl[:], -1.0, ["rl%d" % n for n in range(4)], ["rn"])
        ts(T.cl[:, 0:8], T.itg[:, 0:8], col(0), OP.add, ["itg", "k0", "cl"], ["cl"])
        for n in range(0, 8, 8 // LOTS):
            ts(T.cl[:, 8 + n:8 + n + 8 // LOTS], T.itg[:, 0:8 // LOTS], col(0), OP.add, ["itg", "k0", "cl"], ["cl"])
        ts(T.cl[:, 24:32], T.itg[:, 0:8], col(0), OP.add, ["itg", "k0", "cl"], ["cl"], (), 16.0, OP.mult)

    def rows():
        for n, by in enumerate([-1.0, 2048.0, -2048.0]):
            times(T.bm[:, 128 * n:128 * n + 128], blk, by, ["blk"], ["bm"])

    def constants_2():
        sel(T.e8[:], one, [[-16, 8], [0, 16]], OP.is_equal, 0.0, -8, 1, ["ones"], ["e8"])
        sel(T.an[:], one, [[-16, 8], [1, 16]], OP.is_equal, 0.0, -15, 1, ["ones"], ["an"])
        sel(T.m3[:], one, [[-16, 8], [1, 8], [0, 2]], OP.is_equal, 0.0, -15, 1, ["ones"], ["m3"])
        sel(T.pc[:], blk, DOWN[1:], OP.is_equal, 0.0, -1, -1, ["blk"], ["pc"])
        sel(T.pd[:], blk, DOWN[1:], OP.is_equal, 0.0, 15, -1, ["blk"], ["pd"])
        times(T.ann[:], T.an[:], -1.0, ["an"], ["ann"])
        times(T.mt[:], T.m3[:], -OFF, ["m3"], ["mt"])
        fill(T.cr0[0:2, :], OFF - 2048, "cr0")
        sel(T.cr0[0:2, 0:128], T.cr0[0:2, 0:128], [[0, 128]], OP.is_equal, -1.0, 0, 1, ["cr0"], ["cr1"])
        sel(T.cr0[0:2, 128:256], T.cr0[0:2, 128:256], [[0, 128]], OP.is_equal, 0.0, 0, 1, ["cr0"], ["cr2"])
        times(T.n16[:], idn, -16.0, ["idn"], ["n16"])
        ts(T.base[:, 0:8], T.ones[:, 0:8], 16 * 2048.0, OP.mult, ["ones"], ["base0"])
        for n in range(0, 8, 8 // LOTS):
            ts(T.base[:, 8 + n:8 + n + 8 // LOTS], T.itg[:, 0:8 // LOTS], col(0), OP.add, ["itg", "k0"], ["base1"], (), 128.0 / LOTS + 256 * n, OP.add)
        ts(T.ata[:], T.itg[:, 0:8], col(0), OP.add, ["itg", "k0"], ["ata"], (), 1153.0, OP.add)
        ts(T.base[:, 16:24], T.ata[:], 16.0, OP.mult, ["ata"], ["base2"])
        fill(T.bk[:], 0.0, "bk")
        times(T.bk[:, 15:143:16], T.bj[:, 128:256:16], 2048.0, ["bjt", "bk"], ["bk"])
        fill(T.sj[:], 0.0, "sj")
        for z, by in enumerate([1.0, 2.0, -1.0]):
            times(T.sj[:, 64 * z + 24:64 * z + 32], s1, by, ["blk", "sj"], ["sj"])
        ts(col(5), col(0), 8.0, OP.is_equal, ["k0"], ["q8"])
        ts(col(6), col(0), 9.0, OP.is_ge, ["k0"], ["q9"], (), 1.0, OP.add)
        ts(col(7), col(5), -8.0, OP.mult, ["q8"], ["q7"])
        tt(col(9), col(6), col(7), OP.add, ["q9", "q7"], ["qc"])
        ts(col(14), col(0), 15.0, OP.is_lt, ["k0"], ["qd"], (), 128.0 / LOTS, OP.mult)
        tt(col(11), col(9), col(14), OP.mult, ["qc", "qd"], ["c0"])
        ts(col(12), col(5), 2048.0, OP.mult, ["q8"], ["c8"])
        cp(T.g8[:, 0:1], col(5), ["q8"], ["g8"])
        join(T.m1a[:], [(1, T.e8[:]), (-1, idn)], ["e8"], "m1a")
        join(T.m2b[:], [(1, T.an[:]), (-1, T.e8[:])], ["an", "e8"], "m2a")
        sel(T.m2b[:], T.m2b[:], [[0, 8], [-1, 16]], OP.is_ge, 0.0, 7, 0, ["m2a"], ["m2b"])
        times(T.mo[:], T.m2b[:], OFF, ["m2b"], ["mo"])
        ts(col(20), col(0), 0.5, OP.is_gt, ["k0"], ["q20"])
        ts(col(21), col(0), 9.5, OP.is_lt, ["k0", "q20"], ["q21"], (), col(20), OP.mult)
        times(T.cw[:], T.id2[:], col(21), ["idn", "q21"], ["cw"])
        times(T.ct[:], T.id2[:], col(13), ["idn", "q0"], ["ct"])
        ts(col(15), col(0), 15.0, OP.is_equal, ["k0"], ["q15"])
        times(T.cc[:], T.id2[:], col(15), ["idn", "q15"], ["cc"])
        times(T.cn[:], T.cc[:], -1.0, ["cc"], ["cn"])
        ts(col(22), col(21), -2048.0, OP.mult, ["q21"], ["q22"], (), -OFF, OP.add)
        ts(col(23), col(0), 1.0, OP.is_equal, ["k0"], ["q23"], (), OFF, OP.mult)
        tt(T.g8[:, 2:3], col(22), col(23), OP.add, ["q22", "q23"], ["g82"])
        cp(T.g8[:, 3:4], col(15), ["q15"], ["g83"])
        mm(T.ps7[0:2, 0:128], T.g8[:, 2:4], idn, ["g82", "g83", "idn"], "ps7", True, True, "ps7d")
        act(T.q1[0:2, :], T.ps7[0:2, 0:128], AF.Copy, ["ps7d"], ["q1"], ["ps7"])
        sel(T.pa[:, 0:128], blk, DOWN[1:], OP.is_equal, 0.0, -2, -1, ["blk"], ["pa"])
        join(T.pb[:, 0:128], [(1, T.pa[:, 0:128]), (-1, T.pc[:])], ["pa", "pc"], "pb")
        sel(T.pa[:, 128:256], T.pb[:, 0:128], [[0, 8], [-1, 16]], OP.is_ge, 0.0, 9, 0, ["pb"], ["pa2", "pa"])
        sel(T.pb[:, 128:256], T.m1a[:], [[0, 8], [1, 16]], OP.is_equal, 0.0, -15, 0, ["m1a"], ["pb2", "pb"])
        join(T.mc[:, 0:128], [(1, T.pa[:, 128:256]), (1, T.pb[:, 128:256]), (1, T.pd[:])], ["pa2", "pb2", "pd"], "mc0")
        times(T.mc[:, 128:256], T.mc[:, 0:128], OFF, ["mc0"], ["mc1"])
        times(T.mc[:, 0:128], T.mc[:, 0:128], OFF, ["mc0"], ["mc", "mc0"])

    def window(sem, src, cols, by, dram, win, start, read, name):
        pieces = [(by, 8, 0), (0, by, 128 - 16 * by)][:2 if by else 1]
        lots = len(dram)
        wide = (cols.stop - cols.start) // lots
        dmas("sy", [(lambda a, b, p, h, d, c0: lambda: SY.dma_start(d[a:b, h:h + 16, :], src[p:p + 16 * (b - a), c0:c0 + wide]))(a, b, p, h, d, cols.start + n * wide)
                    for n, d in enumerate(dram) for h in (0, 16) for a, b, p in pieces], sem % 0, [read], [name + "d"], lots * wide)
        for n, d in enumerate(dram):
            dmas("sy", [(lambda k, d, n: lambda: SY.dma_start(win[k:128:16, 16 * wide * n:16 * wide * (n + 1)], d[:, start(k):start(k) + 16, :]))(k, d, n)
                        for k in range(16)], sem % (n + 1), [name + "d"], [name + str(n)], 8 * wide)

    def limits():
        ts(T.two[:, 0:16], T.kt[:, 0:16], col(0), OP.add, ["kt", "k0"], ["two0"], (), 15.0, OP.is_lt)
        ts(T.two[:, 16:32], T.two[:, 0:16], 1.0, OP.add, ["two0"], ["two1"])
        scan(T.two[:, 32:48], T.two[:, 16:32], T.zerf[:, 0:16], 1.0, OP.mult, OP.add, ["two1", "zerf"], ["two"])
        fill(T.tx[:], 0.0, "tx")
        ts(T.tx[:, 0:1], T.thi[:, 0:1], -1.0, OP.mult, ["thi", "tx"], ["tx"], (), 2048.0, OP.add)
        cp(T.tx[:, 1:2], T.two[:, 47:48], ["two", "tx"], ["tx"])
        ts(T.tx[:, 2:3], col(0), 9.0, OP.is_ge, ["k0", "tx"], ["tx"], (), 8192.0, OP.mult)
        window("dx%d", T.tx, slice(0, 8), 0, [T.dx], T.tw, lambda m: 15 - m, "tx", "tw")
        ts(col(17), col(0), 8.0, OP.is_ge, ["k0"], ["k8"], (), 8.0, OP.mult)
        sel(T.bj[:, 128:256], one, [[0, 16], [-16, 8]], OP.is_ge, 0.0, 0, 1, ["ones"], ["bjt"])
        sel(T.bj[:, 0:128], T.bj[:, 128:256], [[0, 16], [16, 8]], OP.is_ge, 0.0, 15, -1, ["bjt"], ["bj"])
        mm(T.ps7[:, 0:128], T.bj[:, 0:128], idn, ["bj", "idn"], "ps7", True, True, "ps7d")
        act(T.bj[:, 128:256], T.ps7[:, 0:128], AF.Copy, ["ps7d"], ["bjt"], ["ps7"])
        for n, out in enumerate([T.cth, T.cw2, T.cw3]):
            ts(T.tl[:, 8 * n:8 * n + 8], T.itg[:, 0:8], col(17), OP.add, ["itg", "k8"], ["tl%d" % n], (), float(n), OP.add)
            tt(out[:], T.tw[:].indirect(T.tl[:, 8 * n:8 * n + 8]), T.bj[:, 0:128], OP.mult, ["tw0", "tl%d" % n, "bj"], ["circ%d" % n], kind="g")

    XR = ["x_lo", "x_hi"]

    def stages(t, c):
        X, Y, Z = ["ps%d" % (3 * c + b) for b in range(3)]
        PX, PY, PZ = T[X], T[Y], T[Z]
        r = lambda name: "%s_%d" % (name, c)
        xr, mx, df = T["xr%d" % c], T["mx%d" % c], T["df%d" % c]
        part = lambda name, n, w=128: T["%s%d" % (name, c)][:, w * n:w * n + w]
        TI, TF, TB, HH = [(lambda name: lambda n: part(name, n))(name) for name in ("ti", "tf", "tb", "hh")]
        UI, UF, UH, LS = [(lambda name: lambda n: part(name, n, 8))(name) for name in ("ui", "uf", "uh", "ls")]
        lu, hh, tb, tf, uf = [T["%s%d" % (name, c)] for name in ("lu", "hh", "tb", "tf", "uf")]
        w0, l0 = CW * (NC * t + c), 8 * (NC * t + c)
        wres, lres, made = "wl%d_%d" % (t, c), "ll%d_%d" % (t, c), r("lo%d" % t)
        LO = lambda lo, hi: T.lo[:, 3 * l0 + 8 * lo:3 * l0 + 8 * hi]
        last = t == VIS - 1
        x0 = TB(7)
        blocks = lambda name, lo, hi: [r("%s%d" % (name, b)) for b in range(lo // 128, hi // 128)]
        sized = lambda js, hs=(0, 1): [r("mx%d.%d" % (j, h)) for j in js for h in hs]
        XRS = blocks("xr", 0, 2048)
        x = T.xs[:, 2048:6144]

        step = lambda u: (u + u // nrank) - (u - 1 + (u - 1) // nrank) if u else 0
        onward = lambda d: slice(128 - 16 * d, 256 - 16 * d)
        moved = onward(step(t + 1))
        zs, ys = T["zs%d" % c], T["ys%d" % c]
        GAPS = [r("d2.%d" % n) for n in range(4)]
        WW = [r("ww") + str(n) for n in range(LOTS)]

        def send(out, src, name, sem, lands, extra):
            rid, pid, _ = topo.addr(nxt)

            def emit():
                sync_for("gp", [name], [], ())
                g.remote_dma(out, src, T.sem[sem], T.sem.sent, pid, rid, topo.mask(core, nxt))
                total["sent"] = total.get("sent", 0) + len(topo.engines(core, nxt))
                total[sem] = len(topo.engines(T.cores[(rank - 1) % nrank], core))
                wrote[lands] = (sem, total[sem], {}, "net")
            moving[len(nodes)] = (750.0 * NET, extra * NET, (900.0 + extra) * NET)
            nodes.append(("gp", emit, [name], [lands], [], 1000.0 * NET))

        def start():
            ts(HH(3), T.wdi[:, CW * c:CW * c + CW], -2048.0, OP.add, ["wdi"], [r("h3")])
            for m in range(16):
                mm(PX[:, 48:56], T.z0[:, 15 - m:143 - m], hh[:, 384 + m:512:16], ["z0", r("h3")], X, m == 0, m == 15, r("w0p"))
            ts(T.ll[:, l0:l0 + 8], PX[:, 48:56], 2048.0, OP.add, [r("w0p")], [lres], [X])
            cp(T.wl[:, w0:w0 + 128], T.wdi[:, CW * c:CW * c + CW], ["wdi"], [wres])

        def first():
            copy(FIRST[c], x0, x.indirect(T.ll[:, l0:l0 + 8]), XR + [lres], [r("x0")], kind="g")

        def lead():
            B = {"X": X, "Z": Z}[LEAD[c]]
            o = T[B][:, 384:512]
            mm(o, T.q1[0:2, :], T.ones[0:2, 0:128], ["q1", "ones"], B, True, False, r("cp"))
            mm(o, T.cw[:, onward(step(t) + step(t + 1))], T.wl[:, w0:w0 + 128], ["cw", wres], B, False, False, r("cp"))
            mm(o, T.cn[:, moved], HH(0), ["cn", r("q")], B, False, False, r("cp"), False)
            mm(o, T.cc[:, moved], HH(1), ["cc", r("ev")], B, False, False, r("cp"), False)
            mm(o, T.ct[:, moved], HH(4), ["ct", r("tl")], B, False, False, r("cp"), False)
            mm(o, T.mc[:, moved], TB(6), ["mc", "mc1", r("P")], B, False, True, r("cp"), False)
            ts(HH(5), o, -2048.0, OP.max, [r("cp")], [r("h5")], [B])

        def lists():
            lo, hi = (1 if last else 0), (2 if FAST[c] == "f" else 3)
            for n, (by, name) in enumerate([(11, "c0"), (12, "c8")][:hi - 1]):
                if STEPS_BY[c] == "s":
                    times(HH(6 + n), TB(6), col(by), [r("P"), name], [r("h%d" % (6 + n))])
                else:
                    ts(HH(6 + n), TB(6), col(by), OP.mult, [r("P"), name], [r("h%d" % (6 + n))], kind="h")
            o = PY[:, 400 + 8 * lo:400 + 8 * hi]
            mm(o, idn, T.base[:, 8 * lo:8 * hi], ["idn", "base0", "base1", "base2"], Y, True, False, r("x0p"))
            if hi == 3:
                mm(PY[:, 416:424], idn, ys[:, 0:128:16], ["idn", r("y")], Y, False, False, r("x0p"))
                mm(PY[:, 416:424], T.n16[:], UH(2), ["n16", r("uq")], Y, False, False, r("x0p"))
            for m in range(16):
                mm(o, T.b0[:, 15 - m:143 - m], hh[:, 640 + 128 * lo + m:640 + 128 * hi:16], ["b0"] + [r("h%d" % (5 + n)) for n in range(lo, hi)],
                   Y, False, m == 15, r("x0p"), m > 0)
            cp(LO(lo, hi), o, [r("x0p")], [made], [Y])
            if not last:
                send(T.ll[:, l0 + 8 * NC:l0 + 8 * NC + 8], LO(0, 1), made, "al%d_%d" % (t + 1, c), "ll%d_%d" % (t + 1, c), 20.0)

        def wwin():
            window("dw%d" + str(c), T.wl, slice(w0, w0 + 128), step(t), [T["dw%d%d" % (c, n)] for n in range(LOTS)], T["ww%d" % c], lambda k: k, wres, r("ww"))

        def pwin():
            if PACK and c == 0:
                return
            window("dp%d" + str(c), T["pk%d" % c], slice(0, 128), 0, [T["dp%d" % c]], T["pw%d" % c], lambda k: k + 1, r("pk"), r("pw"))

        def weigh():
            mm(PX[:, 96:248], idn, T.dg[:], ["idn", "dg"], X, True, False, r("key"))
            for h in range(8):
                mm(PX[:, 96 + 19 * h:112 + 19 * h], T.wb[:], tb[:, 896 + 16 * h:912 + 16 * h], ["wb", r("x0")], X, False, h == 7, r("key"), h > 0, 8)
            if MJ[c]:
                mm(PY[:, 384:512], idn, x0, ["idn", r("x0")], Y, True, True, r("x0p"))

        def relator():
            scan(tf[:, 1024:1176], T.rd[:], PX[:, 96:248], 0.0, OP.add, OP.max, ["rd", r("key")], [r("f1")], [X])
            tt(UF(6), tf[:, 1024 + 15:1176:19], tf[:, 1024 + 18:1176:19], OP.subtract, [r("f1")], [r("u1")])
            tt(UI(2), UF(6), UF(6), OP.mult, [r("u1")], [r("u2")])
            ts(UI(3), UI(2), 5, OP.arith_shift_right, [r("u2")], [r("u3")], (), 2047, OP.bitwise_and)
            cp(LS(1), UI(3), [r("u3")], [r("cl")])
            copy(PICK[c], lu[:, 0:128], T.rts[:].indirect(LS(1)), ["rts", r("cl")], [r("lr")], kind="g")

        def spread():
            plus(SPREAD[c], ys[:, 0:128:16], UF(6), -2640.0, [r("u1")], [r("y")])
            line(SPREAD[c], UH(2), UF(6), 1.0 / 16, 1025.0 - 37 - 15.0 / 32, [r("u1")], [r("uq")])
            together(2)
            scan(ys[:, 144:272], T.keep[:], ys[:, 0:128], 0.0, OP.mult, OP.add, ["keep", r("y")], [r("yk")], kind="h")
            both = [r("k1"), r("k2")]
            mm(PZ[:, 0:256], T.k2[0:1, :], T.oneh[0:1, :], ["k2", "oneh", "oneh2"], Z, True, False, both)
            for n, (up, down) in enumerate([(blk, T.bm[:, 0:128]), (T.bm[:, 128:256], T.bm[:, 256:384])]):
                o = PZ[:, 128 * n:128 * n + 128]
                mm(o, up, ys[:, 1:129], ["blk", "bm", r("y"), r("yk")], Z, False, False, both, False)
                mm(o, up, ys[:, 144:272], ["blk", "bm", r("yk")], Z, False, False, both)
                mm(o, down, ys[:, 145:273], ["bm", r("yk")], Z, False, n == 1, both)

        def gather_r(n):
            lo, hi = 512 * n, 512 * n + 512
            copy((GR if t else GR0)[c][n], xr[:, lo:hi], x.indirect(lu[:, lo // 16:hi // 16]), XR + [r("lr")], blocks("xr", lo, hi), kind="g")

        def letters():
            if not PACK:
                plus(LETTERS[c], T["pk%d" % c][:], lu[:, 0:128], -2048.0, [r("lr")], [r("pk")])
            elif c == 0:
                copy(LETTERS[c], T.pk0[:], lu[:, 0:128], [r("lr")], [r("pk")])
            else:
                act(PZ[:, 384:512], lu[:, 0:128], AF.Copy, [r("lr")], [r("up")], [Z], scale=4096.0)
                tt(T.pk1[:], T.pk0[:], PZ[:, 384:512], OP.add, ["pk_0", r("up")], [r("pk")], [Z])

        def tail():
            tt(TF(6), HH(0), PZ[:, 0:128], OP.mult, [r("q"), r("k1")], [r("f6")], [Z])
            tt(TI(0), TF(6), PZ[:, 128:256], OP.add, [r("f6"), r("k2")], [r("t0")], [Z])
            ts(TI(1), TI(0), 5, OP.arith_shift_right, [r("t0")], [r("t1")], (), 4095, OP.bitwise_and)
            plus(TAIL[c], HH(4), TI(1), -2048.0, [r("t1")], [r("tl")])

        def other():
            ts(TF(3), HH(0), -0.5, OP.add, [r("q")], [r("t3")], (), EVEN, OP.add)
            if OTHER[c] == "s":
                act(HH(1), TF(3), AF.Copy, [r("t3")], [r("ev")], scale=2.0, bias=-2 * EVEN)
            else:
                ts(HH(1), TF(3), -EVEN, OP.add, [r("t3")], [r("ev")], (), 2.0, OP.mult)

        mj = MJ[c]
        spare = [("ps6", "ps6d"), ("ps7", "ps7d")]

        def biggest(h):
            for j in range(mj):
                tt(mx[:, j, 64 * h:64 * h + 64], xr[:, 1024 * h + j:1024 * h + 1024:16], PY[:, 384 + 64 * h:448 + 64 * h], OP.max,
                   XRS[8 * h:8 * h + 8] + [r("x0p")], sized([j], [h]), [Y])
                if j in (mj // 2 - 1, mj - 1):
                    together(mj // 2)

        def apart(h):
            for j0 in range(mj, 16, 8):
                D, tag = spare[(h + (j0 - mj) // 8) % 2]
                js = range(j0, min(j0 + 8, 16))
                for j in js:
                    o = T[D][:, 64 * (j - j0):64 * (j - j0) + 64]
                    mm(o, idn, xr[:, 1024 * h + j:1024 * h + 1024:16], ["idn"] + XRS[8 * h:8 * h + 8], D, True, False, tag, j > j0)
                    mm(o, T.ni[:], tb[:, 896 + 64 * h:960 + 64 * h], ["ni", r("x0")], D, False, True, tag)
                act(mx[:, j0:js[-1] + 1, 64 * h:64 * h + 64], T[D][:, 0:64 * len(js)], AF.Abs, [tag], sized(js, [h]), [D])

        def keys():
            mm(PX[:, 96:240], T.ones[0:1, 0:128], T.ktk[0:1, :], ["ones", "ktk"], X, True, False, r("key"))
            if mj:
                mm(PX[:, 96:240], x0, T["sx%d" % c][:], [r("x0"), r("sx")], X, False, False, r("key"))
            for j in range(mj):
                mm(PX[:, 96 + j:240:18], xr[:, j:2048:16], T.sn[:], XRS + ["sn"], X, False, False, r("key"), j > 0)
            for j in range(16):
                mm(PX[:, 96 + j:240:18], mx[:, j, :], T.s2[:] if j < mj else s1, sized([j]) + ["s2", "blk"], X, False, j == 15,
                   r("key"), j % 4 != mj % 4 and j > 0)

        def least():
            scan(tf[:, 1024:1168], T.rs[:], PX[:, 96:240], 0.0, OP.add, OP.min, ["rs", r("key")], [r("f1")], [X])
            tt(zs[:, 0:128:16], tf[:, 1024 + 15:1168:18], tf[:, 1024 + 17:1168:18], OP.subtract, [r("f1")], [r("zs")])
            scan(zs[:, 144:272], T.keep[:], zs[:, 0:128], 0.0, OP.mult, OP.add, ["keep", r("zs")], [r("sk")], kind="h")
            o, rl = PX[:, 56:88], ["rl%d" % n for n in range(4)]
            mm(o, T.ones[0:1, 0:128], T.row[0:1, :], ["ones"] + ["row%d" % n for n in range(4)], X, True, False, r("slp"))
            mm(o, idn, T.cl[:], ["idn", "cl"], X, False, False, r("slp"))
            mm(o, zs[:, 1:129], T.rl[:], [r("zs")] + rl, X, False, False, r("slp"), False)
            mm(o, zs[:, 144:272], T.rl[:], [r("sk")] + rl, X, False, False, r("slp"), False)
            mm(o, zs[:, 145:273], T.rn[:], [r("sk"), "rn"], X, False, True, r("slp"))
            cp(T["ls%d" % c][:, 16:48], o, [r("slp")], [r("sl")], [X])

        def turn():
            for n in range(LOTS):
                a, b = n * 128 // LOTS, (n + 1) * 128 // LOTS
                copy(TURN[c], lu[:, 128 + a:128 + b], T["ww%d" % c][:, 16 * a:16 * b].indirect(T["ls%d" % c][:, 24 + a // 16:24 + b // 16]),
                   [r("ww") + str(n), r("sl")], [r("lw%d" % h) for h in range(a // 64, b // 64)], kind="g")

        def limit():
            copy(LIMIT[c], TB(2), T.md[:, 0:16].indirect(LS(4)), ["md", r("sl")], [r("one")], kind="g")
            mm(PX[:, 256:384], T.cw2[:], TB(2), ["circ1", r("one")], X, True, True, r("w2"))
            if FAST[c] == "f":
                mm(PZ[:, 256:384], T.cw3[:], TB(2), ["circ2", r("one")], Z, True, True, r("w3"))
                act(TF(5), PZ[:, 256:384], AF.Identity, [r("w3"), "thr"], [r("f5")], [Z], bias=col(10))

        def gather_w(n):
            lo, hi, how = 512 * n, 512 * n + 512, GW[c][n]
            d, m, out = blocks("df", lo, hi), sized(range(4 * n, 4 * n + 4)), mx[:, 4 * n:4 * n + 4, :]
            if how == "s":
                act(df[:, lo:hi], x.indirect(lu[:, 128 + lo // 16:128 + hi // 16]), AF.Copy, XR + [r("lw%d" % (n // 2))], d, kind="g")
                D, tag = spare[n % 2]
                mm(T[D][:], T.ni[:], xr[:, lo:hi], ["ni"] + blocks("xr", lo, hi), D, True, False, tag)
                mm(T[D][:], idn, df[:, lo:hi], ["idn"] + d, D, False, True, tag, False)
                act(out, T[D][:], AF.Abs, [tag], m, [D])
                return
            for a in range(lo, hi, FINE[c]):
                b = a + FINE[c]
                tt(df[:, a:b], x.indirect(lu[:, 128 + a // 16:128 + b // 16]), xr[:, a:b], OP.subtract,
                   XR + [r("lw%d" % (n // 2))] + blocks("xr", a, b), blocks("df", a, b), kind="g")
            if how == "a":
                act(out, df[:, lo:hi], AF.Abs, d, m)
            else:
                ts(out, df[:, lo:hi], 0.0, OP.max, d, m, kind="h")

        def sizes(n):
            lo, relu = 512 * n, GW[c][n] == "r"
            o = lambda k: PY[32 * (k // 4):32 * (k // 4) + 32, 128 + 32 * n:160 + 32 * n]
            by = lambda z, k: T.sj[:, 64 * z + 24 - 8 * (k % 4):64 * z + 56 - 8 * (k % 4)]
            mm(PY[:, 128 + 32 * n:160 + 32 * n], T.cth[:], tb[:, 256 + 32 * n:288 + 32 * n], ["circ0", r("one")], Y, True, False, GAPS[n])
            if relu:
                for k in range(16):
                    mm(o(k), by(2, k), df[:, lo + k:lo + 512:16], ["sj"] + blocks("df", lo, lo + 512), Y, False, False, GAPS[n], k > 0, 8)
            for k in range(16):
                mm(o(k), by(int(relu), k), mx[:, 4 * n:4 * n + 4, k:128:16], ["sj"] + sized(range(4 * n, 4 * n + 4)), Y, False, k % 4 == 3, GAPS[n], k > 0, 8)

        def halves():
            act(TB(3), xr[:].indirect(LS(5)), AF.Copy, XRS + [r("sl")], [r("q15")], kind="g")
            mm(PY[:, 0:128], idn, x0, ["idn", r("x0")], Y, True, False, r("nvp"))
            mm(PY[:, 0:128], idn, TB(3), ["idn", r("q15")], Y, False, True, r("nvp"))
            line(HALVES[c], T.nvi[:, CW * c:CW * c + CW], PY[:, 0:128], 0.5, -0.25, [r("nvp")], [r("nv")], [Y])

        def unpack():
            if PACK:
                by, o = [(4095, OP.bitwise_and), (12, OP.arith_shift_right)][c]
                ts(TI(2), T.pw1[:].indirect(LS(2)), by, o, ["pw_10", r("sl")], [r("t2")], kind="g")
                plus(UNPACK[c], HH(0), TI(2), -2048.0, [r("t2")], [r("q")])
            else:
                copy(UNPACK[c], HH(0), T["pw%d" % c][:].indirect(LS(2)), [r("pw") + "0", r("sl")], [r("q")], kind="g")

        def match():
            if MATCH[c] == "s":
                act(TB(4), PY[:, 128:256], AF.Relu, GAPS + ["thr2"], [r("dis")], [Y], scale=32768.0, bias=col(19))
                tt(TB(5), TB(4), PX[:, 256:384], OP.min, [r("dis"), r("w2")], [r("dw")], [X])
            else:
                ts(TB(4), PY[:, 128:256], col(10), OP.is_gt, GAPS + ["thr"], [r("dis")], [Y])
                tt(TB(5), TB(4), PX[:, 256:384], OP.mult, [r("dis"), r("w2")], [r("dw")], [X])
            mm(PY[:, 256:384], T.bj[:, 128:256], TB(5), ["bjt", r("dw")], Y, True, True, r("pre"))
            ts(TB(6), PY[:, 256:384], T.two[:, 47:48], OP.is_lt, [r("pre"), "two"], [r("P")], [Y])

        def aim(n):
            if n + 1 < len(AIM):
                a, b, uh = 2 * AIM[n], 2 * AIM[n + 1], T["uh%d" % c]
                o, far, tag = PX[:, a:b], r("far%d" % n), r("atp%d" % n)
                tt(tb[:, 1024 + 16 * a:1024 + 16 * b], PY[:, 128 + 16 * a:128 + 16 * b], tf[:, 640 + 16 * a:640 + 16 * b], OP.is_gt,
                   GAPS[AIM[n]:AIM[n + 1]] + [r("f5")], [far], [Y])
                mm(o, idn, T.base[:, 16 + a:16 + b], ["idn", "base2"], X, True, False, tag)
                mm(o, idn, ys[:, 16 * a:16 * b:16], ["idn", r("y")], X, False, False, tag)
                mm(o, T.n16[:], uh[:, 16 + a:16 + b], ["n16", r("uq")], X, False, False, tag)
                for m in range(16):
                    mm(o, T.bk[:, 15 - m:143 - m], tb[:, 1024 + 16 * a + m:1024 + 16 * b:16], ["bk", far], X, False, m == 15, tag, m > 0)
                cp(T["ls%d" % c][:, 64 + a:64 + b], o, [tag], [r("al%d" % n)], [X])

        def masks():
            both = [r("k1"), r("k2")]
            mm(PZ[:, 0:256], T.ones[0:2, 0:128], T.cr0[0:2, :], ["ones", "cr1", "cr2"], Z, True, False, both)
            mm(PZ[:, 0:128], T.an[:], HH(0), ["an", r("q")], Z, False, False, both)
            mm(PZ[:, 0:128], T.ann[:], HH(1), ["ann", r("ev")], Z, False, False, both)
            mm(PZ[:, 128:256], T.ni[:], HH(4), ["ni", r("tl")], Z, False, False, both)
            mm(PZ[:, 0:128], T.mo[:], TB(6), ["mo", r("P")], Z, False, False, both, False)
            mm(PZ[:, 128:256], T.mt[:], TB(6), ["mt", r("P")], Z, False, True, both)

        def write_x(n=0):
            if FAST[c] != "f":
                cp(T.xs[:, 0:4096].indirect(LO(2, 3)), T.nvi[:, CW * c:CW * c + CW], [r("nv"), made], XR[c:c + 1], kind="s")
            elif n + 1 < len(AIM):
                a, b = 2 * AIM[n], 2 * AIM[n + 1]
                cp(T.xs[:, 4096:XW].indirect(T["ls%d" % c][:, 64 + a:64 + b]), T.nvi[:, CW * c + 16 * a:CW * c + 16 * b], [r("nv"), r("al%d" % n)],
                   XR[c:c + 1], kind="s")

        def turned():
            if TURNED[c] != "f":
                copy(TURNED[c], TF(4), T["ww%d" % c][:].indirect(LO(1, 2)), WW + [made], [r("wr")], kind="g")

        def renew():
            if TURNED[c] == "f":
                act(TF(4), PZ[:, 0:128], AF.Copy, [r("k1")], [r("wr")], [Z])
                tt(TF(0), TF(4), PZ[:, 128:256], OP.min, [r("wr"), r("k2")], [r("n1")], [Z])
                tt(TF(2), T["ww%d" % c][:].indirect(LO(1, 2)), TF(0), OP.min, WW + [made, r("n1")], [r("n2")], kind="g")
            else:
                tt(TF(0), TF(4), PZ[:, 0:128], OP.min, [r("wr"), r("k1")], [r("n1")], [Z])
                tt(TF(2), TF(0), PZ[:, 128:256], OP.min, [r("n1"), r("k2")], [r("n2")], [Z])
            if last:
                act(T.ywf[:, CW * c:CW * c + CW], TF(2), AF.Abs, [r("n2")], [r("yw")])
                return
            act(T.wo[:, w0:w0 + CW], TF(2), AF.Abs, [r("n2")], [r("wo%d" % t)])
            send(T.wl[:, w0 + NC * CW:w0 + NC * CW + CW], T.wo[:, w0:w0 + CW], r("wo%d" % t), "ar%d_%d" % (t + 1, c), "wl%d_%d" % (t + 1, c), 550.0)

        def tally():
            mm(PY[:, 256:257], TB(6), T.g8[:, 0:1], [r("P"), "g8"], Y, True, True, r("pre"))
            act(T.cnt[:, c:c + 1], PY[:, 256:257], AF.Copy, [r("pre")], [r("cnt")], [Y])

        return {"start": start, "first": first, "wwin": wwin, "pwin": pwin, "weigh": weigh, "relator": relator, "spread": spread,
                "gather_r": gather_r, "letters": letters, "tail": tail, "other": other, "keys": keys, "least": least, "turn": turn,
                "gather_w": gather_w, "biggest": biggest, "apart": apart, "limit": limit, "aim": aim, "masks": masks,
                "sizes": sizes, "halves": halves, "unpack": unpack, "match": match, "write_x": write_x, "turned": turned,
                "renew": renew, "tally": tally, "lead": lead, "lists": lists}

    def allow():
        o = T.ps0[:, 48:49]
        mm(o, one, T.cnt[:, 0:1], ["ones", "cnt_0"], "ps0", True, False, "w0p_0")
        mm(o, one, T.cnt[:, 1:2], ["ones", "cnt_1"], "ps0", False, True, "w0p_0")
        cp(T.ai[:, 0:1], o, ["w0p_0"], ["ai"], ["ps0"])
        ts(T.aj[:, 0:1], T.ai[:, 0:1], 31, OP.bitwise_and, ["ai"], ["aj"])
        ts(col(10), T.aj[:, 0:1], 8.0, OP.mult, ["aj"], ["thr"], (), 2048.0, OP.add)
        if "s" in MATCH:
            ts(col(19), T.aj[:, 0:1], -8.0 * 32768, OP.mult, ["aj"], ["thr2"], (), -2048.0 * 32768, OP.add)

    def enter(name):
        label.extend([now[0]] * (len(nodes) - len(label)))
        now[0] = name

    parts = [{"a": stages(t, 0), "b": stages(t, 1)} for t in range(VIS)]
    for once in (constants_1, parts[0]["a"]["start"], parts[0]["b"]["start"], limits, rows, constants_2):
        once()
    for t in range(VIS + 1):
        for word in ORDER.split():
            at = t - 1 if word[0] == "-" else t
            chunk, _, name = word.lstrip("-").partition(".")
            name, _, piece = name.partition(":")
            enter((t, word))
            if not 0 <= at < VIS or (at == VIS - 1 and name in ("tally", "offer", "lead")):
                continue
            if chunk == "allow":
                if t > 0:
                    allow()
            elif piece:
                parts[at][chunk][name](int(piece))
            else:
                parts[at][chunk][name]()

    enter((VIS, "out"))
    dmas("sy", [lambda: SY.dma_start(T.yx[:, 0:2048], T.xs[:, 2048:4096])], "outx", XR[:1], [], 512)
    dmas("sy", [lambda: SY.dma_start(T.yx[:, 2048:4096], T.xs[:, 4096:6144])], "outx", XR[1:], [], 512)
    for c in range(NC):
        dmas("s", [(lambda a: lambda: S.dma_start(T.yw[:, a], T.ywf[:, a]))(slice(CW * c, CW * c + CW))], "outw", ["yw_%d" % c], [], 64)
    enter(None)
    if "order" not in PLAN:
        PLAN["len"], PLAN["order"] = tighten(nodes, moving, label, first_placing(nodes, moving))
    for i in PLAN["order"]:
        nodes[i][1]()
    for sem, val in total.items():
        g.wait_ge(T.sem[sem], val)
